import numpy as np, ml_dtypes
CORES = [2,3,42,43,82,83,122,123]
N = 8
BF = ml_dtypes.bfloat16
def gentries(a):
    return np.ascontiguousarray(a.reshape(8, 16, -1).transpose(0, 2, 1)).reshape(8, -1)
def gtable(e):
    e = np.asarray(e); return np.ascontiguousarray(e.reshape(8, -1, 16).transpose(0, 2, 1)).reshape(128, -1).astype(np.int32)
L, LB, HB, J, CAP, M, S, RO = 1024, 10, 13, 2048, 320, 128, 96, 3
H, W, T, TOP = N * L, 2 * L, 2 ** (20 - HB), 2 ** 20 - 1
def shelf(rng, n, full):
    a = np.arange(H).reshape(N, 1, 1, L); b = np.roll(a, 1, axis=0); m = n.reshape(1, 8, 1, 1)
    e = rng.integers(0, T >> 4, (N, 8, 16, W)) + (T >> 4) * np.arange(16).reshape(1, 1, 16, 1)
    k = np.concatenate([a + H * np.where(a < m, e[..., :L] & -2, e[..., :L]), b + H * (e[..., L:] | 1)], axis=3)
    k = np.take_along_axis(k, np.argsort(rng.random(k.shape), axis=2), 2)
    c = np.where(rng.random((N, 8, 1, W)) < full, 16, rng.integers(0, 17, (N, 8, 1, W)))
    k = np.where(np.argsort(rng.random(k.shape), axis=2) < c, k, -1)
    k[..., L:] = np.where(b < m, k[..., L:], -1)
    return k
def lack(rng, k, t, c, n):
    c = np.asarray(c); lo = c < L; a = np.where(lo, t * L + c, ((t - 1) % N) * L + c - L)
    e = rng.integers(0, T, c.shape); e = np.where(lo, np.where(a < n, e & -2, e), e | 1)
    x = a[:, None] + H * ((e[:, None] + 2 * np.arange(17)) % T)
    ok = ~np.any(x[:, :, None] == k[:, c].T[:, None, :], axis=2)
    return x[np.arange(c.size), np.argmax(ok, axis=1)]
def stored(rng, k, shape):
    s = k[k >= 0]
    return s[rng.integers(0, s.size, shape)] if s.size else rng.integers(0, 2 ** 20, shape)
def lanes(rng, k, n, w, miss):
    key = np.zeros((N, 8, J), np.int64)
    for g in range(8):
        u = np.add.accumulate(w[:, g], axis=1)
        t = np.minimum(np.sum(rng.random((N, J, 1)) * u[:, None, -1:] >= u[:, None, :], axis=2), N - 1)
        for d in range(N):
            at = t == d; z = int(np.sum(at)); v = stored(rng, k[d, g], z); m = rng.random(z) < miss[g]
            c = rng.integers(0, L, z); c = np.where((rng.random(z) < 0.5) & (((d - 1) % N) * L + c < n[g]), c + L, c)
            v[m] = lack(rng, k[d, g], d, c[m], n[g]); key[:, g][at] = v
    return key
def draws(rng, k, n, w, miss):
    return np.stack([lanes(rng, k, n, w, miss) for _ in range(RO)], axis=2)
def pays(rng, k, miss):
    p = rng.integers(0, 2 ** 20, k.shape)
    for g in range(8):
        p[:, g] = np.where(rng.random(p[:, g].shape) < miss[g], p[:, g], stored(rng, k[:, g], p[:, g].shape))
    return p
def images(rng, n):
    m = n.reshape(1, 8, 1); z = rng.integers(0, 4, (N, 8, J))
    return np.where(z == 0, 0, np.where(z == 1, m, np.minimum((rng.random((N, 8, J)) * (m + 1)).astype(np.int64), m)))
def pack(k, p, n, key, img, dr):
    return {"tk": np.ascontiguousarray(k.reshape(N, 128, W)).astype(np.int32), "tp": np.ascontiguousarray(p.reshape(N, 128, W)).astype(np.int32),
            "pn": np.tile(np.repeat(n, 16).reshape(1, 128, 1), (N, 1, 1)).astype(np.int32), "lk": np.stack([gtable(a) for a in key]),
            "li": np.stack([gtable(a) for a in img]), "dk": np.stack([gtable(a.reshape(8, -1)) for a in dr])}
def setup_inputs(rng):
    n = rng.permutation(8) * (H >> 3) + rng.integers(1, H >> 3, 8)
    miss = rng.permutation(np.array([0.01, 0.01, 0.02, 0.04, 0.1, 0.2, 0.3, 0.4])); full = rng.choice(np.array([0.2, 0.4, 0.6]), (1, 8, 1, 1))
    k = shelf(rng, n, full); w = np.exp2(rng.integers(-1, 2, (N, 8, N)))
    return pack(k, pays(rng, k, miss), n, lanes(rng, k, n, w, miss), images(rng, n), draws(rng, k, n, w, miss))
def setup_inputs_spread(rng):
    n = np.minimum((H * rng.random(8) ** 2).astype(np.int64), H); k = shelf(rng, n, 0.4); b = (N, 8, 1, W)
    wild = rng.integers(0, 2 ** 16, k.shape) + 65536 * ((np.arange(16).reshape(1, 1, 16, 1) + rng.integers(0, 16, b)) % 16)
    wild = np.where(rng.random(k.shape) < rng.random(b) * 1.3, wild, -1)
    k = np.where(rng.random(b) < 0.4, wild, k); miss = rng.choice(np.array([0.01, 0.05, 0.2]), 8); w = np.exp2(rng.integers(-3, 4, (N, 8, N)))
    p = np.where(rng.random(k.shape) < 0.4, np.minimum(np.exp2(20 * rng.random(k.shape)).astype(np.int64), TOP), pays(rng, k, miss))
    key = np.where(rng.random((N, 8, J)) < 0.2, np.minimum(np.exp2(20 * rng.random((N, 8, J))).astype(np.int64), TOP), lanes(rng, k, n, w, miss))
    return pack(k, p, n, key, images(rng, n), draws(rng, k, n, w, miss))
def setup_inputs_ends(rng):
    n = np.concatenate([rng.permutation(np.array([0, 0, H, H, H, H - 1, H >> 1])), np.array([0])])
    k = shelf(rng, n, 1.0); b = (N, 8, 1, W); x = np.arange(16)
    one = rng.integers(0, 32, b) == x.reshape(1, 1, 16, 1)
    k = np.where(rng.random(b) < 0.68, np.where(one, TOP, -1), k)
    for g in range(8):
        k[0, g, :, 0] = H * (x + 1); k[N - 1, g, :, L - 1] = TOP - H * (x + 1); k[0, g, :, W - 1] = TOP - 2 * H * (x + 1)
        if g % 2 == 1: k[0, g, 15, 0] = 0; k[N - 1, g, 15, L - 1] = TOP; k[0, g, 15, W - 1] = TOP
    q = rng.random(b); p = TOP * np.where(q < 0.3, 1, np.where(q > 0.8, 0, rng.integers(0, 2, k.shape)))
    p[..., W - 1] = TOP; p[..., 2] = TOP; p[..., 5] = 0
    p[N - 1, 1::2, 15, L - 1] = TOP; p[N - 1, 1::2, 0, L - 1] = 0
    w = np.ones((N, 8, N)); miss = np.full(8, 0.7)
    def mix(v):
        z = rng.random(v.shape); return np.where(z < 0.34, 0, np.where(z < 0.68, TOP, v))
    img = np.where(rng.random((N, 8, J)) < 0.5, 0, n.reshape(1, 8, 1))
    return pack(k, p, n, mix(lanes(rng, k, n, w, miss)), img, mix(draws(rng, k, n, w, miss)))
def setup_inputs_corners(rng):
    n = rng.permutation(np.array([0, 1, L - 1, L, H - S, H - 1, H, (N - 1) * L - (S >> 1)])); k = shelf(rng, n, 0.5)
    miss = np.full(8, 0.04); w = np.exp2(rng.integers(-1, 2, (N, 8, N))); p = pays(rng, k, miss)
    key = lanes(rng, k, n, w, miss); img = images(rng, n); dr = draws(rng, k, n, w, miss)
    kind = rng.permutation(np.array([0, 0, 0, 1, 1, 1, 2, 2])); nth = [0, 0, 0]
    for g in range(8):
        i = nth[kind[g]]; nth[kind[g]] += 1
        if kind[g] == 0:
            for q in range(N):
                t = (q + 1) % N; x = int(rng.choice(np.array([0, 1, CAP - 1, CAP, CAP + 1, J])))
                if q == 0: x = (CAP, CAP + 1, CAP - 1)[i]
                to = rng.permutation(np.concatenate([np.full(x, t), (t + 1 + rng.integers(0, N - 1, J - x)) % N])); c = rng.integers(0, L, J)
                v = k[to, g, rng.integers(0, 16, J), c]; v = np.where(v < 0, to * L + c + H * rng.integers(0, T, J), v)
                key[q, g] = v; img[q, g] = np.where(((v >> HB) & 1) == 1, 0, img[q, g])
        elif kind[g] == 1:
            img[:, g] = n[g]; to = np.stack([rng.permutation(np.arange(J) % N) for _ in range(N)]); tot = S + i - 1
            for t in range(N):
                qi, ji = np.nonzero(to == t); v = stored(rng, k[t, g], qi.size); x = (M - 1, M, M + 1)[(t + i) % 3]
                f = rng.permutation(np.flatnonzero(np.all(k[t, g, :, :L] >= 0, axis=0))); c = rng.permutation(np.flatnonzero(np.any(k[t, g, :, :L] < 0, axis=0)))[:x]
                y = tot // N + (tot % N if t == N - 1 else 0); c[rng.permutation(M - 1)[:y]] = f[:y]
                if x > M: c[M] = f[y]
                v[np.sort(rng.permutation(qi.size)[:x])] = lack(rng, k[t, g], t, c, n[g]); key[qi, g, ji] = v
        else:
            a = key[:, g] & (H - 1); z = rng.integers(0, 5, a.shape); m = n[g]
            img[:, g] = np.where(z == 0, 0, np.where(z == 1, m, np.where(z == 2, np.minimum(a, m), np.where(z == 3, np.minimum(a + 1, m), max(int(m) - 1, 0)))))
    return pack(k, p, n, key, img, dr)
def setup_inputs_crowd(rng):
    kd = rng.permutation(8); n = np.concatenate([rng.integers(1, H, 4), np.array([0, 0, H, H >> 1])])[kd]
    k = shelf(rng, n, np.where(kd >= 4, 1.0, 0.5).reshape(1, 8, 1, 1)); miss = np.full(8, 0.1); w = np.ones((N, 8, N)); p = pays(rng, k, miss)
    key = lanes(rng, k, n, w, miss); img = images(rng, n); dr = draws(rng, k, n, w, miss); x = np.arange(16)
    for g in range(8):
        q1, j1 = int(rng.integers(0, N)), int(rng.integers(0, J)); keep = key[q1, g, j1]
        if kd[g] < 4:
            t, c = int(rng.integers(0, N)), int(rng.integers(0, L))
            if kd[g] == 3: t, c = N - 1, L - 1
            a = t * L + c; k[t, g, :, c] = rng.permutation(a + 2 * H * x); other = a + 2 * H * rng.integers(16, T >> 1, (N, J))
            if kd[g] == 0: key[:, g] = k[t, g, 15, c]; p[t, g, 15, c] = k[t, g, 3, c]; p[t, g, 3, c] = other[0, 0]
            elif kd[g] == 2: key[:, g] = other; dr[:, g, 0] = other[:, ::-1]
            else: k[t, g, 15, c] = -1; key[:, g] = a + 32 * H; dr[:, g, 0] = other
            if kd[g] == 3: key[q1, g, j1] = keep
        elif kd[g] < 6:
            if kd[g] == 4:
                for c in (0, S - 1, RO * S - 1): k[0, g, :, c] = c + H * (2 * rng.permutation(16) + 1)
            for t in range(N):
                cols = RO * S + rng.permutation(L - RO * S); sp = cols[-RO:]; cols = cols[:-RO]
                if kd[g] == 5: k[t, g, rng.integers(0, 16, RO), sp] = -1
                for rnd in range(RO + 1):
                    c = np.roll(cols, 7 * rnd)[np.arange(J // N) % cols.size]
                    if kd[g] == 5 and rnd < RO: c[5] = sp[rnd]
                    for q in range(N):
                        v = lack(rng, k[t, g], t, c, 0)
                        if rnd == 0: key[q, g, t::N] = v
                        else: dr[q, g, rnd - 1, t::N] = v
        else:
            t = 0 if kd[g] == 6 else 1; cols = L + rng.integers(0, L, 3)
            if kd[g] == 6: cols[0] = W - 1
            v = np.concatenate([stored(rng, k[t, g][:, cols], 4), lack(rng, k[t, g], t, cols, n[g])])
            img[:, g] = 0; key[:, g] = v[rng.integers(0, v.size, (N, J))]; dr[:, g, 0] = v[rng.integers(0, v.size, (N, J))]
            if kd[g] == 6: k[N - 1, g, 0, cols[2] - L] = v[-1]
            if kd[g] == 7:
                low = rng.random((N, J)) < 0.5
                key[:, g] = np.where(low, stored(rng, k[t, g][:, :L], (N, J)), key[:, g])
                key[q1, g, J - 1] = keep; img[q1, g, J - 1] = n[g]
                j = int(np.flatnonzero(~low[N - 1])[CAP - 1]); z, y = int(k[t, g, 15, cols[0]]), int(k[t, g, 0, cols[0]])
                key[N - 1, g, j] = z; dr[N - 1, g, 0, j] = y; p[t, g, 15, cols[0]] = z; p[t, g, 0, cols[0]] = y
    return pack(k, p, n, key, img, dr)
def setup_inputs_calm(rng):
    v = rng.permutation(np.array([0, 1, 2, 3, 0, 1, 2, 3])); n = np.where(rng.random(8) < 0.5, L * rng.integers(1, N, 8) - 2, rng.integers(16, H - 32, 8))
    few = np.concatenate([np.flatnonzero(v == 0), np.flatnonzero(v == 1)[:1]]); n[few] = np.array([0, 3, 0]); n[np.flatnonzero(v == 3)[0]] = L * int(rng.integers(1, N)) - 2
    k = shelf(rng, n, 0.5)
    for g in few:
        for x in range(3):
            if x < n[g]: k[1, g, :, L + x] = x + H * (2 * rng.permutation(16) + 1)
            else: k[0, g, :, x] = x + H * rng.permutation(16)
    none = np.zeros(8); w = np.ones((N, 8, N)); p = pays(rng, k, none); key = lanes(rng, k, n, w, none); dr = draws(rng, k, n, w, none)
    img = np.where(rng.random((N, 8, J)) < 0.5, np.maximum(n.reshape(1, 8, 1) - rng.integers(0, 4, (N, 8, J)), 0), images(rng, n))
    for g in range(8):
        s = k[:, g][k[:, g] >= 0]; s = s[np.abs((s & (H - 1)) - n[g] - 3) < 9]
        if s.size:
            for a in (p, key): a[:, g] = np.where(rng.random(a[:, g].shape) < 0.15, s[rng.integers(0, s.size, a[:, g].shape)], a[:, g])
        for i in range(int(v[g])):
            t = (i + 1) % N; f = np.flatnonzero(np.all(k[t, g, :, :L] >= 0, axis=0)); f = rng.permutation(f[np.abs(t * L + f - n[g] - 4) > 12])[:RO + 1]
            u = lack(rng, k[t, g], t, f, n[g]); key[i, g, 0] = u[0]; dr[i, g, :, 0] = u[1:]
    for g in few:
        for x in range(3):
            key[:, g, 2 + x] = x + H; p[:, g] = np.where(k[:, g] == x + H, x + H, p[:, g])
    return pack(k, p, n, key, img, dr)
def check_inputs(d):
    bad = []
    for a, lo, hi in (("tk", -1, TOP), ("tp", 0, TOP), ("pn", 0, H), ("lk", 0, TOP), ("li", 0, H), ("dk", 0, TOP)):
        if np.min(d[a]) < lo or np.max(d[a]) > hi: bad.append("range of " + a)
    s = np.sort(d["tk"].reshape(N, 8, 16, W), axis=2)
    if np.any((s[:, :, 1:] == s[:, :, :-1]) & (s[:, :, 1:] >= 0)): bad.append("tk: keys of one bucket differ")
    m = d["pn"].reshape(N, 8, 16)
    if np.any(m != m[:1, :, :1]): bad.append("pn: alike in a group and on all ranks")
    if np.any(d["li"].reshape(N, 8, -1) > m[:, :, :1]): bad.append("li: at most the pointer")
    return bad
def reference(tk, tp, pn, lk, li, dk):
    k = tk.astype(np.int64).reshape(N, 8, 16, W); p = tp.astype(np.int64).reshape(N, 8, 16, W); n = pn[0].astype(np.int64).reshape(8, 16)[:, 0]
    key = np.stack([gentries(a) for a in lk]).astype(np.int64); img = np.stack([gentries(a) for a in li]).astype(np.int64)
    dr = np.stack([gentries(a) for a in dk]).astype(np.int64).reshape(N, 8, RO, J)
    src = np.arange(N).reshape(N, 1, 1); grp = np.arange(8).reshape(1, 8, 1)
    for rnd in range(RO):
        home = key & (H - 1); bit = ((key >> HB) & 1) == 1
        old = bit & (home < img); new = bit & (home < n.reshape(1, 8, 1)); fwd = new & ~old
        to = ((home >> LB) + old) % N
        own = ((home >> LB) + new) % N; col = (home & (L - 1)) + L * new
        place = np.zeros_like(key)
        for d in range(N):
            m = (to == d).astype(np.int64); place = place + m * (np.add.accumulate(m, axis=2) - m)
        go = place < CAP
        eq = k[own, grp, :, col] == key[..., None]; hit = np.any(eq, axis=3)
        val = np.sum(np.where(eq, p[own, grp, :, col], 0), axis=3)
        order = fwd * (N * CAP) + src * CAP + place; miss = go & ~hit; over = np.zeros(8, np.int64)
        for t in range(N):
            for g in range(8):
                m = miss[:, g] & (own[:, g] == t)
                o = np.argsort(order[:, g][m])[:M]; ks = key[:, g][m][o]
                c, first = np.unique(col[:, g][m][o], return_index=True); ks = ks[first]
                e = k[t, g][:, c] == -1; room = np.any(e, axis=0); s = np.argmax(e, axis=0)
                over[g] += np.sum(~room)
                s, c, ks = s[room], c[room], ks[room]
                k[t, g, s, c] = ks; p[t, g, s, c] = (ks & 1023) * 1024 + (ks >> 10)
        key = np.where(go, np.where(hit, val, dr[:, :, rnd]), key); img = np.where(go & fwd, home + 1, img)
        nn = np.minimum(n + np.minimum(over, S), H)
        for g in range(8):
            x = np.arange(n[g], nn[g]); t = x >> LB; c = x & (L - 1); t2 = (t + 1) % N
            kl = k[t, g, :, c]; pl = p[t, g, :, c]; mv = (kl >= 0) & (((kl >> HB) & 1) == 1)
            k[t2, g, :, L + c] = np.where(mv, kl, -1); p[t2, g, :, L + c] = np.where(mv, pl, 0)
            k[t, g, :, c] = np.where(mv, -1, kl); p[t, g, :, c] = np.where(mv, 0, pl)
        n = nn
    return {"yk": k.reshape(N, 128, W).astype(np.float32), "ys": np.sum(p, axis=2).astype(np.float32), "yn": np.tile(np.repeat(n, 16).reshape(1, 128, 1), (N, 1, 1)).astype(np.float32),
            "yl": np.stack([gtable(a) for a in key]).astype(np.float32), "yi": np.stack([gtable(a) for a in img]).astype(np.float32)}

@@ -1,0 +1,875 @@
+from concourse.bass import DstId, RemoteDMATransfer
+from concourse.mybir import AluOpType as A, AxisListType, ActivationFunctionType as F
+
+N, RO, CAP, WIN = 8, 3, 320, 288
+S1, S2, S3, S4, S5, DUMP, TW = 1024, 2048, 3072, 3360, 3648, 3936, 4192
+BIG, P20, P21 = 8192.0, 1048576.0, 2097152.0
+SWW = 6464
+WV = True
+HB_ = (0, 1, 4, 5)
+OWN, LOW, NXT, PRV = 8192.0, 16096.0, 16672.0, 12144.0
+U1, U2, U3, U4, U5 = 5000.0, 3000.0, 5000.0, 3000.0, 5000.0
+SLACK, PASSES, NPK = 100.0, 6, 4
+FIX, WAKE, PE = 40.0, 80.0, 0.6
+SCRATCH = {
+    "lki": ("sbuf", [128, 128], "int32"), "lii": ("sbuf", [128, 128], "int32"), "dki": ("sbuf", [128, 384], "int32"),
+    "pni": ("sbuf", [128, 1], "int32"), "KR": ("sbuf", [128, 3072], "int32"), "PT": ("sbuf", [128, TW], "int32"),
+    "TG": ("sbuf", [128, TW], "float32"), "XT": ("sbuf", [128, TW], "float32"),
+    "SW": ("sbuf", [128, SWW], "bfloat16"), "W": ("sbuf", [128, 2576], "bfloat16"),
+    "Z": ("sbuf", [128, 16, 132], "bfloat16"), "BC": ("sbuf", [128, 16, 128], "bfloat16"),
+    "SQ": ("sbuf", [128, 24, 24], "int32"), "RQ": ("sbuf", [128, 24, 24], "int32"),
+    "SR": ("sbuf", [128, 192, 16], "bfloat16"), "RR": ("sbuf", [128, 3072], "bfloat16"),
+    "SF": ("sbuf", [128, 3, 160], "float32"), "CAT": ("sbuf", [128, 3, 336], "float32"),
+    "UP": ("sbuf", [128, 3, 288], "float32"), "UA": ("sbuf", [128, 3, 288], "float32"), "UB": ("sbuf", [128, 3, 288], "float32"),
+    "WT": ("sbuf", [128, WIN], "float32"), "WQ": ("sbuf", [128, WIN], "int32"),
+    "SO": ("sbuf", [128, 4], "float32"), "RV": ("sbuf", [128, 8, 4], "float32"), "HB": ("sbuf", [128, 512], "int32"),
+    "OY": ("sbuf", [128, 260], "float32"),
+    "TF": ("sbuf", [128, 16000], "float32"), "TI": ("sbuf", [128, 2816], "int32"), "TB": ("sbuf", [128, 16000], "bfloat16"),
+    "TU": ("sbuf", [128, 1024], "uint16"),
+}
+for _b in range(8):
+    SCRATCH["B%d" % _b] = ("psum", [128, 512], "float32")
+SEMAPHORES = (["qv", "qs", "qp", "qg", "aK", "aP", "aW", "aO", "aH"] + ["a%s%d" % (k, r) for k in "QRFAB" for r in range(RO)]
+              + ["d%d" % i for i in range(16)] + ["l%d" % i for i in range(32)])
+
+
+def bits(engs):
+    return sum(1 << e for e in engs)
+
+
+def all_to_all_calls(src, cores, topo):
+    far = [c for c in cores if topo.chip(c) != topo.chip(src)]
+    near = [c for c in cores if c != src and topo.chip(c) == topo.chip(src)]
+    k = cores.index(src)
+    far = far[k % len(far):] + far[:k % len(far)]
+    out_e = topo.engines(src, far[0])
+    in_e = [e for e in topo.engines(src, near[0]) if e not in out_e]
+    first, rest = far[:4], far[4:]
+    w1, w2 = len(out_e) // len(first), len(out_e) // len(rest)
+    c1 = [(d, out_e[i * w1:(i + 1) * w1]) for i, d in enumerate(first)] + [(near[0], in_e)]
+    c2 = [(d, out_e[i * w2:(i + 1) * w2]) for i, d in enumerate(rest)]
+    return [c1, c2]
+
+
+def a2a_count(dst, cores, topo):
+    return sum(len(e) for s in cores if s != dst for call in all_to_all_calls(s, cores, topo) for d, e in call if d == dst)
+
+
+def relays(src, dst, cores, topo):
+    if topo.chip(src) == topo.chip(dst):
+        return []
+    return [h for h in topo.cores_of(src) if h not in cores and topo.die(h) != topo.die(src) and topo.may_write(h, dst)][:2]
+
+
+def halves(src, dst, topo):
+    e = topo.engines(src, dst)
+    return e[:len(e) // 2], e[len(e) // 2:]
+
+
+def side_engines(src, dst, topo, cores):
+    far = [c for c in cores if topo.chip(c) != topo.chip(src)][0]
+    if topo.chip(src) != topo.chip(dst):
+        return topo.engines(src, dst)
+    return [e for e in topo.engines(src, dst) if e not in topo.engines(src, far)]
+
+
+def dst_id(c, topo):
+    rid, pid, _ = topo.addr(c)
+    return DstId(rid=rid, pnc=pid)
+
+
+def relay_program(g, core, T, topo):
+    cores = list(T.cores)
+    for t in range(N):
+        src, dst = cores[t], cores[(t - 1) % N]
+        hs = relays(src, dst, cores, topo)
+        if core in hs:
+            i = hs.index(core)
+            g.wait_ge(T.sem.aH, len(side_engines(src, core, topo, cores)) // 2)
+            rid, pid, _ = topo.addr(dst)
+            g.remote_dma(T.PT[:, S1 + 512 * i:S1 + 512 * (i + 1)], T.HB[:], T.sem.aP, T.sem.l0, pid, rid, topo.mask(core, dst))
+            g.wait_ge(T.sem.l0, len(topo.engines(core, dst)))
+
+
+def rank_program(g, core, T, topo):
+    t = T.rank_of(core)
+    if t is None:
+        relay_program(g, core, T, topo)
+        return
+    cores = list(T.cores)
+    prv, nxt = cores[(t - 1) % N], cores[(t + 1) % N]
+    ENG = {"v": g.vector, "s": g.scalar, "p": g.tensor, "g": g, "y": g.sync}
+    ops, wr, rd, bank, slots = [], {}, {}, {}, {}
+    cnt = {"d": 0, "l": 0, "TF": 0, "TI": 0, "TB": 0, "TU": 0}
+    lastg, boost = [], [0.0]
+
+    def urgent(v, fn, *a):
+        boost[0] = v
+        r = fn(*a)
+        boost[0] = 0.0
+        return r
+
+    def size(x):
+        n = 1
+        for k in x[0].shape[1:]:
+            n *= k
+        return n
+
+    def cost(out, ins, two=False):
+        tk = [k for x in ins for k in x[1]]
+        k = 1.56 if "~" in tk else 2.0 if two and not any(z[0] == "@" for z in tk) else 1.0
+        return FIX + max(64.0, size(out) * k) * 1.04
+
+    def rec(q, fn, R, W, ev=None, cont=False, c=100.0, after=()):
+        me = len(ops)
+        deps = set()
+        for k in set(R + W):
+            if k[0] == "@":
+                b = bank.setdefault(k, [q, [], []])
+                if b[0] != q:
+                    b[0], b[1], b[2] = q, [], b[1]
+                b[1].append(me)
+                deps.update(b[2])
+        R = [k for k in R if k[0] not in "@~"]
+        W = [k for k in W if k[0] != "@"]
+        for k in R:
+            deps.update(wr.get(k, []))
+        for k in W:
+            deps.update(rd.get(k, []))
+            deps.update(o for o in wr.get(k, []) if not (cont and ops[o]["q"] == q))
+        for k in R:
+            rd.setdefault(k, []).append(me)
+        for k in W:
+            wr[k] = (wr.get(k, []) if cont else []) + [me]
+            if not cont:
+                rd[k] = []
+        deps.discard(me)
+        soft = set(after)
+        if q == "g":
+            soft.update(lastg[-1:])
+            lastg.append(me)
+        ops.append({"q": q, "fn": fn, "deps": deps, "ev": ev, "c": c, "up": boost[0], "soft": soft, "lab": (W + ["-"])[0]})
+
+    def o(ap, *tok):
+        return (ap, list(tok))
+
+    def tmp(buf, name, n):
+        if name not in slots:
+            slots[name] = (buf, cnt[buf])
+            cnt[buf] += (n + 15) // 16 * 16
+            assert cnt[buf] <= SCRATCH[buf][1][1]
+        assert slots[name][0] == buf
+        a = slots[name][1]
+        return o(T[buf][:, a:a + n], name)
+
+    def sub(name, a, b, s=1, tok=None):
+        buf, z = slots[name]
+        tk = [name] if tok is None else tok
+        return o(T[buf][:, z + a:z + b:s] if s != 1 else T[buf][:, z + a:z + b], *tk)
+
+    def f(name, n=128):
+        return tmp("TF", name, n)
+
+    def i_(name, n=128):
+        return tmp("TI", name, n)
+
+    def h(name, n=128):
+        return tmp("TB", name, n)
+
+    def u(name, n=128):
+        return tmp("TU", name, n)
+
+    def ps(b, a, e, s=1):
+        ap = T["B%d" % b][:, a:e:s] if s != 1 else T["B%d" % b][:, a:e]
+        return o(ap, "@%d" % b, *["B%d_%d" % (b, k) for k in range(a // 128, (e + 127) // 128)])
+
+    def ind(w, off):
+        return (w[0].indirect(off[0]), w[1] + off[1] + ["~"])
+
+    def sv(x):
+        return x[0] if isinstance(x, tuple) else x
+
+    def st(*xs):
+        return [k for x in xs if isinstance(x, tuple) for k in x[1]]
+
+    def ts(out, a, s1, op0, s2=None, op1=None, c=None):
+        if op1 is None:
+            rec("v", lambda e: e.tensor_scalar(out[0], a[0], sv(s1), None, op0), st(a, s1), out[1], c=c or cost(out, [a]))
+        else:
+            rec("v", lambda e: e.tensor_scalar(out[0], a[0], sv(s1), sv(s2), op0, op1), st(a, s1, s2), out[1], c=cost(out, [a]))
+        return out
+
+    def tt(out, a, b, op):
+        rec("v", lambda e: e.tensor_tensor(out[0], a[0], b[0], op), st(a, b), out[1], c=cost(out, [a, b], True))
+        return out
+
+    def cp(out, a):
+        rec("v", lambda e: e.tensor_copy(out[0], a[0]), st(a), out[1], c=cost(out, [a]))
+        return out
+
+    def scat(w, off, a):
+        rec("v", lambda e: e.tensor_copy(w[0].indirect(off[0]), a[0]), st(a, off), w[1], c=FIX + 3.95 * size(a))
+
+    def ms(out, c):
+        rec("v", lambda e: e.memset(out[0], c), [], out[1], c=cost(out, []))
+        return out
+
+    def scan(out, d0, d1, op0, op1, c=None):
+        rec("v", lambda e: e.tensor_tensor_scan(out[0], d0[0], d1[0], 0.0, op0, op1), st(d0, d1), out[1], c=c or cost(out, []))
+        return out
+
+    def red(out, a):
+        rec("v", lambda e: e.tensor_reduce(out[0], a[0], AxisListType.X, A.add), st(a), out[1])
+        return out
+
+    def act(out, a, func=F.Identity, bias=0.0, scale=1.0, acc=None):
+        if acc is None:
+            rec("s", lambda e: e.activation(out[0], a[0], func, bias=sv(bias), scale=sv(scale)), st(a, bias, scale), out[1], c=cost(out, [a]))
+        else:
+            rec("s", lambda e: e.activation(out[0], a[0], func, bias=sv(bias), scale=sv(scale), accum_out=acc[0]), st(a, bias, scale), out[1] + acc[1], c=cost(out, [a]))
+        return out
+
+    def mm(items, cont=False, c=None):
+        def fn(e):
+            ins = None
+            for x in items:
+                ins = e.matmul(x[0][0], x[1][0], x[2][0], x[3], x[4])
+            return ins
+        R, W = [], []
+        for x in items:
+            R += st(x[1], x[2])
+            W += x[0][1]
+        rec("p", fn, sorted(set(R)), sorted(set(W)), cont=cont, c=100.0 + PE * (c or sum(max(64, size(x[0])) for x in items)))
+
+    def iota(out, pat, base, cm, fl=True):
+        if fl:
+            rec("g", lambda e: e.iota(out[0], pat, base, cm, allow_small_or_imprecise_dtypes=True), [], out[1], c=130 + 2.1 * size(out))
+        else:
+            rec("g", lambda e: e.iota(out[0], pat, base, cm), [], out[1])
+        return out
+
+    def dma(q, out, a):
+        s = "d%d" % cnt["d"]
+        cnt["d"] += 1
+        rec(q, lambda e: e.dma_start(sv(out), sv(a)).then_inc(T.sem[s], 16), st(a), st(out), ev=(s, 16), c=2500.0 + 2.0 * (size((sv(out),))))
+
+    def send(trs):
+        s = "l%d" % cnt["l"]
+        cnt["l"] += 1
+        rec("g", lambda e: e.remote_dma_fused([RemoteDMATransfer(dst_ids=[dst_id(d, topo)], dma_engine_mask=bits(en), remote_sem=T.sem[sm], src=a[0], dst=da)
+                                              for d, da, a, sm, en in trs], local_sem=T.sem[s]),
+            st(*[x[2] for x in trs]), [], ev=(s, sum(len(x[4]) for x in trs)), c=600.0)
+
+    def arrive(sem, n, toks, c=2800.0):
+        rec("x", None, [], toks, ev=(sem, n), c=c, after=lastg[-1:])
+
+    def a2a(src_of, dst_ap, sem):
+        for call in all_to_all_calls(core, cores, topo):
+            send([(d, dst_ap, src_of(cores.index(d)), sem, en) for d, en in call])
+
+    TGa = o(T.TG[:, 0:TW], "TG0", "TG1", "TG2", "TG3", "TG4", "TG5", "TG6")
+    PTa = o(T.PT[:, 0:TW], "PT0", "PT1", "PT2", "PT3", "PT4", "PT5", "PT6")
+    XTa = o(T.XT[:, 0:TW], "XT0", "XT1", "XT2", "XT3", "XT6")
+    SWa = o(T.SW[:, 0:SWW], "SW")
+    AND, SHR, SAR = A.bitwise_and, A.logical_shift_right, A.arith_shift_right
+    ADD, SUB, MUL, MAX, MIN = A.add, A.subtract, A.mult, A.max, A.min
+    EQ, GE, GT, LT = A.is_equal, A.is_ge, A.is_gt, A.is_lt
+
+    dma("y", o(T.lki[:], "lki"), T.lk[:])
+    dma("y", o(T.lii[:], "lii"), T.li[:])
+    dma("y", o(T.pni[:], "pni"), T.pn[:])
+    dma("y", o(T.KR[:, S2:S3], "KR2"), T.tk[:, 1024:2048])
+    dma("y", o(T.PT[:, S2:S3], "PT2"), T.tp[:, 1024:2048])
+    dma("y", o(T.KR[:, 0:S1], "KR0"), T.tk[:, 0:1024])
+    dma("y", o(T.PT[:, 0:S1], "PT0"), T.tp[:, 0:1024])
+    dma("y", o(T.dki[:], "dki"), T.dk[:])
+    pidx = iota(i_("pidx", 1), [[1, 1]], 0, 1, False)
+    IO = f("IO", 1024)
+    iota(sub("IO", 0, 320, tok=["IOa"]), [[1, 320]], 0, 0)
+    gi16 = iota(f("gi16"), [[1, 8], [0, 16]], 0, 0)
+    DJ = iota(f("DJ"), [[16, 128]], int(BIG) + 4288, 1)
+    ri16 = iota(f("ri16"), [[0, 8], [1, 16]], 0, 0)
+    DC = iota(h("DC", 512), [[0, 64], [CAP, 8]], 0, 0)
+    iota(sub("IO", 320, 1024, tok=["IOb"]), [[1, 704]], 320, 0)
+    IO = o(IO[0], "IOa", "IOb")
+
+    def io(a, b):
+        return sub("IO", a, b, tok=["IOa"])
+    ms(o(T.SW[:, 0:2560], "SW"), 0.0)
+    boost[0] = U3
+    pr = cp(f("pr", 1), ts(i_("pri", 1), pidx, 15, AND))
+    pg = cp(f("pg", 1), ts(i_("pgi", 1), pidx, 4, SHR))
+    pf = cp(f("pf", 1), pidx)
+    ts(f("M16", 16), io(0, 16), pr, EQ)
+    Y = ts(h("Y", 144), io(0, 144), ts(f("y15", 1), pg, 16.0, MUL, 15.0, ADD), EQ)
+    for r in range(16):
+        act(o(T.Z[:, r, 0:130], "Z%d" % r), sub("Y", 13, 143), F.Copy, scale=sub("M16", r, r + 1))
+    boost[0] = 0.0
+
+    def sumto(r):
+        return sub("Y", 15 - r, 143 - r)
+    BLK = ts(h("BLK"), gi16, pg, EQ)
+    D = ts(f("D"), io(0, 128), pf, SUB)
+    ID = ts(h("ID"), D, 0.0, EQ)
+    LS = tt(h("LS"), ts(h("lsa"), D, 0.0, GT), BLK, MUL)
+    LB = tt(h("LB"), ts(h("lba"), D, 0.0, EQ, BIG, MUL), LS, ADD)
+    f("MK", 4)
+    for r in range(RO):
+        ts(sub("MK", r, r + 1, tok=["MK%d" % r]), pr, 3.0, EQ, 524288.0 * (r + 1), MUL)
+    RS8 = ms(h("RS8", 512), 1.0)
+    ms(sub("RS8", 0, 512, 8), 0.0)
+    h("R", 1032)
+    ms(sub("R", 0, 8, tok=["R0"]), 0.0)
+    ms(o(T.SQ[:], "SQ0", "SQ1", "SQ2", "SQo0", "SQo1", "SQo2"), 0)
+    n0 = cp(f("n0", 1), o(T.pni[:], "pni"))
+    n288 = ts(f("n288", 1), n0, float(WIN), ADD)
+    cn = ts(f("cn", 1), n0, -1.0, MUL, float(S3), ADD)
+    img = cp(f("img"), o(T.lii[:], "lii"))
+    NN = [n0] + [f("n%d" % (r + 1), 1) for r in range(RO)]
+    C = {}
+
+    def late_consts():
+        C["BLKF"] = act(f("BLKF"), BLK, F.Copy)
+        C["LI"] = tt(h("LI"), LS, ID, ADD)
+        C["GIF"] = ts(f("GIF", 8), io(0, 8), pg, EQ)
+        C["GIB"] = ts(h("GIB", 8), io(0, 8), pg, EQ, P20, MUL)
+        C["HM"] = ts(f("HM", 4), io(0, 4), cp(f("p4", 1), ts(i_("p4i", 1), pidx, 2, SHR, 3, AND)), EQ)
+        C["kA"] = ts(f("kA", 18), io(0, 18), 16.0, MUL, pr, ADD)
+        C["KB"] = act(f("KB", 8), sub("kA", 0, 8), bias=-0.5, scale=-1.0)
+        C["DG"] = ts(h("DG"), ri16, pr, EQ, P21, MUL)
+        C["RS16"] = act(f("RS16"), ri16, F.Sign)
+        C["C128"] = act(h("C128", 320), io(0, 320), bias=128.0, scale=0.0)
+        C["ONE"] = ms(f("ONE", 8), 1.0)
+        C["DM"] = f("DM", 32)
+        for k, v in enumerate((DUMP - OWN, DUMP + 128 - LOW, DUMP - NXT, DUMP - PRV)):
+            act(sub("DM", 8 * k, 8 * k + 8), sub("kA", 0, 8), bias=float(v))
+        h("R2", 336)
+        ms(sub("R2", 0, 1, tok=["R2z"]), 0.0)
+        f("cumM", 336)
+        ms(sub("cumM", 320, 336, tok=["cumz"]), 0.0)
+        ms(o(T.CAT[:, :, 320:336], "CATz"), 0.0)
+        h("EQ", 2624)
+        f("PR", 2624)
+        ms(sub("EQ", 2560, 2624, tok=["EQ5"]), 0.0)
+        ms(sub("PR", 2560, 2624, tok=["PR5"]), 0.0)
+        ms(o(T.W[:, 2560:2576], "Wz"), 0.0)
+        C["IDF"] = act(f("IDF"), ID, F.Copy)
+        C["ID2F"] = act(f("ID2F"), ID, F.Copy, scale=2.0)
+        for nm, v in (("I512", 512.0), ("I144", 144.0), ("I2n", -2.0), ("I4096", 4096.0), ("I4608", 4608.0), ("I8192n", -8192.0)):
+            C[nm] = act(h(nm), ID, F.Copy, scale=v)
+        act(h("Y2", 144), Y, F.Copy, scale=2.0)
+        C["LSI"] = tt(h("LSI"), LS, ID, SUB)
+        C["DG14"] = act(h("DG14"), C["DG"], F.Copy, scale=1.0 / 128)
+        C["KF"] = act(h("KF"), io(0, 128), F.Copy, scale=1.0 / 128)
+        C["kF"] = act(f("kF", 8), sub("kA", 0, 8), F.Copy, scale=1.0 / 128)
+        f("dk2", 384)
+        ts(sub("dk2", 0, 384), o(T.dki[:], "dki"), P20, ADD)
+        ms(o(T.SR[:, :, 3:12:4], "SRz"), 0.0)
+        ms(o(T.SR[:, :, 12:16], "SRy"), 0.0)
+        act(o(T.TG[:, DUMP:TW], "TG6"), io(0, 256), F.Copy, scale=0.0)
+        act(o(T.TG[:, S5:DUMP], "TG5"), io(0, WIN), F.Copy, scale=0.0)
+        ms(o(T.PT[:, S5:TW], "PT5", "PT6"), 0)
+        act(o(T.XT[:, DUMP:TW], "XT6"), io(0, 256), F.Copy, scale=0.0)
+        ms(o(T.SO[:], "SO"), 0.0)
+
+    KH, PH = o(T.KR[:, S2:S3], "KR2"), o(T.PT[:, S2:S3], "PT2")
+    hs = relays(core, prv, cores, topo)
+    if hs:
+        send([(prv, T.KR[:, S1:S2], KH, "aK", topo.engines(core, prv))])
+        en = side_engines(core, hs[0], topo, cores)
+        send([(x, T.HB[:], o(T.PT[:, S2 + 512 * k:S2 + 512 * (k + 1)], "PT2"), "aH", en[k * len(en) // 2:(k + 1) * len(en) // 2]) for k, x in enumerate(hs)])
+    else:
+        ea, eb = halves(core, prv, topo)
+        send([(prv, T.KR[:, S1:S2], KH, "aK", ea), (prv, T.PT[:, S1:S2], PH, "aP", eb)])
+    hn = relays(nxt, core, cores, topo)
+    arrive("aK", len(topo.engines(nxt, core)) if hn else len(halves(nxt, core, topo)[0]), ["KR1"], 9000.0)
+    arrive("aP", sum(len(topo.engines(x, core)) for x in hn) if hn else len(halves(nxt, core, topo)[1]), ["PT1"], 12000.0)
+    na = a2a_count(core, cores, topo)
+    L = {}
+
+    def address(KI):
+        x = ts(i_("x"), KI, 8191, AND)
+        bit = ts(i_("bit"), KI, 13, SHR, 1, AND)
+        lt = tt(ps(7, 0, 128), x, img, LT)
+        rk = ts(i_("rk"), KI, 10, SHR, 7, AND)
+        old = tt(ps(7, 128, 256), lt, bit, MUL)
+        boost[0] = U4
+        la = ts(ps(7, 256, 384), x, n288, LT, 288.0, MUL)
+        lb = ts(f("lb"), x, n0, LT, 736.0, MUL)
+        bo = tt(f("bo"), old, bit, ADD)
+        w = tt(ps(7, 384, 512), la, lb, ADD)
+        zz = ts(f("zz"), rk, 1024.0, MUL, cn, ADD)
+        c10 = ts(i_("c10"), KI, 1023, AND)
+        q = ts(ps(7, 0, 128), w, 288.0, EQ)
+        t2 = tt(ps(7, 256, 384), w, bo, MUL)
+        qz = tt(f("qz"), q, zz, MUL)
+        c1 = tt(ps(7, 384, 512), t2, c10, ADD)
+        tg = ts(i_("tg"), KI, 0xFE000, AND)
+        col = tt(ps(7, 0, 128), c1, qz, ADD)
+        p2 = ts(h("p2"), tg, 0.5, MUL)
+        p1 = cp(h("p1"), col)
+        p0 = tt(h("p0"), col, p1, SUB)
+        boost[0] = 0.0
+        to = ts(i_("to"), tt(i_("s"), old, rk, ADD), 7, AND)
+        L.update(x=x, bit=bit, to=to, pc=(p0, p1, p2))
+
+    def spread(rho):
+        h("SRC", 2048)
+        for b in range(4):
+            mm([(ps(b % 2, 128 * (r % 4), 128 * (r % 4) + 128), o(T.Z[:, r, 2 - k:130 - k], "Z%d" % r), L["pc"][k], k == 0, k == 2) for r in range(4 * b, 4 * b + 4) for k in range(3)])
+            for r in range(4 * b, 4 * b + 4):
+                act(sub("SRC", r, 2048, 16, tok=["SRC%d" % r]), ps(b % 2, 128 * (r % 4), 128 * (r % 4) + 128), bias=sub("MK", rho, rho + 1, tok=["MK%d" % rho]))
+
+    def place():
+        h("OH", 1024)
+        for d in range(8):
+            ts(sub("OH", d, 1024, 8, tok=["OH%d" % d]), L["to"], float(d), EQ)
+        for d in range(8):
+            x = sub("OH", d, 1024, 8, tok=["OH%d" % d])
+            scan(sub("R", 8 + d, 1032, 8, tok=["R%d" % (d + 1)]), x, x, ADD, MAX, c=110.0)
+        thr = ts(f("thr"), L["to"], float(CAP), MUL, BIG + CAP, ADD)
+        oh, rr = ["OH%d" % d for d in range(8)], ["R%d" % d for d in range(9)]
+        for b in range(2):
+            out = ps(4 + b, 0, 512)
+            mm([(out, ID, DC, True, False), (out, LB, sub("OH", 512 * b, 512 * b + 512, tok=oh), False, False),
+                (out, BLK, sub("R", 512 * b, 512 * b + 512, tok=rr), False, True)])
+        f("MS", 1024)
+        for b in range(2):
+            scan(sub("MS", 512 * b, 512 * b + 512, tok=["MS%d" % b]), RS8, ps(4 + b, 0, 512), MUL, MAX)
+        val = sub("MS", 7, 1024, 8, tok=["MS0", "MS1"])
+        ng = L["ng"] = tt(f("ng"), val, thr, GE)
+        mx = tt(f("mx"), tt(ps(7, 128, 256), ng, DJ, MUL), val, MAX)
+        ts(u("off"), mx, -BIG, ADD)
+        ts(u("off2"), mx, -BIG, ADD, 2560.0, MIN)
+
+    def pack():
+        w = 128 // NPK
+        for j in range(NPK):
+            scat(SWa, sub("off", w * j, w * j + w), sub("SRC", 16 * w * j, 16 * w * (j + 1), tok=["SRC%d" % r for r in range(16)]))
+
+    def request(rho):
+        out = ps(6, 0, 160)
+        mm([(out, sumto(r), o(T.SW[:, r:2560:16], "SW"), r == 0, r == 15) for r in range(16)])
+        cp(o(T.SQ[:, 8 * rho:8 * rho + 8, 0:20], "SQ%d" % rho), out)
+        a2a(lambda d: o(T.SQ[:, 8 * rho + d, :], "SQ%d" % rho, "SQo%d" % rho), T.RQ[:, 8 * rho + t, :], "aQ%d" % rho)
+        cp(o(T.RQ[:, 8 * rho + t, :], "RQm%d" % rho), o(T.SQ[:, 8 * rho + t, :], "SQ%d" % rho, "SQo%d" % rho))
+        arrive("aQ%d" % rho, na, ["RQ%d" % rho], 4500.0)
+
+    def lane_prep(rho, KI):
+        dk = sub("dk2", 128 * rho, 128 * rho + 128)
+        if rho == 0:
+            KI = ts(i_("KI"), KI, P20, ADD)
+        d2 = tt(ps(7, 384, 512), tt(ps(7, 256, 384), KI, dk, SUB), L["ng"], MUL)
+        L["base"] = tt(f("base"), d2, dk, ADD)
+
+    def image(rho, out):
+        nw = tt(ps(7, 128, 256), ts(ps(7, 0, 128), L["x"], NN[rho], LT), L["bit"], MUL)
+        fw = tt(f("fw"), nw, L["ng"], GT)
+        tt(out, tt(ps(7, 0, 128), ts(ps(7, 256, 384), L["x"], 1.0, ADD), fw, MUL), img, MAX)
+
+    def unpack(rho):
+        rr = ["RR%d" % rho, "RRm%d" % rho]
+        for b in range(2):
+            mm([(ps(b, 128 * k, 128 * k + 128), o(T.RR[:, 1024 * rho + 128 * (4 * b + k):1024 * rho + 128 * (4 * b + k + 1)], *rr), ID, True, True) for k in range(4)])
+        wt = ["Wz"]
+        for d in range(8):
+            for k in range(3):
+                n = 64 if k == 2 else 128
+                a = CAP * d + 128 * k
+                wt.append("W%d_%d" % (d, k))
+                src = ps(d // 4, 128 * (d % 4), 128 * (d % 4) + n)
+                if d < 4 and WV:
+                    ts(o(T.W[:, a:a + n], wt[-1]), src, sub("HM", k, k + 1), MUL)
+                else:
+                    act(o(T.W[:, a:a + n], wt[-1]), src, F.Copy, scale=sub("HM", k, k + 1))
+        Wa = o(T.W[:, 0:2576], *wt)
+        h("GR", 2048)
+        cp(sub("GR", 0, 1024, tok=["GR0"]), ind(Wa, sub("off2", 0, 64)))
+        act(sub("GR", 1024, 2048, tok=["GR1"]), ind(Wa, sub("off2", 64, 128)))
+        val = ps(4, 0, 128)
+        mm([(val, sumto(r), sub("GR", r, 2048, 16, tok=["GR0", "GR1"]), r == 0, r == 15) for r in range(16)])
+        m = tt(f("nm"), ts(ps(7, 0, 128), val, P20, LT), L["base"], MUL)
+        return tt(i_("KI"), val, m, ADD)
+
+    def decode(rho):
+        rq = o(T.RQ[:, 8 * rho:8 * rho + 8, 0:20], "RQ%d" % rho, "RQm%d" % rho)
+        L["rq"] = rq
+        L["ci"] = ts(i_("ci", 160), rq, 4095, AND)
+        cp(u("offc", 160), L["ci"])
+        ts(h("tb", 160), ts(i_("ti", 160), rq, 12, SHR), -128.0 * (rho + 1), ADD, 8192.0, MUL)
+
+    def pointer(rho, parts):
+        mm([(ps(5, 480, 488), BLK, cp(h("ovb", 8), parts), True, True)])
+        v = red(f("v", 1), ps(5, 480, 488))
+        ts(NN[rho], ts(f("v2", 1), v, 96.0, MIN, NN[rho - 1], ADD), 8192.0, MIN)
+
+    def lookup(rho, fill):
+        f("G", 2560)
+        for k in range(5):
+            act(sub("G", 512 * k, 512 * k + 512, tok=["G%d" % k]), ind(TGa, sub("offc", 32 * k, 32 * k + 32)))
+            mm([(ps(k, r, 512, 16), o(T.BC[:, r, :], "BC%d" % r), sub("tb", 32 * k, 32 * k + 32), True, True) for r in range(16)])
+        fill()
+        blocks = [(s, k) for s in range(8) for k in range(3)]
+        for k in range(5):
+            e = tt(sub("EQ", 512 * k, 512 * k + 512, tok=["EQ%d" % k]), sub("G", 512 * k, 512 * k + 512, tok=["G%d" % k]), ps(k, 0, 512), EQ)
+            tt(sub("PR", 512 * k, 512 * k + 512, tok=["PR%d" % k]), ind(PTa, sub("offc", 32 * k, 32 * k + 32)), e, MUL)
+            items = []
+            for s, j in blocks:
+                a = CAP * s + 128 * j
+                if min((a + 127) // 512, 4) == k:
+                    tk = range(a // 512, (a + 127) // 512 + 1)
+                    out = ps(6, 24 * s + j, 24 * s + 24, 3)
+                    items.append((out, sub("PR", a, a + 128, tok=["PR%d" % z for z in tk]), C["GIF"], True, False))
+                    items.append((out, sub("EQ", a, a + 128, tok=["EQ%d" % z for z in tk]), C["GIB"], False, True))
+            if k == 0:
+                mm(items, c=160 * len(items))
+                head = len(ops) - 1
+            else:
+                mm(items, cont=True, c=160 * len(items))
+                ops[-1]["deps"].update(ops[head]["deps"])
+
+    def reply(rho):
+        z, y = 1024 * rho, 64 * rho
+        val = ps(6, 0, 192)
+        hi = cp(o(T.SR[:, y:y + 64, 0:12:4], "SRa%d" % rho), val)
+        r1 = tt(ps(7, 0, 192), val, hi, SUB)
+        mid = cp(o(T.SR[:, y:y + 64, 1:12:4], "SRb%d" % rho), r1)
+        tt(o(T.SR[:, y:y + 64, 2:12:4], "SRc%d" % rho), r1, mid, SUB)
+        tk = ["SRa%d" % rho, "SRb%d" % rho, "SRc%d" % rho, "SRz", "SRy"]
+        a2a(lambda d: o(T.SR[:, y + 8 * d:y + 8 * d + 8, :], *tk), T.RR[:, z + 128 * t:z + 128 * t + 128], "aR%d" % rho)
+        act(o(T.RR[:, z + 128 * t:z + 128 * t + 128], "RRm%d" % rho), o(T.SR[:, y + 8 * t:y + 8 * t + 8, :], *tk), F.Copy)
+        arrive("aR%d" % rho, na, ["RR%d" % rho], 4500.0)
+
+    def miss_pre(rho):
+        dn = tt(f("dn", 1), NN[rho], n0, SUB)
+        th4 = act(f("th4", 1), dn, bias=S4 - 0.5)
+        L["th3"] = act(f("th3", 1), dn, bias=0.5 - S3, scale=-1.0)
+        cf = cp(f("cf", 160), L["ci"])
+        code = L["code"] = act(f("code", 160), cp(f("vf", 160), L["rq"]), F.Relu, bias=1.0 - 524288.0 * (rho + 1))
+        sg = [act(h("sg0", 160), cf, F.Sign, bias=0.5 - S1), act(h("sg1", 160), cf, F.Sign, bias=S2 - 0.5, scale=-1.0),
+              act(h("sg2", 160), cf, F.Sign, bias=0.5 - S4), act(h("sg3", 160), cf, F.Sign, bias=th4, scale=-1.0)]
+        L["vl"] = act(h("vl", 160), code, F.Sign)
+        wt = [C["I512"], C["I512"], C["I144"], C["I144"]]
+        mm([(ps(5, 320, 480), wt[k], sg[k], k == 0, k == 3) for k in range(4)])
+        L["fl"] = act(h("fl", 160), ps(5, 320, 480), F.Sign)
+        mm([(ps(5, 160, 320), wt[k], sg[k], k == 0, False) for k in range(4)] + [(ps(5, 160, 320), C["IDF"], code, False, True)], c=1280)
+
+    def miss(rho):
+        out = ps(5, 0, 160)
+        mm([(out, sub("Y2", 15 - r, 143 - r), sub("EQ", r, 2560, 16, tok=["EQ%d" % z for z in range(5)]), r == 0, False) for r in range(16)]
+           + [(out, C["I2n"], L["vl"], False, False), (out, ID, L["fl"], False, True)])
+        mf = act(f("mf", 160), act(f("mfa", 160), out, F.Abs, bias=1.0), F.Relu, bias=1.0, scale=-1.0)
+        mi = act(f("mn", 160), out, F.Relu, bias=-1.0, scale=-1.0)
+        sf = tt(o(T.SF[:, rho, :], "SF%d" % rho), ps(5, 160, 320), mf, MUL)
+        send([(nxt, T.CAT[:, rho, 160:320], sf, "aF%d" % rho, topo.engines(core, nxt))])
+        tt(o(T.CAT[:, rho, 0:160], "CN%d" % rho), mi, L["code"], MUL)
+        arrive("aF%d" % rho, len(topo.engines(prv, core)), ["CF%d" % rho])
+
+    def select(rho):
+        m = act(h("m", 320), o(T.CAT[:, rho, 0:320], "CN%d" % rho, "CF%d" % rho), F.Sign)
+        scan(sub("R2", 1, 321), m, C["C128"], ADD, MIN)
+        mm([(ps(6, 0, 320), BLK, sub("R2", 1, 321), True, True)])
+        mm([(ps(3, 0, 320), BLK, sub("R2", 0, 320, tok=["R2", "R2z"]), True, False), (ps(3, 0, 320), C["LI"], m, False, True)])
+        f("ACC", 8)
+        for a in range(8):
+            act(h("junk%d" % (a % 2), 320), ps(6, 0, 320), F.Sign, bias=sub("KB", a, a + 1), acc=sub("ACC", a, a + 1, tok=["ACC%d" % a]))
+        tt(sub("cumM", 0, 320), ps(3, 0, 320), m, MUL)
+        offk = ts(u("offk", 8), sub("ACC", 0, 8, tok=["ACC%d" % a for a in range(8)]), -0.5, MUL, 160.0, ADD)
+        e = tt(f("e"), ind(sub("cumM", 0, 336, tok=["cumM", "cumz"]), offk), io(1, 129), EQ)
+        pc = tt(f("pc"), ind(o(T.CAT[:, rho, :], "CN%d" % rho, "CF%d" % rho, "CATz"), offk), e, MUL)
+        mm([(ps(6, 128, 256), C["BLKF"], pc, True, False), (ps(6, 128, 256), ID, C["DG"], False, True), (ps(6, 0, 128), C["BLKF"], pc, True, True)], c=1152)
+
+    def cand_a(rho):
+        scan(f("cs"), C["RS16"], ps(6, 128, 256), MUL, MAX)
+        ca = ts(i_("ca", 8), sub("cs", 15, 128, 16), -P21 - 1.0, ADD)
+        col = ts(i_("colA", 8), ca, 4095, AND)
+        u("offg", 16)
+        o1 = cp(sub("offg", 0, 8, tok=["og0"]), col)
+        xg = L["xg"] = act(f("xg"), ind(XTa, o1))
+        L["g1"] = act(f("g1"), ind(TGa, o1))
+        cf = L["cf"] = cp(f("colf", 8), col)
+        for nm, b, sc in (("p3u", L["th3"], 1.0), ("n4", S4 - 0.5, -1.0), ("p5", 0.5 - S5, 1.0), ("p6", 0.5 - DUMP, 1.0), ("n5", S5 - 0.5, -1.0), ("n2", S2 - 0.5, -1.0), ("p3", 0.5 - S3, 1.0)):
+            L[nm] = act(h("c" + nm, 8), cf, F.Sign, bias=b, scale=sc)
+        out = ps(6, 384, 392)
+        mm([(out, C["IDF"], cf, True, False)] + [(out, C["I144"], L[nm], False, k == 3) for k, nm in enumerate(("p3u", "n4", "n4", "p5"))], c=512)
+        o2 = cp(sub("offg", 8, 16, tok=["og1"]), out)
+        L["g2"] = act(f("g2"), ind(TGa, o2))
+        tg = ts(i_("tgB"), ts(i_("cb"), ps(6, 0, 128), -1.0, ADD), 12, SAR)
+        mm([(ps(2, 0, 128), C["IDF"], xg, True, False), (ps(2, 0, 128), ID, C["KF"], False, True)], c=640)
+        mm([(ps(3, 0, 128), C["IDF"], xg, True, False), (ps(3, 0, 128), ID, C["KF"], False, False), (ps(3, 0, 128), ID, C["DG14"], False, True)], c=768)
+        scan(f("ys_"), C["RS16"], ps(3, 0, 128), MUL, MAX)
+        b1 = act(f("yb1", 8), sub("ys_", 15, 128, 16), bias=-16384.0 - 1.0 / 256)
+        tt(f("yb2", 8), C["kF"], b1, SUB)
+        f("s1", 8)
+        f("s2", 8)
+        for a in range(8):
+            for nm in ("1", "2"):
+                act(sub("junk%d" % (int(nm) - 1), 0, 16 * a + 16), ps(2, 0, 16 * a + 16), F.Sign, bias=sub("yb" + nm, a, a + 1), scale=-1.0 if nm == "1" else 1.0,
+                    acc=sub("s" + nm, a, a + 1, tok=["s%s_%d" % (nm, a)]))
+        cp(f("pg_", 256), ind(PTa, sub("offg", 0, 16, tok=["og0", "og1"])))
+        key = L["key"] = tt(i_("key"), ts(ps(6, 256, 384), tg, 8192.0, MUL), xg, ADD)
+        lo = ts(ps(6, 128, 256), ts(i_("klo"), key, 1023, AND), 1024.0, MUL)
+        npay = tt(ps(6, 256, 384), lo, ts(i_("khi"), key, 10, SAR), ADD)
+        L["dp"] = tt(f("dp"), npay, sub("pg_", 0, 128), SUB)
+
+    def cand_b(rho, ovout):
+        out = ps(3, 128, 256)
+        xs = [] if rho == RO - 1 else [(out, C["ID2F"], L["xg"], False, False)]
+        mm([(out, C["IDF"], L["g1"], True, False)] + xs + [(out, C["IDF"], L["g2"], False, True)], c=1536)
+        emp = act(h("emp"), out, F.Relu, bias=-1.0, scale=-1.0)
+        mm([(ps(3, 256, 384), C["LSI"], emp, True, True)])
+        L["fs"] = act(f("fs"), ps(3, 256, 384), F.Relu, scale=-1.0)
+
+        def terms(out, start):
+            return [(out, C["IDF"], sub("s1", 0, 8, tok=["s1_%d" % a for a in range(8)]), start, False),
+                    (out, C["IDF"], sub("s2", 0, 8, tok=["s2_%d" % a for a in range(8)]), False, False), (out, ID, L["p6"], False, True)]
+        out = ps(3, 384, 392)
+        mm([(out, sumto(r), sub("emp", r, 128, 16), r == 0, False) for r in range(16)] + terms(out, False) + terms(ps(3, 392, 400), True), c=2200)
+        act(f("ov", 8), out, F.Relu, scale=-1.0, acc=f("ovs", 1))
+        L["tr"] = act(h("tr", 8), ps(3, 392, 400), F.Relu, scale=-1.0)
+        ovout(f("ovs", 1))
+
+    def cand_d(rho):
+        up = "UP%d" % rho
+        fs = L["fs"]
+        items = []
+        for k, extra in enumerate(([], [("I4096", "n4"), ("I4096", "p5")], [("I4096", "n4"), ("I4096", "p5")],
+                                   [("I4608", "n2"), ("I4608", "p3"), ("I4096", "n5"), ("I144", "n5")])):
+            out = ps(3, 400 + 8 * k, 408 + 8 * k)
+            items += [(out, C["IDF"], L["cf"], True, False)] + [(out, C[a], L[b], False, False) for a, b in extra] + [(out, C["I8192n"], L["tr"], False, True)]
+        mm(items, c=1800)
+        tt(o(T.UP[:, rho, 256:288], up + "c"), ps(3, 400, 432), C["DM"], MIN)
+        tt(o(T.UP[:, rho, 0:128], up + "a"), tt(ps(2, 256, 384), ts(ps(2, 128, 256), L["key"], 1.0, ADD), fs, MUL), L["g1"], ADD)
+        f("nP", 256)
+        L["np1"] = tt(o(T.UP[:, rho, 128:256], up + "b"), tt(ps(2, 384, 512), L["dp"], fs, MUL), sub("pg_", 0, 128), ADD)
+        tk = [up + "a", up + "b", up + "c"]
+        trs = [(nxt, T.UA[:, rho, :], o(T.UP[:, rho, :], *tk), "aA%d" % rho, side_engines(core, nxt, topo, cores))]
+        if rho < RO - 1:
+            trs.append((prv, T.UB[:, rho, :], o(T.UP[:, rho, :], *tk), "aB%d" % rho, side_engines(core, prv, topo, cores)))
+        send(trs)
+        arrive("aA%d" % rho, len(side_engines(prv, core, topo, cores)), ["UA%d" % rho])
+        if rho < RO - 1:
+            arrive("aB%d" % rho, len(side_engines(nxt, core, topo, cores)), ["UB%d" % rho])
+
+    def insert(rho):
+        u("offs", 16)
+        up = "UP%d" % rho
+        o1 = ts(sub("offs", 0, 8, tok=["os0"]), o(T.UP[:, rho, 256:264], up + "c"), OWN, ADD)
+        scat(TGa, o1, o(T.UP[:, rho, 0:128], up + "a"))
+        tt(sub("nP", 128, 256, tok=["nP1"]), sub("pg_", 128, 256), act(f("nfs"), L["fs"], bias=1.0, scale=-1.0), MUL)
+        act(sub("nP", 0, 128, tok=["nP0"]), L["np1"], F.Copy)
+        ts(sub("offs", 8, 16, tok=["os1"]), o(T.UP[:, rho, 264:272], up + "c"), LOW, ADD)
+        scat(PTa, sub("offs", 0, 16, tok=["os0", "os1"]), sub("nP", 0, 256, tok=["nP0", "nP1"]))
+
+    def mirror(rho, buf, a, c):
+        tk = "%s%d" % (buf, rho)
+        off = ts(u("offm" + buf, 8), o(T[buf][:, rho, a:a + 8], tk), c, ADD)
+        scat(TGa, off, o(T[buf][:, rho, 0:128], tk))
+        scat(PTa, off, o(T[buf][:, rho, 128:256], tk))
+
+    def homes_psum():
+        for b in range(4):
+            act(ps(HB_[b], 0, 512), sub("IO", 512 * (b % 2), 512 * (b % 2) + 512, tok=["IOa", "IOb"]), bias=float(1024 * (t if b < 2 else (t - 1) % N)))
+
+    KI = o(T.lki[:], "lki")
+    address(KI)
+    spread(0)
+    place()
+    late_consts()
+    homes_psum()
+    nn0 = act(f("nn0", 1), n0, bias=-1.0, scale=-1.0)
+    NX = act(f("NX", WIN), io(0, WIN), bias=nn0, scale=-1.0)
+    for r in range(16):
+        act(o(T.BC[:, r, :], "BC%d" % r), BLK, F.Copy, scale=sub("M16", r, r + 1))
+    for k in range(3):
+        act(o(T.XT[:, S3 + WIN * k:S3 + WIN * (k + 1)], "XT3"), io(0, WIN), bias=n0)
+    for k in range(3):
+        act(o(T.XT[:, 1024 * k:1024 * k + 1024], "XT%d" % k), IO, bias=float(1024 * (t if k < 2 else (t - 1) % N)))
+    pack()
+    for b in (2, 3):
+        tt(o(T.TG[:, S2 + 512 * (b - 2):S2 + 512 * (b - 1)], "TG2"), o(T.KR[:, S2 + 512 * (b - 2):S2 + 512 * (b - 1)], "KR2"), ps(HB_[b], 0, 512), SUB)
+    request(0)
+    xw = ts(f("xw", 18), C["kA"], n0, ADD, -1024.0 * t, ADD)
+    offw = ts(u("offw", 18), xw, 0.0, MAX, 1023.0, MIN)
+    kg = cp(i_("kg", WIN), ind(o(T.KR[:, 0:S1], "KR0"), offw))
+    pgw = cp(f("pgw", WIN), ind(o(T.PT[:, 0:S1], "PT0"), offw))
+    mv = ts(ps(2, 0, WIN), ts(i_("kb", WIN), kg, -2147475456, AND), 8192.0, EQ)
+    k1 = ts(f("wk1", WIN), kg, 1.0, ADD)
+    wa = tt(ps(3, 0, WIN), mv, k1, MUL)
+    t4_ = tt(o(T.TG[:, S4:S5], "TG4"), wa, NX, ADD)
+    p4_ = tt(o(T.PT[:, S4:S5], "PT4"), mv, pgw, MUL)
+    ea, eb = halves(core, nxt, topo)
+    send([(nxt, T.WT[:], t4_, "aW", ea), (nxt, T.WQ[:], p4_, "aW", eb)])
+    arrive("aW", len(topo.engines(prv, core)), ["WT"])
+    tt(o(T.TG[:, S3:S4], "TG3"), tt(ps(2, 0, WIN), k1, wa, SUB), NX, ADD)
+    tt(o(T.PT[:, S3:S4], "PT3"), pgw, p4_, SUB)
+    for k in range(4):
+        tt(o(T.TG[:, 512 * k:512 * k + 512], "TG%d" % (k // 2)), o(T.KR[:, 512 * k:512 * k + 512], "KR%d" % (k // 2)), ps(k % 2, 0, 512), SUB)
+
+    for rho in range(RO):
+        last = rho == RO - 1
+        decode(rho)
+
+        def fill(rho=rho):
+            if rho:
+                urgent(U2, pointer, rho, o(T.RQ[:, 8 * rho:8 * rho + 8, 20], "RQ%d" % rho, "RQm%d" % rho))
+            urgent(U2, miss_pre, rho)
+        lookup(rho, fill)
+        reply(rho)
+        urgent(U2, miss, rho)
+        lane_prep(rho, KI)
+        image(rho, o(T.OY[:, 128:256], "OYi") if last else img)
+        if rho == 0:
+            act(o(T.TG[:, S5:DUMP], "TG5"), o(T.WT[:], "WT"), F.Copy)
+            cp(o(T.PT[:, S5:DUMP], "PT5"), o(T.WQ[:], "WT"))
+        if not last:
+            urgent(U1, select, rho)
+            urgent(U1, cand_a, rho)
+            urgent(U1, cand_b, rho, lambda s, rho=rho: ts(o(T.SQ[:, 8 * rho + 8:8 * rho + 16, 20], "SQo%d" % (rho + 1)), C["ONE"], s, MUL))
+            urgent(U1, cand_d, rho)
+            KI = unpack(rho)
+            address(KI)
+            spread(rho + 1)
+            place()
+            pack()
+            request(rho + 1)
+            insert(rho)
+            mirror(rho, "UA", 272, NXT)
+            mirror(rho, "UB", 280, PRV)
+
+    rho = RO - 1
+    dma("y", T.yi[:], o(T.OY[:, 128:256], "OYi"))
+    homes_psum()
+    for b in range(4):
+        a = (0 if b < 2 else S2) + 512 * (b % 2)
+        x = o(T.TG[:, a:a + 512], "TG0" if b < 2 else "TG2")
+        tt(x, x, ps(HB_[b], 0, 512), ADD)
+    x = o(T.TG[:, S3:DUMP], "TG3", "TG4", "TG5")
+    tt(x, x, o(T.XT[:, S3:DUMP], "XT3"), ADD)
+    urgent(U1, select, rho)
+    for b in range(4):
+        a = (0 if b < 2 else S2) + 512 * (b % 2)
+        cp(sub("G", 512 * b, 512 * b + 512, tok=["G%d" % b]), o(T.PT[:, a:a + 512], "PT0" if b < 2 else "PT2"))
+    urgent(U1, cand_a, rho)
+    for b in range(4):
+        a = (0 if b < 2 else S2) + 512 * (b % 2)
+        mm([(ps(4 + b % 2, 0, 512), C["BLKF"], sub("G", 512 * b, 512 * b + 512, tok=["G%d" % b]), True, True)], c=2048)
+        act(o(T.XT[:, a:a + 512], "XT0" if b < 2 else "XT2"), ps(4 + b % 2, 0, 512), F.Copy)
+
+    def ov_last(s):
+        cp(o(T.SO[:, 0:1], "SO"), s)
+        a2a(lambda d: o(T.SO[:], "SO"), T.RV[:, t, :], "aO")
+        cp(o(T.RV[:, t, :], "RVm"), o(T.SO[:], "SO"))
+        arrive("aO", na, ["RV"], 4500.0)
+    urgent(U1, cand_b, rho, ov_last)
+    cand_d(rho)
+    insert(rho)
+    mm([(ps(4, 0, 128), C["BLKF"], L["np1"], True, True)], c=512)
+    scat(XTa, sub("offs", 0, 8, tok=["os0"]), act(f("sm1"), ps(4, 0, 128), F.Copy))
+    inr = tt(f("inr", 18), ts(f("in0", 18), xw, 0.0, GE), ts(f("in1", 18), xw, 1024.0, LT), MUL)
+    dl = ts(f("dl", 18), C["kA"], float(S1), ADD)
+    u("offf", 36)
+    cp(sub("offf", 0, 18, tok=["of0"]), tt(f("z2", 18), tt(f("z1", 18), tt(f("z0", 18), xw, dl, SUB), inr, MUL), dl, ADD))
+    xh = ts(f("xh", 18), C["kA"], n0, ADD, -1024.0 * ((t - 1) % N), ADD)
+    inh = tt(f("inh", 18), ts(f("in2", 18), xh, 0.0, GE), ts(f("in3", 18), xh, 1024.0, LT), MUL)
+    dh = ts(f("dh", 18), C["kA"], float(S1 + WIN), ADD)
+    zh = tt(f("z4", 18), tt(f("z3", 18), ts(f("xh2", 18), xh, float(S2), ADD), dh, SUB), inh, MUL)
+    KI = unpack(rho)
+    dma("y", T.yl[:], ts(o(T.OY[:, 0:128], "OYl"), KI, -P20, ADD))
+    mirror(rho, "UA", 272, NXT)
+    boost[0] = U5
+    pointer(RO, o(T.RV[:, :, 0], "RV", "RVm"))
+    dn = tt(f("dn", 1), NN[RO], n0, SUB)
+    cp(sub("offf", 18, 36, tok=["of1"]), tt(f("z6", 18), tt(f("z5", 18), ts(f("sp", 18), C["kA"], dn, LT), zh, MUL), dh, ADD))
+    m2 = tt(ps(7, 0, WIN), ts(ps(5, 0, WIN), io(0, WIN), dn, LT, -P21, MUL), o(T.TG[:, S4:S5], "TG4"), ADD)
+    tt(o(T.TG[:, S4:S5], "TG4"), m2, o(T.TG[:, S3:S4], "TG3"), MAX)
+    offf = sub("offf", 0, 36, tok=["of0", "of1"])
+    scat(o(T.TG[:, 0:S3], "TG0", "TG1", "TG2"), offf, o(T.TG[:, S4:DUMP], "TG4", "TG5"))
+    dma("y", T.yk[:, 0:1024], o(T.TG[:, 0:S1], "TG0"))
+    dma("s", T.yk[:, 1024:2048], o(T.TG[:, S2:S3], "TG2"))
+    boost[0] = 0.0
+    p1 = tt(ps(7, 0, WIN), ts(ps(5, 0, WIN), io(0, WIN), dn, GE), o(T.PT[:, S4:S5], "PT4"), MUL)
+    pa = tt(sub("PR", 0, WIN, tok=["PR0"]), p1, o(T.PT[:, S3:S4], "PT3"), ADD)
+    pb = cp(sub("PR", 512, 512 + WIN, tok=["PR1"]), o(T.PT[:, S5:DUMP], "PT5"))
+    for k, x in enumerate((pa, pb)):
+        mm([(ps(k, 0, WIN), C["BLKF"], x, True, True)], c=1152)
+        act(sub("G", WIN * k, WIN * k + WIN, tok=["G0", "G1"] if k else ["G0"]), ps(k, 0, WIN), F.Copy)
+    dma("y", T.yn[:], cp(o(T.OY[:, 256:257], "OYn"), NN[RO]))
+    scat(o(T.XT[:, 0:S3], "XT0", "XT1", "XT2"), offf, sub("G", 0, 2 * WIN, tok=["G0", "G1"]))
+    dma("y", T.ys[:, 0:1024], o(T.XT[0:128:16, 0:S1], "XT0"))
+    dma("s", T.ys[:, 1024:2048], o(T.XT[0:128:16, S2:S3], "XT2"))
+
+    n = len(ops)
+    pre = [op["deps"] | op["soft"] for op in ops]
+    post = [[] for _ in ops]
+    for me in range(n):
+        for d in pre[me]:
+            post[d].append(me)
+
+    def plan(pre, post, prio, sign):
+        left = [len(p) for p in pre]
+        done, free, order = [0.0] * n, {}, []
+        ready = {me: 0.0 for me in range(n) if not left[me]}
+        while ready:
+            start = {me: max(r, free.get(ops[me]["q"], 0.0)) for me, r in ready.items()}
+            first = min(start, key=lambda k: start[k])
+            q = ops[first]["q"]
+            me = max((k for k in ready if ops[k]["q"] == q and start[k] <= start[first] + SLACK), key=lambda k: (prio[k] + sign * ops[k]["up"], -k))
+            done[me] = start[me] + ops[me]["c"]
+            if q != "x":
+                free[q] = done[me] if ops[me]["ev"] is None or q == "g" else start[me] + 60.0
+            order.append(me)
+            del ready[me]
+            for k in post[me]:
+                left[k] -= 1
+                if not left[k]:
+                    ready[k] = max(done[d] for d in pre[k]) + WAKE
+        return done, order
+    prio = [0.0] * n
+    for me in range(n - 1, -1, -1):
+        prio[me] = ops[me]["c"] + max([prio[k] + WAKE for k in post[me]], default=0.0)
+    best = None
+    for _ in range(PASSES):
+        done, order = plan(pre, post, prio, 1.0)
+        if best is None or max(done) < max(best[0]):
+            best = (done, order)
+        prio = plan(post, pre, done, -1.0)[0]
+    done, order = best
+    pos = {me: k for k, me in enumerate(order)}
+    ops = [ops[me] for me in order]
+    for op in ops:
+        op["deps"] = {pos[d] for d in op["deps"]}
+    known = {q: {} for q in ENG}
+    clock, need = [], set()
+    for me, op in enumerate(ops):
+        q = op["q"]
+        op["waits"] = []
+        kn = known.get(q, {})
+        for d in sorted(op["deps"], reverse=True) if q != "x" else []:
+            dq = ops[d]["q"] if ops[d]["ev"] is None else ops[d]["ev"][0]
+            if kn.get(dq, -1) >= d:
+                continue
+            op["waits"].append(d)
+            need.add(d)
+            kn[dq] = d
+            for k, v in clock[d].items():
+                kn[k] = max(kn.get(k, -1), v)
+        clock.append(dict(kn))
+    tick = {"v": 0, "s": 0, "p": 0, "g": 0}
+    evs = []
+    for me, op in enumerate(ops):
+        q = op["q"]
+        if q != "x":
+            e = ENG[q]
+            for d in op["waits"]:
+                e.wait_ge(T.sem[ops[d]["ev"][0]], ops[d]["ev"][1])
+            ins = op["fn"](e)
+            if op["ev"] is None and me in need:
+                tick[q] += 1
+                ins.then_inc(T.sem["q" + q], 1)
+                op["ev"] = ("q" + q, tick[q])
+                continue
+        if op["ev"] is not None:
+            evs.append(op["ev"])
+    for s, k in evs:
+        g.wait_ge(T.sem[s], k)

@@ -6,11 +6,15 @@ S1, S2, S3, S4, S5, DUMP, TW = 1024, 2048, 3072, 3360, 3648, 3936, 4192
 BIG, P20, P21 = 8192.0, 1048576.0, 2097152.0
 SWW = 6464
 WV = True
+PLAN = {}
+AB = True
+LK, LO = 17000.0, 6500.0
+PARTS = {1: (0, 3), 3: (3, 6), 4: (6, 8)}
 HB_ = (0, 1, 4, 5)
 OWN, LOW, NXT, PRV = 8192.0, 16096.0, 16672.0, 12144.0
-U1, U2, U3, U4, U5 = 5000.0, 3000.0, 5000.0, 3000.0, 5000.0
-SLACK, PASSES, NPK = 100.0, 6, 4
-FIX, WAKE, PE = 40.0, 80.0, 0.6
+U1, U2, U3, U4, U5, U6 = 3000.0, 3000.0, 5000.0, 3000.0, 5000.0, 0.0
+SLACK, PASSES, NPK = 60.0, 4, 8
+FIX, WAKE, PE, CY, U7 = 10.0, 140.0, 0.5, 0.9, 5000.0
 SCRATCH = {
     "lki": ("sbuf", [128, 128], "int32"), "lii": ("sbuf", [128, 128], "int32"), "dki": ("sbuf", [128, 384], "int32"),
     "pni": ("sbuf", [128, 1], "int32"), "KR": ("sbuf", [128, 3072], "int32"), "PT": ("sbuf", [128, TW], "int32"),
@@ -18,7 +22,7 @@ SCRATCH = {
     "SW": ("sbuf", [128, SWW], "bfloat16"), "W": ("sbuf", [128, 2576], "bfloat16"),
     "Z": ("sbuf", [128, 16, 132], "bfloat16"), "BC": ("sbuf", [128, 16, 128], "bfloat16"),
     "SQ": ("sbuf", [128, 24, 24], "int32"), "RQ": ("sbuf", [128, 24, 24], "int32"),
-    "SR": ("sbuf", [128, 192, 16], "bfloat16"), "RR": ("sbuf", [128, 3072], "bfloat16"),
+    "SR": ("sbuf", [128, 64, 16], "bfloat16"), "RR": ("sbuf", [128, 576], "float32"), "SA": ("sbuf", [128, 576], "float32"),
     "SF": ("sbuf", [128, 3, 160], "float32"), "CAT": ("sbuf", [128, 3, 336], "float32"),
     "UP": ("sbuf", [128, 3, 288], "float32"), "UA": ("sbuf", [128, 3, 288], "float32"), "UB": ("sbuf", [128, 3, 288], "float32"),
     "WT": ("sbuf", [128, WIN], "float32"), "WQ": ("sbuf", [128, WIN], "int32"),
@@ -49,6 +53,23 @@ def all_to_all_calls(src, cores, topo):
     c1 = [(d, out_e[i * w1:(i + 1) * w1]) for i, d in enumerate(first)] + [(near[0], in_e)]
     c2 = [(d, out_e[i * w2:(i + 1) * w2]) for i, d in enumerate(rest)]
     return [c1, c2]
+
+
+def group_call(src, dsts, cores, topo):
+    far = [c for c in dsts if topo.chip(c) != topo.chip(src)]
+    near = [c for c in dsts if c != src and topo.chip(c) == topo.chip(src)]
+    call = [(c, side_engines(src, c, topo, cores)) for c in near]
+    if far:
+        e = topo.engines(src, far[0])
+        w = 1
+        while 2 * w * len(far) <= len(e):
+            w *= 2
+        call += [(d, e[i * w:(i + 1) * w]) for i, d in enumerate(far)]
+    return call
+
+
+def group_count(dst, cores, topo):
+    return sum(len(e) for s in cores if s != dst for a, b in PARTS.values() for d, e in group_call(s, cores[a:b], cores, topo) if d == dst)
 
 
 def a2a_count(dst, cores, topo):
@@ -118,7 +139,7 @@ def rank_program(g, core, T, topo):
     def cost(out, ins, two=False):
         tk = [k for x in ins for k in x[1]]
         k = 1.56 if "~" in tk else 2.0 if two and not any(z[0] == "@" for z in tk) else 1.0
-        return FIX + max(64.0, size(out) * k) * 1.04
+        return FIX + max(64.0, size(out) * k) * CY
 
     def rec(q, fn, R, W, ev=None, cont=False, c=100.0, after=()):
         me = len(ops)
@@ -208,7 +229,7 @@ def rank_program(g, core, T, topo):
         return out
 
     def scat(w, off, a):
-        rec("v", lambda e: e.tensor_copy(w[0].indirect(off[0]), a[0]), st(a, off), w[1], c=FIX + 3.95 * size(a))
+        rec("v", lambda e: e.tensor_copy(w[0].indirect(off[0]), a[0]), st(a, off), w[1], c=50.0 + 3.8 * CY * size(a))
 
     def ms(out, c):
         rec("v", lambda e: e.memset(out[0], c), [], out[1], c=cost(out, []))
@@ -218,8 +239,8 @@ def rank_program(g, core, T, topo):
         rec("v", lambda e: e.tensor_tensor_scan(out[0], d0[0], d1[0], 0.0, op0, op1), st(d0, d1), out[1], c=c or cost(out, []))
         return out
 
-    def red(out, a):
-        rec("v", lambda e: e.tensor_reduce(out[0], a[0], AxisListType.X, A.add), st(a), out[1])
+    def red(out, a, c=100.0):
+        rec("v", lambda e: e.tensor_reduce(out[0], a[0], AxisListType.X, A.add), st(a), out[1], c=c)
         return out
 
     def act(out, a, func=F.Identity, bias=0.0, scale=1.0, acc=None):
@@ -278,11 +299,14 @@ def rank_program(g, core, T, topo):
     dma("y", o(T.lki[:], "lki"), T.lk[:])
     dma("y", o(T.lii[:], "lii"), T.li[:])
     dma("y", o(T.pni[:], "pni"), T.pn[:])
-    dma("y", o(T.KR[:, S2:S3], "KR2"), T.tk[:, 1024:2048])
     dma("y", o(T.PT[:, S2:S3], "PT2"), T.tp[:, 1024:2048])
+    dma("y", o(T.KR[:, S2:S3], "KR2"), T.tk[:, 1024:2048])
     dma("y", o(T.KR[:, 0:S1], "KR0"), T.tk[:, 0:1024])
     dma("y", o(T.PT[:, 0:S1], "PT0"), T.tp[:, 0:1024])
     dma("y", o(T.dki[:], "dki"), T.dk[:])
+    for k in range(len(ops)):
+        ops[k]["c"] = 2600.0 if k == 0 or 3 <= k <= 6 else 400.0
+        ops[k]["soft"].update([k - 1] if k else [])
     pidx = iota(i_("pidx", 1), [[1, 1]], 0, 1, False)
     IO = f("IO", 1024)
     iota(sub("IO", 0, 320, tok=["IOa"]), [[1, 320]], 0, 0)
@@ -295,7 +319,6 @@ def rank_program(g, core, T, topo):
 
     def io(a, b):
         return sub("IO", a, b, tok=["IOa"])
-    ms(o(T.SW[:, 0:2560], "SW"), 0.0)
     boost[0] = U3
     pr = cp(f("pr", 1), ts(i_("pri", 1), pidx, 15, AND))
     pg = cp(f("pg", 1), ts(i_("pgi", 1), pidx, 4, SHR))
@@ -304,7 +327,6 @@ def rank_program(g, core, T, topo):
     Y = ts(h("Y", 144), io(0, 144), ts(f("y15", 1), pg, 16.0, MUL, 15.0, ADD), EQ)
     for r in range(16):
         act(o(T.Z[:, r, 0:130], "Z%d" % r), sub("Y", 13, 143), F.Copy, scale=sub("M16", r, r + 1))
-    boost[0] = 0.0
 
     def sumto(r):
         return sub("Y", 15 - r, 143 - r)
@@ -318,9 +340,14 @@ def rank_program(g, core, T, topo):
         ts(sub("MK", r, r + 1, tok=["MK%d" % r]), pr, 3.0, EQ, 524288.0 * (r + 1), MUL)
     RS8 = ms(h("RS8", 512), 1.0)
     ms(sub("RS8", 0, 512, 8), 0.0)
+    boost[0] = 4 * U3
+    ms(o(T.SW[:, 0:2560], "SW"), 0.0)
+    ops[-1]["c"] /= 2
+    boost[0] = 0.0
     h("R", 1032)
     ms(sub("R", 0, 8, tok=["R0"]), 0.0)
-    ms(o(T.SQ[:], "SQ0", "SQ1", "SQ2", "SQo0", "SQo1", "SQo2"), 0)
+    ms(o(T.SQ[:, 0:8, 20:24], "SQo0"), 0)
+    ms(o(T.SQ[:, 8:24, 20:24], "SQo1", "SQo2"), 0)
     n0 = cp(f("n0", 1), o(T.pni[:], "pni"))
     n288 = ts(f("n288", 1), n0, float(WIN), ADD)
     cn = ts(f("cn", 1), n0, -1.0, MUL, float(S3), ADD)
@@ -375,15 +402,15 @@ def rank_program(g, core, T, topo):
     KH, PH = o(T.KR[:, S2:S3], "KR2"), o(T.PT[:, S2:S3], "PT2")
     hs = relays(core, prv, cores, topo)
     if hs:
-        send([(prv, T.KR[:, S1:S2], KH, "aK", topo.engines(core, prv))])
         en = side_engines(core, hs[0], topo, cores)
-        send([(x, T.HB[:], o(T.PT[:, S2 + 512 * k:S2 + 512 * (k + 1)], "PT2"), "aH", en[k * len(en) // 2:(k + 1) * len(en) // 2]) for k, x in enumerate(hs)])
+        send([(x, T.HB[:], o(T.PT[:, S2 + 512 * k:S2 + 512 * (k + 1)], "PT2"), "aH", en[k * len(en) // 2:(k + 1) * len(en) // 2]) for k, x in enumerate(hs)]
+             + [(prv, T.KR[:, S1 + 512 * k:S1 + 512 * (k + 1)], o(T.KR[:, S2 + 512 * k:S2 + 512 * (k + 1)], "KR2"), "aK", halves(core, prv, topo)[k]) for k in range(2)])
     else:
         ea, eb = halves(core, prv, topo)
         send([(prv, T.KR[:, S1:S2], KH, "aK", ea), (prv, T.PT[:, S1:S2], PH, "aP", eb)])
     hn = relays(nxt, core, cores, topo)
-    arrive("aK", len(topo.engines(nxt, core)) if hn else len(halves(nxt, core, topo)[0]), ["KR1"], 9000.0)
-    arrive("aP", sum(len(topo.engines(x, core)) for x in hn) if hn else len(halves(nxt, core, topo)[1]), ["PT1"], 12000.0)
+    arrive("aK", len(topo.engines(nxt, core)) if hn else len(halves(nxt, core, topo)[0]), ["KR1"], LK)
+    arrive("aP", sum(len(topo.engines(x, core)) for x in hn) if hn else len(halves(nxt, core, topo)[1]), ["PT1"], 19000.0)
     na = a2a_count(core, cores, topo)
     L = {}
 
@@ -422,12 +449,13 @@ def rank_program(g, core, T, topo):
 
     def place():
         h("OH", 1024)
+        tob = cp(h("tob"), L["to"])
         for d in range(8):
-            ts(sub("OH", d, 1024, 8, tok=["OH%d" % d]), L["to"], float(d), EQ)
+            ts(sub("OH", d, 1024, 8, tok=["OH%d" % d]), tob, float(d), EQ, c=110.0)
         for d in range(8):
             x = sub("OH", d, 1024, 8, tok=["OH%d" % d])
             scan(sub("R", 8 + d, 1032, 8, tok=["R%d" % (d + 1)]), x, x, ADD, MAX, c=110.0)
-        thr = ts(f("thr"), L["to"], float(CAP), MUL, BIG + CAP, ADD)
+        thr = ts(ps(7, 256, 384), L["to"], float(CAP), MUL, BIG + CAP, ADD)
         oh, rr = ["OH%d" % d for d in range(8)], ["R%d" % d for d in range(9)]
         for b in range(2):
             out = ps(4 + b, 0, 512)
@@ -468,9 +496,14 @@ def rank_program(g, core, T, topo):
         tt(out, tt(ps(7, 0, 128), ts(ps(7, 256, 384), L["x"], 1.0, ADD), fw, MUL), img, MAX)
 
     def unpack(rho):
-        rr = ["RR%d" % rho, "RRm%d" % rho]
+        ans = o(T.RR[:, 192 * rho:192 * rho + 192], "RR%d" % rho, "RRm%d" % rho)
+        hi = cp(o(T.SR[:, :, 0:12:4], "SRa"), ans)
+        r1 = tt(ps(7, 0, 192), ans, hi, SUB)
+        mid = cp(o(T.SR[:, :, 1:12:4], "SRb"), r1)
+        tt(o(T.SR[:, :, 2:12:4], "SRc"), r1, mid, SUB)
+        rr = ["SRa", "SRb", "SRc", "SRz", "SRy"]
         for b in range(2):
-            mm([(ps(b, 128 * k, 128 * k + 128), o(T.RR[:, 1024 * rho + 128 * (4 * b + k):1024 * rho + 128 * (4 * b + k + 1)], *rr), ID, True, True) for k in range(4)])
+            mm([(ps(b, 128 * k, 128 * k + 128), o(T.SR[:, 8 * (4 * b + k):8 * (4 * b + k + 1), :], *rr), ID, True, True) for k in range(4)])
         wt = ["Wz"]
         for d in range(8):
             for k in range(3):
@@ -527,18 +560,20 @@ def rank_program(g, core, T, topo):
             else:
                 mm(items, cont=True, c=160 * len(items))
                 ops[-1]["deps"].update(ops[head]["deps"])
+            if k < 4 and k in PARTS:
+                reply(rho, k)
 
-    def reply(rho):
-        z, y = 1024 * rho, 64 * rho
-        val = ps(6, 0, 192)
-        hi = cp(o(T.SR[:, y:y + 64, 0:12:4], "SRa%d" % rho), val)
-        r1 = tt(ps(7, 0, 192), val, hi, SUB)
-        mid = cp(o(T.SR[:, y:y + 64, 1:12:4], "SRb%d" % rho), r1)
-        tt(o(T.SR[:, y:y + 64, 2:12:4], "SRc%d" % rho), r1, mid, SUB)
-        tk = ["SRa%d" % rho, "SRb%d" % rho, "SRc%d" % rho, "SRz", "SRy"]
-        a2a(lambda d: o(T.SR[:, y + 8 * d:y + 8 * d + 8, :], *tk), T.RR[:, z + 128 * t:z + 128 * t + 128], "aR%d" % rho)
-        act(o(T.RR[:, z + 128 * t:z + 128 * t + 128], "RRm%d" % rho), o(T.SR[:, y + 8 * t:y + 8 * t + 8, :], *tk), F.Copy)
-        arrive("aR%d" % rho, na, ["RR%d" % rho], 4500.0)
+    def reply(rho, k=4):
+        z = 192 * rho
+        a, b = PARTS[k]
+        tk = "SA%d_%d" % (rho, k)
+        act(o(T.SA[:, z + 24 * a:z + 24 * b], tk), o(T.B6[:, 24 * a:24 * b], "@6", "B6_0", "B6_1"), F.Copy)
+        send([(d, T.RR[:, z + 24 * t:z + 24 * t + 24], o(T.SA[:, z + 24 * cores.index(d):z + 24 * cores.index(d) + 24], tk), "aR%d" % rho, en)
+              for d, en in group_call(core, cores[a:b], cores, topo)])
+        if a <= t < b:
+            act(o(T.RR[:, z + 24 * t:z + 24 * t + 24], "RRm%d" % rho), o(T.SA[:, z + 24 * t:z + 24 * t + 24], tk), F.Copy)
+        if k == 4:
+            arrive("aR%d" % rho, group_count(core, cores, topo), ["RR%d" % rho], 3300.0)
 
     def miss_pre(rho):
         dn = tt(f("dn", 1), NN[rho], n0, SUB)
@@ -571,10 +606,19 @@ def rank_program(g, core, T, topo):
         mm([(ps(6, 0, 320), BLK, sub("R2", 1, 321), True, True)])
         mm([(ps(3, 0, 320), BLK, sub("R2", 0, 320, tok=["R2", "R2z"]), True, False), (ps(3, 0, 320), C["LI"], m, False, True)])
         f("ACC", 8)
-        for a in range(8):
+        ns = 5 if rho == RO - 1 else 8
+        if ns < 8:
+            mm([(ps(2, 0, 320), BLK, sub("R2", 1, 321), True, True)])
+        for a in range(ns):
             act(h("junk%d" % (a % 2), 320), ps(6, 0, 320), F.Sign, bias=sub("KB", a, a + 1), acc=sub("ACC", a, a + 1, tok=["ACC%d" % a]))
         tt(sub("cumM", 0, 320), ps(3, 0, 320), m, MUL)
-        offk = ts(u("offk", 8), sub("ACC", 0, 8, tok=["ACC%d" % a for a in range(8)]), -0.5, MUL, 160.0, ADD)
+        offk = u("offk", 8)
+        for a in range(ns, 8):
+            x = sub("PR", 512 * (a - ns), 512 * (a - ns) + 320, tok=["PR%d" % (a - ns)])
+            red(sub("ACC", a, a + 1, tok=["ACC%d" % a]), ts(x, ps(2, 0, 320), sub("kA", a, a + 1), GT, 0.5, SUB), 370.0)
+        if ns < 8:
+            ts(sub("offk", ns, 8), sub("ACC", ns, 8, tok=["ACC%d" % a for a in range(ns, 8)]), -1.0, MUL, 160.0, ADD)
+        ts(sub("offk", 0, ns), sub("ACC", 0, ns, tok=["ACC%d" % a for a in range(ns)]), -0.5, MUL, 160.0, ADD)
         e = tt(f("e"), ind(sub("cumM", 0, 336, tok=["cumM", "cumz"]), offk), io(1, 129), EQ)
         pc = tt(f("pc"), ind(o(T.CAT[:, rho, :], "CN%d" % rho, "CF%d" % rho, "CATz"), offk), e, MUL)
         mm([(ps(6, 128, 256), C["BLKF"], pc, True, False), (ps(6, 128, 256), ID, C["DG"], False, True), (ps(6, 0, 128), C["BLKF"], pc, True, True)], c=1152)
@@ -715,8 +759,11 @@ def rank_program(g, core, T, topo):
                 urgent(U2, pointer, rho, o(T.RQ[:, 8 * rho:8 * rho + 8, 20], "RQ%d" % rho, "RQm%d" % rho))
             urgent(U2, miss_pre, rho)
         lookup(rho, fill)
+        if last:
+            urgent(U7, miss, rho)
         reply(rho)
-        urgent(U2, miss, rho)
+        if not last:
+            urgent(U2, miss, rho)
         lane_prep(rho, KI)
         image(rho, o(T.OY[:, 128:256], "OYi") if last else img)
         if rho == 0:
@@ -726,13 +773,16 @@ def rank_program(g, core, T, topo):
             urgent(U1, select, rho)
             urgent(U1, cand_a, rho)
             urgent(U1, cand_b, rho, lambda s, rho=rho: ts(o(T.SQ[:, 8 * rho + 8:8 * rho + 16, 20], "SQo%d" % (rho + 1)), C["ONE"], s, MUL))
-            urgent(U1, cand_d, rho)
+            if AB:
+                urgent(U1, cand_d, rho)
             KI = unpack(rho)
             address(KI)
             spread(rho + 1)
             place()
             pack()
             request(rho + 1)
+            if not AB:
+                cand_d(rho)
             insert(rho)
             mirror(rho, "UA", 272, NXT)
             mirror(rho, "UB", 280, PRV)
@@ -760,7 +810,7 @@ def rank_program(g, core, T, topo):
         cp(o(T.SO[:, 0:1], "SO"), s)
         a2a(lambda d: o(T.SO[:], "SO"), T.RV[:, t, :], "aO")
         cp(o(T.RV[:, t, :], "RVm"), o(T.SO[:], "SO"))
-        arrive("aO", na, ["RV"], 4500.0)
+        arrive("aO", na, ["RV"], LO)
     urgent(U1, cand_b, rho, ov_last)
     cand_d(rho)
     insert(rho)
@@ -776,26 +826,50 @@ def rank_program(g, core, T, topo):
     zh = tt(f("z4", 18), tt(f("z3", 18), ts(f("xh2", 18), xh, float(S2), ADD), dh, SUB), inh, MUL)
     KI = unpack(rho)
     dma("y", T.yl[:], ts(o(T.OY[:, 0:128], "OYl"), KI, -P20, ADD))
-    mirror(rho, "UA", 272, NXT)
-    boost[0] = U5
-    pointer(RO, o(T.RV[:, :, 0], "RV", "RVm"))
-    dn = tt(f("dn", 1), NN[RO], n0, SUB)
+    dn = f("dn", 1)
+    boost[0] = U6
     cp(sub("offf", 18, 36, tok=["of1"]), tt(f("z6", 18), tt(f("z5", 18), ts(f("sp", 18), C["kA"], dn, LT), zh, MUL), dh, ADD))
     m2 = tt(ps(7, 0, WIN), ts(ps(5, 0, WIN), io(0, WIN), dn, LT, -P21, MUL), o(T.TG[:, S4:S5], "TG4"), ADD)
     tt(o(T.TG[:, S4:S5], "TG4"), m2, o(T.TG[:, S3:S4], "TG3"), MAX)
     offf = sub("offf", 0, 36, tok=["of0", "of1"])
     scat(o(T.TG[:, 0:S3], "TG0", "TG1", "TG2"), offf, o(T.TG[:, S4:DUMP], "TG4", "TG5"))
-    dma("y", T.yk[:, 0:1024], o(T.TG[:, 0:S1], "TG0"))
-    dma("s", T.yk[:, 1024:2048], o(T.TG[:, S2:S3], "TG2"))
-    boost[0] = 0.0
     p1 = tt(ps(7, 0, WIN), ts(ps(5, 0, WIN), io(0, WIN), dn, GE), o(T.PT[:, S4:S5], "PT4"), MUL)
     pa = tt(sub("PR", 0, WIN, tok=["PR0"]), p1, o(T.PT[:, S3:S4], "PT3"), ADD)
     pb = cp(sub("PR", 512, 512 + WIN, tok=["PR1"]), o(T.PT[:, S5:DUMP], "PT5"))
     for k, x in enumerate((pa, pb)):
         mm([(ps(k, 0, WIN), C["BLKF"], x, True, True)], c=1152)
         act(sub("G", WIN * k, WIN * k + WIN, tok=["G0", "G1"] if k else ["G0"]), ps(k, 0, WIN), F.Copy)
-    dma("y", T.yn[:], cp(o(T.OY[:, 256:257], "OYn"), NN[RO]))
     scat(o(T.XT[:, 0:S3], "XT0", "XT1", "XT2"), offf, sub("G", 0, 2 * WIN, tok=["G0", "G1"]))
+    k6 = sub("kA", 0, 6)
+    u("offx", 12)
+    f("tg0", 12)
+    f("k12", 12)
+    for k, (sec, r, base) in enumerate(((S3, t, 0), (S5, (t - 1) % N, S2))):
+        ts(sub("offx", 6 * k, 6 * k + 6, tok=["ox%d" % k]), k6, dn, ADD, float(sec), ADD)
+        act(sub("k12", 6 * k, 6 * k + 6, tok=["k12%d" % k]), k6, bias=96.0 * k)
+        xx = ts(f("xx%d" % k, 6), k6, NN[RO - 1], ADD, -1024.0 * r, ADD)
+        ya = tt(f("ya%d" % k, 6), ts(f("yb%d" % k, 6), xx, 0.0, LT, 2 * BIG, MUL), xx, ADD)
+        yc = ts(f("yc%d" % k, 6), xx, 1024.0, GE, BIG, MUL)
+        tt(sub("tg0", 6 * k, 6 * k + 6, tok=["tg0%d" % k]), ts(f("yd%d" % k, 6), ya, float(base), ADD), yc, ADD)
+    dx = act(f("dx", 12), sub("k12", 0, 12, tok=["k120", "k121"]), bias=float(DUMP))
+    i12 = f("i12", 12)
+    for k in range(2):
+        act(sub("i12", 6 * k, 6 * k + 6), k6, F.Copy)
+    mirror(rho, "UA", 272, NXT)
+    offx = sub("offx", 0, 12, tok=["ox0", "ox1"])
+    kx = act(sub("PR", 1024, 1216, tok=["PR2"]), ind(TGa, offx))
+    mm([(ps(4, 0, 192), C["BLKF"], cp(sub("PR", 1536, 1728, tok=["PR3"]), ind(PTa, offx)), True, True)], c=768)
+    sx = act(sub("PR", 2048, 2240, tok=["PR4"]), ps(4, 0, 192), F.Copy)
+    boost[0] = U5
+    pointer(RO, o(T.RV[:, :, 0], "RV", "RVm"))
+    no = ts(f("no", 12), i12, tt(f("dv", 1), NN[RO], NN[RO - 1], SUB), GE, BIG, MUL)
+    offy = cp(u("offy", 12), tt(f("y2", 12), tt(f("y1", 12), no, sub("tg0", 0, 12, tok=["tg00", "tg01"]), ADD), dx, MIN))
+    scat(TGa, offy, kx)
+    dma("y", T.yk[:, 0:1024], o(T.TG[:, 0:S1], "TG0"))
+    dma("s", T.yk[:, 1024:2048], o(T.TG[:, S2:S3], "TG2"))
+    scat(XTa, offy, sx)
+    boost[0] = 0.0
+    dma("y", T.yn[:], cp(o(T.OY[:, 256:257], "OYn"), NN[RO]))
     dma("y", T.ys[:, 0:1024], o(T.XT[0:128:16, 0:S1], "XT0"))
     dma("s", T.ys[:, 1024:2048], o(T.XT[0:128:16, S2:S3], "XT2"))
 
@@ -835,6 +909,7 @@ def rank_program(g, core, T, topo):
             best = (done, order)
         prio = plan(post, pre, done, -1.0)[0]
     done, order = best
+    PLAN[t] = [(ops[m]["q"], ops[m]["lab"], done[m] - ops[m]["c"]) for m in order]
     pos = {me: k for k, me in enumerate(order)}
     ops = [ops[me] for me in order]
     for op in ops:

@@ -2,84 +2,44 @@ from concourse.bass import DstId, RemoteDMATransfer
 from concourse.mybir import AluOpType as A, AxisListType, ActivationFunctionType as F
 
 N, RO, CAP, WIN = 8, 3, 320, 288
-S1, S2, S3, S4, S5, DUMP, TW = 1024, 2048, 3072, 3360, 3648, 3936, 4192
-BIG, P20, P21 = 8192.0, 1048576.0, 2097152.0
-SWW = 6464
-WV = True
+WS = 1024 + WIN
+S3, S1, S4, S2, S5, DUMP, TW = 1024, WS, WS + 1024, 2 * WS, 2 * WS + 1024, 3 * WS, 3 * WS + 256
+BIG, U, P21 = 8192.0, 1048576.0, 2097152.0
+SWW, OS = 6464, 132
+C0, C1, C2, C3 = 8192.0, 16384.0 - WS, 16384.0 + WS, 12288.0 - WS
 PLAN = {}
-AB = True
-LK, LO = 17000.0, 6500.0
-PARTS = {1: (0, 3), 3: (3, 6), 4: (6, 8)}
-HB_ = (0, 1, 4, 5)
-OWN, LOW, NXT, PRV = 8192.0, 16096.0, 16672.0, 12144.0
-U1, U2, U3, U4, U5, U6 = 3000.0, 3000.0, 5000.0, 3000.0, 5000.0, 0.0
-SLACK, PASSES, NPK = 60.0, 4, 8
-FIX, WAKE, PE, CY, U7 = 10.0, 140.0, 0.5, 0.9, 5000.0
+CFG = {"gv": 48, "npk": 8, "slack": 40.0, "passes": 4, "fix": 10.0, "wake": 70.0, "pe": 0.45, "cy": 0.85, "wv": (3,), "sv": (0, 1, 2, 3), "lastv": 3,
+       "u1": 2000.0, "u2": 2000.0, "u3": 5000.0, "u4": 1000.0, "u5": 5000.0, "u7": 5000.0, "far": 2800.0, "near": 2000.0, "lk": 9000.0, "lp": 12000.0, "lo": 4500.0}
 SCRATCH = {
     "lki": ("sbuf", [128, 128], "int32"), "lii": ("sbuf", [128, 128], "int32"), "dki": ("sbuf", [128, 384], "int32"),
-    "pni": ("sbuf", [128, 1], "int32"), "KR": ("sbuf", [128, 3072], "int32"), "PT": ("sbuf", [128, TW], "int32"),
+    "pni": ("sbuf", [128, 1], "int32"), "KR": ("sbuf", [128, 2048], "int32"), "PT": ("sbuf", [128, TW], "int32"),
     "TG": ("sbuf", [128, TW], "float32"), "XT": ("sbuf", [128, TW], "float32"),
     "SW": ("sbuf", [128, SWW], "bfloat16"), "W": ("sbuf", [128, 2576], "bfloat16"),
-    "Z": ("sbuf", [128, 16, 132], "bfloat16"), "BC": ("sbuf", [128, 16, 128], "bfloat16"),
-    "SQ": ("sbuf", [128, 24, 24], "int32"), "RQ": ("sbuf", [128, 24, 24], "int32"),
+    "T2": ("sbuf", [128, 128, 16], "bfloat16"), "BC": ("sbuf", [128, 16, 128], "bfloat16"),
+    "SQ": ("sbuf", [128, 24, 48], "uint16"), "RQ": ("sbuf", [128, 12, 96], "uint16"), "TQ": ("sbuf", [128, 16, 20], "bfloat16"),
     "SR": ("sbuf", [128, 64, 16], "bfloat16"), "RR": ("sbuf", [128, 576], "float32"), "SA": ("sbuf", [128, 576], "float32"),
     "SF": ("sbuf", [128, 3, 160], "float32"), "CAT": ("sbuf", [128, 3, 336], "float32"),
-    "UP": ("sbuf", [128, 3, 288], "float32"), "UA": ("sbuf", [128, 3, 288], "float32"), "UB": ("sbuf", [128, 3, 288], "float32"),
-    "WT": ("sbuf", [128, WIN], "float32"), "WQ": ("sbuf", [128, WIN], "int32"),
+    "UP": ("sbuf", [128, 3, 416], "float32"), "UA": ("sbuf", [128, 3, 288], "float32"), "UB": ("sbuf", [128, 3, 288], "float32"),
     "SO": ("sbuf", [128, 4], "float32"), "RV": ("sbuf", [128, 8, 4], "float32"), "HB": ("sbuf", [128, 512], "int32"),
     "OY": ("sbuf", [128, 260], "float32"),
-    "TF": ("sbuf", [128, 16000], "float32"), "TI": ("sbuf", [128, 2816], "int32"), "TB": ("sbuf", [128, 16000], "bfloat16"),
-    "TU": ("sbuf", [128, 1024], "uint16"),
+    "TF": ("sbuf", [128, 15360], "float32"), "TI": ("sbuf", [128, 1536], "int32"), "TB": ("sbuf", [128, 21504], "bfloat16"),
+    "TU": ("sbuf", [128, 512], "uint16"),
 }
 for _b in range(8):
     SCRATCH["B%d" % _b] = ("psum", [128, 512], "float32")
-SEMAPHORES = (["qv", "qs", "qp", "qg", "aK", "aP", "aW", "aO", "aH"] + ["a%s%d" % (k, r) for k in "QRFAB" for r in range(RO)]
-              + ["d%d" % i for i in range(16)] + ["l%d" % i for i in range(32)])
+SEMAPHORES = (["qv", "qs", "qp", "qg", "aK", "aP", "aW", "aO", "aH", "lr"] + ["a%s%d" % (k, r) for k in "FAB" for r in range(RO)]
+              + ["a%s%d%d" % (k, r, b) for k in "QR" for r in range(RO) for b in range(4)]
+              + ["d%d" % i for i in range(16)] + ["l%d" % i for i in range(48)])
 
 
 def bits(engs):
     return sum(1 << e for e in engs)
 
 
-def all_to_all_calls(src, cores, topo):
-    far = [c for c in cores if topo.chip(c) != topo.chip(src)]
-    near = [c for c in cores if c != src and topo.chip(c) == topo.chip(src)]
-    k = cores.index(src)
-    far = far[k % len(far):] + far[:k % len(far)]
-    out_e = topo.engines(src, far[0])
-    in_e = [e for e in topo.engines(src, near[0]) if e not in out_e]
-    first, rest = far[:4], far[4:]
-    w1, w2 = len(out_e) // len(first), len(out_e) // len(rest)
-    c1 = [(d, out_e[i * w1:(i + 1) * w1]) for i, d in enumerate(first)] + [(near[0], in_e)]
-    c2 = [(d, out_e[i * w2:(i + 1) * w2]) for i, d in enumerate(rest)]
-    return [c1, c2]
-
-
-def group_call(src, dsts, cores, topo):
-    far = [c for c in dsts if topo.chip(c) != topo.chip(src)]
-    near = [c for c in dsts if c != src and topo.chip(c) == topo.chip(src)]
-    call = [(c, side_engines(src, c, topo, cores)) for c in near]
-    if far:
-        e = topo.engines(src, far[0])
-        w = 1
-        while 2 * w * len(far) <= len(e):
-            w *= 2
-        call += [(d, e[i * w:(i + 1) * w]) for i, d in enumerate(far)]
-    return call
-
-
-def group_count(dst, cores, topo):
-    return sum(len(e) for s in cores if s != dst for a, b in PARTS.values() for d, e in group_call(s, cores[a:b], cores, topo) if d == dst)
-
-
-def a2a_count(dst, cores, topo):
-    return sum(len(e) for s in cores if s != dst for call in all_to_all_calls(s, cores, topo) for d, e in call if d == dst)
-
-
-def relays(src, dst, cores, topo):
-    if topo.chip(src) == topo.chip(dst):
-        return []
-    return [h for h in topo.cores_of(src) if h not in cores and topo.die(h) != topo.die(src) and topo.may_write(h, dst)][:2]
+def chip_pairs(cores, topo):
+    pairs = [[i for i, x in enumerate(cores) if topo.chip(x) == topo.chip(c)] for c in cores[::2]]
+    assert pairs == [[2 * k, 2 * k + 1] for k in range(len(cores) // 2)]
+    return pairs
 
 
 def halves(src, dst, topo):
@@ -92,6 +52,24 @@ def side_engines(src, dst, topo, cores):
     if topo.chip(src) != topo.chip(dst):
         return topo.engines(src, dst)
     return [e for e in topo.engines(src, dst) if e not in topo.engines(src, far)]
+
+
+def pair_call(src, pair, cores, topo):
+    dsts = [d for d in pair if cores[d] != src]
+    if len(dsts) == 1:
+        return [(dsts[0], side_engines(src, cores[dsts[0]], topo, cores))]
+    return [(d, halves(src, cores[d], topo)[k]) for k, d in enumerate(dsts)]
+
+
+def pair_count(dst, pair, cores, topo):
+    mine = chip_pairs(cores, topo)[dst // 2]
+    return sum(len(e) for s in pair if s != dst for d, e in pair_call(cores[s], mine, cores, topo) if d == dst)
+
+
+def relays(src, dst, cores, topo):
+    if topo.chip(src) == topo.chip(dst):
+        return []
+    return [h for h in topo.cores_of(src) if h not in cores and topo.die(h) != topo.die(src) and topo.may_write(h, dst)][:2]
 
 
 def dst_id(c, topo):
@@ -108,8 +86,22 @@ def relay_program(g, core, T, topo):
             i = hs.index(core)
             g.wait_ge(T.sem.aH, len(side_engines(src, core, topo, cores)) // 2)
             rid, pid, _ = topo.addr(dst)
-            g.remote_dma(T.PT[:, S1 + 512 * i:S1 + 512 * (i + 1)], T.HB[:], T.sem.aP, T.sem.l0, pid, rid, topo.mask(core, dst))
-            g.wait_ge(T.sem.l0, len(topo.engines(core, dst)))
+            g.remote_dma(T.PT[:, S1 + 512 * i:S1 + 512 * (i + 1)], T.HB[:], T.sem.aP, T.sem.lr, pid, rid, topo.mask(core, dst))
+            g.wait_ge(T.sem.lr, len(topo.engines(core, dst)))
+
+
+def mask_of(shape, idx):
+    idx = list(idx) + [slice(None)] * (len(shape) - len(idx))
+    step, m = 1, 1
+    for n, i in zip(reversed(shape), reversed(idx)):
+        r = range(n)[i] if isinstance(i, slice) else range(i, i + 1)
+        if len(r) > 1 and m.bit_length() <= r.step * step:
+            w = r.step * step
+            m = m * (((1 << (w * len(r))) - 1) // ((1 << w) - 1)) << (r.start * step)
+        else:
+            m = sum(m << (k * step) for k in r)
+        step *= n
+    return m
 
 
 def rank_program(g, core, T, topo):
@@ -118,9 +110,12 @@ def rank_program(g, core, T, topo):
         relay_program(g, core, T, topo)
         return
     cores = list(T.cores)
+    pairs = chip_pairs(cores, topo)
+    NP, me_c, par = len(pairs), t // 2, t % 2
     prv, nxt = cores[(t - 1) % N], cores[(t + 1) % N]
     ENG = {"v": g.vector, "s": g.scalar, "p": g.tensor, "g": g, "y": g.sync}
-    ops, wr, rd, bank, slots = [], {}, {}, {}, {}
+    FIX, WAKE, PE, CY = CFG["fix"], CFG["wake"], CFG["pe"], CFG["cy"]
+    ops, acc, bank, slots = [], {}, {}, {}
     cnt = {"d": 0, "l": 0, "TF": 0, "TI": 0, "TB": 0, "TU": 0}
     lastg, boost = [], [0.0]
 
@@ -136,43 +131,17 @@ def rank_program(g, core, T, topo):
             n *= k
         return n
 
-    def cost(out, ins, two=False):
-        tk = [k for x in ins for k in x[1]]
-        k = 1.56 if "~" in tk else 2.0 if two and not any(z[0] == "@" for z in tk) else 1.0
-        return FIX + max(64.0, size(out) * k) * CY
+    def o(name, *idx):
+        ap = T[name][(slice(None),) + idx]
+        return (ap, [(name, mask_of(SCRATCH[name][1][1:], idx))], "p" if SCRATCH[name][0] == "psum" else "h" if SCRATCH[name][2] in ("bfloat16", "uint16") else "s")
 
-    def rec(q, fn, R, W, ev=None, cont=False, c=100.0, after=()):
-        me = len(ops)
-        deps = set()
-        for k in set(R + W):
-            if k[0] == "@":
-                b = bank.setdefault(k, [q, [], []])
-                if b[0] != q:
-                    b[0], b[1], b[2] = q, [], b[1]
-                b[1].append(me)
-                deps.update(b[2])
-        R = [k for k in R if k[0] not in "@~"]
-        W = [k for k in W if k[0] != "@"]
-        for k in R:
-            deps.update(wr.get(k, []))
-        for k in W:
-            deps.update(rd.get(k, []))
-            deps.update(o for o in wr.get(k, []) if not (cont and ops[o]["q"] == q))
-        for k in R:
-            rd.setdefault(k, []).append(me)
-        for k in W:
-            wr[k] = (wr.get(k, []) if cont else []) + [me]
-            if not cont:
-                rd[k] = []
-        deps.discard(me)
-        soft = set(after)
-        if q == "g":
-            soft.update(lastg[-1:])
-            lastg.append(me)
-        ops.append({"q": q, "fn": fn, "deps": deps, "ev": ev, "c": c, "up": boost[0], "soft": soft, "lab": (W + ["-"])[0]})
+    def cols(name, a, b, s=1):
+        return o(name, slice(a, b, s) if s != 1 else slice(a, b))
 
-    def o(ap, *tok):
-        return (ap, list(tok))
+    def sub(name, a, b, s=1):
+        buf, z = slots[name]
+        ap = T[buf][:, z + a:z + b:s] if s != 1 else T[buf][:, z + a:z + b]
+        return (ap, [(name, mask_of([b], [slice(a, b, s)]))], "h" if buf in ("TB", "TU") else "s")
 
     def tmp(buf, name, n):
         if name not in slots:
@@ -180,13 +149,7 @@ def rank_program(g, core, T, topo):
             cnt[buf] += (n + 15) // 16 * 16
             assert cnt[buf] <= SCRATCH[buf][1][1]
         assert slots[name][0] == buf
-        a = slots[name][1]
-        return o(T[buf][:, a:a + n], name)
-
-    def sub(name, a, b, s=1, tok=None):
-        buf, z = slots[name]
-        tk = [name] if tok is None else tok
-        return o(T[buf][:, z + a:z + b:s] if s != 1 else T[buf][:, z + a:z + b], *tk)
+        return sub(name, 0, n)
 
     def f(name, n=128):
         return tmp("TF", name, n)
@@ -201,11 +164,10 @@ def rank_program(g, core, T, topo):
         return tmp("TU", name, n)
 
     def ps(b, a, e, s=1):
-        ap = T["B%d" % b][:, a:e:s] if s != 1 else T["B%d" % b][:, a:e]
-        return o(ap, "@%d" % b, *["B%d_%d" % (b, k) for k in range(a // 128, (e + 127) // 128)])
+        return cols("B%d" % b, a, e, s)
 
     def ind(w, off):
-        return (w[0].indirect(off[0]), w[1] + off[1] + ["~"])
+        return (w[0].indirect(off[0]), w[1] + off[1], "i")
 
     def sv(x):
         return x[0] if isinstance(x, tuple) else x
@@ -213,11 +175,44 @@ def rank_program(g, core, T, topo):
     def st(*xs):
         return [k for x in xs if isinstance(x, tuple) for k in x[1]]
 
-    def ts(out, a, s1, op0, s2=None, op1=None, c=None):
+    def cost(out, ins, two=False, half=False):
+        kinds = [x[2] for x in ins]
+        if "i" in kinds:
+            return 55.0 + 1.56 * CY * size(out)
+        k = 2.0 if two and "p" not in kinds else 0.5 if half and all(z == "h" for z in kinds + [out[2]]) else 1.0
+        return FIX + max(64.0, size(out) * k) * CY
+
+    def rec(q, fn, R, W, ev=None, c=100.0, after=()):
+        me = len(ops)
+        deps, soft = set(), set(after)
+        for k in set(x[0] for x in R + W):
+            if k in SCRATCH and SCRATCH[k][0] == "psum":
+                b = bank.setdefault(k, [q, [], []])
+                if b[0] != q:
+                    b[0], b[1], b[2] = q, [], b[1]
+                b[1].append(me)
+                deps.update(b[2])
+        for w, xs in ((False, R), (True, W)):
+            for k, m in xs:
+                keep = []
+                for e in acc.get(k, []):
+                    if e[0] & m and (w or e[2]) and e[1] != me:
+                        deps.add(e[1])
+                    if not (w and e[0] & ~m == 0):
+                        keep.append(e)
+                keep.append((m, me, w))
+                acc[k] = keep
+        if q == "g":
+            soft.update(lastg[-1:])
+            lastg.append(me)
+        ops.append({"q": q, "fn": fn, "deps": deps, "ev": ev, "c": c, "up": boost[0], "soft": soft, "lab": (W + [("-", 0)])[0][0]})
+        return me
+
+    def ts(out, a, s1, op0, s2=None, op1=None):
         if op1 is None:
-            rec("v", lambda e: e.tensor_scalar(out[0], a[0], sv(s1), None, op0), st(a, s1), out[1], c=c or cost(out, [a]))
+            rec("v", lambda e: e.tensor_scalar(out[0], a[0], sv(s1), None, op0), st(a, s1), out[1], c=cost(out, [a], half=True))
         else:
-            rec("v", lambda e: e.tensor_scalar(out[0], a[0], sv(s1), sv(s2), op0, op1), st(a, s1, s2), out[1], c=cost(out, [a]))
+            rec("v", lambda e: e.tensor_scalar(out[0], a[0], sv(s1), sv(s2), op0, op1), st(a, s1, s2), out[1], c=cost(out, [a], half=True))
         return out
 
     def tt(out, a, b, op):
@@ -225,653 +220,640 @@ def rank_program(g, core, T, topo):
         return out
 
     def cp(out, a):
-        rec("v", lambda e: e.tensor_copy(out[0], a[0]), st(a), out[1], c=cost(out, [a]))
+        rec("v", lambda e: e.tensor_copy(out[0], a[0]), st(a), out[1], c=cost(out, [a], half=True))
         return out
 
     def scat(w, off, a):
         rec("v", lambda e: e.tensor_copy(w[0].indirect(off[0]), a[0]), st(a, off), w[1], c=50.0 + 3.8 * CY * size(a))
 
     def ms(out, c):
-        rec("v", lambda e: e.memset(out[0], c), [], out[1], c=cost(out, []))
+        rec("v", lambda e: e.memset(out[0], c), [], out[1], c=cost(out, [], half=True))
         return out
 
-    def scan(out, d0, d1, op0, op1, c=None):
-        rec("v", lambda e: e.tensor_tensor_scan(out[0], d0[0], d1[0], 0.0, op0, op1), st(d0, d1), out[1], c=c or cost(out, []))
+    def scan(out, d0, d1, op0, op1, init=0.0):
+        rec("v", lambda e: e.tensor_tensor_scan(out[0], d0[0], d1[0], sv(init), op0, op1), st(d0, d1, init), out[1], c=cost(out, [d0, d1], half=True))
         return out
 
-    def red(out, a, c=100.0):
-        rec("v", lambda e: e.tensor_reduce(out[0], a[0], AxisListType.X, A.add), st(a), out[1], c=c)
+    def red(out, a):
+        rec("v", lambda e: e.tensor_reduce(out[0], a[0], AxisListType.X, A.add), st(a), out[1], c=cost(a, []))
         return out
 
     def act(out, a, func=F.Identity, bias=0.0, scale=1.0, acc=None):
         if acc is None:
             rec("s", lambda e: e.activation(out[0], a[0], func, bias=sv(bias), scale=sv(scale)), st(a, bias, scale), out[1], c=cost(out, [a]))
         else:
-            rec("s", lambda e: e.activation(out[0], a[0], func, bias=sv(bias), scale=sv(scale), accum_out=acc[0]), st(a, bias, scale), out[1] + acc[1], c=cost(out, [a]))
+            rec("s", lambda e: e.activation(out[0], a[0], func, bias=sv(bias), scale=sv(scale), accum_out=acc[0]), st(a, bias, scale), out[1] + acc[1], c=cost(out, [a]) + 20.0)
         return out
 
-    def mm(items, cont=False, c=None):
+    def mm(items):
         def fn(e):
             ins = None
             for x in items:
                 ins = e.matmul(x[0][0], x[1][0], x[2][0], x[3], x[4])
             return ins
-        R, W = [], []
+        R, W = {}, {}
         for x in items:
-            R += st(x[1], x[2])
-            W += x[0][1]
-        rec("p", fn, sorted(set(R)), sorted(set(W)), cont=cont, c=100.0 + PE * (c or sum(max(64, size(x[0])) for x in items)))
+            for d, ks in ((R, st(x[1], x[2])), (W, x[0][1])):
+                for k, m in ks:
+                    d[k] = d.get(k, 0) | m
+        rec("p", fn, list(R.items()), list(W.items()), c=FIX + PE * sum(max(64, size(x[0])) * (1 if x[1][2] == "h" else 4) for x in items))
+
+    def lin(out, terms):
+        return [(out, a, b, k == 0, k == len(terms) - 1) for k, (a, b) in enumerate(terms)]
 
     def iota(out, pat, base, cm, fl=True):
         if fl:
-            rec("g", lambda e: e.iota(out[0], pat, base, cm, allow_small_or_imprecise_dtypes=True), [], out[1], c=130 + 2.1 * size(out))
+            rec("g", lambda e: e.iota(out[0], pat, base, cm, allow_small_or_imprecise_dtypes=True), [], out[1], c=130 + 1.7 * size(out))
         else:
-            rec("g", lambda e: e.iota(out[0], pat, base, cm), [], out[1])
+            rec("g", lambda e: e.iota(out[0], pat, base, cm), [], out[1], c=140.0)
         return out
 
-    def dma(q, out, a):
+    def dma(q, out, a, c=2500.0, after=()):
         s = "d%d" % cnt["d"]
         cnt["d"] += 1
-        rec(q, lambda e: e.dma_start(sv(out), sv(a)).then_inc(T.sem[s], 16), st(a), st(out), ev=(s, 16), c=2500.0 + 2.0 * (size((sv(out),))))
+        return rec(q, lambda e: e.dma_start(sv(out), sv(a)).then_inc(T.sem[s], 16), st(a), st(out), ev=(s, 16), c=c, after=after)
 
     def send(trs):
         s = "l%d" % cnt["l"]
         cnt["l"] += 1
-        rec("g", lambda e: e.remote_dma_fused([RemoteDMATransfer(dst_ids=[dst_id(d, topo)], dma_engine_mask=bits(en), remote_sem=T.sem[sm], src=a[0], dst=da)
-                                              for d, da, a, sm, en in trs], local_sem=T.sem[s]),
-            st(*[x[2] for x in trs]), [], ev=(s, sum(len(x[4]) for x in trs)), c=600.0)
+        return rec("g", lambda e: e.remote_dma_fused([RemoteDMATransfer(dst_ids=[dst_id(d, topo)], dma_engine_mask=bits(en), remote_sem=T.sem[sm], src=a[0], dst=da)
+                                                     for d, da, a, sm, en in trs], local_sem=T.sem[s]),
+                   st(*[x[2] for x in trs]), [], ev=(s, sum(len(x[4]) for x in trs)), c=600.0)
 
-    def arrive(sem, n, toks, c=2800.0):
-        rec("x", None, [], toks, ev=(sem, n), c=c, after=lastg[-1:])
+    def arrive(sem, n, lands, c, after):
+        rec("x", None, [], st(*lands), ev=(sem, n), c=c, after=[after])
 
-    def a2a(src_of, dst_ap, sem):
-        for call in all_to_all_calls(core, cores, topo):
-            send([(d, dst_ap, src_of(cores.index(d)), sem, en) for d, en in call])
-
-    TGa = o(T.TG[:, 0:TW], "TG0", "TG1", "TG2", "TG3", "TG4", "TG5", "TG6")
-    PTa = o(T.PT[:, 0:TW], "PT0", "PT1", "PT2", "PT3", "PT4", "PT5", "PT6")
-    XTa = o(T.XT[:, 0:TW], "XT0", "XT1", "XT2", "XT3", "XT6")
-    SWa = o(T.SW[:, 0:SWW], "SW")
-    AND, SHR, SAR = A.bitwise_and, A.logical_shift_right, A.arith_shift_right
+    TGa, PTa, XTa, SWa = cols("TG", 0, TW), cols("PT", 0, TW), cols("XT", 0, TW), cols("SW", 0, SWW)
+    AND, SHR = A.bitwise_and, A.logical_shift_right
     ADD, SUB, MUL, MAX, MIN = A.add, A.subtract, A.mult, A.max, A.min
     EQ, GE, GT, LT = A.is_equal, A.is_ge, A.is_gt, A.is_lt
 
-    dma("y", o(T.lki[:], "lki"), T.lk[:])
-    dma("y", o(T.lii[:], "lii"), T.li[:])
-    dma("y", o(T.pni[:], "pni"), T.pn[:])
-    dma("y", o(T.PT[:, S2:S3], "PT2"), T.tp[:, 1024:2048])
-    dma("y", o(T.KR[:, S2:S3], "KR2"), T.tk[:, 1024:2048])
-    dma("y", o(T.KR[:, 0:S1], "KR0"), T.tk[:, 0:1024])
-    dma("y", o(T.PT[:, 0:S1], "PT0"), T.tp[:, 0:1024])
-    dma("y", o(T.dki[:], "dki"), T.dk[:])
-    for k in range(len(ops)):
-        ops[k]["c"] = 2600.0 if k == 0 or 3 <= k <= 6 else 400.0
-        ops[k]["soft"].update([k - 1] if k else [])
+    d = dma("y", o("lki"), T.lk[:], 2600.0)
+    for dst, src, c in ((o("pni"), T.pn[:], 300.0), (o("lii"), T.li[:], 300.0), (cols("KR", 1024, 2048), T.tk[:, 1024:2048], 1600.0), (cols("PT", S2, S5), T.tp[:, 1024:2048], 1600.0),
+                        (cols("KR", 0, 1024), T.tk[:, 0:1024], 1600.0), (cols("PT", 0, S3), T.tp[:, 0:1024], 1600.0), (o("dki"), T.dk[:], 700.0)):
+        d = dma("y", dst, src, c, [d])
     pidx = iota(i_("pidx", 1), [[1, 1]], 0, 1, False)
     IO = f("IO", 1024)
-    iota(sub("IO", 0, 320, tok=["IOa"]), [[1, 320]], 0, 0)
+    iota(sub("IO", 0, 320), [[1, 320]], 0, 0)
     gi16 = iota(f("gi16"), [[1, 8], [0, 16]], 0, 0)
-    DJ = iota(f("DJ"), [[16, 128]], int(BIG) + 4288, 1)
-    ri16 = iota(f("ri16"), [[0, 8], [1, 16]], 0, 0)
     DC = iota(h("DC", 512), [[0, 64], [CAP, 8]], 0, 0)
-    iota(sub("IO", 320, 1024, tok=["IOb"]), [[1, 704]], 320, 0)
-    IO = o(IO[0], "IOa", "IOb")
+    DJs = iota(f("DJs"), [[16, 128]], int(BIG) + 4288, 1)
+    ri16 = iota(f("ri16"), [[0, 8], [1, 16]], 0, 0)
+    iota(sub("IO", 320, 1024), [[1, 704]], 320, 0)
 
     def io(a, b):
-        return sub("IO", a, b, tok=["IOa"])
-    boost[0] = U3
+        return sub("IO", a, b)
+    boost[0] = 4 * CFG["u3"]
+    ms(cols("SW", 0, 2560), 0.0)
+    ms(o("T2"), 0.0)
+    ms(h("OH", 9 * OS), 0.0)
+    boost[0] = CFG["u3"]
     pr = cp(f("pr", 1), ts(i_("pri", 1), pidx, 15, AND))
     pg = cp(f("pg", 1), ts(i_("pgi", 1), pidx, 4, SHR))
     pf = cp(f("pf", 1), pidx)
-    ts(f("M16", 16), io(0, 16), pr, EQ)
-    Y = ts(h("Y", 144), io(0, 144), ts(f("y15", 1), pg, 16.0, MUL, 15.0, ADD), EQ)
-    for r in range(16):
-        act(o(T.Z[:, r, 0:130], "Z%d" % r), sub("Y", 13, 143), F.Copy, scale=sub("M16", r, r + 1))
-
-    def sumto(r):
-        return sub("Y", 15 - r, 143 - r)
-    BLK = ts(h("BLK"), gi16, pg, EQ)
     D = ts(f("D"), io(0, 128), pf, SUB)
     ID = ts(h("ID"), D, 0.0, EQ)
+    BLK = ts(h("BLK"), gi16, pg, EQ)
     LS = tt(h("LS"), ts(h("lsa"), D, 0.0, GT), BLK, MUL)
     LB = tt(h("LB"), ts(h("lba"), D, 0.0, EQ, BIG, MUL), LS, ADD)
-    f("MK", 4)
-    for r in range(RO):
-        ts(sub("MK", r, r + 1, tok=["MK%d" % r]), pr, 3.0, EQ, 524288.0 * (r + 1), MUL)
     RS8 = ms(h("RS8", 512), 1.0)
     ms(sub("RS8", 0, 512, 8), 0.0)
-    boost[0] = 4 * U3
-    ms(o(T.SW[:, 0:2560], "SW"), 0.0)
-    ops[-1]["c"] /= 2
+    RSM = ms(h("RSM", 7 * OS), 1.0)
+    ms(sub("RSM", 0, 7 * OS, OS), 0.0)
+    n0i = o("pni")
+    n0 = cp(f("n0", 1), n0i)
+    n288 = ts(f("n288", 1), n0, float(WIN), ADD, 8192.0, MIN)
+    d0 = ts(f("d0", 1), ts(i_("d0i", 1), n0i, 1023, AND), -1.0, MUL, 1024.0, ADD)
+    img = cp(f("img"), o("lii"))
+    KI = ts(i_("KI"), o("lki"), 6 * U + BIG, ADD)
+    DJ = cp(ps(6, 0, 128), DJs)
+    C, diags = {}, {}
+
+    def dg(v, wide=False):
+        if (v, wide) not in diags:
+            nm = "dg%d" % len(diags)
+            diags[(v, wide)] = act((f if wide else h)(nm), ID, F.Copy, scale=float(v))
+        return diags[(v, wide)]
+    IDF = dg(1, True)
+    nn0 = act(f("nn0", 1), n0, F.Copy, scale=-1.0)
+    th0 = act(f("th0", 1), n0, bias=0.5, scale=-1.0)
+    th1 = ts(f("th1", 1), d0, float(WIN), MIN, n0, ADD)
+    th1 = act(f("th1b", 1), th1, bias=0.5, scale=-1.0)
+    th2 = act(f("th2", 1), n0, bias=WIN - 0.5)
+    dh = act(h("dh", 1), d0, F.Copy, scale=0.5)
+    dl = ts(f("dl", 1), d0, 0.5, MUL, dh, SUB)
+    DH = act(h("DH"), ID, F.Copy, scale=act(f("dhf", 1), dh, F.Copy))
+    DL = act(h("DL"), ID, F.Copy, scale=dl)
+    C128 = act(h("C128", 160), io(0, 160), bias=128.0, scale=0.0)
+    for v in (-1024, 1024 + WS, WS, 512, CAP, -8 * CAP, (BIG + CAP) / 128):
+        dg(v)
+    Y = ts(h("Y", 144), io(0, 144), ts(f("y15", 1), pg, 16.0, MUL, 15.0, ADD), EQ)
+    f("MK", 4)
+    for r in range(RO):
+        ts(sub("MK", r, r + 1), pr, 3.0, EQ, 256.0 * (r + 1), MUL)
+    act(h("YC", 144), Y, F.Copy, scale=ts(f("yc", 1), pr, 2.0, LT))
+    act(h("YT", 144), Y, F.Copy, scale=ts(f("yt", 1), cp(f("p2f", 1), ts(i_("p2i", 1), pidx, 1, SHR, 7, AND)), 1.0, EQ))
     boost[0] = 0.0
-    h("R", 1032)
-    ms(sub("R", 0, 8, tok=["R0"]), 0.0)
-    ms(o(T.SQ[:, 0:8, 20:24], "SQo0"), 0)
-    ms(o(T.SQ[:, 8:24, 20:24], "SQo1", "SQo2"), 0)
-    n0 = cp(f("n0", 1), o(T.pni[:], "pni"))
-    n288 = ts(f("n288", 1), n0, float(WIN), ADD)
-    cn = ts(f("cn", 1), n0, -1.0, MUL, float(S3), ADD)
-    img = cp(f("img"), o(T.lii[:], "lii"))
+    ms(o("SQ", slice(None), slice(40, 48) if par else slice(0, 8)), 0)
     NN = [n0] + [f("n%d" % (r + 1), 1) for r in range(RO)]
-    C = {}
+
+    def sumto(r, nm="Y"):
+        return sub(nm, 15 - r, 143 - r)
 
     def late_consts():
+        ts(f("M16", 16), io(0, 16), pr, EQ)
+        for r in range(16):
+            act(o("BC", r), BLK, F.Copy, scale=sub("M16", r, r + 1))
         C["BLKF"] = act(f("BLKF"), BLK, F.Copy)
-        C["LI"] = tt(h("LI"), LS, ID, ADD)
         C["GIF"] = ts(f("GIF", 8), io(0, 8), pg, EQ)
-        C["GIB"] = ts(h("GIB", 8), io(0, 8), pg, EQ, P20, MUL)
+        C["GIB"] = ts(h("GIB", 8), io(0, 8), pg, EQ, 8 * U, MUL)
         C["HM"] = ts(f("HM", 4), io(0, 4), cp(f("p4", 1), ts(i_("p4i", 1), pidx, 2, SHR, 3, AND)), EQ)
         C["kA"] = ts(f("kA", 18), io(0, 18), 16.0, MUL, pr, ADD)
         C["KB"] = act(f("KB", 8), sub("kA", 0, 8), bias=-0.5, scale=-1.0)
         C["DG"] = ts(h("DG"), ri16, pr, EQ, P21, MUL)
         C["RS16"] = act(f("RS16"), ri16, F.Sign)
-        C["C128"] = act(h("C128", 320), io(0, 320), bias=128.0, scale=0.0)
-        C["ONE"] = ms(f("ONE", 8), 1.0)
+        C["ONE"] = act(f("ONE", 8), io(0, 8), bias=1.0, scale=0.0)
+        C["IO1"] = cp(ps(6, 128, 256), io(1, 129))
         C["DM"] = f("DM", 32)
-        for k, v in enumerate((DUMP - OWN, DUMP + 128 - LOW, DUMP - NXT, DUMP - PRV)):
+        for k, v in enumerate((DUMP + 128 - C1, DUMP - C0, DUMP - C2, DUMP - C3)):
             act(sub("DM", 8 * k, 8 * k + 8), sub("kA", 0, 8), bias=float(v))
         h("R2", 336)
-        ms(sub("R2", 0, 1, tok=["R2z"]), 0.0)
+        ms(sub("R2", 0, 1), 0.0)
         f("cumM", 336)
-        ms(sub("cumM", 320, 336, tok=["cumz"]), 0.0)
-        ms(o(T.CAT[:, :, 320:336], "CATz"), 0.0)
-        h("EQ", 2624)
-        f("PR", 2624)
-        ms(sub("EQ", 2560, 2624, tok=["EQ5"]), 0.0)
-        ms(sub("PR", 2560, 2624, tok=["PR5"]), 0.0)
-        ms(o(T.W[:, 2560:2576], "Wz"), 0.0)
-        C["IDF"] = act(f("IDF"), ID, F.Copy)
-        C["ID2F"] = act(f("ID2F"), ID, F.Copy, scale=2.0)
-        for nm, v in (("I512", 512.0), ("I144", 144.0), ("I2n", -2.0), ("I4096", 4096.0), ("I4608", 4608.0), ("I8192n", -8192.0)):
-            C[nm] = act(h(nm), ID, F.Copy, scale=v)
-        act(h("Y2", 144), Y, F.Copy, scale=2.0)
+        act(sub("cumM", 320, 336), io(0, 16), F.Copy, scale=0.0)
+        ms(o("CAT", slice(None), slice(320, 336)), 0.0)
+        act(cols("W", 2560, 2576), io(0, 16), F.Copy, scale=0.0)
+        act(h("YN", 144), Y, F.Copy, scale=-U)
         C["LSI"] = tt(h("LSI"), LS, ID, SUB)
         C["DG14"] = act(h("DG14"), C["DG"], F.Copy, scale=1.0 / 128)
         C["KF"] = act(h("KF"), io(0, 128), F.Copy, scale=1.0 / 128)
         C["kF"] = act(f("kF", 8), sub("kA", 0, 8), F.Copy, scale=1.0 / 128)
         f("dk2", 384)
-        ts(sub("dk2", 0, 384), o(T.dki[:], "dki"), P20, ADD)
-        ms(o(T.SR[:, :, 3:12:4], "SRz"), 0.0)
-        ms(o(T.SR[:, :, 12:16], "SRy"), 0.0)
-        act(o(T.TG[:, DUMP:TW], "TG6"), io(0, 256), F.Copy, scale=0.0)
-        act(o(T.TG[:, S5:DUMP], "TG5"), io(0, WIN), F.Copy, scale=0.0)
-        ms(o(T.PT[:, S5:TW], "PT5", "PT6"), 0)
-        act(o(T.XT[:, DUMP:TW], "XT6"), io(0, 256), F.Copy, scale=0.0)
-        ms(o(T.SO[:], "SO"), 0.0)
+        for r in range(RO):
+            ts(sub("dk2", 128 * r, 128 * r + 128), cols("dki", 128 * r, 128 * r + 128), (RO - 1 - r) * 2 * U + BIG, ADD)
+        act(o("SR"), IO, F.Copy, scale=0.0)
+        act(cols("TG", DUMP, TW), io(0, 256), F.Copy, scale=0.0)
+        ms(cols("PT", DUMP, TW), 0)
+        act(cols("XT", DUMP, TW), io(0, 256), F.Copy, scale=0.0)
+        act(o("SO"), io(0, 4), F.Copy, scale=0.0)
+        for a in (S3, S4, S5):
+            act(cols("XT", a, a + WIN), io(0, WIN), bias=n0)
+        for a, r in ((0, t), (S2, (t - 1) % N), (S1, t)):
+            act(cols("XT", a, a + 1024), IO, bias=float(1024 * r))
 
-    KH, PH = o(T.KR[:, S2:S3], "KR2"), o(T.PT[:, S2:S3], "PT2")
-    hs = relays(core, prv, cores, topo)
-    if hs:
-        en = side_engines(core, hs[0], topo, cores)
-        send([(x, T.HB[:], o(T.PT[:, S2 + 512 * k:S2 + 512 * (k + 1)], "PT2"), "aH", en[k * len(en) // 2:(k + 1) * len(en) // 2]) for k, x in enumerate(hs)]
-             + [(prv, T.KR[:, S1 + 512 * k:S1 + 512 * (k + 1)], o(T.KR[:, S2 + 512 * k:S2 + 512 * (k + 1)], "KR2"), "aK", halves(core, prv, topo)[k]) for k in range(2)])
-    else:
-        ea, eb = halves(core, prv, topo)
-        send([(prv, T.KR[:, S1:S2], KH, "aK", ea), (prv, T.PT[:, S1:S2], PH, "aP", eb)])
-    hn = relays(nxt, core, cores, topo)
-    arrive("aK", len(topo.engines(nxt, core)) if hn else len(halves(nxt, core, topo)[0]), ["KR1"], LK)
-    arrive("aP", sum(len(topo.engines(x, core)) for x in hn) if hn else len(halves(nxt, core, topo)[1]), ["PT1"], 19000.0)
-    na = a2a_count(core, cores, topo)
+    def homes(r):
+        for k, b in enumerate((3, 7)):
+            act(ps(b, 0, 512), io(512 * k, 512 * k + 512), bias=float(1024 * r))
+
+    def relative(a, z):
+        for k, b in enumerate((3, 7)):
+            tt(cols("TG", a + 512 * k, a + 512 * k + 512), cols("KR", z + 512 * k, z + 512 * k + 512), ps(b, 0, 512), SUB)
+
+    def mirror_out():
+        hs, hn = relays(core, prv, cores, topo), relays(nxt, core, cores, topo)
+        if hs:
+            en = side_engines(core, hs[0], topo, cores)
+            s1 = send([(x, T.HB[:], cols("PT", S2 + 512 * k, S2 + 512 * (k + 1)), "aH", en[k * len(en) // 2:(k + 1) * len(en) // 2]) for k, x in enumerate(hs)])
+        else:
+            s1 = send([(prv, T.PT[:, S1:S4], cols("PT", S2, S5), "aP", halves(core, prv, topo)[1])])
+        homes((t - 1) % N)
+        relative(S2, 1024)
+        s2 = send([(prv, T.TG[:, S1:S4], cols("TG", S2, S5), "aK", topo.engines(core, prv) if hs else halves(core, prv, topo)[0])])
+        arrive("aP", sum(len(topo.engines(x, core)) for x in hn) if hn else len(halves(nxt, core, topo)[1]), [cols("PT", S1, S4)], CFG["lp"], s1)
+        arrive("aK", len(topo.engines(nxt, core)) if hn else len(halves(nxt, core, topo)[0]), [cols("TG", S1, S4)], CFG["lk"], s2)
     L = {}
 
     def address(KI):
-        x = ts(i_("x"), KI, 8191, AND)
-        bit = ts(i_("bit"), KI, 13, SHR, 1, AND)
-        lt = tt(ps(7, 0, 128), x, img, LT)
+        w = ts(i_("w"), KI, 16383, AND)
         rk = ts(i_("rk"), KI, 10, SHR, 7, AND)
-        old = tt(ps(7, 128, 256), lt, bit, MUL)
-        boost[0] = U4
-        la = ts(ps(7, 256, 384), x, n288, LT, 288.0, MUL)
-        lb = ts(f("lb"), x, n0, LT, 736.0, MUL)
-        bo = tt(f("bo"), old, bit, ADD)
-        w = tt(ps(7, 384, 512), la, lb, ADD)
-        zz = ts(f("zz"), rk, 1024.0, MUL, cn, ADD)
-        c10 = ts(i_("c10"), KI, 1023, AND)
-        q = ts(ps(7, 0, 128), w, 288.0, EQ)
-        t2 = tt(ps(7, 256, 384), w, bo, MUL)
-        qz = tt(f("qz"), q, zz, MUL)
-        c1 = tt(ps(7, 384, 512), t2, c10, ADD)
-        tg = ts(i_("tg"), KI, 0xFE000, AND)
-        col = tt(ps(7, 0, 128), c1, qz, ADD)
-        p2 = ts(h("p2"), tg, 0.5, MUL)
-        p1 = cp(h("p1"), col)
+        old = tt(h("old"), w, img, LT)
+        s = L["s"] = tt(h("s"), old, rk, ADD)
+        boost[0] = CFG["u4"]
+        xf = L["xf"] = cp(f("xf"), ts(i_("x"), KI, 8191, AND))
+        hb = L["hb"] = ts(h("hb"), w, n288, LT)
+        sg0 = act(h("sg0"), xf, F.Sign, bias=th0)
+        sg1 = act(h("sg1"), xf, F.Sign, bias=th1)
+        sg2 = act(h("sg2"), xf, F.Sign, bias=th2, scale=-1.0)
+        col = ps(2, 128, 256)
+        mm(lin(col, [(IDF, xf), (dg(-1024), s), (dg(1024 + WS), old), (dg(WS), hb), (DH, sg0), (DL, sg0), (dg(512), sg1), (DH, sg2), (DL, sg2), (dg(512), sg2)]))
+        p2 = ts(h("p2"), ts(i_("tg"), KI, 0x1FE000, AND), 1.0 / 8192, MUL)
+        p1 = act(h("p1"), col, F.Copy)
         p0 = tt(h("p0"), col, p1, SUB)
+        L["pc"] = (p0, p1, p2)
         boost[0] = 0.0
-        to = ts(i_("to"), tt(i_("s"), old, rk, ADD), 7, AND)
-        L.update(x=x, bit=bit, to=to, pc=(p0, p1, p2))
 
     def spread(rho):
+        boost[0] = CFG["u4"]
+        mm([(ps(0, 128 * k, 128 * k + 128), L["pc"][k], ID, True, True) for k in range(3)])
+        for k in range(3):
+            act(o("T2", slice(k, 128, 16)), ps(0, 128 * k, 128 * k + 128), F.Copy)
         h("SRC", 2048)
-        for b in range(4):
-            mm([(ps(b % 2, 128 * (r % 4), 128 * (r % 4) + 128), o(T.Z[:, r, 2 - k:130 - k], "Z%d" % r), L["pc"][k], k == 0, k == 2) for r in range(4 * b, 4 * b + 4) for k in range(3)])
-            for r in range(4 * b, 4 * b + 4):
-                act(sub("SRC", r, 2048, 16, tok=["SRC%d" % r]), ps(b % 2, 128 * (r % 4), 128 * (r % 4) + 128), bias=sub("MK", rho, rho + 1, tok=["MK%d" % rho]))
+        for b in range(2):
+            mm([(ps(q % 2, q // 2, 512, 8), o("T2", slice(None), q), sub("ID", 64 * b, 64 * b + 64), True, True) for q in range(16)])
+            for e in range(2):
+                act(sub("SRC", 1024 * b + e, 1024 * b + 1024, 2), ps(e, 0, 512), bias=sub("MK", rho, rho + 1))
+        boost[0] = 0.0
 
     def place():
-        h("OH", 1024)
-        tob = cp(h("tob"), L["to"])
-        for d in range(8):
-            ts(sub("OH", d, 1024, 8, tok=["OH%d" % d]), tob, float(d), EQ, c=110.0)
-        for d in range(8):
-            x = sub("OH", d, 1024, 8, tok=["OH%d" % d])
-            scan(sub("R", 8 + d, 1032, 8, tok=["R%d" % (d + 1)]), x, x, ADD, MAX, c=110.0)
-        thr = ts(ps(7, 256, 384), L["to"], float(CAP), MUL, BIG + CAP, ADD)
-        oh, rr = ["OH%d" % d for d in range(8)], ["R%d" % d for d in range(9)]
+        s = L["s"]
+
+        def oh(d, a=0, b=128):
+            return sub("OH", OS * d + 1 + a, OS * d + 1 + b)
+        for d in (0, 8, 1, 2, 3, 4, 5, 6, 7):
+            ts(oh(d), s, float(d), EQ)
+        h("R", 8 * OS)
+        scan(sub("R", 0, 129), sub("OH", 0, 129), sub("OH", 8 * OS, 8 * OS + 129), ADD, ADD)
+        scan(sub("R", OS, 8 * OS), RSM, sub("OH", OS, 8 * OS), MUL, ADD)
         for b in range(2):
-            out = ps(4 + b, 0, 512)
-            mm([(out, ID, DC, True, False), (out, LB, sub("OH", 512 * b, 512 * b + 512, tok=oh), False, False),
-                (out, BLK, sub("R", 512 * b, 512 * b + 512, tok=rr), False, True)])
+            items = [(ps(4 + b, 0, 512), ID, DC, True, False), (ps(4 + b, 0, 512, 8), LB, oh(8, 64 * b, 64 * b + 64), False, False)]
+            for d in range(8):
+                out = ps(4 + b, d, 512, 8)
+                items += [(out, LB, oh(d, 64 * b, 64 * b + 64), False, False), (out, BLK, sub("R", OS * d + 64 * b, OS * d + 64 * b + 64), False, d == 7)]
+            mm(items)
+        thr = ps(2, 256, 384)
+        mm(lin(thr, [(dg((BIG + CAP) / 128), sub("C128", 0, 128)), (dg(CAP), s), (dg(-8 * CAP), oh(8))]))
         f("MS", 1024)
         for b in range(2):
-            scan(sub("MS", 512 * b, 512 * b + 512, tok=["MS%d" % b]), RS8, ps(4 + b, 0, 512), MUL, MAX)
-        val = sub("MS", 7, 1024, 8, tok=["MS0", "MS1"])
-        ng = L["ng"] = tt(f("ng"), val, thr, GE)
-        mx = tt(f("mx"), tt(ps(7, 128, 256), ng, DJ, MUL), val, MAX)
+            scan(sub("MS", 512 * b, 512 * b + 512), RS8, ps(4 + b, 0, 512), MUL, MAX)
+        val = sub("MS", 7, 1024, 8)
+        ng = L["ng"] = tt(h("ng"), val, thr, GE)
+        mx = L["mx"] = tt(f("mx"), tt(ps(6, 256, 384), ng, DJ, MUL), val, MAX)
         ts(u("off"), mx, -BIG, ADD)
-        ts(u("off2"), mx, -BIG, ADD, 2560.0, MIN)
 
     def pack():
-        w = 128 // NPK
-        for j in range(NPK):
-            scat(SWa, sub("off", w * j, w * j + w), sub("SRC", 16 * w * j, 16 * w * (j + 1), tok=["SRC%d" % r for r in range(16)]))
+        w = 128 // CFG["npk"]
+        for j in range(CFG["npk"]):
+            scat(SWa, sub("off", w * j, w * j + w), sub("SRC", 16 * w * j, 16 * w * (j + 1)))
 
     def request(rho):
-        out = ps(6, 0, 160)
-        mm([(out, sumto(r), o(T.SW[:, r:2560:16], "SW"), r == 0, r == 15) for r in range(16)])
-        cp(o(T.SQ[:, 8 * rho:8 * rho + 8, 0:20], "SQ%d" % rho), out)
-        a2a(lambda d: o(T.SQ[:, 8 * rho + d, :], "SQ%d" % rho, "SQo%d" % rho), T.RQ[:, 8 * rho + t, :], "aQ%d" % rho)
-        cp(o(T.RQ[:, 8 * rho + t, :], "RQm%d" % rho), o(T.SQ[:, 8 * rho + t, :], "SQ%d" % rho, "SQo%d" % rho))
-        arrive("aQ%d" % rho, na, ["RQ%d" % rho], 4500.0)
+        ca, ta = (0, 20) if par else (28, 8)
+        for k in range(NP):
+            c = (me_c + 1 + k) % NP
+            b = k % 2
+            mm(lin(ps(b, 0, 40), [(sumto(q, "YC"), cols("SW", 640 * c + q, 640 * c + 640, 16)) for q in range(16)])
+               + lin(ps(b, 40, 80), [(sumto(q, "YT"), cols("SW", 640 * c + q, 640 * c + 640, 16)) for q in range(16)]))
+            z = slice(8 * rho + 2 * c, 8 * rho + 2 * c + 2)
+            cp(o("SQ", z, slice(ca, ca + 20)), ps(b, 0, 40))
+            cp(o("SQ", z, slice(ta, ta + 20)), ps(b, 40, 80))
+            s = send([(cores[d], T.RQ[:, 4 * rho + me_c, 48 * par:48 * par + 48], o("SQ", 8 * rho + d), "aQ%d%d" % (rho, k), en) for d, en in pair_call(core, pairs[c], cores, topo)])
+            cs = (me_c - 1 - k) % NP
+            if cs == me_c:
+                cp(o("RQ", 4 * rho + me_c, slice(48 * par, 48 * par + 48)), o("SQ", 8 * rho + t))
+                arrive("aQ%d%d" % (rho, k), pair_count(t, pairs[cs], cores, topo), [o("RQ", 4 * rho + cs, slice(48 - 48 * par, 96 - 48 * par))], CFG["near"], s)
+            else:
+                arrive("aQ%d%d" % (rho, k), pair_count(t, pairs[cs], cores, topo), [o("RQ", 4 * rho + cs)], CFG["far"], s)
 
     def lane_prep(rho, KI):
-        dk = sub("dk2", 128 * rho, 128 * rho + 128)
-        if rho == 0:
-            KI = ts(i_("KI"), KI, P20, ADD)
-        d2 = tt(ps(7, 384, 512), tt(ps(7, 256, 384), KI, dk, SUB), L["ng"], MUL)
-        L["base"] = tt(f("base"), d2, dk, ADD)
+        ts(u("off2"), L["mx"], -BIG, ADD, 2560.0, MIN)
+        gate = act(ps(2, 384, 512), L["ng"], bias=-16 * U, scale=16 * U)
+        L["base"] = tt(f("base"), tt(ps(6, 384, 512), KI, gate, ADD), sub("dk2", 128 * rho, 128 * rho + 128), MAX)
 
     def image(rho, out):
-        nw = tt(ps(7, 128, 256), ts(ps(7, 0, 128), L["x"], NN[rho], LT), L["bit"], MUL)
-        fw = tt(f("fw"), nw, L["ng"], GT)
-        tt(out, tt(ps(7, 0, 128), ts(ps(7, 256, 384), L["x"], 1.0, ADD), fw, MUL), img, MAX)
+        nb = act(f("nb", 1), NN[rho], bias=16385.0, scale=-1.0)
+        mm(lin(ps(4, 128, 256), [(IDF, L["xf"]), (dg(-16384), L["hb"]), (dg(16384), L["ng"])]))
+        no = act(h("imno"), ps(4, 128, 256), F.Relu, bias=nb)
+        mm(lin(ps(4, 256, 384), [(IDF, L["xf"]), (dg(1.0 / 128), sub("C128", 0, 128)), (dg(-16384), no)]))
+        tt(out, ps(4, 256, 384), img, MAX)
+
+    def unpack_block(rho, k):
+        c = (me_c + 1 + k) % NP
+        ans = cols("RR", 192 * rho + 48 * c, 192 * rho + 48 * c + 48)
+        z = slice(16 * c, 16 * c + 16)
+        copy = cp if k in CFG["sv"] else lambda a, b: act(a, b, F.Copy)
+        hi = copy(o("SR", z, slice(0, 12, 4)), ans)
+        r1 = tt(f("r1%d" % k, 48), ans, hi, SUB)
+        mid = copy(o("SR", z, slice(1, 12, 4)), r1)
+        tt(o("SR", z, slice(2, 12, 4)), r1, mid, SUB)
+        b, a0 = k % 2, 256 * (k // 2)
+        mm([(ps(b, a0 + 128 * s, a0 + 128 * s + 128), o("SR", slice(16 * c + 8 * s, 16 * c + 8 * s + 8)), ID, True, True) for s in range(2)])
+        for s in range(2):
+            for j in range(3):
+                a, n, lo = CAP * (2 * c + s) + 128 * j, 64 if j == 2 else 128, 64 if j == 2 else 0
+                src = ps(b, a0 + 128 * s + lo, a0 + 128 * s + lo + n)
+                if k in CFG["wv"]:
+                    ts(cols("W", a, a + n), src, sub("HM", j, j + 1), MUL)
+                else:
+                    act(cols("W", a, a + n), src, F.Copy, scale=sub("HM", j, j + 1))
 
     def unpack(rho):
-        ans = o(T.RR[:, 192 * rho:192 * rho + 192], "RR%d" % rho, "RRm%d" % rho)
-        hi = cp(o(T.SR[:, :, 0:12:4], "SRa"), ans)
-        r1 = tt(ps(7, 0, 192), ans, hi, SUB)
-        mid = cp(o(T.SR[:, :, 1:12:4], "SRb"), r1)
-        tt(o(T.SR[:, :, 2:12:4], "SRc"), r1, mid, SUB)
-        rr = ["SRa", "SRb", "SRc", "SRz", "SRy"]
-        for b in range(2):
-            mm([(ps(b, 128 * k, 128 * k + 128), o(T.SR[:, 8 * (4 * b + k):8 * (4 * b + k + 1), :], *rr), ID, True, True) for k in range(4)])
-        wt = ["Wz"]
-        for d in range(8):
-            for k in range(3):
-                n = 64 if k == 2 else 128
-                a = CAP * d + 128 * k
-                wt.append("W%d_%d" % (d, k))
-                src = ps(d // 4, 128 * (d % 4), 128 * (d % 4) + n)
-                if d < 4 and WV:
-                    ts(o(T.W[:, a:a + n], wt[-1]), src, sub("HM", k, k + 1), MUL)
-                else:
-                    act(o(T.W[:, a:a + n], wt[-1]), src, F.Copy, scale=sub("HM", k, k + 1))
-        Wa = o(T.W[:, 0:2576], *wt)
+        for k in range(NP):
+            unpack_block(rho, k)
+        Wa, gv = cols("W", 0, 2576), CFG["gv"]
         h("GR", 2048)
-        cp(sub("GR", 0, 1024, tok=["GR0"]), ind(Wa, sub("off2", 0, 64)))
-        act(sub("GR", 1024, 2048, tok=["GR1"]), ind(Wa, sub("off2", 64, 128)))
-        val = ps(4, 0, 128)
-        mm([(val, sumto(r), sub("GR", r, 2048, 16, tok=["GR0", "GR1"]), r == 0, r == 15) for r in range(16)])
-        m = tt(f("nm"), ts(ps(7, 0, 128), val, P20, LT), L["base"], MUL)
-        return tt(i_("KI"), val, m, ADD)
-
-    def decode(rho):
-        rq = o(T.RQ[:, 8 * rho:8 * rho + 8, 0:20], "RQ%d" % rho, "RQm%d" % rho)
-        L["rq"] = rq
-        L["ci"] = ts(i_("ci", 160), rq, 4095, AND)
-        cp(u("offc", 160), L["ci"])
-        ts(h("tb", 160), ts(i_("ti", 160), rq, 12, SHR), -128.0 * (rho + 1), ADD, 8192.0, MUL)
+        cp(sub("GR", 0, 16 * gv), ind(Wa, sub("off2", 0, gv)))
+        act(sub("GR", 16 * gv, 2048), ind(Wa, sub("off2", gv, 128)))
+        val = ps(2, 0, 128)
+        mm(lin(val, [(sumto(r), sub("GR", r, 2048, 16)) for r in range(16)]))
+        return tt(i_("KI"), val, L["base"], MAX)
 
     def pointer(rho, parts):
-        mm([(ps(5, 480, 488), BLK, cp(h("ovb", 8), parts), True, True)])
-        v = red(f("v", 1), ps(5, 480, 488))
+        mm([(ps(7, 320, 328), BLK, cp(h("ovb", 8), parts), True, True)])
+        v = red(f("v", 1), ps(7, 320, 328))
         ts(NN[rho], ts(f("v2", 1), v, 96.0, MIN, NN[rho - 1], ADD), 8192.0, MIN)
 
-    def lookup(rho, fill):
+    def lookup(rho, k):
+        c = (me_c - 1 - k) % NP
+        a, top = 640 * c, S5 if rho == 0 else TW
         f("G", 2560)
-        for k in range(5):
-            act(sub("G", 512 * k, 512 * k + 512, tok=["G%d" % k]), ind(TGa, sub("offc", 32 * k, 32 * k + 32)))
-            mm([(ps(k, r, 512, 16), o(T.BC[:, r, :], "BC%d" % r), sub("tb", 32 * k, 32 * k + 32), True, True) for r in range(16)])
-        fill()
-        blocks = [(s, k) for s in range(8) for k in range(3)]
-        for k in range(5):
-            e = tt(sub("EQ", 512 * k, 512 * k + 512, tok=["EQ%d" % k]), sub("G", 512 * k, 512 * k + 512, tok=["G%d" % k]), ps(k, 0, 512), EQ)
-            tt(sub("PR", 512 * k, 512 * k + 512, tok=["PR%d" % k]), ind(PTa, sub("offc", 32 * k, 32 * k + 32)), e, MUL)
-            items = []
-            for s, j in blocks:
-                a = CAP * s + 128 * j
-                if min((a + 127) // 512, 4) == k:
-                    tk = range(a // 512, (a + 127) // 512 + 1)
-                    out = ps(6, 24 * s + j, 24 * s + 24, 3)
-                    items.append((out, sub("PR", a, a + 128, tok=["PR%d" % z for z in tk]), C["GIF"], True, False))
-                    items.append((out, sub("EQ", a, a + 128, tok=["EQ%d" % z for z in tk]), C["GIB"], False, True))
-            if k == 0:
-                mm(items, c=160 * len(items))
-                head = len(ops) - 1
-            else:
-                mm(items, cont=True, c=160 * len(items))
-                ops[-1]["deps"].update(ops[head]["deps"])
-            if k < 4 and k in PARTS:
-                reply(rho, k)
-
-    def reply(rho, k=4):
+        h("EQ", 2560)
+        f("PR", 2560)
+        offs = o("RQ", 4 * rho + c, slice(28, 68))
+        ts(o("TQ", slice(4 * c, 4 * c + 4)), o("RQ", 4 * rho + c, slice(8, 88)), -256.0 * (rho + 1) - 1.0, ADD, 8192.0, MUL)
+        act(sub("G", a, a + 640), ind(cols("TG", 0, top), offs))
+        b0 = 2 * (k % 2)
+        mm([(ps(b0 + q % 2, q // 2, 320, 8), o("BC", q), o("TQ", slice(4 * c, 4 * c + 4, 3)), True, True) for q in range(16)])
+        for e in range(2):
+            tt(sub("EQ", a + e, a + 640, 2), sub("G", a + e, a + 640, 2), ps(b0 + e, 0, 320), EQ)
+        tt(sub("PR", a, a + 640), ind(cols("PT", 0, top), offs), sub("EQ", a, a + 640), MUL)
+        b = 4 + k % 2
+        items = []
+        for s in range(2):
+            for j, z in enumerate((0, 128, 192)):
+                z += a + CAP * s
+                items += lin(ps(b, 24 * s + j, 24 * s + 24, 3), [(sub("PR", z, z + 128), C["GIF"]), (sub("EQ", z, z + 128), C["GIB"])])
+        mm(items)
         z = 192 * rho
-        a, b = PARTS[k]
-        tk = "SA%d_%d" % (rho, k)
-        act(o(T.SA[:, z + 24 * a:z + 24 * b], tk), o(T.B6[:, 24 * a:24 * b], "@6", "B6_0", "B6_1"), F.Copy)
-        send([(d, T.RR[:, z + 24 * t:z + 24 * t + 24], o(T.SA[:, z + 24 * cores.index(d):z + 24 * cores.index(d) + 24], tk), "aR%d" % rho, en)
-              for d, en in group_call(core, cores[a:b], cores, topo)])
-        if a <= t < b:
-            act(o(T.RR[:, z + 24 * t:z + 24 * t + 24], "RRm%d" % rho), o(T.SA[:, z + 24 * t:z + 24 * t + 24], tk), F.Copy)
-        if k == 4:
-            arrive("aR%d" % rho, group_count(core, cores, topo), ["RR%d" % rho], 3300.0)
+        act(cols("SA", z + 48 * c, z + 48 * c + 48), ps(b, 0, 48), bias=BIG)
+        s = send([(cores[d], T.RR[:, z + 24 * t:z + 24 * t + 24], cols("SA", z + 24 * d, z + 24 * d + 24), "aR%d%d" % (rho, k), en)
+                  for d, en in pair_call(core, pairs[c], cores, topo)])
+        cs = (me_c + 1 + k) % NP
+        if cs == me_c:
+            act(cols("RR", z + 24 * t, z + 24 * t + 24), ps(b, 24 * par, 24 * par + 24), bias=BIG)
+            x = t + 1 - 2 * par
+            arrive("aR%d%d" % (rho, k), pair_count(t, pairs[cs], cores, topo), [cols("RR", z + 24 * x, z + 24 * x + 24)], CFG["near"], s)
+        else:
+            arrive("aR%d%d" % (rho, k), pair_count(t, pairs[cs], cores, topo), [cols("RR", z + 48 * cs, z + 48 * cs + 48)], CFG["far"], s)
 
     def miss_pre(rho):
-        dn = tt(f("dn", 1), NN[rho], n0, SUB)
+        dn = L["dn"] = act(f("dn", 1), NN[rho], bias=nn0)
         th4 = act(f("th4", 1), dn, bias=S4 - 0.5)
         L["th3"] = act(f("th3", 1), dn, bias=0.5 - S3, scale=-1.0)
-        cf = cp(f("cf", 160), L["ci"])
-        code = L["code"] = act(f("code", 160), cp(f("vf", 160), L["rq"]), F.Relu, bias=1.0 - 524288.0 * (rho + 1))
-        sg = [act(h("sg0", 160), cf, F.Sign, bias=0.5 - S1), act(h("sg1", 160), cf, F.Sign, bias=S2 - 0.5, scale=-1.0),
-              act(h("sg2", 160), cf, F.Sign, bias=0.5 - S4), act(h("sg3", 160), cf, F.Sign, bias=th4, scale=-1.0)]
-        L["vl"] = act(h("vl", 160), code, F.Sign)
-        wt = [C["I512"], C["I512"], C["I144"], C["I144"]]
-        mm([(ps(5, 320, 480), wt[k], sg[k], k == 0, k == 3) for k in range(4)])
-        L["fl"] = act(h("fl", 160), ps(5, 320, 480), F.Sign)
-        mm([(ps(5, 160, 320), wt[k], sg[k], k == 0, False) for k in range(4)] + [(ps(5, 160, 320), C["IDF"], code, False, True)], c=1280)
+        cf = cp(f("cf", 160), o("RQ", slice(4 * rho, 4 * rho + 4), slice(28, 68)))
+        sa = act(h("sa", 160), cf, F.Sign, bias=0.5 - S1)
+        sb = act(h("sb", 160), cf, F.Sign, bias=th4, scale=-1.0)
+        for k, (nm, sgn, bias) in enumerate((("cF", 1, 2048.5 + WS - U), ("cN", -1, 2048.5))):
+            out = ps(7, 160 * k, 160 * k + 160)
+            mm([(out, IDF, cf, True, False), (out, dg(sgn * U / 2), sa, False, False), (out, dg(sgn * U / 2), sb, False, False)]
+               + [(ps(7, 160 * k + 40 * c, 160 * k + 40 * c + 40), dg(0.5), o("TQ", slice(4 * c, 4 * c + 4, 3)), False, c == NP - 1) for c in range(NP)])
+        for k, (nm, bias) in enumerate((("cF", 2048.5 + WS - U), ("cN", 2048.5))):
+            L[nm] = act(f(nm, 160), ps(7, 160 * k, 160 * k + 160), F.Relu, bias=bias)
 
     def miss(rho):
-        out = ps(5, 0, 160)
-        mm([(out, sub("Y2", 15 - r, 143 - r), sub("EQ", r, 2560, 16, tok=["EQ%d" % z for z in range(5)]), r == 0, False) for r in range(16)]
-           + [(out, C["I2n"], L["vl"], False, False), (out, ID, L["fl"], False, True)])
-        mf = act(f("mf", 160), act(f("mfa", 160), out, F.Abs, bias=1.0), F.Relu, bias=1.0, scale=-1.0)
-        mi = act(f("mn", 160), out, F.Relu, bias=-1.0, scale=-1.0)
-        sf = tt(o(T.SF[:, rho, :], "SF%d" % rho), ps(5, 160, 320), mf, MUL)
-        send([(nxt, T.CAT[:, rho, 160:320], sf, "aF%d" % rho, topo.engines(core, nxt))])
-        tt(o(T.CAT[:, rho, 0:160], "CN%d" % rho), mi, L["code"], MUL)
-        arrive("aF%d" % rho, len(topo.engines(prv, core)), ["CF%d" % rho])
+        out = ps(7, 328, 488)
+        mm(lin(out, [(dg(8192), C128)] + [(sumto(r, "YN"), sub("EQ", r, 2560, 16)) for r in range(16)]))
+        sf = tt(o("SF", rho), out, L["cF"], MIN)
+        s = send([(nxt, T.CAT[:, rho, 160:320], sf, "aF%d" % rho, topo.engines(core, nxt))])
+        tt(o("CAT", rho, slice(0, 160)), out, L["cN"], MIN)
+        arrive("aF%d" % rho, len(topo.engines(prv, core)), [o("CAT", rho, slice(160, 320))], CFG["far"], s)
 
-    def select(rho):
-        m = act(h("m", 320), o(T.CAT[:, rho, 0:320], "CN%d" % rho, "CF%d" % rho), F.Sign)
-        scan(sub("R2", 1, 321), m, C["C128"], ADD, MIN)
-        mm([(ps(6, 0, 320), BLK, sub("R2", 1, 321), True, True)])
-        mm([(ps(3, 0, 320), BLK, sub("R2", 0, 320, tok=["R2", "R2z"]), True, False), (ps(3, 0, 320), C["LI"], m, False, True)])
-        f("ACC", 8)
-        ns = 5 if rho == RO - 1 else 8
-        if ns < 8:
-            mm([(ps(2, 0, 320), BLK, sub("R2", 1, 321), True, True)])
-        for a in range(ns):
-            act(h("junk%d" % (a % 2), 320), ps(6, 0, 320), F.Sign, bias=sub("KB", a, a + 1), acc=sub("ACC", a, a + 1, tok=["ACC%d" % a]))
-        tt(sub("cumM", 0, 320), ps(3, 0, 320), m, MUL)
-        offk = u("offk", 8)
-        for a in range(ns, 8):
-            x = sub("PR", 512 * (a - ns), 512 * (a - ns) + 320, tok=["PR%d" % (a - ns)])
-            red(sub("ACC", a, a + 1, tok=["ACC%d" % a]), ts(x, ps(2, 0, 320), sub("kA", a, a + 1), GT, 0.5, SUB), 370.0)
-        if ns < 8:
-            ts(sub("offk", ns, 8), sub("ACC", ns, 8, tok=["ACC%d" % a for a in range(ns, 8)]), -1.0, MUL, 160.0, ADD)
-        ts(sub("offk", 0, ns), sub("ACC", 0, ns, tok=["ACC%d" % a for a in range(ns)]), -0.5, MUL, 160.0, ADD)
-        e = tt(f("e"), ind(sub("cumM", 0, 336, tok=["cumM", "cumz"]), offk), io(1, 129), EQ)
-        pc = tt(f("pc"), ind(o(T.CAT[:, rho, :], "CN%d" % rho, "CF%d" % rho, "CATz"), offk), e, MUL)
-        mm([(ps(6, 128, 256), C["BLKF"], pc, True, False), (ps(6, 128, 256), ID, C["DG"], False, True), (ps(6, 0, 128), C["BLKF"], pc, True, True)], c=1152)
+    def count(rho, k):
+        a = 160 * k
+        h("m", 320)
+        f("ACC", 16)
+        m = act(sub("m", a, a + 160), o("CAT", rho, slice(a, a + 160)), F.Sign)
+        scan(sub("R2", a + 1, a + 161), m, C128, ADD, MIN, sub("R2", a, a + 1) if k else 0.0)
+        nv = CFG["lastv"] if k and rho == RO - 1 else 0
+        mm([(ps(3, a, a + 160), BLK, sub("R2", a + 1, a + 161), True, True)])
+        if nv:
+            mm([(ps(2, 0, 160), BLK, sub("R2", a + 1, a + 161), True, True)])
+        mm(lin(ps(7, a, a + 160), [(BLK, sub("R2", a, a + 160)), (LB, m)]))
+        for j in range(8 - nv):
+            act(h("junk%d" % (j % 2), 160), ps(3, a, a + 160), F.Sign, bias=sub("KB", j, j + 1), acc=sub("ACC", 8 * k + j, 8 * k + j + 1))
+        for j in range(8 - nv, 8):
+            x = ts(f("jv%d" % j, 160), ps(2, 0, 160), sub("kA", j, j + 1), GT, 0.5, SUB)
+            ts(sub("ACC", 8 * k + j, 8 * k + j + 1), red(f("jr%d" % j, 1), x), 2.0, MUL)
+        act(sub("cumM", a, a + 160), ps(7, a, a + 160), F.Relu, bias=1.0 - BIG)
+
+    def pick(rho):
+        offk = ts(u("offk", 8), tt(f("acs", 8), sub("ACC", 0, 8), sub("ACC", 8, 16), ADD), -0.5, MUL, 160.0, ADD)
+        g1 = act(f("sg1_"), ind(sub("cumM", 0, 336), offk))
+        g2 = act(f("sg2_"), ind(o("CAT", rho), offk))
+        pc = tt(f("pc"), g2, tt(ps(6, 256, 384), g1, C["IO1"], EQ), MUL)
+        mm(lin(ps(7, 320, 448), [(C["BLKF"], pc), (ID, C["DG"])]))
+        mm([(ps(3, 320, 448), C["BLKF"], pc, True, True)])
 
     def cand_a(rho):
-        scan(f("cs"), C["RS16"], ps(6, 128, 256), MUL, MAX)
-        ca = ts(i_("ca", 8), sub("cs", 15, 128, 16), -P21 - 1.0, ADD)
+        scan(f("cs"), C["RS16"], ps(7, 320, 448), MUL, MAX)
+        ca = ts(i_("ca", 8), sub("cs", 15, 128, 16), 2047.5 - P21, ADD, 4095.0, MAX)
         col = ts(i_("colA", 8), ca, 4095, AND)
         u("offg", 16)
-        o1 = cp(sub("offg", 0, 8, tok=["og0"]), col)
+        o1 = cp(sub("offg", 8, 16), col)
+        cf = L["cf"] = cp(f("colf", 8), col)
         xg = L["xg"] = act(f("xg"), ind(XTa, o1))
         L["g1"] = act(f("g1"), ind(TGa, o1))
-        cf = L["cf"] = cp(f("colf", 8), col)
-        for nm, b, sc in (("p3u", L["th3"], 1.0), ("n4", S4 - 0.5, -1.0), ("p5", 0.5 - S5, 1.0), ("p6", 0.5 - DUMP, 1.0), ("n5", S5 - 0.5, -1.0), ("n2", S2 - 0.5, -1.0), ("p3", 0.5 - S3, 1.0)):
+        for nm, b, sc in (("a1", L["th3"], 1.0), ("a2", S1 - 0.5, -1.0), ("b1", 0.5 - S4, 1.0), ("b2", S2 - 0.5, -1.0), ("p6", 0.5 - DUMP, 1.0)):
             L[nm] = act(h("c" + nm, 8), cf, F.Sign, bias=b, scale=sc)
-        out = ps(6, 384, 392)
-        mm([(out, C["IDF"], cf, True, False)] + [(out, C["I144"], L[nm], False, k == 3) for k, nm in enumerate(("p3u", "n4", "n4", "p5"))], c=512)
-        o2 = cp(sub("offg", 8, 16, tok=["og1"]), out)
+        out = ps(7, 448, 456)
+        mm(lin(out, [(IDF, cf), (dg(WS // 2), L["a1"]), (dg(WS // 2), L["a2"]), (dg(-WS // 2), L["b1"]), (dg(-WS // 2), L["b2"])]))
+        o2 = cp(sub("offg", 0, 8), out)
         L["g2"] = act(f("g2"), ind(TGa, o2))
-        tg = ts(i_("tgB"), ts(i_("cb"), ps(6, 0, 128), -1.0, ADD), 12, SAR)
-        mm([(ps(2, 0, 128), C["IDF"], xg, True, False), (ps(2, 0, 128), ID, C["KF"], False, True)], c=640)
-        mm([(ps(3, 0, 128), C["IDF"], xg, True, False), (ps(3, 0, 128), ID, C["KF"], False, False), (ps(3, 0, 128), ID, C["DG14"], False, True)], c=768)
-        scan(f("ys_"), C["RS16"], ps(3, 0, 128), MUL, MAX)
+        tagb = act(h("tagb"), ps(3, 320, 448), bias=128.0, scale=1.0 / 4096)
+        L["tagv"] = act(h("tagv"), tagb, bias=-129.0)
+        mm(lin(ps(7, 0, 128), [(IDF, xg), (ID, C["KF"]), (ID, C["DG14"])]))
+        mm(lin(ps(3, 0, 128), [(IDF, xg), (ID, C["KF"])]))
+        scan(f("ys_"), C["RS16"], ps(7, 0, 128), MUL, MAX)
         b1 = act(f("yb1", 8), sub("ys_", 15, 128, 16), bias=-16384.0 - 1.0 / 256)
         tt(f("yb2", 8), C["kF"], b1, SUB)
         f("s1", 8)
         f("s2", 8)
         for a in range(8):
             for nm in ("1", "2"):
-                act(sub("junk%d" % (int(nm) - 1), 0, 16 * a + 16), ps(2, 0, 16 * a + 16), F.Sign, bias=sub("yb" + nm, a, a + 1), scale=-1.0 if nm == "1" else 1.0,
-                    acc=sub("s" + nm, a, a + 1, tok=["s%s_%d" % (nm, a)]))
-        cp(f("pg_", 256), ind(PTa, sub("offg", 0, 16, tok=["og0", "og1"])))
-        key = L["key"] = tt(i_("key"), ts(ps(6, 256, 384), tg, 8192.0, MUL), xg, ADD)
-        lo = ts(ps(6, 128, 256), ts(i_("klo"), key, 1023, AND), 1024.0, MUL)
-        npay = tt(ps(6, 256, 384), lo, ts(i_("khi"), key, 10, SAR), ADD)
-        L["dp"] = tt(f("dp"), npay, sub("pg_", 0, 128), SUB)
+                act(sub("junk%d" % (int(nm) - 1), 0, 16 * a + 16), ps(3, 0, 16 * a + 16), F.Sign, bias=sub("yb" + nm, a, a + 1), scale=-1.0 if nm == "1" else 1.0,
+                    acc=sub("s" + nm, a, a + 1))
+        L["pg"] = cp(f("pg_", 256), ind(PTa, sub("offg", 0, 16)))
+        rkb = act(h("rkb"), xg, bias=192.0 - 511.5 / 1024, scale=1.0 / 1024)
+        L["rkv"] = act(h("rkv"), rkb, bias=-192.0)
 
     def cand_b(rho, ovout):
-        out = ps(3, 128, 256)
-        xs = [] if rho == RO - 1 else [(out, C["ID2F"], L["xg"], False, False)]
-        mm([(out, C["IDF"], L["g1"], True, False)] + xs + [(out, C["IDF"], L["g2"], False, True)], c=1536)
+        out = ps(7, 128, 256)
+        mm(lin(out, [(IDF, L["g1"])] + ([] if rho == RO - 1 else [(dg(2, True), L["xg"])]) + [(IDF, L["g2"])]))
         emp = act(h("emp"), out, F.Relu, bias=-1.0, scale=-1.0)
-        mm([(ps(3, 256, 384), C["LSI"], emp, True, True)])
-        L["fs"] = act(f("fs"), ps(3, 256, 384), F.Relu, scale=-1.0)
-
-        def terms(out, start):
-            return [(out, C["IDF"], sub("s1", 0, 8, tok=["s1_%d" % a for a in range(8)]), start, False),
-                    (out, C["IDF"], sub("s2", 0, 8, tok=["s2_%d" % a for a in range(8)]), False, False), (out, ID, L["p6"], False, True)]
-        out = ps(3, 384, 392)
-        mm([(out, sumto(r), sub("emp", r, 128, 16), r == 0, False) for r in range(16)] + terms(out, False) + terms(ps(3, 392, 400), True), c=2200)
-        act(f("ov", 8), out, F.Relu, scale=-1.0, acc=f("ovs", 1))
-        L["tr"] = act(h("tr", 8), ps(3, 392, 400), F.Relu, scale=-1.0)
+        mm([(ps(7, 256, 384), C["LSI"], emp, True, True)])
+        L["nfs"] = act(h("nfs"), ps(7, 256, 384), F.Sign, bias=1.0)
+        terms = [(IDF, sub("s1", 0, 8)), (IDF, sub("s2", 0, 8)), (ID, L["p6"])]
+        mm(lin(ps(7, 384, 392), [(sumto(r), sub("emp", r, 128, 16)) for r in range(16)] + terms) + lin(ps(7, 392, 400), terms))
+        act(f("ov", 8), ps(7, 384, 392), F.Relu, scale=-1.0, acc=f("ovs", 1))
+        L["tr"] = act(h("tr", 8), ps(7, 392, 400), F.Relu, scale=-1.0)
         ovout(f("ovs", 1))
 
     def cand_d(rho):
-        up = "UP%d" % rho
-        fs = L["fs"]
-        items = []
-        for k, extra in enumerate(([], [("I4096", "n4"), ("I4096", "p5")], [("I4096", "n4"), ("I4096", "p5")],
-                                   [("I4608", "n2"), ("I4608", "p3"), ("I4096", "n5"), ("I144", "n5")])):
-            out = ps(3, 400 + 8 * k, 408 + 8 * k)
-            items += [(out, C["IDF"], L["cf"], True, False)] + [(out, C[a], L[b], False, False) for a, b in extra] + [(out, C["I8192n"], L["tr"], False, True)]
-        mm(items, c=1800)
-        tt(o(T.UP[:, rho, 256:288], up + "c"), ps(3, 400, 432), C["DM"], MIN)
-        tt(o(T.UP[:, rho, 0:128], up + "a"), tt(ps(2, 256, 384), ts(ps(2, 128, 256), L["key"], 1.0, ADD), fs, MUL), L["g1"], ADD)
-        f("nP", 256)
-        L["np1"] = tt(o(T.UP[:, rho, 128:256], up + "b"), tt(ps(2, 384, 512), L["dp"], fs, MUL), sub("pg_", 0, 128), ADD)
-        tk = [up + "a", up + "b", up + "c"]
-        trs = [(nxt, T.UA[:, rho, :], o(T.UP[:, rho, :], *tk), "aA%d" % rho, side_engines(core, nxt, topo, cores))]
+        nfs, xg = L["nfs"], L["xg"]
+        mm(lin(ps(3, 128, 256), [(IDF, sub("pg_", 0, 128)), (dg(P21), nfs)]) + lin(ps(3, 256, 384), [(IDF, sub("pg_", 128, 256)), (dg(P21), nfs)]))
+        act(o("UP", rho, slice(0, 128)), ps(3, 128, 256), F.Relu, bias=-P21)
+        kept = act(f("kept"), ps(3, 256, 384), F.Relu, bias=-P21)
+        s4 = [(IDF, L["cf"]), (dg(-4096), L["b1"]), (dg(-4096), L["b2"]), (dg(-8192), L["tr"])]
+        mm(lin(ps(7, 0, 128), [(dg(8192), L["tagv"])] + ([(IDF, xg)] if rho == RO - 1 else []) + [(dg(-P21), nfs)])
+           + lin(ps(7, 128, 256), [(dg(-U), L["rkv"]), (dg(1024, True), xg), (ID, L["rkv"]), (dg(8), L["tagv"]), (dg(-P21), nfs)])
+           + lin(ps(7, 400, 408), s4) + lin(ps(7, 408, 416), [(IDF, L["cf"]), (dg(-8192), L["tr"])]) + lin(ps(7, 416, 424), s4)
+           + lin(ps(7, 424, 432), [(IDF, L["cf"]), (dg(4096), L["b2"]), (dg(-8192), L["tr"])]))
+        tt(o("UP", rho, slice(384, 416)), ps(7, 400, 432), C["DM"], MIN)
+        tt(o("UP", rho, slice(256, 384)), ps(7, 0, 128), L["g1"], MAX)
+        L["np1"] = tt(o("UP", rho, slice(128, 256)), ps(7, 128, 256), kept, MAX)
+        msg = o("UP", rho, slice(128, 416))
+        trs = [(nxt, T.UA[:, rho, :], msg, "aA%d" % rho, side_engines(core, nxt, topo, cores))]
         if rho < RO - 1:
-            trs.append((prv, T.UB[:, rho, :], o(T.UP[:, rho, :], *tk), "aB%d" % rho, side_engines(core, prv, topo, cores)))
-        send(trs)
-        arrive("aA%d" % rho, len(side_engines(prv, core, topo, cores)), ["UA%d" % rho])
+            trs.append((prv, T.UB[:, rho, :], msg, "aB%d" % rho, side_engines(core, prv, topo, cores)))
+        s = send(trs)
+        arrive("aA%d" % rho, len(side_engines(prv, core, topo, cores)), [o("UA", rho)], CFG["far"], s)
         if rho < RO - 1:
-            arrive("aB%d" % rho, len(side_engines(nxt, core, topo, cores)), ["UB%d" % rho])
+            arrive("aB%d" % rho, len(side_engines(nxt, core, topo, cores)), [o("UB", rho)], CFG["far"], s)
 
     def insert(rho):
         u("offs", 16)
-        up = "UP%d" % rho
-        o1 = ts(sub("offs", 0, 8, tok=["os0"]), o(T.UP[:, rho, 256:264], up + "c"), OWN, ADD)
-        scat(TGa, o1, o(T.UP[:, rho, 0:128], up + "a"))
-        tt(sub("nP", 128, 256, tok=["nP1"]), sub("pg_", 128, 256), act(f("nfs"), L["fs"], bias=1.0, scale=-1.0), MUL)
-        act(sub("nP", 0, 128, tok=["nP0"]), L["np1"], F.Copy)
-        ts(sub("offs", 8, 16, tok=["os1"]), o(T.UP[:, rho, 264:272], up + "c"), LOW, ADD)
-        scat(PTa, sub("offs", 0, 16, tok=["os0", "os1"]), sub("nP", 0, 256, tok=["nP0", "nP1"]))
+        o1 = ts(sub("offs", 8, 16), o("UP", rho, slice(392, 400)), C0, ADD)
+        scat(TGa, o1, o("UP", rho, slice(256, 384)))
+        ts(sub("offs", 0, 8), o("UP", rho, slice(384, 392)), C1, ADD)
+        scat(PTa, sub("offs", 0, 16), o("UP", rho, slice(0, 256)))
 
     def mirror(rho, buf, a, c):
-        tk = "%s%d" % (buf, rho)
-        off = ts(u("offm" + buf, 8), o(T[buf][:, rho, a:a + 8], tk), c, ADD)
-        scat(TGa, off, o(T[buf][:, rho, 0:128], tk))
-        scat(PTa, off, o(T[buf][:, rho, 128:256], tk))
+        off = ts(u("offm" + buf, 8), o(buf, rho, slice(a, a + 8)), c, ADD)
+        scat(TGa, off, o(buf, rho, slice(128, 256)))
+        scat(PTa, off, o(buf, rho, slice(0, 128)))
 
-    def homes_psum():
-        for b in range(4):
-            act(ps(HB_[b], 0, 512), sub("IO", 512 * (b % 2), 512 * (b % 2) + 512, tok=["IOa", "IOb"]), bias=float(1024 * (t if b < 2 else (t - 1) % N)))
-
-    KI = o(T.lki[:], "lki")
+    urgent(CFG["u2"], mirror_out)
     address(KI)
     spread(0)
     place()
     late_consts()
-    homes_psum()
-    nn0 = act(f("nn0", 1), n0, bias=-1.0, scale=-1.0)
-    NX = act(f("NX", WIN), io(0, WIN), bias=nn0, scale=-1.0)
-    for r in range(16):
-        act(o(T.BC[:, r, :], "BC%d" % r), BLK, F.Copy, scale=sub("M16", r, r + 1))
-    for k in range(3):
-        act(o(T.XT[:, S3 + WIN * k:S3 + WIN * (k + 1)], "XT3"), io(0, WIN), bias=n0)
-    for k in range(3):
-        act(o(T.XT[:, 1024 * k:1024 * k + 1024], "XT%d" % k), IO, bias=float(1024 * (t if k < 2 else (t - 1) % N)))
     pack()
-    for b in (2, 3):
-        tt(o(T.TG[:, S2 + 512 * (b - 2):S2 + 512 * (b - 1)], "TG2"), o(T.KR[:, S2 + 512 * (b - 2):S2 + 512 * (b - 1)], "KR2"), ps(HB_[b], 0, 512), SUB)
     request(0)
+    homes(t)
+    relative(0, 0)
     xw = ts(f("xw", 18), C["kA"], n0, ADD, -1024.0 * t, ADD)
     offw = ts(u("offw", 18), xw, 0.0, MAX, 1023.0, MIN)
-    kg = cp(i_("kg", WIN), ind(o(T.KR[:, 0:S1], "KR0"), offw))
-    pgw = cp(f("pgw", WIN), ind(o(T.PT[:, 0:S1], "PT0"), offw))
-    mv = ts(ps(2, 0, WIN), ts(i_("kb", WIN), kg, -2147475456, AND), 8192.0, EQ)
-    k1 = ts(f("wk1", WIN), kg, 1.0, ADD)
-    wa = tt(ps(3, 0, WIN), mv, k1, MUL)
-    t4_ = tt(o(T.TG[:, S4:S5], "TG4"), wa, NX, ADD)
-    p4_ = tt(o(T.PT[:, S4:S5], "PT4"), mv, pgw, MUL)
+    NX = act(f("NX", WIN), cols("XT", S3, S1), bias=-1.0, scale=-1.0)
+    kg = cp(i_("kg", WIN), ind(cols("KR", 0, 1024), offw))
+    pgw = cp(f("pgw", WIN), ind(cols("PT", 0, S3), offw))
+    gw = act(f("gw", WIN), ind(cols("TG", 0, S3), offw))
+    mv = ts(h("mv", WIN), ts(i_("kb", WIN), kg, -2147475456, AND), 8192.0, EQ)
+    nmv = act(h("nmv", WIN), mv, bias=1.0, scale=-1.0)
+    mvp, nmvp = act(ps(4, 0, WIN), mv, F.Copy), act(ps(5, 0, WIN), nmv, F.Copy)
+    mm(lin(ps(3, 0, WIN), [(IDF, gw), (dg(-P21), nmv)]))
+    mm(lin(ps(7, 0, WIN), [(IDF, gw), (dg(-P21), mv)]))
+    t4 = tt(cols("TG", S4, S2), ps(3, 0, WIN), NX, MAX)
+    p4 = tt(cols("PT", S4, S2), pgw, mvp, MUL)
     ea, eb = halves(core, nxt, topo)
-    send([(nxt, T.WT[:], t4_, "aW", ea), (nxt, T.WQ[:], p4_, "aW", eb)])
-    arrive("aW", len(topo.engines(prv, core)), ["WT"])
-    tt(o(T.TG[:, S3:S4], "TG3"), tt(ps(2, 0, WIN), k1, wa, SUB), NX, ADD)
-    tt(o(T.PT[:, S3:S4], "PT3"), pgw, p4_, SUB)
-    for k in range(4):
-        tt(o(T.TG[:, 512 * k:512 * k + 512], "TG%d" % (k // 2)), o(T.KR[:, 512 * k:512 * k + 512], "KR%d" % (k // 2)), ps(k % 2, 0, 512), SUB)
+    s = send([(nxt, T.TG[:, S5:DUMP], t4, "aW", ea), (nxt, T.PT[:, S5:DUMP], p4, "aW", eb)])
+    arrive("aW", len(topo.engines(prv, core)), [cols("TG", S5, DUMP), cols("PT", S5, DUMP)], CFG["far"], s)
+    tt(cols("TG", S3, S1), ps(7, 0, WIN), NX, MAX)
+    tt(cols("PT", S3, S1), pgw, nmvp, MUL)
 
     for rho in range(RO):
         last = rho == RO - 1
-        decode(rho)
-
-        def fill(rho=rho):
-            if rho:
-                urgent(U2, pointer, rho, o(T.RQ[:, 8 * rho:8 * rho + 8, 20], "RQ%d" % rho, "RQm%d" % rho))
-            urgent(U2, miss_pre, rho)
-        lookup(rho, fill)
-        if last:
-            urgent(U7, miss, rho)
-        reply(rho)
-        if not last:
-            urgent(U2, miss, rho)
         lane_prep(rho, KI)
-        image(rho, o(T.OY[:, 128:256], "OYi") if last else img)
-        if rho == 0:
-            act(o(T.TG[:, S5:DUMP], "TG5"), o(T.WT[:], "WT"), F.Copy)
-            cp(o(T.PT[:, S5:DUMP], "PT5"), o(T.WQ[:], "WT"))
+        for k in range(NP):
+            lookup(rho, k)
+        if rho:
+            urgent(CFG["u2"], pointer, rho, o("RQ", slice(4 * rho, 4 * rho + 4), slice(0, 96, 88)))
+        urgent(CFG["u2"], miss_pre, rho)
+        urgent(CFG["u7"] if last else CFG["u2"], miss, rho)
+        image(rho, cols("OY", 128, 256) if last else img)
         if not last:
-            urgent(U1, select, rho)
-            urgent(U1, cand_a, rho)
-            urgent(U1, cand_b, rho, lambda s, rho=rho: ts(o(T.SQ[:, 8 * rho + 8:8 * rho + 16, 20], "SQo%d" % (rho + 1)), C["ONE"], s, MUL))
-            if AB:
-                urgent(U1, cand_d, rho)
+            for k in range(2):
+                urgent(CFG["u1"], count, rho, k)
+            urgent(CFG["u1"], pick, rho)
+            urgent(CFG["u1"], cand_a, rho)
+            urgent(CFG["u1"], cand_b, rho, lambda s, rho=rho: ts(o("SQ", slice(8 * rho + 8, 8 * rho + 16), 40 * par), C["ONE"], s, MUL))
+            urgent(CFG["u1"], cand_d, rho)
             KI = unpack(rho)
             address(KI)
             spread(rho + 1)
             place()
             pack()
             request(rho + 1)
-            if not AB:
-                cand_d(rho)
             insert(rho)
-            mirror(rho, "UA", 272, NXT)
-            mirror(rho, "UB", 280, PRV)
+            mirror(rho, "UA", 272, C2)
+            mirror(rho, "UB", 280, C3)
 
     rho = RO - 1
-    dma("y", T.yi[:], o(T.OY[:, 128:256], "OYi"))
-    homes_psum()
+    dma("y", T.yi[:], cols("OY", 128, 256))
+    for a, r in ((0, t), (S2, (t - 1) % N)):
+        for k in range(2):
+            act(ps(k, 0, 512), io(512 * k, 512 * k + 512), bias=float(1024 * r))
+        for k in range(2):
+            x = cols("TG", a + 512 * k, a + 512 * k + 512)
+            tt(x, x, ps(k, 0, 512), ADD)
+    act(ps(0, 0, WIN), io(0, WIN), bias=n0)
+    for a in (S3, S4, S5):
+        x = cols("TG", a, a + WIN)
+        tt(x, x, ps(0, 0, WIN), ADD)
+    for k in range(2):
+        urgent(CFG["u1"], count, rho, k)
+    urgent(CFG["u1"], pick, rho)
     for b in range(4):
         a = (0 if b < 2 else S2) + 512 * (b % 2)
-        x = o(T.TG[:, a:a + 512], "TG0" if b < 2 else "TG2")
-        tt(x, x, ps(HB_[b], 0, 512), ADD)
-    x = o(T.TG[:, S3:DUMP], "TG3", "TG4", "TG5")
-    tt(x, x, o(T.XT[:, S3:DUMP], "XT3"), ADD)
-    urgent(U1, select, rho)
+        cp(sub("G", 512 * b, 512 * b + 512), cols("PT", a, a + 512))
+    urgent(CFG["u1"], cand_a, rho)
     for b in range(4):
         a = (0 if b < 2 else S2) + 512 * (b % 2)
-        cp(sub("G", 512 * b, 512 * b + 512, tok=["G%d" % b]), o(T.PT[:, a:a + 512], "PT0" if b < 2 else "PT2"))
-    urgent(U1, cand_a, rho)
-    for b in range(4):
-        a = (0 if b < 2 else S2) + 512 * (b % 2)
-        mm([(ps(4 + b % 2, 0, 512), C["BLKF"], sub("G", 512 * b, 512 * b + 512, tok=["G%d" % b]), True, True)], c=2048)
-        act(o(T.XT[:, a:a + 512], "XT0" if b < 2 else "XT2"), ps(4 + b % 2, 0, 512), F.Copy)
+        mm([(ps(4 + b % 2, 0, 512), C["BLKF"], sub("G", 512 * b, 512 * b + 512), True, True)])
+        act(cols("XT", a, a + 512), ps(4 + b % 2, 0, 512), F.Copy)
 
     def ov_last(s):
-        cp(o(T.SO[:, 0:1], "SO"), s)
-        a2a(lambda d: o(T.SO[:], "SO"), T.RV[:, t, :], "aO")
-        cp(o(T.RV[:, t, :], "RVm"), o(T.SO[:], "SO"))
-        arrive("aO", na, ["RV"], LO)
-    urgent(U1, cand_b, rho, ov_last)
+        act(cols("SO", 0, 1), s, F.Copy)
+        for k in range(NP):
+            x = send([(cores[d], T.RV[:, t, :], o("SO"), "aO", en) for d, en in pair_call(core, pairs[(me_c + 1 + k) % NP], cores, topo)])
+        act(o("RV", t), o("SO"), F.Copy)
+        arrive("aO", sum(pair_count(t, p, cores, topo) for p in pairs), [o("RV", d) for d in range(N) if d != t], CFG["far"], x)
+    urgent(CFG["u1"], cand_b, rho, ov_last)
     cand_d(rho)
     insert(rho)
-    mm([(ps(4, 0, 128), C["BLKF"], L["np1"], True, True)], c=512)
-    scat(XTa, sub("offs", 0, 8, tok=["os0"]), act(f("sm1"), ps(4, 0, 128), F.Copy))
+    mm([(ps(4, 0, 128), C["BLKF"], L["np1"], True, True)])
+    scat(XTa, sub("offs", 8, 16), act(f("sm1"), ps(4, 0, 128), F.Copy))
+    dn = L["dn"]
     inr = tt(f("inr", 18), ts(f("in0", 18), xw, 0.0, GE), ts(f("in1", 18), xw, 1024.0, LT), MUL)
-    dl = ts(f("dl", 18), C["kA"], float(S1), ADD)
-    u("offf", 36)
-    cp(sub("offf", 0, 18, tok=["of0"]), tt(f("z2", 18), tt(f("z1", 18), tt(f("z0", 18), xw, dl, SUB), inr, MUL), dl, ADD))
-    xh = ts(f("xh", 18), C["kA"], n0, ADD, -1024.0 * ((t - 1) % N), ADD)
-    inh = tt(f("inh", 18), ts(f("in2", 18), xh, 0.0, GE), ts(f("in3", 18), xh, 1024.0, LT), MUL)
-    dh = ts(f("dh", 18), C["kA"], float(S1 + WIN), ADD)
-    zh = tt(f("z4", 18), tt(f("z3", 18), ts(f("xh2", 18), xh, float(S2), ADD), dh, SUB), inh, MUL)
+    dl_ = act(f("dl_", 18), C["kA"], bias=float(S1))
+    offl = cp(u("offl", 18), tt(f("z2", 18), tt(f("z1", 18), tt(f("z0", 18), xw, dl_, SUB), inr, MUL), dl_, ADD))
+    k12 = sub("kA", 0, 12)
+    xh = ts(f("xh", 12), k12, n0, ADD, -1024.0 * ((t - 1) % N), ADD)
+    inh = tt(f("inh", 12), ts(f("in2", 12), xh, 0.0, GE), ts(f("in3", 12), xh, 1024.0, LT), MUL)
+    dh_ = act(f("dh_", 12), k12, bias=float(WIN))
+    zh = tt(f("z4", 12), tt(f("z3", 12), ts(f("xh2", 12), xh, float(WS), ADD), dh_, SUB), inh, MUL)
+    offh = cp(u("offh", 12), tt(f("z6", 12), tt(f("z5", 12), ts(f("sp", 12), k12, dn, LT), zh, MUL), dh_, ADD))
     KI = unpack(rho)
-    dma("y", T.yl[:], ts(o(T.OY[:, 0:128], "OYl"), KI, -P20, ADD))
-    dn = f("dn", 1)
-    boost[0] = U6
-    cp(sub("offf", 18, 36, tok=["of1"]), tt(f("z6", 18), tt(f("z5", 18), ts(f("sp", 18), C["kA"], dn, LT), zh, MUL), dh, ADD))
-    m2 = tt(ps(7, 0, WIN), ts(ps(5, 0, WIN), io(0, WIN), dn, LT, -P21, MUL), o(T.TG[:, S4:S5], "TG4"), ADD)
-    tt(o(T.TG[:, S4:S5], "TG4"), m2, o(T.TG[:, S3:S4], "TG3"), MAX)
-    offf = sub("offf", 0, 36, tok=["of0", "of1"])
-    scat(o(T.TG[:, 0:S3], "TG0", "TG1", "TG2"), offf, o(T.TG[:, S4:DUMP], "TG4", "TG5"))
-    p1 = tt(ps(7, 0, WIN), ts(ps(5, 0, WIN), io(0, WIN), dn, GE), o(T.PT[:, S4:S5], "PT4"), MUL)
-    pa = tt(sub("PR", 0, WIN, tok=["PR0"]), p1, o(T.PT[:, S3:S4], "PT3"), ADD)
-    pb = cp(sub("PR", 512, 512 + WIN, tok=["PR1"]), o(T.PT[:, S5:DUMP], "PT5"))
-    for k, x in enumerate((pa, pb)):
-        mm([(ps(k, 0, WIN), C["BLKF"], x, True, True)], c=1152)
-        act(sub("G", WIN * k, WIN * k + WIN, tok=["G0", "G1"] if k else ["G0"]), ps(k, 0, WIN), F.Copy)
-    scat(o(T.XT[:, 0:S3], "XT0", "XT1", "XT2"), offf, sub("G", 0, 2 * WIN, tok=["G0", "G1"]))
+    dma("y", T.yl[:], cp(cols("OY", 0, 128), ts(i_("w"), ts(i_("x"), KI, -BIG, ADD), 1048575, AND)))
+    m2 = tt(ps(6, 128, 128 + WIN), ts(ps(5, 0, WIN), io(0, WIN), dn, LT, -P21, MUL), cols("TG", S4, S2), ADD)
+    low = tt(f("NX", WIN), m2, cols("TG", S3, S1), MAX)
+    scat(cols("TG", 0, S4), offl, low)
+    scat(cols("TG", S1, S5), offh, cols("TG", S5, S5 + 192))
+    p1 = tt(ps(6, 128, 128 + WIN), ts(ps(5, 0, WIN), io(0, WIN), dn, GE), cols("PT", S4, S2), MUL)
+    pa = tt(sub("PR", 0, WIN), p1, cols("PT", S3, S1), ADD)
+    pb = cp(sub("PR", 512, 512 + 192), cols("PT", S5, S5 + 192))
+    for k, (x, n) in enumerate(((pa, WIN), (pb, 192))):
+        mm([(ps(k, 0, n), C["BLKF"], x, True, True)])
+        act(sub("G", 512 * k, 512 * k + n), ps(k, 0, n), F.Copy)
+    scat(cols("XT", 0, S4), offl, sub("G", 0, WIN))
+    scat(cols("XT", S1, S5), offh, sub("G", 512, 512 + 192))
     k6 = sub("kA", 0, 6)
     u("offx", 12)
     f("tg0", 12)
-    f("k12", 12)
+    f("dx", 12)
+    f("i12", 12)
     for k, (sec, r, base) in enumerate(((S3, t, 0), (S5, (t - 1) % N, S2))):
-        ts(sub("offx", 6 * k, 6 * k + 6, tok=["ox%d" % k]), k6, dn, ADD, float(sec), ADD)
-        act(sub("k12", 6 * k, 6 * k + 6, tok=["k12%d" % k]), k6, bias=96.0 * k)
+        ts(sub("offx", 6 * k, 6 * k + 6), k6, dn, ADD, float(sec), ADD)
+        act(sub("dx", 6 * k, 6 * k + 6), k6, bias=96.0 * k + DUMP)
+        act(sub("i12", 6 * k, 6 * k + 6), k6, F.Copy)
         xx = ts(f("xx%d" % k, 6), k6, NN[RO - 1], ADD, -1024.0 * r, ADD)
         ya = tt(f("ya%d" % k, 6), ts(f("yb%d" % k, 6), xx, 0.0, LT, 2 * BIG, MUL), xx, ADD)
         yc = ts(f("yc%d" % k, 6), xx, 1024.0, GE, BIG, MUL)
-        tt(sub("tg0", 6 * k, 6 * k + 6, tok=["tg0%d" % k]), ts(f("yd%d" % k, 6), ya, float(base), ADD), yc, ADD)
-    dx = act(f("dx", 12), sub("k12", 0, 12, tok=["k120", "k121"]), bias=float(DUMP))
-    i12 = f("i12", 12)
-    for k in range(2):
-        act(sub("i12", 6 * k, 6 * k + 6), k6, F.Copy)
-    mirror(rho, "UA", 272, NXT)
-    offx = sub("offx", 0, 12, tok=["ox0", "ox1"])
-    kx = act(sub("PR", 1024, 1216, tok=["PR2"]), ind(TGa, offx))
-    mm([(ps(4, 0, 192), C["BLKF"], cp(sub("PR", 1536, 1728, tok=["PR3"]), ind(PTa, offx)), True, True)], c=768)
-    sx = act(sub("PR", 2048, 2240, tok=["PR4"]), ps(4, 0, 192), F.Copy)
-    boost[0] = U5
-    pointer(RO, o(T.RV[:, :, 0], "RV", "RVm"))
-    no = ts(f("no", 12), i12, tt(f("dv", 1), NN[RO], NN[RO - 1], SUB), GE, BIG, MUL)
-    offy = cp(u("offy", 12), tt(f("y2", 12), tt(f("y1", 12), no, sub("tg0", 0, 12, tok=["tg00", "tg01"]), ADD), dx, MIN))
+        tt(sub("tg0", 6 * k, 6 * k + 6), ts(f("yd%d" % k, 6), ya, float(base), ADD), yc, ADD)
+    mirror(rho, "UA", 272, C2)
+    offx = sub("offx", 0, 12)
+    kx = act(sub("PR", 1024, 1216), ind(TGa, offx))
+    mm([(ps(4, 0, 192), C["BLKF"], cp(sub("PR", 1536, 1728), ind(PTa, offx)), True, True)])
+    sx = act(sub("PR", 2048, 2240), ps(4, 0, 192), F.Copy)
+    boost[0] = CFG["u5"]
+    pointer(RO, o("RV", slice(None), 0))
+    no = ts(f("no", 12), sub("i12", 0, 12), act(f("dv", 1), NN[RO], bias=act(f("nn2", 1), NN[RO - 1], F.Copy, scale=-1.0)), GE, BIG, MUL)
+    offy = cp(u("offy", 12), tt(f("y2", 12), tt(f("y1", 12), no, sub("tg0", 0, 12), ADD), sub("dx", 0, 12), MIN))
     scat(TGa, offy, kx)
-    dma("y", T.yk[:, 0:1024], o(T.TG[:, 0:S1], "TG0"))
-    dma("s", T.yk[:, 1024:2048], o(T.TG[:, S2:S3], "TG2"))
+    dma("y", T.yk[:, 0:1024], cols("TG", 0, S3), 4000.0)
+    dma("s", T.yk[:, 1024:2048], cols("TG", S2, S5), 4000.0)
     scat(XTa, offy, sx)
     boost[0] = 0.0
-    dma("y", T.yn[:], cp(o(T.OY[:, 256:257], "OYn"), NN[RO]))
-    dma("y", T.ys[:, 0:1024], o(T.XT[0:128:16, 0:S1], "XT0"))
-    dma("s", T.ys[:, 1024:2048], o(T.XT[0:128:16, S2:S3], "XT2"))
+    dma("y", T.yn[:], cp(cols("OY", 256, 257), NN[RO]))
+    dma("y", T.ys[:, 0:1024], (T.XT[0:128:16, 0:S3], cols("XT", 0, S3)[1], "s"))
+    dma("s", T.ys[:, 1024:2048], (T.XT[0:128:16, S2:S5], cols("XT", S2, S5)[1], "s"))
 
     n = len(ops)
     pre = [op["deps"] | op["soft"] for op in ops]
@@ -888,7 +870,7 @@ def rank_program(g, core, T, topo):
             start = {me: max(r, free.get(ops[me]["q"], 0.0)) for me, r in ready.items()}
             first = min(start, key=lambda k: start[k])
             q = ops[first]["q"]
-            me = max((k for k in ready if ops[k]["q"] == q and start[k] <= start[first] + SLACK), key=lambda k: (prio[k] + sign * ops[k]["up"], -k))
+            me = max((k for k in ready if ops[k]["q"] == q and start[k] <= start[first] + CFG["slack"]), key=lambda k: (prio[k] + sign * ops[k]["up"], -k))
             done[me] = start[me] + ops[me]["c"]
             if q != "x":
                 free[q] = done[me] if ops[me]["ev"] is None or q == "g" else start[me] + 60.0
@@ -903,7 +885,7 @@ def rank_program(g, core, T, topo):
     for me in range(n - 1, -1, -1):
         prio[me] = ops[me]["c"] + max([prio[k] + WAKE for k in post[me]], default=0.0)
     best = None
-    for _ in range(PASSES):
+    for _ in range(CFG["passes"]):
         done, order = plan(pre, post, prio, 1.0)
         if best is None or max(done) < max(best[0]):
             best = (done, order)

@@ -3,31 +3,32 @@ from concourse.mybir import AluOpType as A, AxisListType, ActivationFunctionType
 
 N, RO, CAP, WIN = 8, 3, 320, 288
 WS = 1024 + WIN
-S3, S1, S4, S2, S5, DUMP, TW = 1024, WS, WS + 1024, 2 * WS, 2 * WS + 1024, 3 * WS, 3 * WS + 256
+S3, S1, S4, S2, S5, DUMP, ZC, TW = 1024, WS, WS + 1024, 2 * WS, 2 * WS + 1024, 3 * WS, 3 * WS + 256, 3 * WS + 272
 BIG, U, P21 = 8192.0, 1048576.0, 2097152.0
-SWW, OS = 6464, 132
+SWW, OS, PARTS = 6464, 132, 2
 C0, C1, C2, C3 = 8192.0, 16384.0 - WS, 16384.0 + WS, 12288.0 - WS
-PLAN = {}
-CFG = {"gv": 48, "npk": 8, "slack": 40.0, "passes": 4, "fix": 10.0, "wake": 70.0, "pe": 0.45, "cy": 0.85, "wv": (3,), "sv": (0, 1, 2, 3), "lastv": 3,
-       "u1": 2000.0, "u2": 2000.0, "u3": 5000.0, "u4": 1000.0, "u5": 5000.0, "u7": 5000.0, "far": 2800.0, "near": 2000.0, "lk": 9000.0, "lp": 12000.0, "lo": 4500.0}
+PEER = (2, 3, 1, 0)
+PLAN, ORDERS = {}, {}
+CFG = {"gv": 64, "npk": 4, "tol": 0.0, "passes": 2, "g0": 16, "fix": 45.0, "fixs": 60.0, "least": 16.0, "wake": 70.0, "pe": 0.45, "cy": 0.85, "wv": (4, 6), "apart": (2,), "look": 400.0, "gaps": False, "mend": 4000, "warm": 40.0, "lam": 1.0, "send": 700.0,
+       "u1": 0.0, "u2": 0.0, "u3": 0.0, "u4": 0.0, "u5": 0.0, "u7": 0.0, "far": 2800.0, "near": 2200.0, "lk": 7000.0, "lp": 10000.0, "ld": 2400.0, "ld2": 8000.0, "st": 6500.0}
 SCRATCH = {
     "lki": ("sbuf", [128, 128], "int32"), "lii": ("sbuf", [128, 128], "int32"), "dki": ("sbuf", [128, 384], "int32"),
     "pni": ("sbuf", [128, 1], "int32"), "KR": ("sbuf", [128, 2048], "int32"), "PT": ("sbuf", [128, TW], "int32"),
-    "TG": ("sbuf", [128, TW], "float32"), "XT": ("sbuf", [128, TW], "float32"),
+    "TG": ("sbuf", [128, TW], "float32"), "XT": ("sbuf", [128, TW], "float32"), "YS": ("sbuf", [128, TW], "float32"),
     "SW": ("sbuf", [128, SWW], "bfloat16"), "W": ("sbuf", [128, 2576], "bfloat16"),
     "T2": ("sbuf", [128, 128, 16], "bfloat16"), "BC": ("sbuf", [128, 16, 128], "bfloat16"),
     "SQ": ("sbuf", [128, 24, 48], "uint16"), "RQ": ("sbuf", [128, 12, 96], "uint16"), "TQ": ("sbuf", [128, 16, 20], "bfloat16"),
-    "SR": ("sbuf", [128, 64, 16], "bfloat16"), "RR": ("sbuf", [128, 576], "float32"), "SA": ("sbuf", [128, 576], "float32"),
-    "SF": ("sbuf", [128, 3, 160], "float32"), "CAT": ("sbuf", [128, 3, 336], "float32"),
-    "UP": ("sbuf", [128, 3, 416], "float32"), "UA": ("sbuf", [128, 3, 288], "float32"), "UB": ("sbuf", [128, 3, 288], "float32"),
-    "SO": ("sbuf", [128, 4], "float32"), "RV": ("sbuf", [128, 8, 4], "float32"), "HB": ("sbuf", [128, 512], "int32"),
+    "SR": ("sbuf", [128, 192, 16], "bfloat16"), "RR": ("sbuf", [128, 576], "float32"), "SA": ("sbuf", [128, 192], "float32"),
+    "SF": ("sbuf", [128, 160], "float32"), "CAT": ("sbuf", [128, 3, 336], "float32"),
+    "UP": ("sbuf", [128, 424], "float32"), "UA": ("sbuf", [128, 3, 288], "float32"), "UB": ("sbuf", [128, 2, 288], "float32"),
+    "SO": ("sbuf", [128, 4], "float32"), "RV": ("sbuf", [128, 8, 4], "float32"),
     "OY": ("sbuf", [128, 260], "float32"),
-    "TF": ("sbuf", [128, 15360], "float32"), "TI": ("sbuf", [128, 1536], "int32"), "TB": ("sbuf", [128, 21504], "bfloat16"),
+    "TF": ("sbuf", [128, 14848], "float32"), "TI": ("sbuf", [128, 1408], "int32"), "TB": ("sbuf", [128, 20992], "bfloat16"),
     "TU": ("sbuf", [128, 512], "uint16"),
 }
 for _b in range(8):
     SCRATCH["B%d" % _b] = ("psum", [128, 512], "float32")
-SEMAPHORES = (["qv", "qs", "qp", "qg", "aK", "aP", "aW", "aO", "aH", "lr"] + ["a%s%d" % (k, r) for k in "FAB" for r in range(RO)]
+SEMAPHORES = (["qv", "qs", "qp", "qg", "aK", "aP", "aW", "aO", "go0", "go1", "lr"] + ["aH%d" % j for j in range(PARTS)] + ["a%s%d" % (k, r) for k in "FAB" for r in range(RO)]
               + ["a%s%d%d" % (k, r, b) for k in "QR" for r in range(RO) for b in range(4)]
               + ["d%d" % i for i in range(16)] + ["l%d" % i for i in range(48)])
 
@@ -84,10 +85,12 @@ def relay_program(g, core, T, topo):
         hs = relays(src, dst, cores, topo)
         if core in hs:
             i = hs.index(core)
-            g.wait_ge(T.sem.aH, len(side_engines(src, core, topo, cores)) // 2)
             rid, pid, _ = topo.addr(dst)
-            g.remote_dma(T.PT[:, S1 + 512 * i:S1 + 512 * (i + 1)], T.HB[:], T.sem.aP, T.sem.lr, pid, rid, topo.mask(core, dst))
-            g.wait_ge(T.sem.lr, len(topo.engines(core, dst)))
+            w = 512 // PARTS
+            for j in range(PARTS):
+                g.wait_ge(T.sem["aH%d" % j], len(side_engines(src, core, topo, cores)) // 2)
+                g.remote_dma(T.PT[:, S1 + 512 * i + w * j:S1 + 512 * i + w * j + w], T.KR[:, w * j:w * j + w], T.sem.aP, T.sem.lr, pid, rid, topo.mask(core, dst))
+            g.wait_ge(T.sem.lr, PARTS * len(topo.engines(core, dst)))
 
 
 def mask_of(shape, idx):
@@ -175,12 +178,12 @@ def rank_program(g, core, T, topo):
     def st(*xs):
         return [k for x in xs if isinstance(x, tuple) for k in x[1]]
 
-    def cost(out, ins, two=False, half=False):
+    def cost(out, ins, two=False, half=False, fix=FIX):
         kinds = [x[2] for x in ins]
         if "i" in kinds:
             return 55.0 + 1.56 * CY * size(out)
         k = 2.0 if two and "p" not in kinds else 0.5 if half and all(z == "h" for z in kinds + [out[2]]) else 1.0
-        return FIX + max(64.0, size(out) * k) * CY
+        return fix + max(CFG["least"], size(out) * k) * CY
 
     def rec(q, fn, R, W, ev=None, c=100.0, after=()):
         me = len(ops)
@@ -240,23 +243,29 @@ def rank_program(g, core, T, topo):
 
     def act(out, a, func=F.Identity, bias=0.0, scale=1.0, acc=None):
         if acc is None:
-            rec("s", lambda e: e.activation(out[0], a[0], func, bias=sv(bias), scale=sv(scale)), st(a, bias, scale), out[1], c=cost(out, [a]))
+            rec("s", lambda e: e.activation(out[0], a[0], func, bias=sv(bias), scale=sv(scale)), st(a, bias, scale), out[1], c=cost(out, [a], fix=CFG["fixs"]))
         else:
-            rec("s", lambda e: e.activation(out[0], a[0], func, bias=sv(bias), scale=sv(scale), accum_out=acc[0]), st(a, bias, scale), out[1] + acc[1], c=cost(out, [a]) + 20.0)
+            rec("s", lambda e: e.activation(out[0], a[0], func, bias=sv(bias), scale=sv(scale), accum_out=acc[0]), st(a, bias, scale), out[1] + acc[1], c=cost(out, [a], fix=CFG["fixs"]) + 20.0)
         return out
 
-    def mm(items):
+    def opens(b, terms):
+        mm([(x, y, z, k == 0, False) for k, (x, y, z) in enumerate(terms)], ps(b, 0, 512)[1])
+
+    def closes(b, terms):
+        mm([(x, y, z, False, k == len(terms) - 1) for k, (x, y, z) in enumerate(terms)], ps(b, 0, 512)[1])
+
+    def mm(items, whole=()):
         def fn(e):
             ins = None
             for x in items:
                 ins = e.matmul(x[0][0], x[1][0], x[2][0], x[3], x[4])
             return ins
-        R, W = {}, {}
+        R, W = {}, dict(whole)
         for x in items:
             for d, ks in ((R, st(x[1], x[2])), (W, x[0][1])):
                 for k, m in ks:
                     d[k] = d.get(k, 0) | m
-        rec("p", fn, list(R.items()), list(W.items()), c=FIX + PE * sum(max(64, size(x[0])) * (1 if x[1][2] == "h" else 4) for x in items))
+        rec("p", fn, list(R.items()), list(W.items()), c=10.0 + PE * sum(max(64, size(x[0])) * (1 if x[1][2] == "h" else 4) for x in items))
 
     def lin(out, terms):
         return [(out, a, b, k == 0, k == len(terms) - 1) for k, (a, b) in enumerate(terms)]
@@ -268,55 +277,55 @@ def rank_program(g, core, T, topo):
             rec("g", lambda e: e.iota(out[0], pat, base, cm), [], out[1], c=140.0)
         return out
 
-    def dma(q, out, a, c=2500.0, after=()):
+    def keep_if(out, a, op, fill):
+        rec("g", lambda e: e.affine_select(out[0], a[0], [[1, 128]], op, fill, 0, -1), st(a), out[1], c=400.0)
+        return out
+
+    def dma(q, out, a, c=2500.0, after=(), reads=()):
         s = "d%d" % cnt["d"]
         cnt["d"] += 1
-        return rec(q, lambda e: e.dma_start(sv(out), sv(a)).then_inc(T.sem[s], 16), st(a), st(out), ev=(s, 16), c=c, after=after)
+        return rec(q, lambda e: e.dma_start(sv(out), sv(a)).then_inc(T.sem[s], 16), st(a) + list(reads), st(out), ev=(s, 16), c=c, after=after)
 
     def send(trs):
         s = "l%d" % cnt["l"]
         cnt["l"] += 1
         return rec("g", lambda e: e.remote_dma_fused([RemoteDMATransfer(dst_ids=[dst_id(d, topo)], dma_engine_mask=bits(en), remote_sem=T.sem[sm], src=a[0], dst=da)
                                                      for d, da, a, sm, en in trs], local_sem=T.sem[s]),
-                   st(*[x[2] for x in trs]), [], ev=(s, sum(len(x[4]) for x in trs)), c=600.0)
+                   st(*[x[2] for x in trs]), [], ev=(s, sum(len(x[4]) for x in trs)), c=CFG["send"])
 
     def arrive(sem, n, lands, c, after):
         rec("x", None, [], st(*lands), ev=(sem, n), c=c, after=[after])
 
-    TGa, PTa, XTa, SWa = cols("TG", 0, TW), cols("PT", 0, TW), cols("XT", 0, TW), cols("SW", 0, SWW)
+    TGa, PTa, XTa, YSa, SWa = cols("TG", 0, TW), cols("PT", 0, TW), cols("XT", 0, TW), cols("YS", 0, TW), cols("SW", 0, SWW)
     AND, SHR = A.bitwise_and, A.logical_shift_right
     ADD, SUB, MUL, MAX, MIN = A.add, A.subtract, A.mult, A.max, A.min
     EQ, GE, GT, LT = A.is_equal, A.is_ge, A.is_gt, A.is_lt
 
     d = dma("y", o("lki"), T.lk[:], 2600.0)
-    for dst, src, c in ((o("pni"), T.pn[:], 300.0), (o("lii"), T.li[:], 300.0), (cols("KR", 1024, 2048), T.tk[:, 1024:2048], 1600.0), (cols("PT", S2, S5), T.tp[:, 1024:2048], 1600.0),
-                        (cols("KR", 0, 1024), T.tk[:, 0:1024], 1600.0), (cols("PT", 0, S3), T.tp[:, 0:1024], 1600.0), (o("dki"), T.dk[:], 700.0)):
+    for dst, src, c in ((o("pni"), T.pn[:], 300.0), (o("lii"), T.li[:], 300.0), (cols("PT", S2, S5), T.tp[:, 1024:2048], CFG["ld"]),
+                        (cols("KR", 1024, 2048), T.tk[:, 1024:2048], CFG["ld"]), (cols("KR", 0, 1024), T.tk[:, 0:1024], CFG["ld"])):
         d = dma("y", dst, src, c, [d])
     pidx = iota(i_("pidx", 1), [[1, 1]], 0, 1, False)
     IO = f("IO", 1024)
     iota(sub("IO", 0, 320), [[1, 320]], 0, 0)
     gi16 = iota(f("gi16"), [[1, 8], [0, 16]], 0, 0)
-    DC = iota(h("DC", 512), [[0, 64], [CAP, 8]], 0, 0)
     DJs = iota(f("DJs"), [[16, 128]], int(BIG) + 4288, 1)
-    ri16 = iota(f("ri16"), [[0, 8], [1, 16]], 0, 0)
-    iota(sub("IO", 320, 1024), [[1, 704]], 320, 0)
 
     def io(a, b):
         return sub("IO", a, b)
-    boost[0] = 4 * CFG["u3"]
-    ms(cols("SW", 0, 2560), 0.0)
-    ms(o("T2"), 0.0)
-    ms(h("OH", 9 * OS), 0.0)
     boost[0] = CFG["u3"]
+    ms(cols("SW", 0, 2560), 0.0)
+    act(o("T2"), cols("SW", 0, 2048), F.Copy)
+    ms(h("OH", 9 * OS), 0.0)
     pr = cp(f("pr", 1), ts(i_("pri", 1), pidx, 15, AND))
     pg = cp(f("pg", 1), ts(i_("pgi", 1), pidx, 4, SHR))
-    pf = cp(f("pf", 1), pidx)
-    D = ts(f("D"), io(0, 128), pf, SUB)
-    ID = ts(h("ID"), D, 0.0, EQ)
+    ID = ts(h("ID"), io(0, 128), cp(f("pf", 1), pidx), EQ)
     BLK = ts(h("BLK"), gi16, pg, EQ)
-    LS = tt(h("LS"), ts(h("lsa"), D, 0.0, GT), BLK, MUL)
-    LB = tt(h("LB"), ts(h("lba"), D, 0.0, EQ, BIG, MUL), LS, ADD)
-    RS8 = ms(h("RS8", 512), 1.0)
+    LS = keep_if(h("LS"), BLK, GT, 0.0)
+    LB = [keep_if(h("LB%d" % d), LS, A.not_equal, BIG + CAP * d) for d in range(8)]
+    for k in range(1, 4):
+        act(io(256 * k + 64 * (k == 1), 256 * k + 256), io(64 * (k == 1), 256), bias=256.0 * k)
+    RS8 = act(h("RS8", 512), cols("SW", 0, 512), bias=1.0)
     ms(sub("RS8", 0, 512, 8), 0.0)
     RSM = ms(h("RSM", 7 * OS), 1.0)
     ms(sub("RSM", 0, 7 * OS, OS), 0.0)
@@ -344,7 +353,7 @@ def rank_program(g, core, T, topo):
     dl = ts(f("dl", 1), d0, 0.5, MUL, dh, SUB)
     DH = act(h("DH"), ID, F.Copy, scale=act(f("dhf", 1), dh, F.Copy))
     DL = act(h("DL"), ID, F.Copy, scale=dl)
-    C128 = act(h("C128", 160), io(0, 160), bias=128.0, scale=0.0)
+    act(h("C128", 320), io(0, 320), bias=128.0, scale=0.0)
     for v in (-1024, 1024 + WS, WS, 512, CAP, -8 * CAP, (BIG + CAP) / 128):
         dg(v)
     Y = ts(h("Y", 144), io(0, 144), ts(f("y15", 1), pg, 16.0, MUL, 15.0, ADD), EQ)
@@ -360,22 +369,34 @@ def rank_program(g, core, T, topo):
     def sumto(r, nm="Y"):
         return sub(nm, 15 - r, 143 - r)
 
+    fin_lo, fin_hi = -1024.0 * t, S2 - 1024.0 * ((t - 1) % N)
+    C4 = (fin_lo + fin_hi) / 2 + 1.0 / 256 + 16384.0
+
     def late_consts():
+        ri16 = iota(f("ri16"), [[0, 8], [1, 16]], 0, 0)
+        C["LSI"] = keep_if(h("LSI"), LS, A.not_equal, -1.0)
         ts(f("M16", 16), io(0, 16), pr, EQ)
         for r in range(16):
             act(o("BC", r), BLK, F.Copy, scale=sub("M16", r, r + 1))
         C["BLKF"] = act(f("BLKF"), BLK, F.Copy)
-        C["GIF"] = ts(f("GIF", 8), io(0, 8), pg, EQ)
-        C["GIB"] = ts(h("GIB", 8), io(0, 8), pg, EQ, 8 * U, MUL)
-        C["HM"] = ts(f("HM", 4), io(0, 4), cp(f("p4", 1), ts(i_("p4i", 1), pidx, 2, SHR, 3, AND)), EQ)
+        f("GIF", 16)
+        h("GIB", 16)
+        for k in (0, 8):
+            act(sub("GIF", k, k + 8), sub("BLK", 0, 128, 16), F.Copy)
+            act(sub("GIB", k, k + 8), sub("BLK", 0, 128, 16), F.Copy, scale=8 * U)
         C["kA"] = ts(f("kA", 18), io(0, 18), 16.0, MUL, pr, ADD)
+        act(h("ZB", 40), io(0, 40), F.Copy, scale=0.0)
+        act(sub("ZB", 0, 8), io(0, 8), bias=C1 - C0, scale=0.0)
         C["KB"] = act(f("KB", 8), sub("kA", 0, 8), bias=-0.5, scale=-1.0)
         C["DG"] = ts(h("DG"), ri16, pr, EQ, P21, MUL)
-        C["RS16"] = act(f("RS16"), ri16, F.Sign)
+        f("RS16", 256)
+        for k in (0, 128):
+            act(sub("RS16", k, k + 128), ri16, F.Sign)
+        C["RS16"] = sub("RS16", 0, 128)
         C["ONE"] = act(f("ONE", 8), io(0, 8), bias=1.0, scale=0.0)
         C["IO1"] = cp(ps(6, 128, 256), io(1, 129))
-        C["DM"] = f("DM", 32)
-        for k, v in enumerate((DUMP + 128 - C1, DUMP - C0, DUMP - C2, DUMP - C3)):
+        C["DM"] = f("DM", 40)
+        for k, v in enumerate((DUMP + 128 - C0, DUMP - C0, DUMP - C2, DUMP - C3, DUMP - C4)):
             act(sub("DM", 8 * k, 8 * k + 8), sub("kA", 0, 8), bias=float(v))
         h("R2", 336)
         ms(sub("R2", 0, 1), 0.0)
@@ -384,22 +405,14 @@ def rank_program(g, core, T, topo):
         ms(o("CAT", slice(None), slice(320, 336)), 0.0)
         act(cols("W", 2560, 2576), io(0, 16), F.Copy, scale=0.0)
         act(h("YN", 144), Y, F.Copy, scale=-U)
-        C["LSI"] = tt(h("LSI"), LS, ID, SUB)
         C["DG14"] = act(h("DG14"), C["DG"], F.Copy, scale=1.0 / 128)
         C["KF"] = act(h("KF"), io(0, 128), F.Copy, scale=1.0 / 128)
-        C["kF"] = act(f("kF", 8), sub("kA", 0, 8), F.Copy, scale=1.0 / 128)
-        f("dk2", 384)
-        for r in range(RO):
-            ts(sub("dk2", 128 * r, 128 * r + 128), cols("dki", 128 * r, 128 * r + 128), (RO - 1 - r) * 2 * U + BIG, ADD)
-        act(o("SR"), IO, F.Copy, scale=0.0)
-        act(cols("TG", DUMP, TW), io(0, 256), F.Copy, scale=0.0)
+        act(cols("TG", DUMP, TW), io(0, TW - DUMP), F.Copy, scale=0.0)
         ms(cols("PT", DUMP, TW), 0)
-        act(cols("XT", DUMP, TW), io(0, 256), F.Copy, scale=0.0)
+        act(cols("XT", DUMP, TW), io(0, TW - DUMP), F.Copy, scale=0.0)
         act(o("SO"), io(0, 4), F.Copy, scale=0.0)
         for a in (S3, S4, S5):
             act(cols("XT", a, a + WIN), io(0, WIN), bias=n0)
-        for a, r in ((0, t), (S2, (t - 1) % N), (S1, t)):
-            act(cols("XT", a, a + 1024), IO, bias=float(1024 * r))
 
     def homes(r):
         for k, b in enumerate((3, 7)):
@@ -409,22 +422,30 @@ def rank_program(g, core, T, topo):
         for k, b in enumerate((3, 7)):
             tt(cols("TG", a + 512 * k, a + 512 * k + 512), cols("KR", z + 512 * k, z + 512 * k + 512), ps(b, 0, 512), SUB)
 
+    def behind(sem, dst, src, c):
+        go = f(sem, 1)
+        rec("g", lambda e: e.sem_inc(T.sem[sem], 1), [], go[1], ev=(sem, 1), c=50.0)
+        dma("y", dst, src, c, reads=go[1])
+
     def mirror_out():
         hs, hn = relays(core, prv, cores, topo), relays(nxt, core, cores, topo)
         if hs:
-            en = side_engines(core, hs[0], topo, cores)
-            s1 = send([(x, T.HB[:], cols("PT", S2 + 512 * k, S2 + 512 * (k + 1)), "aH", en[k * len(en) // 2:(k + 1) * len(en) // 2]) for k, x in enumerate(hs)])
+            en, w = side_engines(core, hs[0], topo, cores), 512 // PARTS
+            for j in range(PARTS):
+                s1 = send([(x, T.KR[:, w * j:w * j + w], cols("PT", S2 + 512 * k + w * j, S2 + 512 * k + w * j + w), "aH%d" % j, en[k * len(en) // 2:(k + 1) * len(en) // 2])
+                           for k, x in enumerate(hs)])
         else:
             s1 = send([(prv, T.PT[:, S1:S4], cols("PT", S2, S5), "aP", halves(core, prv, topo)[1])])
         homes((t - 1) % N)
         relative(S2, 1024)
         s2 = send([(prv, T.TG[:, S1:S4], cols("TG", S2, S5), "aK", topo.engines(core, prv) if hs else halves(core, prv, topo)[0])])
-        arrive("aP", sum(len(topo.engines(x, core)) for x in hn) if hn else len(halves(nxt, core, topo)[1]), [cols("PT", S1, S4)], CFG["lp"], s1)
+        behind("go0", cols("PT", 0, S3), T.tp[:, 0:1024], CFG["ld2"])
+        arrive("aP", PARTS * sum(len(topo.engines(x, core)) for x in hn) if hn else len(halves(nxt, core, topo)[1]), [cols("PT", S1, S4)], CFG["lp"], s1)
         arrive("aK", len(topo.engines(nxt, core)) if hn else len(halves(nxt, core, topo)[0]), [cols("TG", S1, S4)], CFG["lk"], s2)
     L = {}
 
     def address(KI):
-        w = ts(i_("w"), KI, 16383, AND)
+        w = L["w"] = ts(i_("w"), KI, 16383, AND)
         rk = ts(i_("rk"), KI, 10, SHR, 7, AND)
         old = tt(h("old"), w, img, LT)
         s = L["s"] = tt(h("s"), old, rk, ADD)
@@ -464,14 +485,13 @@ def rank_program(g, core, T, topo):
         h("R", 8 * OS)
         scan(sub("R", 0, 129), sub("OH", 0, 129), sub("OH", 8 * OS, 8 * OS + 129), ADD, ADD)
         scan(sub("R", OS, 8 * OS), RSM, sub("OH", OS, 8 * OS), MUL, ADD)
-        for b in range(2):
-            items = [(ps(4 + b, 0, 512), ID, DC, True, False), (ps(4 + b, 0, 512, 8), LB, oh(8, 64 * b, 64 * b + 64), False, False)]
-            for d in range(8):
-                out = ps(4 + b, d, 512, 8)
-                items += [(out, LB, oh(d, 64 * b, 64 * b + 64), False, False), (out, BLK, sub("R", OS * d + 64 * b, OS * d + 64 * b + 64), False, d == 7)]
-            mm(items)
         thr = ps(2, 256, 384)
         mm(lin(thr, [(dg((BIG + CAP) / 128), sub("C128", 0, 128)), (dg(CAP), s), (dg(-8 * CAP), oh(8))]))
+        for b in range(2):
+            items = []
+            for d in range(8):
+                items += lin(ps(4 + b, d, 512, 8), [(LB[d], oh(x, 64 * b, 64 * b + 64)) for x in ([d] if d else [0, 8])] + [(BLK, sub("R", OS * d + 64 * b, OS * d + 64 * b + 64))])
+            mm(items)
         f("MS", 1024)
         for b in range(2):
             scan(sub("MS", 512 * b, 512 * b + 512), RS8, ps(4 + b, 0, 512), MUL, MAX)
@@ -487,145 +507,169 @@ def rank_program(g, core, T, topo):
 
     def request(rho):
         ca, ta = (0, 20) if par else (28, 8)
-        for k in range(NP):
-            c = (me_c + 1 + k) % NP
-            b = k % 2
-            mm(lin(ps(b, 0, 40), [(sumto(q, "YC"), cols("SW", 640 * c + q, 640 * c + 640, 16)) for q in range(16)])
-               + lin(ps(b, 40, 80), [(sumto(q, "YT"), cols("SW", 640 * c + q, 640 * c + 640, 16)) for q in range(16)]))
-            z = slice(8 * rho + 2 * c, 8 * rho + 2 * c + 2)
-            cp(o("SQ", z, slice(ca, ca + 20)), ps(b, 0, 40))
-            cp(o("SQ", z, slice(ta, ta + 20)), ps(b, 40, 80))
-            s = send([(cores[d], T.RQ[:, 4 * rho + me_c, 48 * par:48 * par + 48], o("SQ", 8 * rho + d), "aQ%d%d" % (rho, k), en) for d, en in pair_call(core, pairs[c], cores, topo)])
-            cs = (me_c - 1 - k) % NP
-            if cs == me_c:
-                cp(o("RQ", 4 * rho + me_c, slice(48 * par, 48 * par + 48)), o("SQ", 8 * rho + t))
-                arrive("aQ%d%d" % (rho, k), pair_count(t, pairs[cs], cores, topo), [o("RQ", 4 * rho + cs, slice(48 - 48 * par, 96 - 48 * par))], CFG["near"], s)
-            else:
-                arrive("aQ%d%d" % (rho, k), pair_count(t, pairs[cs], cores, topo), [o("RQ", 4 * rho + cs)], CFG["far"], s)
+        for b in range(2):
+            a = (me_c ^ PEER[2 * b]) // 2
+            for k, (nm, z) in enumerate((("YC", ca), ("YT", ta))):
+                mm(lin(ps(2 * k + b, 0, 80), [(sumto(q, nm), cols("SW", 1280 * a + q, 1280 * a + 1280, 16)) for q in range(16)]))
+                cp(o("SQ", slice(8 * rho + 4 * a, 8 * rho + 4 * a + 4), slice(z, z + 20)), ps(2 * k + b, 0, 80))
+            for ks in ([2, 3],) if b else ([0], [1]):
+                s = send([(cores[d], T.RQ[:, 4 * rho + me_c, 48 * par:48 * par + 48], o("SQ", 8 * rho + d), "aQ%d%d" % (rho, k), en)
+                          for k in ks for d, en in pair_call(core, pairs[me_c ^ PEER[k]], cores, topo)])
+                for k in ks:
+                    c = me_c ^ PEER[k]
+                    land = o("RQ", 4 * rho + c, slice(48 - 48 * par, 96 - 48 * par)) if c == me_c else o("RQ", 4 * rho + c)
+                    arrive("aQ%d%d" % (rho, k), pair_count(t, pairs[c], cores, topo), [land], CFG["near" if c == me_c else "far"], s)
+        cp(o("RQ", 4 * rho + me_c, slice(48 * par, 48 * par + 48)), o("SQ", 8 * rho + t))
 
     def lane_prep(rho, KI):
         ts(u("off2"), L["mx"], -BIG, ADD, 2560.0, MIN)
         gate = act(ps(2, 384, 512), L["ng"], bias=-16 * U, scale=16 * U)
+        far = act(ps(2, 128, 256), L["ng"], bias=1.0, scale=16384.0)
         L["base"] = tt(f("base"), tt(ps(6, 384, 512), KI, gate, ADD), sub("dk2", 128 * rho, 128 * rho + 128), MAX)
+        L["y1"] = tt(f("y1_"), L["w"], far, ADD)
 
     def image(rho, out):
-        nb = act(f("nb", 1), NN[rho], bias=16385.0, scale=-1.0)
-        mm(lin(ps(4, 128, 256), [(IDF, L["xf"]), (dg(-16384), L["hb"]), (dg(16384), L["ng"])]))
-        no = act(h("imno"), ps(4, 128, 256), F.Relu, bias=nb)
-        mm(lin(ps(4, 256, 384), [(IDF, L["xf"]), (dg(1.0 / 128), sub("C128", 0, 128)), (dg(-16384), no)]))
-        tt(out, ps(4, 256, 384), img, MAX)
+        nb = act(f("nb", 1), NN[rho], bias=16384.0, scale=16384.0)
+        yes = act(f("imy"), L["y1"], bias=nb, scale=-16384.0)
+        tt(out, tt(ps(6, 384, 512), yes, L["y1"], MIN), img, MAX)
 
     def unpack_block(rho, k):
-        c = (me_c + 1 + k) % NP
-        ans = cols("RR", 192 * rho + 48 * c, 192 * rho + 48 * c + 48)
-        z = slice(16 * c, 16 * c + 16)
-        copy = cp if k in CFG["sv"] else lambda a, b: act(a, b, F.Copy)
-        hi = copy(o("SR", z, slice(0, 12, 4)), ans)
-        r1 = tt(f("r1%d" % k, 48), ans, hi, SUB)
-        mid = copy(o("SR", z, slice(1, 12, 4)), r1)
-        tt(o("SR", z, slice(2, 12, 4)), r1, mid, SUB)
-        b, a0 = k % 2, 256 * (k // 2)
-        mm([(ps(b, a0 + 128 * s, a0 + 128 * s + 128), o("SR", slice(16 * c + 8 * s, 16 * c + 8 * s + 8)), ID, True, True) for s in range(2)])
-        for s in range(2):
-            for j in range(3):
-                a, n, lo = CAP * (2 * c + s) + 128 * j, 64 if j == 2 else 128, 64 if j == 2 else 0
-                src = ps(b, a0 + 128 * s + lo, a0 + 128 * s + lo + n)
-                if k in CFG["wv"]:
-                    ts(cols("W", a, a + n), src, sub("HM", j, j + 1), MUL)
-                else:
-                    act(cols("W", a, a + n), src, F.Copy, scale=sub("HM", j, j + 1))
+        c = (me_c ^ PEER[2 * k]) // 2
+        ans = cols("RR", 192 * rho + 96 * c, 192 * rho + 96 * c + 96)
+        z = slice(96 * c, 96 * c + 96)
+        up = ts(f("r1%d" % k, 96), ans, 1.5 * 2.0 ** 31, ADD, 1.5 * 2.0 ** 31, SUB)
+        hi = ts(o("SR", z, 0), ans, 1.5 * 2.0 ** 39, ADD, 1.5 * 2.0 ** 39, SUB)
+        tt(o("SR", z, 2), ans, up, SUB)
+        tt(o("SR", z, 1), up, hi, SUB)
+        for s in range(4):
+            d, b = 4 * c + s, (0, 4, 1, 5)[s] if k else s % 2
+            mm([(ps(b, a, a + n), o("SR", slice(24 * d + 8 * j, 24 * d + 8 * j + 8)), sub("ID", lo, lo + n), True, True)
+                for j, (a, n, lo) in enumerate(((0, 64, 64), (64, 128, 0), (192, 128, 0)) if par else ((0, 128, 0), (128, 128, 0), (256, 64, 0)))])
+            if 4 * k + s in CFG["wv"] and rho < RO - 1:
+                cp(cols("W", CAP * d, CAP * d + CAP), ps(b, 0, CAP))
+            else:
+                act(cols("W", CAP * d, CAP * d + CAP), ps(b, 0, CAP), F.Copy)
 
     def unpack(rho):
-        for k in range(NP):
+        for k in range(2):
             unpack_block(rho, k)
         Wa, gv = cols("W", 0, 2576), CFG["gv"]
         h("GR", 2048)
-        cp(sub("GR", 0, 16 * gv), ind(Wa, sub("off2", 0, gv)))
-        act(sub("GR", 16 * gv, 2048), ind(Wa, sub("off2", gv, 128)))
-        val = ps(2, 0, 128)
-        mm(lin(val, [(sumto(r), sub("GR", r, 2048, 16)) for r in range(16)]))
-        return tt(i_("KI"), val, L["base"], MAX)
+        if rho == RO - 1:
+            for a in range(0, 128, 16):
+                act(sub("GR", 16 * a, 16 * a + 256), ind(Wa, sub("off2", a, a + 16)))
+        else:
+            cp(sub("GR", 0, 16 * gv), ind(Wa, sub("off2", 0, gv)))
+            act(sub("GR", 16 * gv, 2048), ind(Wa, sub("off2", gv, 128)))
+        for a, b in ((0, gv), (gv, 128)):
+            mm(lin(ps(2, a, b), [(sumto(r), sub("GR", 16 * a + r, 16 * b, 16)) for r in range(16)]))
+        return tt(i_("KI"), ps(2, 0, 128), L["base"], MAX)
 
     def pointer(rho, parts):
-        mm([(ps(7, 320, 328), BLK, cp(h("ovb", 8), parts), True, True)])
-        v = red(f("v", 1), ps(7, 320, 328))
-        ts(NN[rho], ts(f("v2", 1), v, 96.0, MIN, NN[rho - 1], ADD), 8192.0, MIN)
+        room = act(f("room", 1), NN[rho - 1], bias=8192.0 - 96.0, scale=-1.0)
+        ovb = cp(h("ovb", 8), parts)
+        L["ahead"] = [len(ops) - 1]
+        mm([(ps(7, 320, 328), BLK, ovb, True, True)])
+        act(f("v8", 8), ps(7, 320, 328), F.Copy, acc=f("v", 1))
+        a = act(f("v2", 1), f("v", 1), F.Relu, bias=96.0, scale=-1.0)
+        act(NN[rho], act(f("v3", 1), a, F.Relu, bias=room), bias=8192.0, scale=-1.0)
 
-    def lookup(rho, k):
-        c = (me_c - 1 - k) % NP
+    def lookup(rho, k, between=None):
+        c = me_c ^ PEER[k]
         a, top = 640 * c, S5 if rho == 0 else TW
         f("G", 2560)
         h("EQ", 2560)
         f("PR", 2560)
-        offs = o("RQ", 4 * rho + c, slice(28, 68))
-        ts(o("TQ", slice(4 * c, 4 * c + 4)), o("RQ", 4 * rho + c, slice(8, 88)), -256.0 * (rho + 1) - 1.0, ADD, 8192.0, MUL)
-        act(sub("G", a, a + 640), ind(cols("TG", 0, top), offs))
+        both = slice(4 * rho + c // 2 * 2, 4 * rho + c // 2 * 2 + 2)
+        if k < 2:
+            ts(o("TQ", slice(4 * c, 4 * c + 4)), o("RQ", 4 * rho + c, slice(8, 88)), -256.0 * (rho + 1) - 1.0, ADD, 8192.0, MUL)
+        elif k == 2:
+            ts(o("TQ", slice(c // 2 * 8, c // 2 * 8 + 8)), o("RQ", both, slice(8, 88)), -256.0 * (rho + 1) - 1.0, ADD, 8192.0, MUL)
+        gv = 0 if k else CFG["g0"]
+        if gv:
+            cp(sub("G", a, a + 16 * gv), ind(cols("TG", 0, top), o("RQ", 4 * rho + c, slice(28, 28 + gv))))
+        act(sub("G", a + 16 * gv, a + 640), ind(cols("TG", 0, top), o("RQ", 4 * rho + c, slice(28 + gv, 68))))
         b0 = 2 * (k % 2)
         mm([(ps(b0 + q % 2, q // 2, 320, 8), o("BC", q), o("TQ", slice(4 * c, 4 * c + 4, 3)), True, True) for q in range(16)])
+        ahead = []
+        if k == 2:
+            cp(f("cf", 160), o("RQ", slice(4 * rho, 4 * rho + 4), slice(28, 68)))
+            ahead = [len(ops) - 1] + L.pop("ahead", [])
         for e in range(2):
             tt(sub("EQ", a + e, a + 640, 2), sub("G", a + e, a + 640, 2), ps(b0 + e, 0, 320), EQ)
-        tt(sub("PR", a, a + 640), ind(cols("PT", 0, top), offs), sub("EQ", a, a + 640), MUL)
-        b = 4 + k % 2
-        items = []
-        for s in range(2):
-            for j, z in enumerate((0, 128, 192)):
-                z += a + CAP * s
-                items += lin(ps(b, 24 * s + j, 24 * s + 24, 3), [(sub("PR", z, z + 128), C["GIF"]), (sub("EQ", z, z + 128), C["GIB"])])
-        mm(items)
+            ops[-1]["soft"].update(ahead)
+        if k % 2:
+            found(c // 2)
+        if between:
+            between()
         z = 192 * rho
-        act(cols("SA", z + 48 * c, z + 48 * c + 48), ps(b, 0, 48), bias=BIG)
-        s = send([(cores[d], T.RR[:, z + 24 * t:z + 24 * t + 24], cols("SA", z + 24 * d, z + 24 * d + 24), "aR%d%d" % (rho, k), en)
-                  for d, en in pair_call(core, pairs[c], cores, topo)])
-        cs = (me_c + 1 + k) % NP
-        if cs == me_c:
-            act(cols("RR", z + 24 * t, z + 24 * t + 24), ps(b, 24 * par, 24 * par + 24), bias=BIG)
-            x = t + 1 - 2 * par
-            arrive("aR%d%d" % (rho, k), pair_count(t, pairs[cs], cores, topo), [cols("RR", z + 24 * x, z + 24 * x + 24)], CFG["near"], s)
+
+        b = 4 + k % 2
+
+        def answers(lo, hi):
+            tt(sub("PR", a + 128 * lo, a + 128 * hi), ind(cols("PT", 0, top), o("RQ", 4 * rho + c, slice(28 + 8 * lo, 28 + 8 * hi))), sub("EQ", a + 128 * lo, a + 128 * hi), MUL)
+            items = []
+            for j in range(lo, hi):
+                y, x0 = a + 128 * j, 8 * j + 8 * (j > 2)
+                n = 16 if j == 2 else 8
+                items += lin(ps(b, x0, x0 + n), [(sub("EQ", y, y + 128), sub("GIB", 0, n)), (sub("PR", y, y + 128), sub("GIF", 0, n))])
+            mm(items)
+        x = t + 1 - 2 * par
+        if c == me_c:
+            answers(*((0, 3) if par else (2, 5)))
+            act(cols("SA", 24 * x, 24 * x + 24), ps(b, 24 - 24 * par, 48 - 24 * par), bias=BIG)
         else:
-            arrive("aR%d%d" % (rho, k), pair_count(t, pairs[cs], cores, topo), [cols("RR", z + 48 * cs, z + 48 * cs + 48)], CFG["far"], s)
+            answers(0, 5)
+            act(cols("SA", 48 * c, 48 * c + 48), ps(b, 0, 48), bias=BIG)
+        s = send([(cores[d], T.RR[:, z + 24 * t:z + 24 * t + 24], cols("SA", 24 * d, 24 * d + 24), "aR%d%d" % (rho, k), en)
+                  for d, en in pair_call(core, pairs[c], cores, topo)])
+        if c == me_c:
+            answers(*((3, 5) if par else (0, 2)))
+            act(cols("RR", z + 24 * t, z + 24 * t + 24), ps(b, 24 * par, 24 * par + 24), bias=BIG)
+            arrive("aR%d%d" % (rho, k), pair_count(t, pairs[c], cores, topo), [cols("RR", z + 24 * x, z + 24 * x + 24)], CFG["near"], s)
+        else:
+            arrive("aR%d%d" % (rho, k), pair_count(t, pairs[c], cores, topo), [cols("RR", z + 48 * c, z + 48 * c + 48)], CFG["far"], s)
 
     def miss_pre(rho):
         dn = L["dn"] = act(f("dn", 1), NN[rho], bias=nn0)
         th4 = act(f("th4", 1), dn, bias=S4 - 0.5)
         L["th3"] = act(f("th3", 1), dn, bias=0.5 - S3, scale=-1.0)
-        cf = cp(f("cf", 160), o("RQ", slice(4 * rho, 4 * rho + 4), slice(28, 68)))
-        sa = act(h("sa", 160), cf, F.Sign, bias=0.5 - S1)
-        sb = act(h("sb", 160), cf, F.Sign, bias=th4, scale=-1.0)
-        for k, (nm, sgn, bias) in enumerate((("cF", 1, 2048.5 + WS - U), ("cN", -1, 2048.5))):
-            out = ps(7, 160 * k, 160 * k + 160)
-            mm([(out, IDF, cf, True, False), (out, dg(sgn * U / 2), sa, False, False), (out, dg(sgn * U / 2), sb, False, False)]
-               + [(ps(7, 160 * k + 40 * c, 160 * k + 40 * c + 40), dg(0.5), o("TQ", slice(4 * c, 4 * c + 4, 3)), False, c == NP - 1) for c in range(NP)])
-        for k, (nm, bias) in enumerate((("cF", 2048.5 + WS - U), ("cN", 2048.5))):
-            L[nm] = act(f(nm, 160), ps(7, 160 * k, 160 * k + 160), F.Relu, bias=bias)
+        L["sa"] = act(h("sa", 160), f("cf", 160), F.Sign, bias=0.5 - S1)
+        L["sb"] = act(h("sb", 160), f("cf", 160), F.Sign, bias=th4, scale=-1.0)
+
+    def code(nm, sgn, bias):
+        mm([(ps(7, 0, 160), IDF, f("cf", 160), True, False), (ps(7, 0, 160), dg(sgn * U / 2), L["sa"], False, False), (ps(7, 0, 160), dg(sgn * U / 2), L["sb"], False, False)]
+           + [(ps(7, 40 * c, 40 * c + 40), dg(0.5), o("TQ", slice(4 * c, 4 * c + 4, 3)), False, c == NP - 1) for c in range(NP)])
+        return act(f(nm, 160), ps(7, 0, 160), F.Relu, bias=bias)
+
+    def found(a):
+        mm(lin(ps(6, 256 + 80 * a, 336 + 80 * a), [(dg(8192), sub("C128", 0, 80))] + [(sumto(r, "YN"), sub("EQ", 1280 * a + r, 1280 * a + 1280, 16)) for r in range(16)]))
 
     def miss(rho):
-        out = ps(7, 328, 488)
-        mm(lin(out, [(dg(8192), C128)] + [(sumto(r, "YN"), sub("EQ", r, 2560, 16)) for r in range(16)]))
-        sf = tt(o("SF", rho), out, L["cF"], MIN)
+        out = ps(6, 256, 416)
+        sf = tt(o("SF"), out, code("cF", 1, 2048.5 + WS - U), MIN)
         s = send([(nxt, T.CAT[:, rho, 160:320], sf, "aF%d" % rho, topo.engines(core, nxt))])
-        tt(o("CAT", rho, slice(0, 160)), out, L["cN"], MIN)
+        tt(o("CAT", rho, slice(0, 160)), out, code("cN", -1, 2048.5), MIN)
         arrive("aF%d" % rho, len(topo.engines(prv, core)), [o("CAT", rho, slice(160, 320))], CFG["far"], s)
 
     def count(rho, k):
-        a = 160 * k
+        a, b = (160 * k, 160 * k + 160) if rho in CFG["apart"] else (0, 320)
+        if a != 160 * k:
+            return
         h("m", 320)
         f("ACC", 16)
-        m = act(sub("m", a, a + 160), o("CAT", rho, slice(a, a + 160)), F.Sign)
-        scan(sub("R2", a + 1, a + 161), m, C128, ADD, MIN, sub("R2", a, a + 1) if k else 0.0)
-        nv = CFG["lastv"] if k and rho == RO - 1 else 0
-        mm([(ps(3, a, a + 160), BLK, sub("R2", a + 1, a + 161), True, True)])
-        if nv:
-            mm([(ps(2, 0, 160), BLK, sub("R2", a + 1, a + 161), True, True)])
-        mm(lin(ps(7, a, a + 160), [(BLK, sub("R2", a, a + 160)), (LB, m)]))
-        for j in range(8 - nv):
-            act(h("junk%d" % (j % 2), 160), ps(3, a, a + 160), F.Sign, bias=sub("KB", j, j + 1), acc=sub("ACC", 8 * k + j, 8 * k + j + 1))
-        for j in range(8 - nv, 8):
-            x = ts(f("jv%d" % j, 160), ps(2, 0, 160), sub("kA", j, j + 1), GT, 0.5, SUB)
-            ts(sub("ACC", 8 * k + j, 8 * k + j + 1), red(f("jr%d" % j, 1), x), 2.0, MUL)
-        act(sub("cumM", a, a + 160), ps(7, a, a + 160), F.Relu, bias=1.0 - BIG)
+        m = act(sub("m", a, b), o("CAT", rho, slice(a, b)), F.Sign)
+        scan(sub("R2", a + 1, b + 1), m, sub("C128", 0, b - a), ADD, MIN, sub("R2", a, a + 1) if k else 0.0)
+        mm([(ps(3, a, b), BLK, sub("R2", a + 1, b + 1), True, True)])
+        mm(lin(ps(7, a, b), [(BLK, sub("R2", a, b)), (LB[0], m)]))
+        for j in range(8):
+            h("junk%d" % (j % 2), 320)
+            act(sub("junk%d" % (j % 2), 0, b - a), ps(3, a, b), F.Sign, bias=sub("KB", j, j + 1), acc=sub("ACC", 8 * k + j, 8 * k + j + 1))
+        act(sub("cumM", a, b), ps(7, a, b), F.Relu, bias=1.0 - BIG)
 
     def pick(rho):
-        offk = ts(u("offk", 8), tt(f("acs", 8), sub("ACC", 0, 8), sub("ACC", 8, 16), ADD), -0.5, MUL, 160.0, ADD)
+        signs = tt(f("acs", 8), sub("ACC", 0, 8), sub("ACC", 8, 16), ADD) if rho in CFG["apart"] else sub("ACC", 0, 8)
+        offk = ts(u("offk", 8), signs, -0.5, MUL, 160.0, ADD)
         g1 = act(f("sg1_"), ind(sub("cumM", 0, 336), offk))
         g2 = act(f("sg2_"), ind(o("CAT", rho), offk))
         pc = tt(f("pc"), g2, tt(ps(6, 256, 384), g1, C["IO1"], EQ), MUL)
@@ -636,24 +680,25 @@ def rank_program(g, core, T, topo):
         scan(f("cs"), C["RS16"], ps(7, 320, 448), MUL, MAX)
         ca = ts(i_("ca", 8), sub("cs", 15, 128, 16), 2047.5 - P21, ADD, 4095.0, MAX)
         col = ts(i_("colA", 8), ca, 4095, AND)
-        u("offg", 16)
+        u("offg", 24)
         o1 = cp(sub("offg", 8, 16), col)
         cf = L["cf"] = cp(f("colf", 8), col)
         xg = L["xg"] = act(f("xg"), ind(XTa, o1))
         L["g1"] = act(f("g1"), ind(TGa, o1))
         for nm, b, sc in (("a1", L["th3"], 1.0), ("a2", S1 - 0.5, -1.0), ("b1", 0.5 - S4, 1.0), ("b2", S2 - 0.5, -1.0), ("p6", 0.5 - DUMP, 1.0)):
             L[nm] = act(h("c" + nm, 8), cf, F.Sign, bias=b, scale=sc)
-        out = ps(7, 448, 456)
-        mm(lin(out, [(IDF, cf), (dg(WS // 2), L["a1"]), (dg(WS // 2), L["a2"]), (dg(-WS // 2), L["b1"]), (dg(-WS // 2), L["b2"])]))
-        o2 = cp(sub("offg", 0, 8), out)
+        other = [(IDF, cf), (dg(WS // 2), L["a1"]), (dg(WS // 2), L["a2"]), (dg(-WS // 2), L["b1"]), (dg(-WS // 2), L["b2"])]
+        mm(lin(ps(7, 448, 456), other) + lin(ps(7, 456, 464), other + [(dg(-4096), L[x]) for x in ("a1", "a2", "b1", "b2")]))
+        o2 = cp(sub("offg", 16, 24), ps(7, 448, 456))
+        ts(sub("offg", 0, 8), ps(7, 456, 464), 8192.0, ADD, float(ZC), MIN)
         L["g2"] = act(f("g2"), ind(TGa, o2))
         tagb = act(h("tagb"), ps(3, 320, 448), bias=128.0, scale=1.0 / 4096)
         L["tagv"] = act(h("tagv"), tagb, bias=-129.0)
-        mm(lin(ps(7, 0, 128), [(IDF, xg), (ID, C["KF"]), (ID, C["DG14"])]))
+        mm(lin(ps(7, 0, 128), [(IDF, xg), (ID, C["KF"]), (ID, C["DG14"])]) + lin(ps(7, 128, 256), [(IDF, xg), (ID, C["DG14"])]))
         mm(lin(ps(3, 0, 128), [(IDF, xg), (ID, C["KF"])]))
-        scan(f("ys_"), C["RS16"], ps(7, 0, 128), MUL, MAX)
-        b1 = act(f("yb1", 8), sub("ys_", 15, 128, 16), bias=-16384.0 - 1.0 / 256)
-        tt(f("yb2", 8), C["kF"], b1, SUB)
+        scan(f("ys_", 256), sub("RS16", 0, 256), ps(7, 0, 256), MUL, MAX)
+        act(f("yb1", 8), sub("ys_", 15, 128, 16), bias=-16384.0 - 1.0 / 256)
+        act(f("yb2", 8), sub("ys_", 143, 256, 16), bias=16384.0 + 1.0 / 256, scale=-1.0)
         f("s1", 8)
         f("s2", 8)
         for a in range(8):
@@ -670,26 +715,36 @@ def rank_program(g, core, T, topo):
         emp = act(h("emp"), out, F.Relu, bias=-1.0, scale=-1.0)
         mm([(ps(7, 256, 384), C["LSI"], emp, True, True)])
         L["nfs"] = act(h("nfs"), ps(7, 256, 384), F.Sign, bias=1.0)
-        terms = [(IDF, sub("s1", 0, 8)), (IDF, sub("s2", 0, 8)), (ID, L["p6"])]
-        mm(lin(ps(7, 384, 392), [(sumto(r), sub("emp", r, 128, 16)) for r in range(16)] + terms) + lin(ps(7, 392, 400), terms))
-        act(f("ov", 8), ps(7, 384, 392), F.Relu, scale=-1.0, acc=f("ovs", 1))
-        L["tr"] = act(h("tr", 8), ps(7, 392, 400), F.Relu, scale=-1.0)
+        twice = [(IDF, sub("s1", 0, 8)), (IDF, sub("s2", 0, 8))]
+        ov, tr = ps(2, 0, 8), ps(7, 392, 400)
+        opens(2, [(ov, ID, L["p6"])] + [(ov, sumto(r), sub("emp", r, 128, 16)) for r in range(16)])
+        closes(2, [(ov, a, b) for a, b in twice])
+        mm(lin(tr, [(ID, L["p6"])] + twice))
+        act(f("ov", 8), ov, F.Relu, scale=-1.0, acc=f("ovs", 1))
+        L["tr"] = act(h("tr", 8), tr, F.Relu, scale=-1.0)
         ovout(f("ovs", 1))
 
     def cand_d(rho):
         nfs, xg = L["nfs"], L["xg"]
-        mm(lin(ps(3, 128, 256), [(IDF, sub("pg_", 0, 128)), (dg(P21), nfs)]) + lin(ps(3, 256, 384), [(IDF, sub("pg_", 128, 256)), (dg(P21), nfs)]))
-        act(o("UP", rho, slice(0, 128)), ps(3, 128, 256), F.Relu, bias=-P21)
-        kept = act(f("kept"), ps(3, 256, 384), F.Relu, bias=-P21)
-        s4 = [(IDF, L["cf"]), (dg(-4096), L["b1"]), (dg(-4096), L["b2"]), (dg(-8192), L["tr"])]
-        mm(lin(ps(7, 0, 128), [(dg(8192), L["tagv"])] + ([(IDF, xg)] if rho == RO - 1 else []) + [(dg(-P21), nfs)])
-           + lin(ps(7, 128, 256), [(dg(-U), L["rkv"]), (dg(1024, True), xg), (ID, L["rkv"]), (dg(8), L["tagv"]), (dg(-P21), nfs)])
-           + lin(ps(7, 400, 408), s4) + lin(ps(7, 408, 416), [(IDF, L["cf"]), (dg(-8192), L["tr"])]) + lin(ps(7, 416, 424), s4)
-           + lin(ps(7, 424, 432), [(IDF, L["cf"]), (dg(4096), L["b2"]), (dg(-8192), L["tr"])]))
-        tt(o("UP", rho, slice(384, 416)), ps(7, 400, 432), C["DM"], MIN)
-        tt(o("UP", rho, slice(256, 384)), ps(7, 0, 128), L["g1"], MAX)
-        L["np1"] = tt(o("UP", rho, slice(128, 256)), ps(7, 128, 256), kept, MAX)
-        msg = o("UP", rho, slice(128, 416))
+        last = rho == RO - 1
+        w = 40 if last else 32
+        key, pay = ps(0, 0, 128), ps(1, 0, 128)
+        opens(0, [(key, dg(8192), L["tagv"])] + ([(key, IDF, xg)] if last else []))
+        opens(1, [(pay, a, b) for a, b in ((dg(-U), L["rkv"]), (dg(1024, True), xg), (ID, L["rkv"]), (dg(8), L["tagv"]))])
+        opens(4, [(ps(4, 0, 256), IDF, sub("pg_", 0, 256))])
+        s4 = [(IDF, L["cf"]), (dg(-4096), L["b1"]), (dg(-4096), L["b2"])]
+        lists = [s4, s4[:1], s4, [(IDF, L["cf"]), (dg(4096), L["b2"])], [(dg(-1, True), sub("yb2", 0, 8)), (dg((fin_lo - fin_hi) / 2), L["b2"])]][:w // 8]
+        opens(5, [(ps(5, 0, w), ID, sub("ZB", 0, w))] + [(ps(5, 8 * k, 8 * k + 8), a, b) for k, x in enumerate(lists) for a, b in x])
+        closes(4, [(ps(4, a, a + 128), dg(P21), nfs) for a in (128, 0)])
+        closes(0, [(key, dg(-P21), nfs)])
+        closes(1, [(pay, dg(-P21), nfs)])
+        closes(5, [(ps(5, 8 * k, 8 * k + 8), dg(-16384 if k == 4 else -8192), L["tr"]) for k in range(w // 8)])
+        kept = act(f("kept"), ps(4, 128, 256), F.Relu, bias=-P21)
+        act(cols("UP", 0, 128), ps(4, 0, 128), F.Relu, bias=-P21)
+        tt(cols("UP", 256, 384), key, L["g1"], MAX)
+        L["np1"] = tt(cols("UP", 128, 256), pay, kept, MAX)
+        tt(cols("UP", 384, 384 + w), ps(5, 0, w), sub("DM", 0, w), MIN)
+        msg = cols("UP", 128, 416)
         trs = [(nxt, T.UA[:, rho, :], msg, "aA%d" % rho, side_engines(core, nxt, topo, cores))]
         if rho < RO - 1:
             trs.append((prv, T.UB[:, rho, :], msg, "aB%d" % rho, side_engines(core, prv, topo, cores)))
@@ -700,10 +755,23 @@ def rank_program(g, core, T, topo):
 
     def insert(rho):
         u("offs", 16)
-        o1 = ts(sub("offs", 8, 16), o("UP", rho, slice(392, 400)), C0, ADD)
-        scat(TGa, o1, o("UP", rho, slice(256, 384)))
-        ts(sub("offs", 0, 8), o("UP", rho, slice(384, 392)), C1, ADD)
-        scat(PTa, sub("offs", 0, 16), o("UP", rho, slice(0, 256)))
+        ts(sub("offs", 0, 16), cols("UP", 384, 400), C0, ADD)
+        scat(TGa, sub("offs", 8, 16), cols("UP", 256, 384))
+        scat(PTa, sub("offs", 0, 16), cols("UP", 0, 256))
+
+    def sums(step):
+        for b in range(8):
+            a = (0 if b < 4 else S2) + 256 * (b % 4)
+            x = cols("YS", a, a + 256)
+            if step:
+                mm([(ps(4 + b % 2, 0, 256), C["BLKF"], x, True, True)])
+                act(x, ps(4 + b % 2, 0, 256), F.Copy)
+            else:
+                cp(x, cols("PT", a, a + 256))
+
+    def sums_of(parts, off):
+        mm(lin(ps(4, 0, 128), [(C["BLKF"], x) for x in parts]))
+        scat(YSa, off, act(f("sm1"), ps(4, 0, 128), F.Copy))
 
     def mirror(rho, buf, a, c):
         off = ts(u("offm" + buf, 8), o(buf, rho, slice(a, a + 8)), c, ADD)
@@ -717,6 +785,11 @@ def rank_program(g, core, T, topo):
     late_consts()
     pack()
     request(0)
+    behind("go1", o("dki"), T.dk[:], 4000.0)
+    iota(o("SR"), [[0, 3072]], 0, 0)
+    f("dk2", 384)
+    for r in range(RO):
+        ts(sub("dk2", 128 * r, 128 * r + 128), cols("dki", 128 * r, 128 * r + 128), (RO - 1 - r) * 2 * U + BIG, ADD)
     homes(t)
     relative(0, 0)
     xw = ts(f("xw", 18), C["kA"], n0, ADD, -1024.0 * t, ADD)
@@ -741,65 +814,55 @@ def rank_program(g, core, T, topo):
     for rho in range(RO):
         last = rho == RO - 1
         lane_prep(rho, KI)
-        for k in range(NP):
-            lookup(rho, k)
         if rho:
             urgent(CFG["u2"], pointer, rho, o("RQ", slice(4 * rho, 4 * rho + 4), slice(0, 96, 88)))
-        urgent(CFG["u2"], miss_pre, rho)
-        urgent(CFG["u7"] if last else CFG["u2"], miss, rho)
+        for k in range(NP - 1):
+            lookup(rho, k)
+
+        def forward(rho=rho):
+            urgent(CFG["u2"], miss_pre, rho)
+            urgent(CFG["u7"], miss, rho)
+        lookup(rho, NP - 1, forward if last else None)
+        if not last:
+            forward()
+        if not rho:
+            for a, r in ((0, t), (S2, (t - 1) % N), (S1, t)):
+                iota(cols("XT", a, a + 1024), [[1, 1024]], 1024 * r, 0)
         image(rho, cols("OY", 128, 256) if last else img)
+        if rho == RO - 2:
+            sums(0)
         if not last:
             for k in range(2):
                 urgent(CFG["u1"], count, rho, k)
             urgent(CFG["u1"], pick, rho)
             urgent(CFG["u1"], cand_a, rho)
-            urgent(CFG["u1"], cand_b, rho, lambda s, rho=rho: ts(o("SQ", slice(8 * rho + 8, 8 * rho + 16), 40 * par), C["ONE"], s, MUL))
-            urgent(CFG["u1"], cand_d, rho)
             KI = unpack(rho)
             address(KI)
             spread(rho + 1)
             place()
+            urgent(CFG["u1"], cand_b, rho, lambda s, rho=rho: ts(o("SQ", slice(8 * rho + 8, 8 * rho + 16), 40 * par), C["ONE"], s, MUL))
+            urgent(CFG["u1"], cand_d, rho)
             pack()
             request(rho + 1)
+            if rho == RO - 2:
+                sums(1)
             insert(rho)
             mirror(rho, "UA", 272, C2)
             mirror(rho, "UB", 280, C3)
 
     rho = RO - 1
     dma("y", T.yi[:], cols("OY", 128, 256))
+    sums_of([L["np1"]], sub("offs", 8, 16))
     for a, r in ((0, t), (S2, (t - 1) % N)):
         for k in range(2):
             act(ps(k, 0, 512), io(512 * k, 512 * k + 512), bias=float(1024 * r))
-        for k in range(2):
-            x = cols("TG", a + 512 * k, a + 512 * k + 512)
-            tt(x, x, ps(k, 0, 512), ADD)
+        for k in range(4):
+            x = cols("TG", a + 256 * k, a + 256 * k + 256)
+            tt(x, x, ps(k // 2, 256 * (k % 2), 256 * (k % 2) + 256), ADD)
     act(ps(0, 0, WIN), io(0, WIN), bias=n0)
     for a in (S3, S4, S5):
         x = cols("TG", a, a + WIN)
         tt(x, x, ps(0, 0, WIN), ADD)
-    for k in range(2):
-        urgent(CFG["u1"], count, rho, k)
-    urgent(CFG["u1"], pick, rho)
-    for b in range(4):
-        a = (0 if b < 2 else S2) + 512 * (b % 2)
-        cp(sub("G", 512 * b, 512 * b + 512), cols("PT", a, a + 512))
-    urgent(CFG["u1"], cand_a, rho)
-    for b in range(4):
-        a = (0 if b < 2 else S2) + 512 * (b % 2)
-        mm([(ps(4 + b % 2, 0, 512), C["BLKF"], sub("G", 512 * b, 512 * b + 512), True, True)])
-        act(cols("XT", a, a + 512), ps(4 + b % 2, 0, 512), F.Copy)
-
-    def ov_last(s):
-        act(cols("SO", 0, 1), s, F.Copy)
-        for k in range(NP):
-            x = send([(cores[d], T.RV[:, t, :], o("SO"), "aO", en) for d, en in pair_call(core, pairs[(me_c + 1 + k) % NP], cores, topo)])
-        act(o("RV", t), o("SO"), F.Copy)
-        arrive("aO", sum(pair_count(t, p, cores, topo) for p in pairs), [o("RV", d) for d in range(N) if d != t], CFG["far"], x)
-    urgent(CFG["u1"], cand_b, rho, ov_last)
-    cand_d(rho)
-    insert(rho)
-    mm([(ps(4, 0, 128), C["BLKF"], L["np1"], True, True)])
-    scat(XTa, sub("offs", 8, 16), act(f("sm1"), ps(4, 0, 128), F.Copy))
     dn = L["dn"]
     inr = tt(f("inr", 18), ts(f("in0", 18), xw, 0.0, GE), ts(f("in1", 18), xw, 1024.0, LT), MUL)
     dl_ = act(f("dl_", 18), C["kA"], bias=float(S1))
@@ -810,20 +873,41 @@ def rank_program(g, core, T, topo):
     dh_ = act(f("dh_", 12), k12, bias=float(WIN))
     zh = tt(f("z4", 12), tt(f("z3", 12), ts(f("xh2", 12), xh, float(WS), ADD), dh_, SUB), inh, MUL)
     offh = cp(u("offh", 12), tt(f("z6", 12), tt(f("z5", 12), ts(f("sp", 12), k12, dn, LT), zh, MUL), dh_, ADD))
+    half = act(f("half", 1), dn, bias=-0.5)
+    done_ = act(h("mv", WIN), io(0, WIN), F.Sign, bias=half, scale=-1.0)
+    m2 = tt(ps(5, 0, WIN), act(ps(1, 0, WIN), done_, bias=-U, scale=-U), cols("TG", S4, S2), ADD)
+    low = tt(f("NX", WIN), m2, cols("TG", S3, S1), MAX)
+    for a, b in ((0, 10), (10, 18)):
+        scat(cols("TG", 0, S4), sub("offl", a, b), sub("NX", 16 * a, 16 * b))
+    scat(cols("TG", S1, S5), offh, cols("TG", S5, S5 + 192))
+    for k in range(2):
+        urgent(CFG["u1"], count, rho, k)
+    urgent(CFG["u1"], pick, rho)
+    urgent(CFG["u1"], cand_a, rho)
+    p1 = tt(sub("PR", 512, 512 + WIN), act(ps(1, 0, WIN), done_, bias=0.5, scale=-0.5), cols("PT", S4, S2), MUL)
+    pa = cp(sub("PR", 0, WIN), cols("PT", S3, S1))
+    pb = cp(sub("PR", 1024, 1024 + 192), cols("PT", S5, S5 + 192))
+    for k, (x, n) in enumerate((([pa, p1], WIN), ([pb], 192))):
+        mm(lin(ps(4 + k, 0, n), [(C["BLKF"], y) for y in x]))
+        act(sub("G", 512 * k, 512 * k + n), ps(4 + k, 0, n), F.Copy)
+    for a, b in ((0, 10), (10, 18)):
+        scat(cols("YS", 0, S4), sub("offl", a, b), sub("G", 16 * a, 16 * b))
+    scat(cols("YS", S1, S5), offh, sub("G", 512, 512 + 192))
+
+    def ov_last(s):
+        act(cols("SO", 0, 1), s, F.Copy)
+        for ks in ([0, 3], [1], [2]):
+            x = send([(cores[d], T.RV[:, t, :], o("SO"), "aO", en) for k in ks for d, en in pair_call(core, pairs[me_c ^ PEER[k]], cores, topo)])
+        act(o("RV", t), o("SO"), F.Copy)
+        arrive("aO", sum(pair_count(t, p, cores, topo) for p in pairs), [o("RV", d) for d in range(N) if d != t], CFG["far"], x)
+    urgent(CFG["u1"], cand_b, rho, ov_last)
+    cand_d(rho)
+    insert(rho)
+    offf = ts(u("offf", 8), cols("UP", 416, 424), C4, ADD)
+    scat(TGa, offf, tt(f("whole"), cols("UP", 256, 384), L["g2"], MAX))
+    sums_of([L["np1"], cols("UP", 0, 128)], offf)
     KI = unpack(rho)
     dma("y", T.yl[:], cp(cols("OY", 0, 128), ts(i_("w"), ts(i_("x"), KI, -BIG, ADD), 1048575, AND)))
-    m2 = tt(ps(6, 128, 128 + WIN), ts(ps(5, 0, WIN), io(0, WIN), dn, LT, -P21, MUL), cols("TG", S4, S2), ADD)
-    low = tt(f("NX", WIN), m2, cols("TG", S3, S1), MAX)
-    scat(cols("TG", 0, S4), offl, low)
-    scat(cols("TG", S1, S5), offh, cols("TG", S5, S5 + 192))
-    p1 = tt(ps(6, 128, 128 + WIN), ts(ps(5, 0, WIN), io(0, WIN), dn, GE), cols("PT", S4, S2), MUL)
-    pa = tt(sub("PR", 0, WIN), p1, cols("PT", S3, S1), ADD)
-    pb = cp(sub("PR", 512, 512 + 192), cols("PT", S5, S5 + 192))
-    for k, (x, n) in enumerate(((pa, WIN), (pb, 192))):
-        mm([(ps(k, 0, n), C["BLKF"], x, True, True)])
-        act(sub("G", 512 * k, 512 * k + n), ps(k, 0, n), F.Copy)
-    scat(cols("XT", 0, S4), offl, sub("G", 0, WIN))
-    scat(cols("XT", S1, S5), offh, sub("G", 512, 512 + 192))
     k6 = sub("kA", 0, 6)
     u("offx", 12)
     f("tg0", 12)
@@ -834,7 +918,7 @@ def rank_program(g, core, T, topo):
         act(sub("dx", 6 * k, 6 * k + 6), k6, bias=96.0 * k + DUMP)
         act(sub("i12", 6 * k, 6 * k + 6), k6, F.Copy)
         xx = ts(f("xx%d" % k, 6), k6, NN[RO - 1], ADD, -1024.0 * r, ADD)
-        ya = tt(f("ya%d" % k, 6), ts(f("yb%d" % k, 6), xx, 0.0, LT, 2 * BIG, MUL), xx, ADD)
+        ya = tt(f("ya%d" % k, 6), ts(f("yq%d" % k, 6), xx, 0.0, LT, 2 * BIG, MUL), xx, ADD)
         yc = ts(f("yc%d" % k, 6), xx, 1024.0, GE, BIG, MUL)
         tt(sub("tg0", 6 * k, 6 * k + 6), ts(f("yd%d" % k, 6), ya, float(base), ADD), yc, ADD)
     mirror(rho, "UA", 272, C2)
@@ -842,18 +926,21 @@ def rank_program(g, core, T, topo):
     kx = act(sub("PR", 1024, 1216), ind(TGa, offx))
     mm([(ps(4, 0, 192), C["BLKF"], cp(sub("PR", 1536, 1728), ind(PTa, offx)), True, True)])
     sx = act(sub("PR", 2048, 2240), ps(4, 0, 192), F.Copy)
+    cap = act(f("cap", 1), NN[RO - 1], bias=8192.0, scale=-1.0)
+    tg1 = tt(f("tg1", 12), ts(f("tg2", 12), sub("i12", 0, 12), cap, GE, BIG, MUL), sub("tg0", 0, 12), ADD)
     boost[0] = CFG["u5"]
-    pointer(RO, o("RV", slice(None), 0))
-    no = ts(f("no", 12), sub("i12", 0, 12), act(f("dv", 1), NN[RO], bias=act(f("nn2", 1), NN[RO - 1], F.Copy, scale=-1.0)), GE, BIG, MUL)
-    offy = cp(u("offy", 12), tt(f("y2", 12), tt(f("y1", 12), no, sub("tg0", 0, 12), ADD), sub("dx", 0, 12), MIN))
+    v = ps(7, 320, 321)
+    mm([(v, C["BLKF"], red(f("v", 1), o("RV", slice(None), 0)), True, True)])
+    no = ts(f("no", 12), sub("i12", 0, 12), v, GE, BIG, MUL)
+    offy = cp(u("offy", 12), tt(f("y2", 12), tt(ps(6, 384, 396), no, tg1, ADD), sub("dx", 0, 12), MIN))
     scat(TGa, offy, kx)
-    dma("y", T.yk[:, 0:1024], cols("TG", 0, S3), 4000.0)
-    dma("s", T.yk[:, 1024:2048], cols("TG", S2, S5), 4000.0)
-    scat(XTa, offy, sx)
+    dma("y", T.yk[:, 0:1024], cols("TG", 0, S3), CFG["st"])
+    dma("s", T.yk[:, 1024:2048], cols("TG", S2, S5), CFG["st"])
+    scat(YSa, offy, sx)
     boost[0] = 0.0
-    dma("y", T.yn[:], cp(cols("OY", 256, 257), NN[RO]))
-    dma("y", T.ys[:, 0:1024], (T.XT[0:128:16, 0:S3], cols("XT", 0, S3)[1], "s"))
-    dma("s", T.ys[:, 1024:2048], (T.XT[0:128:16, S2:S5], cols("XT", S2, S5)[1], "s"))
+    dma("y", T.yn[:], ts(cols("OY", 256, 257), ts(f("v2", 1), v, 96.0, MIN, NN[RO - 1], ADD), 8192.0, MIN))
+    dma("y", T.ys[:, 0:1024], (T.YS[0:128:16, 0:S3], cols("YS", 0, S3)[1], "s"))
+    dma("s", T.ys[:, 1024:2048], (T.YS[0:128:16, S2:S5], cols("YS", S2, S5)[1], "s"))
 
     n = len(ops)
     pre = [op["deps"] | op["soft"] for op in ops]
@@ -864,13 +951,43 @@ def rank_program(g, core, T, topo):
 
     def plan(pre, post, prio, sign):
         left = [len(p) for p in pre]
+        done, taken = [0.0] * n, {q: [] for q in ENG}
+        ready = {me for me in range(n) if not left[me]}
+        while ready:
+            me = max(ready, key=lambda k: (prio[k] + sign * ops[k]["up"], -k))
+            ready.remove(me)
+            q = ops[me]["q"]
+            at = max([done[d] + WAKE for d in pre[me]], default=0.0)
+            if q != "x":
+                hold = ops[me]["c"] if ops[me]["ev"] is None or q == "g" else 60.0
+                row, k = taken[q], 0
+                while k < len(row) and row[k][0] < at + hold - CFG["tol"]:
+                    at = max(at, row[k][1])
+                    k += 1
+                row.insert(k, (at, at + hold))
+            done[me] = at + ops[me]["c"]
+            for k in post[me]:
+                left[k] -= 1
+                if not left[k]:
+                    ready.add(k)
+        return done, sorted(range(n), key=lambda k: done[k] - ops[k]["c"])
+
+    def greedy(pre, post, prio, sign):
+        left = [len(p) for p in pre]
         done, free, order = [0.0] * n, {}, []
         ready = {me: 0.0 for me in range(n) if not left[me]}
         while ready:
             start = {me: max(r, free.get(ops[me]["q"], 0.0)) for me, r in ready.items()}
             first = min(start, key=lambda k: start[k])
             q = ops[first]["q"]
-            me = max((k for k in ready if ops[k]["q"] == q and start[k] <= start[first] + CFG["slack"]), key=lambda k: (prio[k] + sign * ops[k]["up"], -k))
+            mine = [k for k in ready if ops[k]["q"] == q and start[k] <= start[first] + CFG["look"]]
+            val = {k: prio[k] + sign * ops[k]["up"] for k in mine}
+            me = top = max(mine, key=lambda k: (val[k], -k))
+            if start[top] > start[first] and q != "x":
+                late = {k: max(start[k] + val[k], max(start[top], start[k] + ops[k]["c"]) + val[top]) for k in mine if start[k] < start[top]}
+                other = min(late, key=lambda k: (late[k], -val[k], k))
+                if late[other] <= max(start[top] + val[top], start[top] + ops[top]["c"] + val[other]) + 30.0:
+                    me = other
             done[me] = start[me] + ops[me]["c"]
             if q != "x":
                 free[q] = done[me] if ops[me]["ev"] is None or q == "g" else start[me] + 60.0
@@ -881,17 +998,99 @@ def rank_program(g, core, T, topo):
                 if not left[k]:
                     ready[k] = max(done[d] for d in pre[k]) + WAKE
         return done, order
-    prio = [0.0] * n
-    for me in range(n - 1, -1, -1):
-        prio[me] = ops[me]["c"] + max([prio[k] + WAKE for k in post[me]], default=0.0)
-    best = None
-    for _ in range(CFG["passes"]):
-        done, order = plan(pre, post, prio, 1.0)
-        if best is None or max(done) < max(best[0]):
-            best = (done, order)
-        prio = plan(post, pre, done, -1.0)[0]
-    done, order = best
-    PLAN[t] = [(ops[m]["q"], ops[m]["lab"], done[m] - ops[m]["c"]) for m in order]
+    if not CFG["gaps"]:
+        plan = greedy
+
+    def first_order():
+        prio = [0.0] * n
+        for me in range(n - 1, -1, -1):
+            prio[me] = ops[me]["c"] + max([prio[k] + WAKE for k in post[me]], default=0.0)
+        best = None
+        for _ in range(CFG["passes"]):
+            done, order = plan(pre, post, prio, 1.0)
+            CFG.setdefault("log", []).append(int(max(done)))
+            if best is None or max(done) < max(best[0]):
+                best = (done, order)
+            prio = plan(post, pre, done, -1.0)[0]
+        return best[1]
+
+    def clocked(rows):
+        before, after_ = [-1] * n, [-1] * n
+        for row in rows.values():
+            for a, b in zip(row, row[1:]):
+                before[b], after_[a] = a, b
+        left = [len(pre[k]) + (before[k] >= 0) for k in range(n)]
+        at, why, seen = [0.0] * n, [-1] * n, [k for k in range(n) if not left[k]]
+        for k in seen:
+            e = at[k] + cost_[k] + WAKE
+            for j in post[k]:
+                if e > at[j]:
+                    at[j], why[j] = e, k
+                left[j] -= 1
+                if not left[j]:
+                    seen.append(j)
+            j = after_[k]
+            if j >= 0:
+                if at[k] + hold[k] > at[j]:
+                    at[j], why[j] = at[k] + hold[k], k
+                left[j] -= 1
+                if not left[j]:
+                    seen.append(j)
+        if len(seen) < n:
+            return None
+        end = max(at[k] + cost_[k] for k in range(n))
+        return end, at, why, seen, end + CFG["lam"] * sum(at[k] for k in marks) / len(marks)
+    marks = [k for k in range(n) if ops[k]["q"] == "g" and ops[k]["ev"]]
+    kids = [set(p) for p in post]
+
+    def mend(order):
+        rows = {q: [k for k in order if ops[k]["q"] == q] for q in "vspy"}
+        now = top = clocked(rows)
+        seed = 1
+        for step in range(CFG["mend"]):
+            seed = (seed * 1103515245 + 12345) % 2147483648
+            k, edges = max(range(n), key=lambda k: now[1][k] + cost_[k]) if (seed >> 12) % 4 else marks[(seed >> 14) % len(marks)], []
+            while now[2][k] >= 0:
+                if now[2][k] not in pre[k]:
+                    edges.append((now[2][k], k))
+                k = now[2][k]
+            if not edges:
+                continue
+            seed = (seed * 1103515245 + 12345) % 2147483648
+            a, b = edges[(seed >> 8) % len(edges)]
+            row = rows[ops[a]["q"]]
+            i = row.index(a)
+            old = list(row)
+            if (seed >> 16) % 2:
+                j = i + 1
+                while j < len(row) and j - i < 24 and row[j] not in kids[a]:
+                    j += 1
+                row.insert(i + 1 + (seed >> 18) % (j - i - 1) if (seed >> 17) % 2 and j > i + 1 else j - 1, row.pop(i))
+            else:
+                j = i
+                while j >= 0 and i - j < 24 and row[j] not in pre[b]:
+                    j -= 1
+                row.insert(i - (seed >> 18) % (i - j), row.pop(i + 1))
+            new = clocked(rows)
+            if new is None or new[4] > now[4] + CFG["warm"] * (1 - step / CFG["mend"]):
+                row[:] = old
+            else:
+                now = new
+                if new[0] < top[0]:
+                    top = new
+        place_ = {k: i for i, k in enumerate(top[3])}
+        CFG["log"].append(int(top[0]))
+        return sorted(range(n), key=lambda k: (top[1][k], place_[k]))
+    cost_ = [op["c"] for op in ops]
+    hold = [op["c"] if op["ev"] is None else 60.0 for op in ops]
+    shape = tuple((op["q"], op["c"]) for op in ops)
+    again = clocked({q: [k for k in ORDERS[shape] if ops[k]["q"] == q] for q in "vspy"}) if shape in ORDERS else None
+    if again:
+        place_ = {k: i for i, k in enumerate(again[3])}
+        order = sorted(range(n), key=lambda k: (again[1][k], place_[k]))
+    else:
+        order = ORDERS[shape] = mend(first_order())
+    PLAN.update(slots)
     pos = {me: k for k, me in enumerate(order)}
     ops = [ops[me] for me in order]
     for op in ops:

@@ -9,8 +9,8 @@ SWW, OS, PARTS = 6464, 132, 2
 C0, C1, C2, C3 = 8192.0, 16384.0 - WS, 16384.0 + WS, 12288.0 - WS
 PEER = (2, 3, 1, 0)
 PLAN, ORDERS = {}, {}
-CFG = {"gv": 64, "npk": 4, "tol": 0.0, "passes": 2, "g0": 16, "fix": 45.0, "fixs": 60.0, "least": 16.0, "wake": 70.0, "pe": 0.45, "cy": 0.85, "wv": (4, 6), "apart": (2,), "look": 400.0, "gaps": False, "mend": 4000, "warm": 40.0, "lam": 1.0, "send": 700.0,
-       "u1": 0.0, "u2": 0.0, "u3": 0.0, "u4": 0.0, "u5": 0.0, "u7": 0.0, "far": 2800.0, "near": 2200.0, "lk": 7000.0, "lp": 10000.0, "ld": 2400.0, "ld2": 8000.0, "st": 6500.0}
+CFG = {"gv": 72, "cuts": (0, 32, 64, 128), "wl": (), "gl": (), "gconv": True, "tol": 0.0, "passes": 2, "g0": 0, "fix": 45.0, "fixs": 60.0, "least": 16.0, "wake": 90.0, "pe": 0.45, "cy": 0.85, "wv": (5, 7), "apart": (0, 1, 2), "prk": 0, "early": 0, "fine": True, "pgk": 3, "upk": False, "lp0": False, "nv": 4, "nd": 0, "ysl": True, "tb": 1, "late": 9, "looks": (120.0, 180.0, 250.0, 320.0, 400.0, 500.0), "gaps": False, "mend": 200, "warm": 150.0, "lam": 0.0, "bar": 12, "send": 750.0,
+       "u1": 0.0, "u2": 0.0, "u3": 0.0, "u4": 0.0, "u5": 0.0, "u7": 0.0, "u6": 3000.0, "u8": 0.0, "u9": 0.0, "ao": 1, "ff": (2,), "far": 2600.0, "near": 2000.0, "q0": 300.0, "qk": 300.0, "a0": 400.0, "a1": 1500.0, "lk": 7000.0, "lp": 10000.0, "ld": 2400.0, "ld2": 8000.0, "st": 4300.0}
 SCRATCH = {
     "lki": ("sbuf", [128, 128], "int32"), "lii": ("sbuf", [128, 128], "int32"), "dki": ("sbuf", [128, 384], "int32"),
     "pni": ("sbuf", [128, 1], "int32"), "KR": ("sbuf", [128, 2048], "int32"), "PT": ("sbuf", [128, TW], "int32"),
@@ -23,7 +23,7 @@ SCRATCH = {
     "UP": ("sbuf", [128, 424], "float32"), "UA": ("sbuf", [128, 3, 288], "float32"), "UB": ("sbuf", [128, 2, 288], "float32"),
     "SO": ("sbuf", [128, 4], "float32"), "RV": ("sbuf", [128, 8, 4], "float32"),
     "OY": ("sbuf", [128, 260], "float32"),
-    "TF": ("sbuf", [128, 14848], "float32"), "TI": ("sbuf", [128, 1408], "int32"), "TB": ("sbuf", [128, 20992], "bfloat16"),
+    "TF": ("sbuf", [128, 14720], "float32"), "TI": ("sbuf", [128, 1408], "int32"), "TB": ("sbuf", [128, 22784], "bfloat16"),
     "TU": ("sbuf", [128, 512], "uint16"),
 }
 for _b in range(8):
@@ -120,7 +120,7 @@ def rank_program(g, core, T, topo):
     FIX, WAKE, PE, CY = CFG["fix"], CFG["wake"], CFG["pe"], CFG["cy"]
     ops, acc, bank, slots = [], {}, {}, {}
     cnt = {"d": 0, "l": 0, "TF": 0, "TI": 0, "TB": 0, "TU": 0}
-    lastg, boost = [], [0.0]
+    lastg, boost, later = [], [0.0], []
 
     def urgent(v, fn, *a):
         boost[0] = v
@@ -205,6 +205,8 @@ def rank_program(g, core, T, topo):
                         keep.append(e)
                 keep.append((m, me, w))
                 acc[k] = keep
+        if q == "s":
+            soft.update(later)
         if q == "g":
             soft.update(lastg[-1:])
             lastg.append(me)
@@ -274,11 +276,17 @@ def rank_program(g, core, T, topo):
         if fl:
             rec("g", lambda e: e.iota(out[0], pat, base, cm, allow_small_or_imprecise_dtypes=True), [], out[1], c=130 + 1.7 * size(out))
         else:
-            rec("g", lambda e: e.iota(out[0], pat, base, cm), [], out[1], c=140.0)
+            rec("g", lambda e: e.iota(out[0], pat, base, cm), [], out[1], c=130 + 1.7 * size(out))
         return out
 
     def keep_if(out, a, op, fill):
         rec("g", lambda e: e.affine_select(out[0], a[0], [[1, 128]], op, fill, 0, -1), st(a), out[1], c=400.0)
+        return out
+
+    def as_float(out, a):
+        if not CFG["gconv"]:
+            return cp(out, a)
+        rec("g", lambda e: e.affine_select(out[0], a[0], [[0, size(out)]], A.is_equal, 0.0, 0, 0), st(a), out[1], c=170.0 + 1.7 * size(out))
         return out
 
     def dma(q, out, a, c=2500.0, after=(), reads=()):
@@ -315,7 +323,8 @@ def rank_program(g, core, T, topo):
         return sub("IO", a, b)
     boost[0] = CFG["u3"]
     ms(cols("SW", 0, 2560), 0.0)
-    act(o("T2"), cols("SW", 0, 2048), F.Copy)
+    for k in range(4):
+        act(o("T2", slice(32 * k, 32 * k + 32)), cols("SW", 0, 512), F.Copy)
     ms(h("OH", 9 * OS), 0.0)
     pr = cp(f("pr", 1), ts(i_("pri", 1), pidx, 15, AND))
     pg = cp(f("pg", 1), ts(i_("pgi", 1), pidx, 4, SHR))
@@ -333,15 +342,23 @@ def rank_program(g, core, T, topo):
     n0 = cp(f("n0", 1), n0i)
     n288 = ts(f("n288", 1), n0, float(WIN), ADD, 8192.0, MIN)
     d0 = ts(f("d0", 1), ts(i_("d0i", 1), n0i, 1023, AND), -1.0, MUL, 1024.0, ADD)
-    img = cp(f("img"), o("lii"))
+    L = {"img": o("lii")}
     KI = ts(i_("KI"), o("lki"), 6 * U + BIG, ADD)
     DJ = cp(ps(6, 0, 128), DJs)
     C, diags = {}, {}
 
-    def dg(v, wide=False):
+    def dg(v, wide=False, own=0):
+        if own:
+            own = "dgo%d" % own
+            if own not in slots:
+                keep_if(h(own), C["ZT"], A.not_equal, float(v))
+            return h(own)
         if (v, wide) not in diags:
             nm = "dg%d" % len(diags)
-            diags[(v, wide)] = act((f if wide else h)(nm), ID, F.Copy, scale=float(v))
+            if "ZT" in C and not wide:
+                diags[(v, wide)] = keep_if(h(nm), C["ZT"], A.not_equal, float(v))
+            else:
+                diags[(v, wide)] = act((f if wide else h)(nm), ID, F.Copy, scale=float(v))
         return diags[(v, wide)]
     IDF = dg(1, True)
     nn0 = act(f("nn0", 1), n0, F.Copy, scale=-1.0)
@@ -373,11 +390,8 @@ def rank_program(g, core, T, topo):
     C4 = (fin_lo + fin_hi) / 2 + 1.0 / 256 + 16384.0
 
     def late_consts():
-        ri16 = iota(f("ri16"), [[0, 8], [1, 16]], 0, 0)
-        C["LSI"] = keep_if(h("LSI"), LS, A.not_equal, -1.0)
-        ts(f("M16", 16), io(0, 16), pr, EQ)
-        for r in range(16):
-            act(o("BC", r), BLK, F.Copy, scale=sub("M16", r, r + 1))
+        iota(o("SR", slice(0, 128)), [[0, 2048]], 0, 0)
+        rec("g", lambda e: e.affine_select(T.BC[:], T.SR[:, 0:128, :], [[-1, 16], [-16, 8], [0, 16]], A.not_equal, 1.0, 0, 1), o("SR", slice(0, 128))[1], o("BC")[1], c=3650.0)
         C["BLKF"] = act(f("BLKF"), BLK, F.Copy)
         f("GIF", 16)
         h("GIB", 16)
@@ -388,38 +402,39 @@ def rank_program(g, core, T, topo):
         act(h("ZB", 40), io(0, 40), F.Copy, scale=0.0)
         act(sub("ZB", 0, 8), io(0, 8), bias=C1 - C0, scale=0.0)
         C["KB"] = act(f("KB", 8), sub("kA", 0, 8), bias=-0.5, scale=-1.0)
-        C["DG"] = ts(h("DG"), ri16, pr, EQ, P21, MUL)
-        f("RS16", 256)
-        for k in (0, 128):
-            act(sub("RS16", k, k + 128), ri16, F.Sign)
-        C["RS16"] = sub("RS16", 0, 128)
+        h("kF", 16)
+        act(sub("kF", 0, 8), sub("kA", 0, 8), F.Copy, scale=1.0 / 128)
+        act(sub("kF", 8, 16), sub("kA", 0, 8), F.Copy, scale=0.0)
+        nh = act(h("nh", 1), n0, F.Copy, scale=0.5)
+        C["NH"] = act(h("NH"), ID, F.Copy, scale=act(f("nhf", 1), nh, F.Copy))
+        C["NL"] = act(h("NL"), ID, F.Copy, scale=ts(f("nl", 1), n0, 0.5, MUL, nh, SUB))
+        C["bx1"] = act(f("bx1", 1), n0, bias=512.0 * t - 512 - WS - 1.0 / 256, scale=0.5)
+        C["bx2"] = act(f("bx2", 1), n0, bias=512.0 + WS - 512 * t + 1.0 / 256, scale=-0.5)
         C["ONE"] = act(f("ONE", 8), io(0, 8), bias=1.0, scale=0.0)
         C["IO1"] = cp(ps(6, 128, 256), io(1, 129))
         C["DM"] = f("DM", 40)
         for k, v in enumerate((DUMP + 128 - C0, DUMP - C0, DUMP - C2, DUMP - C3, DUMP - C4)):
             act(sub("DM", 8 * k, 8 * k + 8), sub("kA", 0, 8), bias=float(v))
         h("R2", 336)
-        ms(sub("R2", 0, 1), 0.0)
+        act(sub("R2", 0, 1), io(0, 1), F.Copy, scale=0.0)
         f("cumM", 336)
         act(sub("cumM", 320, 336), io(0, 16), F.Copy, scale=0.0)
-        ms(o("CAT", slice(None), slice(320, 336)), 0.0)
+        act(o("CAT", slice(None), slice(320, 336)), io(0, 48), F.Copy, scale=0.0)
         act(cols("W", 2560, 2576), io(0, 16), F.Copy, scale=0.0)
         act(h("YN", 144), Y, F.Copy, scale=-U)
-        C["DG14"] = act(h("DG14"), C["DG"], F.Copy, scale=1.0 / 128)
         C["KF"] = act(h("KF"), io(0, 128), F.Copy, scale=1.0 / 128)
         act(cols("TG", DUMP, TW), io(0, TW - DUMP), F.Copy, scale=0.0)
-        ms(cols("PT", DUMP, TW), 0)
         act(cols("XT", DUMP, TW), io(0, TW - DUMP), F.Copy, scale=0.0)
         act(o("SO"), io(0, 4), F.Copy, scale=0.0)
         for a in (S3, S4, S5):
             act(cols("XT", a, a + WIN), io(0, WIN), bias=n0)
 
-    def homes(r):
-        for k, b in enumerate((3, 7)):
+    def homes(r, banks):
+        for k, b in enumerate(banks):
             act(ps(b, 0, 512), io(512 * k, 512 * k + 512), bias=float(1024 * r))
 
-    def relative(a, z):
-        for k, b in enumerate((3, 7)):
+    def relative(a, z, banks):
+        for k, b in enumerate(banks):
             tt(cols("TG", a + 512 * k, a + 512 * k + 512), cols("KR", z + 512 * k, z + 512 * k + 512), ps(b, 0, 512), SUB)
 
     def behind(sem, dst, src, c):
@@ -436,18 +451,17 @@ def rank_program(g, core, T, topo):
                            for k, x in enumerate(hs)])
         else:
             s1 = send([(prv, T.PT[:, S1:S4], cols("PT", S2, S5), "aP", halves(core, prv, topo)[1])])
-        homes((t - 1) % N)
-        relative(S2, 1024)
+        homes((t - 1) % N, (3, 7))
+        relative(S2, 1024, (3, 7))
         s2 = send([(prv, T.TG[:, S1:S4], cols("TG", S2, S5), "aK", topo.engines(core, prv) if hs else halves(core, prv, topo)[0])])
         behind("go0", cols("PT", 0, S3), T.tp[:, 0:1024], CFG["ld2"])
         arrive("aP", PARTS * sum(len(topo.engines(x, core)) for x in hn) if hn else len(halves(nxt, core, topo)[1]), [cols("PT", S1, S4)], CFG["lp"], s1)
         arrive("aK", len(topo.engines(nxt, core)) if hn else len(halves(nxt, core, topo)[0]), [cols("TG", S1, S4)], CFG["lk"], s2)
-    L = {}
 
     def address(KI):
         w = L["w"] = ts(i_("w"), KI, 16383, AND)
         rk = ts(i_("rk"), KI, 10, SHR, 7, AND)
-        old = tt(h("old"), w, img, LT)
+        old = tt(h("old"), w, L["img"], LT)
         s = L["s"] = tt(h("s"), old, rk, ADD)
         boost[0] = CFG["u4"]
         xf = L["xf"] = cp(f("xf"), ts(i_("x"), KI, 8191, AND))
@@ -501,9 +515,12 @@ def rank_program(g, core, T, topo):
         ts(u("off"), mx, -BIG, ADD)
 
     def pack():
-        w = 128 // CFG["npk"]
-        for j in range(CFG["npk"]):
-            scat(SWa, sub("off", w * j, w * j + w), sub("SRC", 16 * w * j, 16 * w * (j + 1)))
+        for a, b in zip(CFG["cuts"], CFG["cuts"][1:]):
+            scat(SWa, sub("off", a, b), sub("SRC", 16 * a, 16 * b))
+            if a == CFG["cuts"][CFG["pgk"]] and "pgop" in L:
+                ops[-1]["soft"].add(L["pgop"])
+            if b == 128 and "upop" in L and CFG["upk"]:
+                ops[-1]["soft"].update(L["upop"])
 
     def request(rho):
         ca, ta = (0, 20) if par else (28, 8)
@@ -518,49 +535,59 @@ def rank_program(g, core, T, topo):
                 for k in ks:
                     c = me_c ^ PEER[k]
                     land = o("RQ", 4 * rho + c, slice(48 - 48 * par, 96 - 48 * par)) if c == me_c else o("RQ", 4 * rho + c)
-                    arrive("aQ%d%d" % (rho, k), pair_count(t, pairs[c], cores, topo), [land], CFG["near" if c == me_c else "far"], s)
+                    arrive("aQ%d%d" % (rho, k), pair_count(t, pairs[c], cores, topo), [land], CFG["near"] if c == me_c else CFG["far"] + CFG["q0"] + CFG["qk"] * k, s)
         cp(o("RQ", 4 * rho + me_c, slice(48 * par, 48 * par + 48)), o("SQ", 8 * rho + t))
 
     def lane_prep(rho, KI):
         ts(u("off2"), L["mx"], -BIG, ADD, 2560.0, MIN)
-        gate = act(ps(2, 384, 512), L["ng"], bias=-16 * U, scale=16 * U)
-        far = act(ps(2, 128, 256), L["ng"], bias=1.0, scale=16384.0)
+        gate = act(ps(2, 384, 512), L["ng"], bias=-16 * U - BIG * (rho == RO - 1), scale=16 * U)
         L["base"] = tt(f("base"), tt(ps(6, 384, 512), KI, gate, ADD), sub("dk2", 128 * rho, 128 * rho + 128), MAX)
-        L["y1"] = tt(f("y1_"), L["w"], far, ADD)
+        mm(lin(ps(7, 0, 128), [(IDF, L["xf"]), (dg(-16384), L["hb"]), (dg(16384), L["ng"])]))
+        L["y1"] = act(f("y1_"), ps(7, 0, 128), bias=16385.0)
+        L["y1op"] = ops[-1]
 
     def image(rho, out):
         nb = act(f("nb", 1), NN[rho], bias=16384.0, scale=16384.0)
-        yes = act(f("imy"), L["y1"], bias=nb, scale=-16384.0)
-        tt(out, tt(ps(6, 384, 512), yes, L["y1"], MIN), img, MAX)
+        yes = act(ps(4, 128, 256), L["y1"], bias=nb, scale=-16384.0)
+        L["img"] = tt(out, tt(ps(6, 384, 512), yes, L["y1"], MIN), L["img"], MAX)
 
-    def unpack_block(rho, k):
-        c = (me_c ^ PEER[2 * k]) // 2
-        ans = cols("RR", 192 * rho + 96 * c, 192 * rho + 96 * c + 96)
-        z = slice(96 * c, 96 * c + 96)
-        up = ts(f("r1%d" % k, 96), ans, 1.5 * 2.0 ** 31, ADD, 1.5 * 2.0 ** 31, SUB)
+    def unpack_block(rho, k, d0, nd):
+        ans = cols("RR", 192 * rho + 24 * d0, 192 * rho + 24 * (d0 + nd))
+        z = slice(24 * d0, 24 * (d0 + nd))
+        f("r1", 192)
+        up = ts(sub("r1", 24 * d0, 24 * (d0 + nd)), ans, 1.5 * 2.0 ** 31, ADD, 1.5 * 2.0 ** 31, SUB)
         hi = ts(o("SR", z, 0), ans, 1.5 * 2.0 ** 39, ADD, 1.5 * 2.0 ** 39, SUB)
         tt(o("SR", z, 2), ans, up, SUB)
         tt(o("SR", z, 1), up, hi, SUB)
-        for s in range(4):
-            d, b = 4 * c + s, (0, 4, 1, 5)[s] if k else s % 2
+        for s in range(nd):
+            d, b = d0 + s, (0, 1, 0, 1, 0, 4, 1, 5)[k + s]
             mm([(ps(b, a, a + n), o("SR", slice(24 * d + 8 * j, 24 * d + 8 * j + 8)), sub("ID", lo, lo + n), True, True)
                 for j, (a, n, lo) in enumerate(((0, 64, 64), (64, 128, 0), (192, 128, 0)) if par else ((0, 128, 0), (128, 128, 0), (256, 64, 0)))])
-            if 4 * k + s in CFG["wv"] and rho < RO - 1:
+            if k + s in CFG["wv" if rho < RO - 1 else "wl"]:
                 cp(cols("W", CAP * d, CAP * d + CAP), ps(b, 0, CAP))
             else:
                 act(cols("W", CAP * d, CAP * d + CAP), ps(b, 0, CAP), F.Copy)
+                if CFG["early"] and rho < RO - 1:
+                    ops[-1]["soft"].add(L["m0"])
 
     def unpack(rho):
-        for k in range(2):
-            unpack_block(rho, k)
+        unpack_block(rho, 0, (me_c ^ PEER[0]) // 2 * 4, 4)
+        if rho < RO - 1 and CFG["fine"]:
+            unpack_block(rho, 4, t, 1)
+            unpack_block(rho, 5, 2 * (me_c ^ PEER[2]), 2)
+            unpack_block(rho, 7, t + 1 - 2 * par, 1)
+        else:
+            unpack_block(rho, 4, me_c // 2 * 4, 4)
         Wa, gv = cols("W", 0, 2576), CFG["gv"]
         h("GR", 2048)
         if rho == RO - 1:
             for a in range(0, 128, 16):
-                act(sub("GR", 16 * a, 16 * a + 256), ind(Wa, sub("off2", a, a + 16)))
+                (cp if a // 16 in CFG["gl"] else act)(sub("GR", 16 * a, 16 * a + 256), ind(Wa, sub("off2", a, a + 16)))
         else:
             cp(sub("GR", 0, 16 * gv), ind(Wa, sub("off2", 0, gv)))
             act(sub("GR", 16 * gv, 2048), ind(Wa, sub("off2", gv, 128)))
+            if CFG["early"] > 1:
+                ops[-1]["soft"].add(L["n0"][CFG["early"] - 2])
         for a, b in ((0, gv), (gv, 128)):
             mm(lin(ps(2, a, b), [(sumto(r), sub("GR", 16 * a + r, 16 * b, 16)) for r in range(16)]))
         return tt(i_("KI"), ps(2, 0, 128), L["base"], MAX)
@@ -585,16 +612,25 @@ def rank_program(g, core, T, topo):
             ts(o("TQ", slice(4 * c, 4 * c + 4)), o("RQ", 4 * rho + c, slice(8, 88)), -256.0 * (rho + 1) - 1.0, ADD, 8192.0, MUL)
         elif k == 2:
             ts(o("TQ", slice(c // 2 * 8, c // 2 * 8 + 8)), o("RQ", both, slice(8, 88)), -256.0 * (rho + 1) - 1.0, ADD, 8192.0, MUL)
+            ops[-1]["soft"].add(L["pr"])
         gv = 0 if k else CFG["g0"]
         if gv:
             cp(sub("G", a, a + 16 * gv), ind(cols("TG", 0, top), o("RQ", 4 * rho + c, slice(28, 28 + gv))))
         act(sub("G", a + 16 * gv, a + 640), ind(cols("TG", 0, top), o("RQ", 4 * rho + c, slice(28 + gv, 68))))
+        if not k and "y1op" in L:
+            L.pop("y1op")["soft"].add(len(ops) - 1)
+        if not rho and k == CFG["late"]:
+            later.append(len(ops) - 1)
+            for op in lc:
+                op["soft"].update(later)
         b0 = 2 * (k % 2)
         mm([(ps(b0 + q % 2, q // 2, 320, 8), o("BC", q), o("TQ", slice(4 * c, 4 * c + 4, 3)), True, True) for q in range(16)])
         ahead = []
         if k == 2:
             cp(f("cf", 160), o("RQ", slice(4 * rho, 4 * rho + 4), slice(28, 68)))
             ahead = [len(ops) - 1] + L.pop("ahead", [])
+            for x in ahead:
+                ops[x]["soft"].add(L["pr"])
         for e in range(2):
             tt(sub("EQ", a + e, a + 640, 2), sub("G", a + e, a + 640, 2), ps(b0 + e, 0, 320), EQ)
             ops[-1]["soft"].update(ahead)
@@ -608,24 +644,26 @@ def rank_program(g, core, T, topo):
 
         def answers(lo, hi):
             tt(sub("PR", a + 128 * lo, a + 128 * hi), ind(cols("PT", 0, top), o("RQ", 4 * rho + c, slice(28 + 8 * lo, 28 + 8 * hi))), sub("EQ", a + 128 * lo, a + 128 * hi), MUL)
+            if k == CFG["prk"]:
+                L["pr"] = len(ops) - 1
             items = []
             for j in range(lo, hi):
                 y, x0 = a + 128 * j, 8 * j + 8 * (j > 2)
                 n = 16 if j == 2 else 8
                 items += lin(ps(b, x0, x0 + n), [(sub("EQ", y, y + 128), sub("GIB", 0, n)), (sub("PR", y, y + 128), sub("GIF", 0, n))])
             mm(items)
-        x = t + 1 - 2 * par
+        x, more = t + 1 - 2 * par, BIG * (rho < RO - 1)
         if c == me_c:
             answers(*((0, 3) if par else (2, 5)))
-            act(cols("SA", 24 * x, 24 * x + 24), ps(b, 24 - 24 * par, 48 - 24 * par), bias=BIG)
+            act(cols("SA", 24 * x, 24 * x + 24), ps(b, 24 - 24 * par, 48 - 24 * par), bias=more)
         else:
             answers(0, 5)
-            act(cols("SA", 48 * c, 48 * c + 48), ps(b, 0, 48), bias=BIG)
+            act(cols("SA", 48 * c, 48 * c + 48), ps(b, 0, 48), bias=more)
         s = send([(cores[d], T.RR[:, z + 24 * t:z + 24 * t + 24], cols("SA", 24 * d, 24 * d + 24), "aR%d%d" % (rho, k), en)
                   for d, en in pair_call(core, pairs[c], cores, topo)])
         if c == me_c:
             answers(*((3, 5) if par else (0, 2)))
-            act(cols("RR", z + 24 * t, z + 24 * t + 24), ps(b, 24 * par, 24 * par + 24), bias=BIG)
+            act(cols("RR", z + 24 * t, z + 24 * t + 24), ps(b, 24 * par, 24 * par + 24), bias=more)
             arrive("aR%d%d" % (rho, k), pair_count(t, pairs[c], cores, topo), [cols("RR", z + 24 * x, z + 24 * x + 24)], CFG["near"], s)
         else:
             arrive("aR%d%d" % (rho, k), pair_count(t, pairs[c], cores, topo), [cols("RR", z + 48 * c, z + 48 * c + 48)], CFG["far"], s)
@@ -643,7 +681,7 @@ def rank_program(g, core, T, topo):
         return act(f(nm, 160), ps(7, 0, 160), F.Relu, bias=bias)
 
     def found(a):
-        mm(lin(ps(6, 256 + 80 * a, 336 + 80 * a), [(dg(8192), sub("C128", 0, 80))] + [(sumto(r, "YN"), sub("EQ", 1280 * a + r, 1280 * a + 1280, 16)) for r in range(16)]))
+        mm(lin(ps(6, 256 + 80 * a, 336 + 80 * a), [(dg(8192), sub("C128", 0, 80))] + [(sumto(r, "YN"), sub("EQ", 1280 * a + r, 1280 * a + 1280, 16)) for r in range(16)]), ps(6, 256, 416)[1])
 
     def miss(rho):
         out = ps(6, 256, 416)
@@ -659,12 +697,24 @@ def rank_program(g, core, T, topo):
         h("m", 320)
         f("ACC", 16)
         m = act(sub("m", a, b), o("CAT", rho, slice(a, b)), F.Sign)
+        if not k:
+            L["m0"], L["n0"] = len(ops) - 1, []
         scan(sub("R2", a + 1, b + 1), m, sub("C128", 0, b - a), ADD, MIN, sub("R2", a, a + 1) if k else 0.0)
         mm([(ps(3, a, b), BLK, sub("R2", a + 1, b + 1), True, True)])
         mm(lin(ps(7, a, b), [(BLK, sub("R2", a, b)), (LB[0], m)]))
-        for j in range(8):
+        nv = CFG["nv"] if k and rho == RO - 1 else 0
+        if nv:
+            cum, z = act(h("cumb", 160), ps(3, a, b), F.Copy), 640 * (me_c ^ PEER[0])
+            for j in range(nv):
+                ts(sub("EQ", z + 160 * j, z + 160 * j + 160), cum, sub("kB", j + 8 - nv, j + 9 - nv), GT)
+            y = 640 * (me_c ^ PEER[1])
+            scan(sub("EQ", y, y + 160 * nv), sub("RS160", 0, 160 * nv), sub("EQ", z, z + 160 * nv), MUL, ADD)
+            ts(sub("ACC", 16 - nv, 16), sub("EQ", y + 159, y + 160 * nv, 160), 2.0, MUL, -160.0, ADD)
+        for j in range(8 - nv):
             h("junk%d" % (j % 2), 320)
             act(sub("junk%d" % (j % 2), 0, b - a), ps(3, a, b), F.Sign, bias=sub("KB", j, j + 1), acc=sub("ACC", 8 * k + j, 8 * k + j + 1))
+            if not k:
+                L["n0"].append(len(ops) - 1)
         act(sub("cumM", a, b), ps(7, a, b), F.Relu, bias=1.0 - BIG)
 
     def pick(rho):
@@ -682,36 +732,52 @@ def rank_program(g, core, T, topo):
         col = ts(i_("colA", 8), ca, 4095, AND)
         u("offg", 24)
         o1 = cp(sub("offg", 8, 16), col)
-        cf = L["cf"] = cp(f("colf", 8), col)
+        cf2 = f("colf", 16)
+        cf = L["cf"] = cp(sub("colf", 0, 8), col)
+        cp(sub("colf", 8, 16), col)
         xg = L["xg"] = act(f("xg"), ind(XTa, o1))
         L["g1"] = act(f("g1"), ind(TGa, o1))
-        for nm, b, sc in (("a1", L["th3"], 1.0), ("a2", S1 - 0.5, -1.0), ("b1", 0.5 - S4, 1.0), ("b2", S2 - 0.5, -1.0), ("p6", 0.5 - DUMP, 1.0)):
+        for nm, b, sc in (("c1", 0.5 - S3, 1.0), ("b1", 0.5 - S4, 1.0), ("b2", S2 - 0.5, -1.0), ("c4", 0.5 - S5, 1.0)):
+            act(h("c" + nm, 16), cf2, F.Sign, bias=b, scale=sc)
+            L[nm] = sub("c" + nm, 0, 8)
+        tp = (t - 1) % N + 1
+        mm(lin(ps(7, 0, 16), [(IDF, cf2), (ID, h("kF", 16)), (dg(-512 * (t + 1), own=1), h("cc1", 16)), (dg(-WS // 2), h("cb1", 16)),
+                              (dg(WS // 2 - 512 * tp, own=2), h("cb2", 16)), (dg(-512 * tp, own=3), h("cc4", 16))] + [(C[a], h(b, 16)) for a in ("NH", "NL") for b in ("cc1", "cb2", "cc4")]))
+        act(f("yb1", 8), ps(7, 0, 8), bias=C["bx1"])
+        act(f("yb2", 8), ps(7, 8, 16), bias=C["bx2"], scale=-1.0)
+        for nm, b, sc in (("a1", L["th3"], 1.0), ("a2", S1 - 0.5, -1.0), ("p6", 0.5 - DUMP, 1.0)):
             L[nm] = act(h("c" + nm, 8), cf, F.Sign, bias=b, scale=sc)
         other = [(IDF, cf), (dg(WS // 2), L["a1"]), (dg(WS // 2), L["a2"]), (dg(-WS // 2), L["b1"]), (dg(-WS // 2), L["b2"])]
         mm(lin(ps(7, 448, 456), other) + lin(ps(7, 456, 464), other + [(dg(-4096), L[x]) for x in ("a1", "a2", "b1", "b2")]))
         o2 = cp(sub("offg", 16, 24), ps(7, 448, 456))
         ts(sub("offg", 0, 8), ps(7, 456, 464), 8192.0, ADD, float(ZC), MIN)
         L["g2"] = act(f("g2"), ind(TGa, o2))
-        tagb = act(h("tagb"), ps(3, 320, 448), bias=128.0, scale=1.0 / 4096)
-        L["tagv"] = act(h("tagv"), tagb, bias=-129.0)
-        mm(lin(ps(7, 0, 128), [(IDF, xg), (ID, C["KF"]), (ID, C["DG14"])]) + lin(ps(7, 128, 256), [(IDF, xg), (ID, C["DG14"])]))
-        mm(lin(ps(3, 0, 128), [(IDF, xg), (ID, C["KF"])]))
-        scan(f("ys_", 256), sub("RS16", 0, 256), ps(7, 0, 256), MUL, MAX)
-        act(f("yb1", 8), sub("ys_", 15, 128, 16), bias=-16384.0 - 1.0 / 256)
-        act(f("yb2", 8), sub("ys_", 143, 256, 16), bias=16384.0 + 1.0 / 256, scale=-1.0)
+        L["tagb"] = act(h("tagb"), ps(3, 320, 448), bias=128.0, scale=1.0 / 4096)
+        mm(lin(ps(3, 0, 128), [(ID, C["KF"]), (IDF, xg)]))
         f("s1", 8)
         f("s2", 8)
-        for a in range(8):
+        nd = CFG["nd"] if rho == RO - 1 else 0
+        if nd:
+            mm(lin(ps(6, 0, 128), [(ID, C["KF"]), (IDF, xg)]))
+            act(f("yb3", 8), sub("yb2", 0, 8), F.Copy, scale=-1.0)
+            act(sub("s2", 8 - nd, 8), io(0, nd), F.Copy, scale=0.0)
+            z = 640 * (me_c ^ PEER[3])
+            for a in range(8 - nd, 8):
+                n, y = 16 * a + 16, z + 256 * (a % 2)
+                ts(sub("G", y, y + n), ps(6, 0, n), sub("yb1", a, a + 1), LT, 2.0, MUL)
+                ts(sub("G", y + n, y + 2 * n), ps(6, 0, n), sub("yb3", a, a + 1), LT, -2.0, MUL)
+                red(sub("s1", a, a + 1), sub("G", y, y + 2 * n))
+        for a in range(8 - nd):
             for nm in ("1", "2"):
                 act(sub("junk%d" % (int(nm) - 1), 0, 16 * a + 16), ps(3, 0, 16 * a + 16), F.Sign, bias=sub("yb" + nm, a, a + 1), scale=-1.0 if nm == "1" else 1.0,
                     acc=sub("s" + nm, a, a + 1))
         L["pg"] = cp(f("pg_", 256), ind(PTa, sub("offg", 0, 16)))
-        rkb = act(h("rkb"), xg, bias=192.0 - 511.5 / 1024, scale=1.0 / 1024)
-        L["rkv"] = act(h("rkv"), rkb, bias=-192.0)
+        L["pgop"] = len(ops) - 1
+        L["rkb"] = act(h("rkb"), xg, bias=192.0 - 511.5 / 1024, scale=1.0 / 1024)
 
     def cand_b(rho, ovout):
         out = ps(7, 128, 256)
-        mm(lin(out, [(IDF, L["g1"])] + ([] if rho == RO - 1 else [(dg(2, True), L["xg"])]) + [(IDF, L["g2"])]))
+        mm(lin(out, [(dg(2, True), L["xg"]), (IDF, L["g1"]), (IDF, L["g2"])]))
         emp = act(h("emp"), out, F.Relu, bias=-1.0, scale=-1.0)
         mm([(ps(7, 256, 384), C["LSI"], emp, True, True)])
         L["nfs"] = act(h("nfs"), ps(7, 256, 384), F.Sign, bias=1.0)
@@ -729,29 +795,32 @@ def rank_program(g, core, T, topo):
         last = rho == RO - 1
         w = 40 if last else 32
         key, pay = ps(0, 0, 128), ps(1, 0, 128)
-        opens(0, [(key, dg(8192), L["tagv"])] + ([(key, IDF, xg)] if last else []))
-        opens(1, [(pay, a, b) for a, b in ((dg(-U), L["rkv"]), (dg(1024, True), xg), (ID, L["rkv"]), (dg(8), L["tagv"]))])
+        c128 = sub("C128", 0, 128)
+        opens(0, [(key, dg(8192), L["tagb"]), (key, dg(-129 * 64), c128)])
+        opens(1, [(pay, a, b) for a, b in ((dg(192 * U / 128), c128), (dg(-U), L["rkb"]), (dg(1024, True), xg), (ID, L["rkb"]), (dg(8), L["tagb"]), (dg(-(192 + 8 * 129) / 128), c128))])
         opens(4, [(ps(4, 0, 256), IDF, sub("pg_", 0, 256))])
         s4 = [(IDF, L["cf"]), (dg(-4096), L["b1"]), (dg(-4096), L["b2"])]
-        lists = [s4, s4[:1], s4, [(IDF, L["cf"]), (dg(4096), L["b2"])], [(dg(-1, True), sub("yb2", 0, 8)), (dg((fin_lo - fin_hi) / 2), L["b2"])]][:w // 8]
+        lists = [s4, s4[:1], s4, [(IDF, L["cf"]), (dg(4096), L["b2"])], [(dg(-1, True), sub("yb2", 0, 8)), (dg((fin_lo - fin_hi) / 2, own=4), L["b2"])]][:w // 8]
         opens(5, [(ps(5, 0, w), ID, sub("ZB", 0, w))] + [(ps(5, 8 * k, 8 * k + 8), a, b) for k, x in enumerate(lists) for a, b in x])
         closes(4, [(ps(4, a, a + 128), dg(P21), nfs) for a in (128, 0)])
         closes(0, [(key, dg(-P21), nfs)])
         closes(1, [(pay, dg(-P21), nfs)])
         closes(5, [(ps(5, 8 * k, 8 * k + 8), dg(-16384 if k == 4 else -8192), L["tr"]) for k in range(w // 8)])
         kept = act(f("kept"), ps(4, 128, 256), F.Relu, bias=-P21)
+        L["keptop"] = len(ops) - 1
         act(cols("UP", 0, 128), ps(4, 0, 128), F.Relu, bias=-P21)
         tt(cols("UP", 256, 384), key, L["g1"], MAX)
         L["np1"] = tt(cols("UP", 128, 256), pay, kept, MAX)
         tt(cols("UP", 384, 384 + w), ps(5, 0, w), sub("DM", 0, w), MIN)
+        L["upop"] = range(len(ops) - 3, len(ops))
         msg = cols("UP", 128, 416)
         trs = [(nxt, T.UA[:, rho, :], msg, "aA%d" % rho, side_engines(core, nxt, topo, cores))]
         if rho < RO - 1:
             trs.append((prv, T.UB[:, rho, :], msg, "aB%d" % rho, side_engines(core, prv, topo, cores)))
         s = send(trs)
-        arrive("aA%d" % rho, len(side_engines(prv, core, topo, cores)), [o("UA", rho)], CFG["far"], s)
+        arrive("aA%d" % rho, len(side_engines(prv, core, topo, cores)), [o("UA", rho)], CFG["far"] + CFG["a1" if last else "a0"], s)
         if rho < RO - 1:
-            arrive("aB%d" % rho, len(side_engines(nxt, core, topo, cores)), [o("UB", rho)], CFG["far"], s)
+            arrive("aB%d" % rho, len(side_engines(nxt, core, topo, cores)), [o("UB", rho)], CFG["far"] + CFG["a0"], s)
 
     def insert(rho):
         u("offs", 16)
@@ -767,7 +836,7 @@ def rank_program(g, core, T, topo):
                 mm([(ps(4 + b % 2, 0, 256), C["BLKF"], x, True, True)])
                 act(x, ps(4 + b % 2, 0, 256), F.Copy)
             else:
-                cp(x, cols("PT", a, a + 256))
+                as_float(x, cols("PT", a, a + 256))
 
     def sums_of(parts, off):
         mm(lin(ps(4, 0, 128), [(C["BLKF"], x) for x in parts]))
@@ -782,16 +851,27 @@ def rank_program(g, core, T, topo):
     address(KI)
     spread(0)
     place()
+    lc = len(ops)
     late_consts()
+    lc = [op for op in ops[lc:] if op["q"] == "s" and op["lab"] not in ("XT", "GIF", "GIB", "YN")]
+    for v in (8192, U / 2, -U / 2, 0.5):
+        dg(v)
     pack()
     request(0)
     behind("go1", o("dki"), T.dk[:], 4000.0)
-    iota(o("SR"), [[0, 3072]], 0, 0)
+    iota(o("SR", slice(128, 192)), [[0, 1024]], 0, 0)
+    ri16 = iota(f("ri16"), [[0, 8], [1, 16]], 0, 0)
+    C["LSI"] = keep_if(h("LSI"), LS, A.not_equal, -1.0)
+    C["DG"] = ts(h("DG"), ri16, pr, EQ, P21, MUL)
+    C["RS16"] = act(f("RS16"), ri16, F.Sign)
     f("dk2", 384)
     for r in range(RO):
-        ts(sub("dk2", 128 * r, 128 * r + 128), cols("dki", 128 * r, 128 * r + 128), (RO - 1 - r) * 2 * U + BIG, ADD)
-    homes(t)
-    relative(0, 0)
+        ts(sub("dk2", 128 * r, 128 * r + 128), cols("dki", 128 * r, 128 * r + 128), (RO - 1 - r) * 2 * U + BIG * (r < RO - 1), ADD)
+    dk_ops = ops[-RO:] if CFG["lp0"] else []
+    boost[0] = CFG["u6"]
+    homes(t, (4, 5))
+    boost[0] = CFG["u8"]
+    relative(0, 0, (4, 5))
     xw = ts(f("xw", 18), C["kA"], n0, ADD, -1024.0 * t, ADD)
     offw = ts(u("offw", 18), xw, 0.0, MAX, 1023.0, MIN)
     NX = act(f("NX", WIN), cols("XT", S3, S1), bias=-1.0, scale=-1.0)
@@ -801,19 +881,21 @@ def rank_program(g, core, T, topo):
     mv = ts(h("mv", WIN), ts(i_("kb", WIN), kg, -2147475456, AND), 8192.0, EQ)
     nmv = act(h("nmv", WIN), mv, bias=1.0, scale=-1.0)
     mvp, nmvp = act(ps(4, 0, WIN), mv, F.Copy), act(ps(5, 0, WIN), nmv, F.Copy)
-    mm(lin(ps(3, 0, WIN), [(IDF, gw), (dg(-P21), nmv)]))
     mm(lin(ps(7, 0, WIN), [(IDF, gw), (dg(-P21), mv)]))
+    tt(cols("TG", S3, S1), ps(7, 0, WIN), NX, MAX)
+    mm(lin(ps(3, 0, WIN), [(IDF, gw), (dg(-P21), nmv)]))
     t4 = tt(cols("TG", S4, S2), ps(3, 0, WIN), NX, MAX)
     p4 = tt(cols("PT", S4, S2), pgw, mvp, MUL)
     ea, eb = halves(core, nxt, topo)
     s = send([(nxt, T.TG[:, S5:DUMP], t4, "aW", ea), (nxt, T.PT[:, S5:DUMP], p4, "aW", eb)])
     arrive("aW", len(topo.engines(prv, core)), [cols("TG", S5, DUMP), cols("PT", S5, DUMP)], CFG["far"], s)
-    tt(cols("TG", S3, S1), ps(7, 0, WIN), NX, MAX)
     tt(cols("PT", S3, S1), pgw, nmvp, MUL)
+    boost[0] = 0.0
 
     for rho in range(RO):
         last = rho == RO - 1
-        lane_prep(rho, KI)
+        if rho or not CFG["lp0"]:
+            lane_prep(rho, KI)
         if rho:
             urgent(CFG["u2"], pointer, rho, o("RQ", slice(4 * rho, 4 * rho + 4), slice(0, 96, 88)))
         for k in range(NP - 1):
@@ -822,13 +904,27 @@ def rank_program(g, core, T, topo):
         def forward(rho=rho):
             urgent(CFG["u2"], miss_pre, rho)
             urgent(CFG["u7"], miss, rho)
-        lookup(rho, NP - 1, forward if last else None)
-        if not last:
+        lookup(rho, NP - 1, forward if rho in CFG["ff"] else None)
+        if rho not in CFG["ff"]:
             forward()
         if not rho:
+            first = L["pr"]
+            for op in dk_ops:
+                op["soft"].add(first)
+            if CFG["lp0"]:
+                lane_prep(rho, KI)
+            iota(cols("PT", DUMP, TW), [[0, TW - DUMP]], 0, 0, False)
+            C["ZT"] = act(h("ZT"), ID, F.Copy, scale=0.0)
+            tp = (t - 1) % N + 1
+            for k, v in enumerate((-512 * (t + 1), WS // 2 - 512 * tp, -512 * tp, (fin_lo - fin_hi) / 2)):
+                dg(v, own=k + 1)
+            for v in (-WS // 2, WS // 2, -4096):
+                dg(v)
             for a, r in ((0, t), (S2, (t - 1) % N), (S1, t)):
                 iota(cols("XT", a, a + 1024), [[1, 1024]], 1024 * r, 0)
-        image(rho, cols("OY", 128, 256) if last else img)
+            for v in (4096, -129 * 64, 192 * U / 128, -U, 8, -(192 + 8 * 129) / 128, P21, -8192):
+                dg(v)
+        image(rho, cols("OY", 128, 256) if last else f("img"))
         if rho == RO - 2:
             sums(0)
         if not last:
@@ -852,27 +948,28 @@ def rank_program(g, core, T, topo):
 
     rho = RO - 1
     dma("y", T.yi[:], cols("OY", 128, 256))
+    z = len(ops)
+    act(h("kB", 8), sub("kA", 0, 8), F.Copy)
+    act(h("RS160", 640), io(0, 640), bias=1.0, scale=0.0)
+    act(sub("RS160", 0, 640, 160), io(0, 4), F.Copy, scale=0.0)
+    for op in ops[z:]:
+        op["soft"].add(first)
     sums_of([L["np1"]], sub("offs", 8, 16))
-    for a, r in ((0, t), (S2, (t - 1) % N)):
-        for k in range(2):
-            act(ps(k, 0, 512), io(512 * k, 512 * k + 512), bias=float(1024 * r))
-        for k in range(4):
-            x = cols("TG", a + 256 * k, a + 256 * k + 256)
-            tt(x, x, ps(k // 2, 256 * (k % 2), 256 * (k % 2) + 256), ADD)
-    act(ps(0, 0, WIN), io(0, WIN), bias=n0)
-    for a in (S3, S4, S5):
-        x = cols("TG", a, a + WIN)
-        tt(x, x, ps(0, 0, WIN), ADD)
     dn = L["dn"]
-    inr = tt(f("inr", 18), ts(f("in0", 18), xw, 0.0, GE), ts(f("in1", 18), xw, 1024.0, LT), MUL)
-    dl_ = act(f("dl_", 18), C["kA"], bias=float(S1))
-    offl = cp(u("offl", 18), tt(f("z2", 18), tt(f("z1", 18), tt(f("z0", 18), xw, dl_, SUB), inr, MUL), dl_, ADD))
+
+    def outside(nm, x, n):
+        return act(f(nm, n), act(f(nm + "a", n), x, F.Abs, bias=-511.5), F.Relu, bias=-512.0 * 32768, scale=32768.0)
+
+    def from_on(nm, x, first, n):
+        return act(f(nm, n), x, F.Relu, bias=act(f(nm + "a", 1), first, bias=16384.0, scale=-16384.0), scale=16384.0)
     k12 = sub("kA", 0, 12)
-    xh = ts(f("xh", 12), k12, n0, ADD, -1024.0 * ((t - 1) % N), ADD)
-    inh = tt(f("inh", 12), ts(f("in2", 12), xh, 0.0, GE), ts(f("in3", 12), xh, 1024.0, LT), MUL)
-    dh_ = act(f("dh_", 12), k12, bias=float(WIN))
-    zh = tt(f("z4", 12), tt(f("z3", 12), ts(f("xh2", 12), xh, float(WS), ADD), dh_, SUB), inh, MUL)
-    offh = cp(u("offh", 12), tt(f("z6", 12), tt(f("z5", 12), ts(f("sp", 12), k12, dn, LT), zh, MUL), dh_, ADD))
+    offl = cp(u("offl", 18), tt(f("z2", 18), tt(f("z1", 18), xw, outside("z0", xw, 18), ADD), act(f("dl_", 18), C["kA"], bias=float(S1)), MIN))
+    for op in ops[-6:]:
+        op["soft"].add(first)
+    xh = act(f("xh", 12), k12, bias=act(f("xh0", 1), n0, bias=-1024.0 * ((t - 1) % N)))
+    ops[-1]["soft"].add(first)
+    zh = tt(f("z5", 12), tt(f("z4", 12), xh, outside("z3", xh, 12), SUB), from_on("sp", k12, dn, 12), SUB)
+    offh = ts(u("offh", 12), tt(f("z6", 12), zh, act(f("dh_", 12), k12, bias=float(WIN - WS)), MAX), float(WS), ADD)
     half = act(f("half", 1), dn, bias=-0.5)
     done_ = act(h("mv", WIN), io(0, WIN), F.Sign, bias=half, scale=-1.0)
     m2 = tt(ps(5, 0, WIN), act(ps(1, 0, WIN), done_, bias=-U, scale=-U), cols("TG", S4, S2), ADD)
@@ -881,53 +978,78 @@ def rank_program(g, core, T, topo):
         scat(cols("TG", 0, S4), sub("offl", a, b), sub("NX", 16 * a, 16 * b))
     scat(cols("TG", S1, S5), offh, cols("TG", S5, S5 + 192))
     for k in range(2):
-        urgent(CFG["u1"], count, rho, k)
-    urgent(CFG["u1"], pick, rho)
-    urgent(CFG["u1"], cand_a, rho)
-    p1 = tt(sub("PR", 512, 512 + WIN), act(ps(1, 0, WIN), done_, bias=0.5, scale=-0.5), cols("PT", S4, S2), MUL)
-    pa = cp(sub("PR", 0, WIN), cols("PT", S3, S1))
-    pb = cp(sub("PR", 1024, 1024 + 192), cols("PT", S5, S5 + 192))
-    for k, (x, n) in enumerate((([pa, p1], WIN), ([pb], 192))):
-        mm(lin(ps(4 + k, 0, n), [(C["BLKF"], y) for y in x]))
-        act(sub("G", 512 * k, 512 * k + n), ps(4 + k, 0, n), F.Copy)
+        urgent(CFG["u9"], count, rho, k)
+    urgent(CFG["u9"], pick, rho)
+    urgent(CFG["u9"], cand_a, rho)
+
+    def free(nm, k, a, b):
+        return sub(nm, 640 * (me_c ^ PEER[k]) + a, 640 * (me_c ^ PEER[k]) + b)
+    p1 = tt(free("PR", 0, 320, 320 + WIN), act(ps(1, 0, WIN), done_, bias=0.5, scale=-0.5), cols("PT", S4, S2), MUL)
+    pa = as_float(free("PR", 0, 0, WIN), cols("PT", S3, S1))
+    pb = as_float(free("PR", 1, 0, 192), cols("PT", S5, S5 + 192))
+    for a in (0, 96, 192):
+        mm(lin(ps(4, a, a + 96), [(C["BLKF"], free("PR", 0, z + a, z + a + 96)) for z in (0, 320)]))
+    for a in (0, 96):
+        mm([(ps(5, a, a + 96), C["BLKF"], free("PR", 1, a, a + 96), True, True)])
+    for k, n in enumerate((WIN, 192)):
+        act(free("G", k, 0, n), ps(4 + k, 0, n), F.Copy)
     for a, b in ((0, 10), (10, 18)):
-        scat(cols("YS", 0, S4), sub("offl", a, b), sub("G", 16 * a, 16 * b))
-    scat(cols("YS", S1, S5), offh, sub("G", 512, 512 + 192))
+        scat(cols("YS", 0, S4), sub("offl", a, b), free("G", 0, 16 * a, 16 * b))
+        if CFG["ysl"]:
+            ops[-1]["soft"].add(L["pgop"])
+    scat(cols("YS", S1, S5), offh, free("G", 1, 0, 192))
 
     def ov_last(s):
         act(cols("SO", 0, 1), s, F.Copy)
-        for ks in ([0, 3], [1], [2]):
-            x = send([(cores[d], T.RV[:, t, :], o("SO"), "aO", en) for k in ks for d, en in pair_call(core, pairs[me_c ^ PEER[k]], cores, topo)])
+        calls = [pair_call(core, pairs[me_c ^ x], cores, topo) for x in PEER]
+        thin = [(d, en[k * len(en) // 2:(k + 1) * len(en) // 2]) for k in range(2) for d, en in calls[k]]
+        L["calls"] = [thin + calls[3], calls[2]]
+        for call in L["calls"][:CFG["ao"]]:
+            L["ao"] = send([(cores[d], T.RV[:, t, :], o("SO"), "aO", en) for d, en in call])
         act(o("RV", t), o("SO"), F.Copy)
-        arrive("aO", sum(pair_count(t, p, cores, topo) for p in pairs), [o("RV", d) for d in range(N) if d != t], CFG["far"], x)
     urgent(CFG["u1"], cand_b, rho, ov_last)
     cand_d(rho)
+    for call in L["calls"][CFG["ao"]:]:
+        L["ao"] = send([(cores[d], T.RV[:, t, :], o("SO"), "aO", en) for d, en in call])
+    arrive("aO", sum(len(en) for call in L["calls"] for d, en in call), [o("RV", d) for d in range(N) if d != t], CFG["far"] + CFG["a1"], L["ao"])
     insert(rho)
     offf = ts(u("offf", 8), cols("UP", 416, 424), C4, ADD)
     scat(TGa, offf, tt(f("whole"), cols("UP", 256, 384), L["g2"], MAX))
-    sums_of([L["np1"], cols("UP", 0, 128)], offf)
+    back = []
+    for a in (0, S2):
+        for k in range(2):
+            for z in (0, 256):
+                mm([(ps(2 + k, z, z + 256), IDF, cols("XT", a + 512 * k + z, a + 512 * k + z + 256), True, True)])
+                back.append(ops[-1])
+        for k in range(2):
+            x = cols("TG", a + 512 * k, a + 512 * k + 512)
+            tt(x, x, ps(2 + k, 0, 512), ADD)
+    z = len(ops)
     KI = unpack(rho)
-    dma("y", T.yl[:], cp(cols("OY", 0, 128), ts(i_("w"), ts(i_("x"), KI, -BIG, ADD), 1048575, AND)))
+    turns = [k for k in range(z, len(ops)) if ops[k]["q"] == "p"]
+    for k, op in enumerate(back):
+        op["soft"].add(turns[min(k + CFG["tb"], 7)])
+    sums_of([L["np1"], cols("UP", 0, 128)], offf)
+    dma("y", T.yl[:], cp(cols("OY", 0, 128), ts(i_("w"), KI, 1048575, AND)))
     k6 = sub("kA", 0, 6)
-    u("offx", 12)
-    f("tg0", 12)
-    f("dx", 12)
-    f("i12", 12)
+    for nm in ("sec", "xx", "xb", "dx", "i12"):
+        f(nm, 12)
     for k, (sec, r, base) in enumerate(((S3, t, 0), (S5, (t - 1) % N, S2))):
-        ts(sub("offx", 6 * k, 6 * k + 6), k6, dn, ADD, float(sec), ADD)
+        act(sub("sec", 6 * k, 6 * k + 6), k6, bias=float(sec))
         act(sub("dx", 6 * k, 6 * k + 6), k6, bias=96.0 * k + DUMP)
         act(sub("i12", 6 * k, 6 * k + 6), k6, F.Copy)
-        xx = ts(f("xx%d" % k, 6), k6, NN[RO - 1], ADD, -1024.0 * r, ADD)
-        ya = tt(f("ya%d" % k, 6), ts(f("yq%d" % k, 6), xx, 0.0, LT, 2 * BIG, MUL), xx, ADD)
-        yc = ts(f("yc%d" % k, 6), xx, 1024.0, GE, BIG, MUL)
-        tt(sub("tg0", 6 * k, 6 * k + 6), ts(f("yd%d" % k, 6), ya, float(base), ADD), yc, ADD)
+        xx = act(sub("xx", 6 * k, 6 * k + 6), k6, bias=act(f("xx%d" % k, 1), NN[RO - 1], bias=-1024.0 * r))
+        act(sub("xb", 6 * k, 6 * k + 6), xx, bias=float(base))
+    offx = ts(u("offx", 12), f("sec", 12), dn, ADD)
+    tt(f("tg0", 12), f("xb", 12), outside("xo", f("xx", 12), 12), ADD)
     mirror(rho, "UA", 272, C2)
-    offx = sub("offx", 0, 12)
-    kx = act(sub("PR", 1024, 1216), ind(TGa, offx))
-    mm([(ps(4, 0, 192), C["BLKF"], cp(sub("PR", 1536, 1728), ind(PTa, offx)), True, True)])
-    sx = act(sub("PR", 2048, 2240), ps(4, 0, 192), F.Copy)
+    for k in range(2):
+        act(ps(7, 96 * k, 96 * k + 96), io(0, 96), bias=NN[RO - 1])
+    kx = tt(free("PR", 1, 320, 512), act(free("G", 2, 0, 192), ind(TGa, offx)), ps(7, 0, 192), ADD)
+    mm([(ps(4, 0, 192), C["BLKF"], cp(free("PR", 2, 0, 192), ind(PTa, offx)), True, True)])
+    sx = act(free("PR", 2, 320, 512), ps(4, 0, 192), F.Copy)
     cap = act(f("cap", 1), NN[RO - 1], bias=8192.0, scale=-1.0)
-    tg1 = tt(f("tg1", 12), ts(f("tg2", 12), sub("i12", 0, 12), cap, GE, BIG, MUL), sub("tg0", 0, 12), ADD)
+    tg1 = tt(f("tg1", 12), from_on("tg2", f("i12", 12), cap, 12), f("tg0", 12), ADD)
     boost[0] = CFG["u5"]
     v = ps(7, 320, 321)
     mm([(v, C["BLKF"], red(f("v", 1), o("RV", slice(None), 0)), True, True)])
@@ -1001,7 +1123,8 @@ def rank_program(g, core, T, topo):
     if not CFG["gaps"]:
         plan = greedy
 
-    def first_order():
+    def first_order(look):
+        CFG["look"] = look
         prio = [0.0] * n
         for me in range(n - 1, -1, -1):
             prio[me] = ops[me]["c"] + max([prio[k] + WAKE for k in post[me]], default=0.0)
@@ -1043,44 +1166,67 @@ def rank_program(g, core, T, topo):
     marks = [k for k in range(n) if ops[k]["q"] == "g" and ops[k]["ev"]]
     kids = [set(p) for p in post]
 
-    def mend(order):
+    def mend(order, steps):
         rows = {q: [k for k in order if ops[k]["q"] == q] for q in "vspy"}
         now = top = clocked(rows)
-        seed = 1
-        for step in range(CFG["mend"]):
-            seed = (seed * 1103515245 + 12345) % 2147483648
-            k, edges = max(range(n), key=lambda k: now[1][k] + cost_[k]) if (seed >> 12) % 4 else marks[(seed >> 14) % len(marks)], []
-            while now[2][k] >= 0:
-                if now[2][k] not in pre[k]:
-                    edges.append((now[2][k], k))
-                k = now[2][k]
-            if not edges:
-                continue
-            seed = (seed * 1103515245 + 12345) % 2147483648
-            a, b = edges[(seed >> 8) % len(edges)]
-            row = rows[ops[a]["q"]]
-            i = row.index(a)
-            old = list(row)
-            if (seed >> 16) % 2:
-                j = i + 1
-                while j < len(row) and j - i < 24 and row[j] not in kids[a]:
-                    j += 1
-                row.insert(i + 1 + (seed >> 18) % (j - i - 1) if (seed >> 17) % 2 and j > i + 1 else j - 1, row.pop(i))
-            else:
-                j = i
-                while j >= 0 and i - j < 24 and row[j] not in pre[b]:
-                    j -= 1
-                row.insert(i - (seed >> 18) % (i - j), row.pop(i + 1))
-            new = clocked(rows)
-            if new is None or new[4] > now[4] + CFG["warm"] * (1 - step / CFG["mend"]):
-                row[:] = old
-            else:
-                now = new
-                if new[0] < top[0]:
-                    top = new
+        barred = {}
+        for step in range(steps):
+            end, at, why, seen = now[:4]
+            where = {k: i for row in rows.values() for i, k in enumerate(row)}
+            tail, own = [0.0] * n, [0.0] * n
+            for k in reversed(seen):
+                own[k] = cost_[k] + max([WAKE + tail[j] for j in post[k]], default=0.0)
+                row = rows.get(ops[k]["q"])
+                tail[k] = max(own[k], hold[k] + tail[row[where[k] + 1]]) if row and where[k] + 1 < len(row) else own[k]
+            k, runs, run = max(range(n), key=lambda k: at[k] + cost_[k]), [], []
+            while k >= 0:
+                if why[k] >= 0 and why[k] not in pre[k]:
+                    run = run or [k]
+                    run.append(why[k])
+                elif run:
+                    runs.append(run[::-1])
+                    run = []
+                k = why[k]
+            moves = []
+            for run in runs:
+                row, m = rows[ops[run[0]]["q"]], len(run)
+                ready = {k: max([at[d] + cost_[d] + WAKE for d in pre[k]], default=0.0) for k in run}
+                for i in range(m - 1):
+                    for j in sorted({i + 1, i + 2, i + 4, i + 8, m - 1}):
+                        if j >= m:
+                            continue
+                        part = run[i:j + 1]
+                        for back in (0, 1) if j > i + 1 else (0,):
+                            x = part[-1] if back else part[0]
+                            if barred.get(x, -1) >= step or (pre[x] if back else kids[x]) & set(part):
+                                continue
+                            new, p0, p1 = [x] + part[:-1] if back else part[1:] + [x], where[part[0]], where[part[-1]]
+                            p, heads = at[row[p0 - 1]] + hold[row[p0 - 1]] if p0 else 0.0, []
+                            for w in new:
+                                p = max(p, ready[w])
+                                heads.append(p)
+                                p += hold[w]
+                            p, worst = tail[row[p1 + 1]] if p1 + 1 < len(row) else 0.0, 0.0
+                            for w, a in zip(reversed(new), reversed(heads)):
+                                p = max(own[w], hold[w] + p)
+                                worst = max(worst, a + p)
+                            moves.append((worst, x, p0, new))
+            moves.sort(key=lambda z: z[:3])
+            for worst, x, p0, new in moves[:6]:
+                row = rows[ops[x]["q"]]
+                old = row[p0:p0 + len(new)]
+                row[p0:p0 + len(new)] = new
+                barred[x] = step + CFG["bar"]
+                after = clocked(rows)
+                if after and after[0] <= end + CFG["warm"]:
+                    now = after
+                    break
+                row[p0:p0 + len(new)] = old
+            if now[0] < top[0]:
+                top = now
         place_ = {k: i for i, k in enumerate(top[3])}
         CFG["log"].append(int(top[0]))
-        return sorted(range(n), key=lambda k: (top[1][k], place_[k]))
+        return top[0], sorted(range(n), key=lambda k: (top[1][k], place_[k]))
     cost_ = [op["c"] for op in ops]
     hold = [op["c"] if op["ev"] is None else 60.0 for op in ops]
     shape = tuple((op["q"], op["c"]) for op in ops)
@@ -1089,7 +1235,7 @@ def rank_program(g, core, T, topo):
         place_ = {k: i for i, k in enumerate(again[3])}
         order = sorted(range(n), key=lambda k: (again[1][k], place_[k]))
     else:
-        order = ORDERS[shape] = mend(first_order())
+        order = ORDERS[shape] = mend(min(mend(first_order(x), CFG["mend"] // 4) for x in CFG["looks"])[1], CFG["mend"])[1]
     PLAN.update(slots)
     pos = {me: k for k, me in enumerate(order)}
     ops = [ops[me] for me in order]

from concourse.bass import DstId, RemoteDMATransfer
from concourse.mybir import AluOpType as A, AxisListType, ActivationFunctionType as F

N, RO, CAP, WIN = 8, 3, 320, 288
WS = 1024 + WIN
S3, S1, S4, S2, S5, DUMP, ZC, TW = 1024, WS, WS + 1024, 2 * WS, 2 * WS + 1024, 3 * WS, 3 * WS + 256, 3 * WS + 272
BIG, U, P21 = 8192.0, 1048576.0, 2097152.0
SWW, OS, PARTS = 6464, 132, 2
C0, C1, C2, C3 = 8192.0, 16384.0 - WS, 16384.0 + WS, 12288.0 - WS
PEER = (2, 3, 1, 0)
PLAN, ORDERS = {}, {}
CFG = {"gv": 72, "cuts": (0, 32, 64, 128), "wl": (), "gl": (), "gconv": True, "tol": 0.0, "passes": 2, "g0": 0, "fix": 45.0, "fixs": 60.0, "least": 16.0, "wake": 90.0, "pe": 0.45, "cy": 0.85, "wv": (5, 7), "apart": (0, 1, 2), "prk": 0, "early": 0, "fine": True, "pgk": 3, "upk": False, "lp0": False, "nv": 4, "nd": 0, "ysl": True, "tb": 1, "late": 9, "looks": (120.0, 180.0, 250.0, 320.0, 400.0, 500.0), "gaps": False, "mend": 200, "warm": 150.0, "lam": 0.0, "bar": 12, "send": 750.0,
       "u1": 0.0, "u2": 0.0, "u3": 0.0, "u4": 0.0, "u5": 0.0, "u7": 0.0, "u6": 3000.0, "u8": 0.0, "u9": 0.0, "ao": 1, "ff": (2,), "far": 2600.0, "near": 2000.0, "q0": 300.0, "qk": 300.0, "a0": 400.0, "a1": 1500.0, "lk": 7000.0, "lp": 10000.0, "ld": 2400.0, "ld2": 8000.0, "st": 4300.0}
SCRATCH = {
    "lki": ("sbuf", [128, 128], "int32"), "lii": ("sbuf", [128, 128], "int32"), "dki": ("sbuf", [128, 384], "int32"),
    "pni": ("sbuf", [128, 1], "int32"), "KR": ("sbuf", [128, 2048], "int32"), "PT": ("sbuf", [128, TW], "int32"),
    "TG": ("sbuf", [128, TW], "float32"), "XT": ("sbuf", [128, TW], "float32"), "YS": ("sbuf", [128, TW], "float32"),
    "SW": ("sbuf", [128, SWW], "bfloat16"), "W": ("sbuf", [128, 2576], "bfloat16"),
    "T2": ("sbuf", [128, 128, 16], "bfloat16"), "BC": ("sbuf", [128, 16, 128], "bfloat16"),
    "SQ": ("sbuf", [128, 24, 48], "uint16"), "RQ": ("sbuf", [128, 12, 96], "uint16"), "TQ": ("sbuf", [128, 16, 20], "bfloat16"),
    "SR": ("sbuf", [128, 192, 16], "bfloat16"), "RR": ("sbuf", [128, 576], "float32"), "SA": ("sbuf", [128, 192], "float32"),
    "SF": ("sbuf", [128, 160], "float32"), "CAT": ("sbuf", [128, 3, 336], "float32"),
    "UP": ("sbuf", [128, 424], "float32"), "UA": ("sbuf", [128, 3, 288], "float32"), "UB": ("sbuf", [128, 2, 288], "float32"),
    "SO": ("sbuf", [128, 4], "float32"), "RV": ("sbuf", [128, 8, 4], "float32"),
    "OY": ("sbuf", [128, 260], "float32"),
    "TF": ("sbuf", [128, 14720], "float32"), "TI": ("sbuf", [128, 1408], "int32"), "TB": ("sbuf", [128, 22784], "bfloat16"),
    "TU": ("sbuf", [128, 512], "uint16"),
}
for _b in range(8):
    SCRATCH["B%d" % _b] = ("psum", [128, 512], "float32")
SEMAPHORES = (["qv", "qs", "qp", "qg", "aK", "aP", "aW", "aO", "go0", "go1", "lr"] + ["aH%d" % j for j in range(PARTS)] + ["a%s%d" % (k, r) for k in "FAB" for r in range(RO)]
              + ["a%s%d%d" % (k, r, b) for k in "QR" for r in range(RO) for b in range(4)]
              + ["d%d" % i for i in range(16)] + ["l%d" % i for i in range(48)])


def bits(engs):
    return sum(1 << e for e in engs)


def chip_pairs(cores, topo):
    pairs = [[i for i, x in enumerate(cores) if topo.chip(x) == topo.chip(c)] for c in cores[::2]]
    assert pairs == [[2 * k, 2 * k + 1] for k in range(len(cores) // 2)]
    return pairs


def halves(src, dst, topo):
    e = topo.engines(src, dst)
    return e[:len(e) // 2], e[len(e) // 2:]


def side_engines(src, dst, topo, cores):
    far = [c for c in cores if topo.chip(c) != topo.chip(src)][0]
    if topo.chip(src) != topo.chip(dst):
        return topo.engines(src, dst)
    return [e for e in topo.engines(src, dst) if e not in topo.engines(src, far)]


def pair_call(src, pair, cores, topo):
    dsts = [d for d in pair if cores[d] != src]
    if len(dsts) == 1:
        return [(dsts[0], side_engines(src, cores[dsts[0]], topo, cores))]
    return [(d, halves(src, cores[d], topo)[k]) for k, d in enumerate(dsts)]


def pair_count(dst, pair, cores, topo):
    mine = chip_pairs(cores, topo)[dst // 2]
    return sum(len(e) for s in pair if s != dst for d, e in pair_call(cores[s], mine, cores, topo) if d == dst)


def relays(src, dst, cores, topo):
    if topo.chip(src) == topo.chip(dst):
        return []
    return [h for h in topo.cores_of(src) if h not in cores and topo.die(h) != topo.die(src) and topo.may_write(h, dst)][:2]


def dst_id(c, topo):
    rid, pid, _ = topo.addr(c)
    return DstId(rid=rid, pnc=pid)


def relay_program(g, core, T, topo):
    cores = list(T.cores)
    for t in range(N):
        src, dst = cores[t], cores[(t - 1) % N]
        hs = relays(src, dst, cores, topo)
        if core in hs:
            i = hs.index(core)
            rid, pid, _ = topo.addr(dst)
            w = 512 // PARTS
            for j in range(PARTS):
                g.wait_ge(T.sem["aH%d" % j], len(side_engines(src, core, topo, cores)) // 2)
                g.remote_dma(T.PT[:, S1 + 512 * i + w * j:S1 + 512 * i + w * j + w], T.KR[:, w * j:w * j + w], T.sem.aP, T.sem.lr, pid, rid, topo.mask(core, dst))
            g.wait_ge(T.sem.lr, PARTS * len(topo.engines(core, dst)))


def mask_of(shape, idx):
    idx = list(idx) + [slice(None)] * (len(shape) - len(idx))
    step, m = 1, 1
    for n, i in zip(reversed(shape), reversed(idx)):
        r = range(n)[i] if isinstance(i, slice) else range(i, i + 1)
        if len(r) > 1 and m.bit_length() <= r.step * step:
            w = r.step * step
            m = m * (((1 << (w * len(r))) - 1) // ((1 << w) - 1)) << (r.start * step)
        else:
            m = sum(m << (k * step) for k in r)
        step *= n
    return m


def rank_program(g, core, T, topo):
    t = T.rank_of(core)
    if t is None:
        relay_program(g, core, T, topo)
        return
    cores = list(T.cores)
    pairs = chip_pairs(cores, topo)
    NP, me_c, par = len(pairs), t // 2, t % 2
    prv, nxt = cores[(t - 1) % N], cores[(t + 1) % N]
    ENG = {"v": g.vector, "s": g.scalar, "p": g.tensor, "g": g, "y": g.sync}
    FIX, WAKE, PE, CY = CFG["fix"], CFG["wake"], CFG["pe"], CFG["cy"]
    ops, acc, bank, slots = [], {}, {}, {}
    cnt = {"d": 0, "l": 0, "TF": 0, "TI": 0, "TB": 0, "TU": 0}
    lastg, boost, later = [], [0.0], []

    def urgent(v, fn, *a):
        boost[0] = v
        r = fn(*a)
        boost[0] = 0.0
        return r

    def size(x):
        n = 1
        for k in x[0].shape[1:]:
            n *= k
        return n

    def o(name, *idx):
        ap = T[name][(slice(None),) + idx]
        return (ap, [(name, mask_of(SCRATCH[name][1][1:], idx))], "p" if SCRATCH[name][0] == "psum" else "h" if SCRATCH[name][2] in ("bfloat16", "uint16") else "s")

    def cols(name, a, b, s=1):
        return o(name, slice(a, b, s) if s != 1 else slice(a, b))

    def sub(name, a, b, s=1):
        buf, z = slots[name]
        ap = T[buf][:, z + a:z + b:s] if s != 1 else T[buf][:, z + a:z + b]
        return (ap, [(name, mask_of([b], [slice(a, b, s)]))], "h" if buf in ("TB", "TU") else "s")

    def tmp(buf, name, n):
        if name not in slots:
            slots[name] = (buf, cnt[buf])
            cnt[buf] += (n + 15) // 16 * 16
            assert cnt[buf] <= SCRATCH[buf][1][1]
        assert slots[name][0] == buf
        return sub(name, 0, n)

    def f(name, n=128):
        return tmp("TF", name, n)

    def i_(name, n=128):
        return tmp("TI", name, n)

    def h(name, n=128):
        return tmp("TB", name, n)

    def u(name, n=128):
        return tmp("TU", name, n)

    def ps(b, a, e, s=1):
        return cols("B%d" % b, a, e, s)

    def ind(w, off):
        return (w[0].indirect(off[0]), w[1] + off[1], "i")

    def sv(x):
        return x[0] if isinstance(x, tuple) else x

    def st(*xs):
        return [k for x in xs if isinstance(x, tuple) for k in x[1]]

    def cost(out, ins, two=False, half=False, fix=FIX):
        kinds = [x[2] for x in ins]
        if "i" in kinds:
            return 55.0 + 1.56 * CY * size(out)
        k = 2.0 if two and "p" not in kinds else 0.5 if half and all(z == "h" for z in kinds + [out[2]]) else 1.0
        return fix + max(CFG["least"], size(out) * k) * CY

    def rec(q, fn, R, W, ev=None, c=100.0, after=()):
        me = len(ops)
        deps, soft = set(), set(after)
        for k in set(x[0] for x in R + W):
            if k in SCRATCH and SCRATCH[k][0] == "psum":
                b = bank.setdefault(k, [q, [], []])
                if b[0] != q:
                    b[0], b[1], b[2] = q, [], b[1]
                b[1].append(me)
                deps.update(b[2])
        for w, xs in ((False, R), (True, W)):
            for k, m in xs:
                keep = []
                for e in acc.get(k, []):
                    if e[0] & m and (w or e[2]) and e[1] != me:
                        deps.add(e[1])
                    if not (w and e[0] & ~m == 0):
                        keep.append(e)
                keep.append((m, me, w))
                acc[k] = keep
        if q == "s":
            soft.update(later)
        if q == "g":
            soft.update(lastg[-1:])
            lastg.append(me)
        ops.append({"q": q, "fn": fn, "deps": deps, "ev": ev, "c": c, "up": boost[0], "soft": soft, "lab": (W + [("-", 0)])[0][0]})
        return me

    def ts(out, a, s1, op0, s2=None, op1=None):
        if op1 is None:
            rec("v", lambda e: e.tensor_scalar(out[0], a[0], sv(s1), None, op0), st(a, s1), out[1], c=cost(out, [a], half=True))
        else:
            rec("v", lambda e: e.tensor_scalar(out[0], a[0], sv(s1), sv(s2), op0, op1), st(a, s1, s2), out[1], c=cost(out, [a], half=True))
        return out

    def tt(out, a, b, op):
        rec("v", lambda e: e.tensor_tensor(out[0], a[0], b[0], op), st(a, b), out[1], c=cost(out, [a, b], True))
        return out

    def cp(out, a):
        rec("v", lambda e: e.tensor_copy(out[0], a[0]), st(a), out[1], c=cost(out, [a], half=True))
        return out

    def scat(w, off, a):
        rec("v", lambda e: e.tensor_copy(w[0].indirect(off[0]), a[0]), st(a, off), w[1], c=50.0 + 3.8 * CY * size(a))

    def ms(out, c):
        rec("v", lambda e: e.memset(out[0], c), [], out[1], c=cost(out, [], half=True))
        return out

    def scan(out, d0, d1, op0, op1, init=0.0):
        rec("v", lambda e: e.tensor_tensor_scan(out[0], d0[0], d1[0], sv(init), op0, op1), st(d0, d1, init), out[1], c=cost(out, [d0, d1], half=True))
        return out

    def red(out, a):
        rec("v", lambda e: e.tensor_reduce(out[0], a[0], AxisListType.X, A.add), st(a), out[1], c=cost(a, []))
        return out

    def act(out, a, func=F.Identity, bias=0.0, scale=1.0, acc=None):
        if acc is None:
            rec("s", lambda e: e.activation(out[0], a[0], func, bias=sv(bias), scale=sv(scale)), st(a, bias, scale), out[1], c=cost(out, [a], fix=CFG["fixs"]))
        else:
            rec("s", lambda e: e.activation(out[0], a[0], func, bias=sv(bias), scale=sv(scale), accum_out=acc[0]), st(a, bias, scale), out[1] + acc[1], c=cost(out, [a], fix=CFG["fixs"]) + 20.0)
        return out

    def opens(b, terms):
        mm([(x, y, z, k == 0, False) for k, (x, y, z) in enumerate(terms)], ps(b, 0, 512)[1])

    def closes(b, terms):
        mm([(x, y, z, False, k == len(terms) - 1) for k, (x, y, z) in enumerate(terms)], ps(b, 0, 512)[1])

    def mm(items, whole=()):
        def fn(e):
            ins = None
            for x in items:
                ins = e.matmul(x[0][0], x[1][0], x[2][0], x[3], x[4])
            return ins
        R, W = {}, dict(whole)
        for x in items:
            for d, ks in ((R, st(x[1], x[2])), (W, x[0][1])):
                for k, m in ks:
                    d[k] = d.get(k, 0) | m
        rec("p", fn, list(R.items()), list(W.items()), c=10.0 + PE * sum(max(64, size(x[0])) * (1 if x[1][2] == "h" else 4) for x in items))

    def lin(out, terms):
        return [(out, a, b, k == 0, k == len(terms) - 1) for k, (a, b) in enumerate(terms)]

    def iota(out, pat, base, cm, fl=True):
        if fl:
            rec("g", lambda e: e.iota(out[0], pat, base, cm, allow_small_or_imprecise_dtypes=True), [], out[1], c=130 + 1.7 * size(out))
        else:
            rec("g", lambda e: e.iota(out[0], pat, base, cm), [], out[1], c=130 + 1.7 * size(out))
        return out

    def keep_if(out, a, op, fill):
        rec("g", lambda e: e.affine_select(out[0], a[0], [[1, 128]], op, fill, 0, -1), st(a), out[1], c=400.0)
        return out

    def as_float(out, a):
        if not CFG["gconv"]:
            return cp(out, a)
        rec("g", lambda e: e.affine_select(out[0], a[0], [[0, size(out)]], A.is_equal, 0.0, 0, 0), st(a), out[1], c=170.0 + 1.7 * size(out))
        return out

    def dma(q, out, a, c=2500.0, after=(), reads=()):
        s = "d%d" % cnt["d"]
        cnt["d"] += 1
        return rec(q, lambda e: e.dma_start(sv(out), sv(a)).then_inc(T.sem[s], 16), st(a) + list(reads), st(out), ev=(s, 16), c=c, after=after)

    def send(trs):
        s = "l%d" % cnt["l"]
        cnt["l"] += 1
        return rec("g", lambda e: e.remote_dma_fused([RemoteDMATransfer(dst_ids=[dst_id(d, topo)], dma_engine_mask=bits(en), remote_sem=T.sem[sm], src=a[0], dst=da)
                                                     for d, da, a, sm, en in trs], local_sem=T.sem[s]),
                   st(*[x[2] for x in trs]), [], ev=(s, sum(len(x[4]) for x in trs)), c=CFG["send"])

    def arrive(sem, n, lands, c, after):
        rec("x", None, [], st(*lands), ev=(sem, n), c=c, after=[after])

    TGa, PTa, XTa, YSa, SWa = cols("TG", 0, TW), cols("PT", 0, TW), cols("XT", 0, TW), cols("YS", 0, TW), cols("SW", 0, SWW)
    AND, SHR = A.bitwise_and, A.logical_shift_right
    ADD, SUB, MUL, MAX, MIN = A.add, A.subtract, A.mult, A.max, A.min
    EQ, GE, GT, LT = A.is_equal, A.is_ge, A.is_gt, A.is_lt

    d = dma("y", o("lki"), T.lk[:], 2600.0)
    for dst, src, c in ((o("pni"), T.pn[:], 300.0), (o("lii"), T.li[:], 300.0), (cols("PT", S2, S5), T.tp[:, 1024:2048], CFG["ld"]),
                        (cols("KR", 1024, 2048), T.tk[:, 1024:2048], CFG["ld"]), (cols("KR", 0, 1024), T.tk[:, 0:1024], CFG["ld"])):
        d = dma("y", dst, src, c, [d])
    pidx = iota(i_("pidx", 1), [[1, 1]], 0, 1, False)
    IO = f("IO", 1024)
    iota(sub("IO", 0, 320), [[1, 320]], 0, 0)
    gi16 = iota(f("gi16"), [[1, 8], [0, 16]], 0, 0)
    DJs = iota(f("DJs"), [[16, 128]], int(BIG) + 4288, 1)

    def io(a, b):
        return sub("IO", a, b)
    boost[0] = CFG["u3"]
    ms(cols("SW", 0, 2560), 0.0)
    for k in range(4):
        act(o("T2", slice(32 * k, 32 * k + 32)), cols("SW", 0, 512), F.Copy)
    ms(h("OH", 9 * OS), 0.0)
    pr = cp(f("pr", 1), ts(i_("pri", 1), pidx, 15, AND))
    pg = cp(f("pg", 1), ts(i_("pgi", 1), pidx, 4, SHR))
    ID = ts(h("ID"), io(0, 128), cp(f("pf", 1), pidx), EQ)
    BLK = ts(h("BLK"), gi16, pg, EQ)
    LS = keep_if(h("LS"), BLK, GT, 0.0)
    LB = [keep_if(h("LB%d" % d), LS, A.not_equal, BIG + CAP * d) for d in range(8)]
    for k in range(1, 4):
        act(io(256 * k + 64 * (k == 1), 256 * k + 256), io(64 * (k == 1), 256), bias=256.0 * k)
    RS8 = act(h("RS8", 512), cols("SW", 0, 512), bias=1.0)
    ms(sub("RS8", 0, 512, 8), 0.0)
    RSM = ms(h("RSM", 7 * OS), 1.0)
    ms(sub("RSM", 0, 7 * OS, OS), 0.0)
    n0i = o("pni")
    n0 = cp(f("n0", 1), n0i)
    n288 = ts(f("n288", 1), n0, float(WIN), ADD, 8192.0, MIN)
    d0 = ts(f("d0", 1), ts(i_("d0i", 1), n0i, 1023, AND), -1.0, MUL, 1024.0, ADD)
    L = {"img": o("lii")}
    KI = ts(i_("KI"), o("lki"), 6 * U + BIG, ADD)
    DJ = cp(ps(6, 0, 128), DJs)
    C, diags = {}, {}

    def dg(v, wide=False, own=0):
        if own:
            own = "dgo%d" % own
            if own not in slots:
                keep_if(h(own), C["ZT"], A.not_equal, float(v))
            return h(own)
        if (v, wide) not in diags:
            nm = "dg%d" % len(diags)
            if "ZT" in C and not wide:
                diags[(v, wide)] = keep_if(h(nm), C["ZT"], A.not_equal, float(v))
            else:
                diags[(v, wide)] = act((f if wide else h)(nm), ID, F.Copy, scale=float(v))
        return diags[(v, wide)]
    IDF = dg(1, True)
    nn0 = act(f("nn0", 1), n0, F.Copy, scale=-1.0)
    th0 = act(f("th0", 1), n0, bias=0.5, scale=-1.0)
    th1 = ts(f("th1", 1), d0, float(WIN), MIN, n0, ADD)
    th1 = act(f("th1b", 1), th1, bias=0.5, scale=-1.0)
    th2 = act(f("th2", 1), n0, bias=WIN - 0.5)
    dh = act(h("dh", 1), d0, F.Copy, scale=0.5)
    dl = ts(f("dl", 1), d0, 0.5, MUL, dh, SUB)
    DH = act(h("DH"), ID, F.Copy, scale=act(f("dhf", 1), dh, F.Copy))
    DL = act(h("DL"), ID, F.Copy, scale=dl)
    act(h("C128", 320), io(0, 320), bias=128.0, scale=0.0)
    for v in (-1024, 1024 + WS, WS, 512, CAP, -8 * CAP, (BIG + CAP) / 128):
        dg(v)
    Y = ts(h("Y", 144), io(0, 144), ts(f("y15", 1), pg, 16.0, MUL, 15.0, ADD), EQ)
    f("MK", 4)
    for r in range(RO):
        ts(sub("MK", r, r + 1), pr, 3.0, EQ, 256.0 * (r + 1), MUL)
    act(h("YC", 144), Y, F.Copy, scale=ts(f("yc", 1), pr, 2.0, LT))
    act(h("YT", 144), Y, F.Copy, scale=ts(f("yt", 1), cp(f("p2f", 1), ts(i_("p2i", 1), pidx, 1, SHR, 7, AND)), 1.0, EQ))
    boost[0] = 0.0
    ms(o("SQ", slice(None), slice(40, 48) if par else slice(0, 8)), 0)
    NN = [n0] + [f("n%d" % (r + 1), 1) for r in range(RO)]

    def sumto(r, nm="Y"):
        return sub(nm, 15 - r, 143 - r)

    fin_lo, fin_hi = -1024.0 * t, S2 - 1024.0 * ((t - 1) % N)
    C4 = (fin_lo + fin_hi) / 2 + 1.0 / 256 + 16384.0

    def late_consts():
        iota(o("SR", slice(0, 128)), [[0, 2048]], 0, 0)
        rec("g", lambda e: e.affine_select(T.BC[:], T.SR[:, 0:128, :], [[-1, 16], [-16, 8], [0, 16]], A.not_equal, 1.0, 0, 1), o("SR", slice(0, 128))[1], o("BC")[1], c=3650.0)
        C["BLKF"] = act(f("BLKF"), BLK, F.Copy)
        f("GIF", 16)
        h("GIB", 16)
        for k in (0, 8):
            act(sub("GIF", k, k + 8), sub("BLK", 0, 128, 16), F.Copy)
            act(sub("GIB", k, k + 8), sub("BLK", 0, 128, 16), F.Copy, scale=8 * U)
        C["kA"] = ts(f("kA", 18), io(0, 18), 16.0, MUL, pr, ADD)
        act(h("ZB", 40), io(0, 40), F.Copy, scale=0.0)
        act(sub("ZB", 0, 8), io(0, 8), bias=C1 - C0, scale=0.0)
        C["KB"] = act(f("KB", 8), sub("kA", 0, 8), bias=-0.5, scale=-1.0)
        h("kF", 16)
        act(sub("kF", 0, 8), sub("kA", 0, 8), F.Copy, scale=1.0 / 128)
        act(sub("kF", 8, 16), sub("kA", 0, 8), F.Copy, scale=0.0)
        nh = act(h("nh", 1), n0, F.Copy, scale=0.5)
        C["NH"] = act(h("NH"), ID, F.Copy, scale=act(f("nhf", 1), nh, F.Copy))
        C["NL"] = act(h("NL"), ID, F.Copy, scale=ts(f("nl", 1), n0, 0.5, MUL, nh, SUB))
        C["bx1"] = act(f("bx1", 1), n0, bias=512.0 * t - 512 - WS - 1.0 / 256, scale=0.5)
        C["bx2"] = act(f("bx2", 1), n0, bias=512.0 + WS - 512 * t + 1.0 / 256, scale=-0.5)
        C["ONE"] = act(f("ONE", 8), io(0, 8), bias=1.0, scale=0.0)
        C["IO1"] = cp(ps(6, 128, 256), io(1, 129))
        C["DM"] = f("DM", 40)
        for k, v in enumerate((DUMP + 128 - C0, DUMP - C0, DUMP - C2, DUMP - C3, DUMP - C4)):
            act(sub("DM", 8 * k, 8 * k + 8), sub("kA", 0, 8), bias=float(v))
        h("R2", 336)
        act(sub("R2", 0, 1), io(0, 1), F.Copy, scale=0.0)
        f("cumM", 336)
        act(sub("cumM", 320, 336), io(0, 16), F.Copy, scale=0.0)
        act(o("CAT", slice(None), slice(320, 336)), io(0, 48), F.Copy, scale=0.0)
        act(cols("W", 2560, 2576), io(0, 16), F.Copy, scale=0.0)
        act(h("YN", 144), Y, F.Copy, scale=-U)
        C["KF"] = act(h("KF"), io(0, 128), F.Copy, scale=1.0 / 128)
        act(cols("TG", DUMP, TW), io(0, TW - DUMP), F.Copy, scale=0.0)
        act(cols("XT", DUMP, TW), io(0, TW - DUMP), F.Copy, scale=0.0)
        act(o("SO"), io(0, 4), F.Copy, scale=0.0)
        for a in (S3, S4, S5):
            act(cols("XT", a, a + WIN), io(0, WIN), bias=n0)

    def homes(r, banks):
        for k, b in enumerate(banks):
            act(ps(b, 0, 512), io(512 * k, 512 * k + 512), bias=float(1024 * r))

    def relative(a, z, banks):
        for k, b in enumerate(banks):
            tt(cols("TG", a + 512 * k, a + 512 * k + 512), cols("KR", z + 512 * k, z + 512 * k + 512), ps(b, 0, 512), SUB)

    def behind(sem, dst, src, c):
        go = f(sem, 1)
        rec("g", lambda e: e.sem_inc(T.sem[sem], 1), [], go[1], ev=(sem, 1), c=50.0)
        dma("y", dst, src, c, reads=go[1])

    def mirror_out():
        hs, hn = relays(core, prv, cores, topo), relays(nxt, core, cores, topo)
        if hs:
            en, w = side_engines(core, hs[0], topo, cores), 512 // PARTS
            for j in range(PARTS):
                s1 = send([(x, T.KR[:, w * j:w * j + w], cols("PT", S2 + 512 * k + w * j, S2 + 512 * k + w * j + w), "aH%d" % j, en[k * len(en) // 2:(k + 1) * len(en) // 2])
                           for k, x in enumerate(hs)])
        else:
            s1 = send([(prv, T.PT[:, S1:S4], cols("PT", S2, S5), "aP", halves(core, prv, topo)[1])])
        homes((t - 1) % N, (3, 7))
        relative(S2, 1024, (3, 7))
        s2 = send([(prv, T.TG[:, S1:S4], cols("TG", S2, S5), "aK", topo.engines(core, prv) if hs else halves(core, prv, topo)[0])])
        behind("go0", cols("PT", 0, S3), T.tp[:, 0:1024], CFG["ld2"])
        arrive("aP", PARTS * sum(len(topo.engines(x, core)) for x in hn) if hn else len(halves(nxt, core, topo)[1]), [cols("PT", S1, S4)], CFG["lp"], s1)
        arrive("aK", len(topo.engines(nxt, core)) if hn else len(halves(nxt, core, topo)[0]), [cols("TG", S1, S4)], CFG["lk"], s2)

    def address(KI):
        w = L["w"] = ts(i_("w"), KI, 16383, AND)
        rk = ts(i_("rk"), KI, 10, SHR, 7, AND)
        old = tt(h("old"), w, L["img"], LT)
        s = L["s"] = tt(h("s"), old, rk, ADD)
        boost[0] = CFG["u4"]
        xf = L["xf"] = cp(f("xf"), ts(i_("x"), KI, 8191, AND))
        hb = L["hb"] = ts(h("hb"), w, n288, LT)
        sg0 = act(h("sg0"), xf, F.Sign, bias=th0)
        sg1 = act(h("sg1"), xf, F.Sign, bias=th1)
        sg2 = act(h("sg2"), xf, F.Sign, bias=th2, scale=-1.0)
        col = ps(2, 128, 256)
        mm(lin(col, [(IDF, xf), (dg(-1024), s), (dg(1024 + WS), old), (dg(WS), hb), (DH, sg0), (DL, sg0), (dg(512), sg1), (DH, sg2), (DL, sg2), (dg(512), sg2)]))
        p2 = ts(h("p2"), ts(i_("tg"), KI, 0x1FE000, AND), 1.0 / 8192, MUL)
        p1 = act(h("p1"), col, F.Copy)
        p0 = tt(h("p0"), col, p1, SUB)
        L["pc"] = (p0, p1, p2)
        boost[0] = 0.0

    def spread(rho):
        boost[0] = CFG["u4"]
        mm([(ps(0, 128 * k, 128 * k + 128), L["pc"][k], ID, True, True) for k in range(3)])
        for k in range(3):
            act(o("T2", slice(k, 128, 16)), ps(0, 128 * k, 128 * k + 128), F.Copy)
        h("SRC", 2048)
        for b in range(2):
            mm([(ps(q % 2, q // 2, 512, 8), o("T2", slice(None), q), sub("ID", 64 * b, 64 * b + 64), True, True) for q in range(16)])
            for e in range(2):
                act(sub("SRC", 1024 * b + e, 1024 * b + 1024, 2), ps(e, 0, 512), bias=sub("MK", rho, rho + 1))
        boost[0] = 0.0

    def place():
        s = L["s"]

        def oh(d, a=0, b=128):
            return sub("OH", OS * d + 1 + a, OS * d + 1 + b)
        for d in (0, 8, 1, 2, 3, 4, 5, 6, 7):
            ts(oh(d), s, float(d), EQ)
        h("R", 8 * OS)
        scan(sub("R", 0, 129), sub("OH", 0, 129), sub("OH", 8 * OS, 8 * OS + 129), ADD, ADD)
        scan(sub("R", OS, 8 * OS), RSM, sub("OH", OS, 8 * OS), MUL, ADD)
        thr = ps(2, 256, 384)
        mm(lin(thr, [(dg((BIG + CAP) / 128), sub("C128", 0, 128)), (dg(CAP), s), (dg(-8 * CAP), oh(8))]))
        for b in range(2):
            items = []
            for d in range(8):
                items += lin(ps(4 + b, d, 512, 8), [(LB[d], oh(x, 64 * b, 64 * b + 64)) for x in ([d] if d else [0, 8])] + [(BLK, sub("R", OS * d + 64 * b, OS * d + 64 * b + 64))])
            mm(items)
        f("MS", 1024)
        for b in range(2):
            scan(sub("MS", 512 * b, 512 * b + 512), RS8, ps(4 + b, 0, 512), MUL, MAX)
        val = sub("MS", 7, 1024, 8)
        ng = L["ng"] = tt(h("ng"), val, thr, GE)
        mx = L["mx"] = tt(f("mx"), tt(ps(6, 256, 384), ng, DJ, MUL), val, MAX)
        ts(u("off"), mx, -BIG, ADD)

    def pack():
        for a, b in zip(CFG["cuts"], CFG["cuts"][1:]):
            scat(SWa, sub("off", a, b), sub("SRC", 16 * a, 16 * b))
            if a == CFG["cuts"][CFG["pgk"]] and "pgop" in L:
                ops[-1]["soft"].add(L["pgop"])
            if b == 128 and "upop" in L and CFG["upk"]:
                ops[-1]["soft"].update(L["upop"])

    def request(rho):
        ca, ta = (0, 20) if par else (28, 8)
        for b in range(2):
            a = (me_c ^ PEER[2 * b]) // 2
            for k, (nm, z) in enumerate((("YC", ca), ("YT", ta))):
                mm(lin(ps(2 * k + b, 0, 80), [(sumto(q, nm), cols("SW", 1280 * a + q, 1280 * a + 1280, 16)) for q in range(16)]))
                cp(o("SQ", slice(8 * rho + 4 * a, 8 * rho + 4 * a + 4), slice(z, z + 20)), ps(2 * k + b, 0, 80))
            for ks in ([2, 3],) if b else ([0], [1]):
                s = send([(cores[d], T.RQ[:, 4 * rho + me_c, 48 * par:48 * par + 48], o("SQ", 8 * rho + d), "aQ%d%d" % (rho, k), en)
                          for k in ks for d, en in pair_call(core, pairs[me_c ^ PEER[k]], cores, topo)])
                for k in ks:
                    c = me_c ^ PEER[k]
                    land = o("RQ", 4 * rho + c, slice(48 - 48 * par, 96 - 48 * par)) if c == me_c else o("RQ", 4 * rho + c)
                    arrive("aQ%d%d" % (rho, k), pair_count(t, pairs[c], cores, topo), [land], CFG["near"] if c == me_c else CFG["far"] + CFG["q0"] + CFG["qk"] * k, s)
        cp(o("RQ", 4 * rho + me_c, slice(48 * par, 48 * par + 48)), o("SQ", 8 * rho + t))

    def lane_prep(rho, KI):
        ts(u("off2"), L["mx"], -BIG, ADD, 2560.0, MIN)
        gate = act(ps(2, 384, 512), L["ng"], bias=-16 * U - BIG * (rho == RO - 1), scale=16 * U)
        L["base"] = tt(f("base"), tt(ps(6, 384, 512), KI, gate, ADD), sub("dk2", 128 * rho, 128 * rho + 128), MAX)
        mm(lin(ps(7, 0, 128), [(IDF, L["xf"]), (dg(-16384), L["hb"]), (dg(16384), L["ng"])]))
        L["y1"] = act(f("y1_"), ps(7, 0, 128), bias=16385.0)
        L["y1op"] = ops[-1]

    def image(rho, out):
        nb = act(f("nb", 1), NN[rho], bias=16384.0, scale=16384.0)
        yes = act(ps(4, 128, 256), L["y1"], bias=nb, scale=-16384.0)
        L["img"] = tt(out, tt(ps(6, 384, 512), yes, L["y1"], MIN), L["img"], MAX)

    def unpack_block(rho, k, d0, nd):
        ans = cols("RR", 192 * rho + 24 * d0, 192 * rho + 24 * (d0 + nd))
        z = slice(24 * d0, 24 * (d0 + nd))
        f("r1", 192)
        up = ts(sub("r1", 24 * d0, 24 * (d0 + nd)), ans, 1.5 * 2.0 ** 31, ADD, 1.5 * 2.0 ** 31, SUB)
        hi = ts(o("SR", z, 0), ans, 1.5 * 2.0 ** 39, ADD, 1.5 * 2.0 ** 39, SUB)
        tt(o("SR", z, 2), ans, up, SUB)
        tt(o("SR", z, 1), up, hi, SUB)
        for s in range(nd):
            d, b = d0 + s, (0, 1, 0, 1, 0, 4, 1, 5)[k + s]
            mm([(ps(b, a, a + n), o("SR", slice(24 * d + 8 * j, 24 * d + 8 * j + 8)), sub("ID", lo, lo + n), True, True)
                for j, (a, n, lo) in enumerate(((0, 64, 64), (64, 128, 0), (192, 128, 0)) if par else ((0, 128, 0), (128, 128, 0), (256, 64, 0)))])
            if k + s in CFG["wv" if rho < RO - 1 else "wl"]:
                cp(cols("W", CAP * d, CAP * d + CAP), ps(b, 0, CAP))
            else:
                act(cols("W", CAP * d, CAP * d + CAP), ps(b, 0, CAP), F.Copy)
                if CFG["early"] and rho < RO - 1:
                    ops[-1]["soft"].add(L["m0"])

    def unpack(rho):
        unpack_block(rho, 0, (me_c ^ PEER[0]) // 2 * 4, 4)
        if rho < RO - 1 and CFG["fine"]:
            unpack_block(rho, 4, t, 1)
            unpack_block(rho, 5, 2 * (me_c ^ PEER[2]), 2)
            unpack_block(rho, 7, t + 1 - 2 * par, 1)
        else:
            unpack_block(rho, 4, me_c // 2 * 4, 4)
        Wa, gv = cols("W", 0, 2576), CFG["gv"]
        h("GR", 2048)
        if rho == RO - 1:
            for a in range(0, 128, 16):
                (cp if a // 16 in CFG["gl"] else act)(sub("GR", 16 * a, 16 * a + 256), ind(Wa, sub("off2", a, a + 16)))
        else:
            cp(sub("GR", 0, 16 * gv), ind(Wa, sub("off2", 0, gv)))
            act(sub("GR", 16 * gv, 2048), ind(Wa, sub("off2", gv, 128)))
            if CFG["early"] > 1:
                ops[-1]["soft"].add(L["n0"][CFG["early"] - 2])
        for a, b in ((0, gv), (gv, 128)):
            mm(lin(ps(2, a, b), [(sumto(r), sub("GR", 16 * a + r, 16 * b, 16)) for r in range(16)]))
        return tt(i_("KI"), ps(2, 0, 128), L["base"], MAX)

    def pointer(rho, parts):
        room = act(f("room", 1), NN[rho - 1], bias=8192.0 - 96.0, scale=-1.0)
        ovb = cp(h("ovb", 8), parts)
        L["ahead"] = [len(ops) - 1]
        mm([(ps(7, 320, 328), BLK, ovb, True, True)])
        act(f("v8", 8), ps(7, 320, 328), F.Copy, acc=f("v", 1))
        a = act(f("v2", 1), f("v", 1), F.Relu, bias=96.0, scale=-1.0)
        act(NN[rho], act(f("v3", 1), a, F.Relu, bias=room), bias=8192.0, scale=-1.0)

    def lookup(rho, k, between=None):
        c = me_c ^ PEER[k]
        a, top = 640 * c, S5 if rho == 0 else TW
        f("G", 2560)
        h("EQ", 2560)
        f("PR", 2560)
        both = slice(4 * rho + c // 2 * 2, 4 * rho + c // 2 * 2 + 2)
        if k < 2:
            ts(o("TQ", slice(4 * c, 4 * c + 4)), o("RQ", 4 * rho + c, slice(8, 88)), -256.0 * (rho + 1) - 1.0, ADD, 8192.0, MUL)
        elif k == 2:
            ts(o("TQ", slice(c // 2 * 8, c // 2 * 8 + 8)), o("RQ", both, slice(8, 88)), -256.0 * (rho + 1) - 1.0, ADD, 8192.0, MUL)
            ops[-1]["soft"].add(L["pr"])
        gv = 0 if k else CFG["g0"]
        if gv:
            cp(sub("G", a, a + 16 * gv), ind(cols("TG", 0, top), o("RQ", 4 * rho + c, slice(28, 28 + gv))))
        act(sub("G", a + 16 * gv, a + 640), ind(cols("TG", 0, top), o("RQ", 4 * rho + c, slice(28 + gv, 68))))
        if not k and "y1op" in L:
            L.pop("y1op")["soft"].add(len(ops) - 1)
        if not rho and k == CFG["late"]:
            later.append(len(ops) - 1)
            for op in lc:
                op["soft"].update(later)
        b0 = 2 * (k % 2)
        mm([(ps(b0 + q % 2, q // 2, 320, 8), o("BC", q), o("TQ", slice(4 * c, 4 * c + 4, 3)), True, True) for q in range(16)])
        ahead = []
        if k == 2:
            cp(f("cf", 160), o("RQ", slice(4 * rho, 4 * rho + 4), slice(28, 68)))
            ahead = [len(ops) - 1] + L.pop("ahead", [])
            for x in ahead:
                ops[x]["soft"].add(L["pr"])
        for e in range(2):
            tt(sub("EQ", a + e, a + 640, 2), sub("G", a + e, a + 640, 2), ps(b0 + e, 0, 320), EQ)
            ops[-1]["soft"].update(ahead)
        if k % 2:
            found(c // 2)
        if between:
            between()
        z = 192 * rho

        b = 4 + k % 2

        def answers(lo, hi):
            tt(sub("PR", a + 128 * lo, a + 128 * hi), ind(cols("PT", 0, top), o("RQ", 4 * rho + c, slice(28 + 8 * lo, 28 + 8 * hi))), sub("EQ", a + 128 * lo, a + 128 * hi), MUL)
            if k == CFG["prk"]:
                L["pr"] = len(ops) - 1
            items = []
            for j in range(lo, hi):
                y, x0 = a + 128 * j, 8 * j + 8 * (j > 2)
                n = 16 if j == 2 else 8
                items += lin(ps(b, x0, x0 + n), [(sub("EQ", y, y + 128), sub("GIB", 0, n)), (sub("PR", y, y + 128), sub("GIF", 0, n))])
            mm(items)
        x, more = t + 1 - 2 * par, BIG * (rho < RO - 1)
        if c == me_c:
            answers(*((0, 3) if par else (2, 5)))
            act(cols("SA", 24 * x, 24 * x + 24), ps(b, 24 - 24 * par, 48 - 24 * par), bias=more)
        else:
            answers(0, 5)
            act(cols("SA", 48 * c, 48 * c + 48), ps(b, 0, 48), bias=more)
        s = send([(cores[d], T.RR[:, z + 24 * t:z + 24 * t + 24], cols("SA", 24 * d, 24 * d + 24), "aR%d%d" % (rho, k), en)
                  for d, en in pair_call(core, pairs[c], cores, topo)])
        if c == me_c:
            answers(*((3, 5) if par else (0, 2)))
            act(cols("RR", z + 24 * t, z + 24 * t + 24), ps(b, 24 * par, 24 * par + 24), bias=more)
            arrive("aR%d%d" % (rho, k), pair_count(t, pairs[c], cores, topo), [cols("RR", z + 24 * x, z + 24 * x + 24)], CFG["near"], s)
        else:
            arrive("aR%d%d" % (rho, k), pair_count(t, pairs[c], cores, topo), [cols("RR", z + 48 * c, z + 48 * c + 48)], CFG["far"], s)

    def miss_pre(rho):
        dn = L["dn"] = act(f("dn", 1), NN[rho], bias=nn0)
        th4 = act(f("th4", 1), dn, bias=S4 - 0.5)
        L["th3"] = act(f("th3", 1), dn, bias=0.5 - S3, scale=-1.0)
        L["sa"] = act(h("sa", 160), f("cf", 160), F.Sign, bias=0.5 - S1)
        L["sb"] = act(h("sb", 160), f("cf", 160), F.Sign, bias=th4, scale=-1.0)

    def code(nm, sgn, bias):
        mm([(ps(7, 0, 160), IDF, f("cf", 160), True, False), (ps(7, 0, 160), dg(sgn * U / 2), L["sa"], False, False), (ps(7, 0, 160), dg(sgn * U / 2), L["sb"], False, False)]
           + [(ps(7, 40 * c, 40 * c + 40), dg(0.5), o("TQ", slice(4 * c, 4 * c + 4, 3)), False, c == NP - 1) for c in range(NP)])
        return act(f(nm, 160), ps(7, 0, 160), F.Relu, bias=bias)

    def found(a):
        mm(lin(ps(6, 256 + 80 * a, 336 + 80 * a), [(dg(8192), sub("C128", 0, 80))] + [(sumto(r, "YN"), sub("EQ", 1280 * a + r, 1280 * a + 1280, 16)) for r in range(16)]), ps(6, 256, 416)[1])

    def miss(rho):
        out = ps(6, 256, 416)
        sf = tt(o("SF"), out, code("cF", 1, 2048.5 + WS - U), MIN)
        s = send([(nxt, T.CAT[:, rho, 160:320], sf, "aF%d" % rho, topo.engines(core, nxt))])
        tt(o("CAT", rho, slice(0, 160)), out, code("cN", -1, 2048.5), MIN)
        arrive("aF%d" % rho, len(topo.engines(prv, core)), [o("CAT", rho, slice(160, 320))], CFG["far"], s)

    def count(rho, k):
        a, b = (160 * k, 160 * k + 160) if rho in CFG["apart"] else (0, 320)
        if a != 160 * k:
            return
        h("m", 320)
        f("ACC", 16)
        m = act(sub("m", a, b), o("CAT", rho, slice(a, b)), F.Sign)
        if not k:
            L["m0"], L["n0"] = len(ops) - 1, []
        scan(sub("R2", a + 1, b + 1), m, sub("C128", 0, b - a), ADD, MIN, sub("R2", a, a + 1) if k else 0.0)
        mm([(ps(3, a, b), BLK, sub("R2", a + 1, b + 1), True, True)])
        mm(lin(ps(7, a, b), [(BLK, sub("R2", a, b)), (LB[0], m)]))
        nv = CFG["nv"] if k and rho == RO - 1 else 0
        if nv:
            cum, z = act(h("cumb", 160), ps(3, a, b), F.Copy), 640 * (me_c ^ PEER[0])
            for j in range(nv):
                ts(sub("EQ", z + 160 * j, z + 160 * j + 160), cum, sub("kB", j + 8 - nv, j + 9 - nv), GT)
            y = 640 * (me_c ^ PEER[1])
            scan(sub("EQ", y, y + 160 * nv), sub("RS160", 0, 160 * nv), sub("EQ", z, z + 160 * nv), MUL, ADD)
            ts(sub("ACC", 16 - nv, 16), sub("EQ", y + 159, y + 160 * nv, 160), 2.0, MUL, -160.0, ADD)
        for j in range(8 - nv):
            h("junk%d" % (j % 2), 320)
            act(sub("junk%d" % (j % 2), 0, b - a), ps(3, a, b), F.Sign, bias=sub("KB", j, j + 1), acc=sub("ACC", 8 * k + j, 8 * k + j + 1))
            if not k:
                L["n0"].append(len(ops) - 1)
        act(sub("cumM", a, b), ps(7, a, b), F.Relu, bias=1.0 - BIG)

    def pick(rho):
        signs = tt(f("acs", 8), sub("ACC", 0, 8), sub("ACC", 8, 16), ADD) if rho in CFG["apart"] else sub("ACC", 0, 8)
        offk = ts(u("offk", 8), signs, -0.5, MUL, 160.0, ADD)
        g1 = act(f("sg1_"), ind(sub("cumM", 0, 336), offk))
        g2 = act(f("sg2_"), ind(o("CAT", rho), offk))
        pc = tt(f("pc"), g2, tt(ps(6, 256, 384), g1, C["IO1"], EQ), MUL)
        mm(lin(ps(7, 320, 448), [(C["BLKF"], pc), (ID, C["DG"])]))
        mm([(ps(3, 320, 448), C["BLKF"], pc, True, True)])

    def cand_a(rho):
        scan(f("cs"), C["RS16"], ps(7, 320, 448), MUL, MAX)
        ca = ts(i_("ca", 8), sub("cs", 15, 128, 16), 2047.5 - P21, ADD, 4095.0, MAX)
        col = ts(i_("colA", 8), ca, 4095, AND)
        u("offg", 24)
        o1 = cp(sub("offg", 8, 16), col)
        cf2 = f("colf", 16)
        cf = L["cf"] = cp(sub("colf", 0, 8), col)
        cp(sub("colf", 8, 16), col)
        xg = L["xg"] = act(f("xg"), ind(XTa, o1))
        L["g1"] = act(f("g1"), ind(TGa, o1))
        for nm, b, sc in (("c1", 0.5 - S3, 1.0), ("b1", 0.5 - S4, 1.0), ("b2", S2 - 0.5, -1.0), ("c4", 0.5 - S5, 1.0)):
            act(h("c" + nm, 16), cf2, F.Sign, bias=b, scale=sc)
            L[nm] = sub("c" + nm, 0, 8)
        tp = (t - 1) % N + 1
        mm(lin(ps(7, 0, 16), [(IDF, cf2), (ID, h("kF", 16)), (dg(-512 * (t + 1), own=1), h("cc1", 16)), (dg(-WS // 2), h("cb1", 16)),
                              (dg(WS // 2 - 512 * tp, own=2), h("cb2", 16)), (dg(-512 * tp, own=3), h("cc4", 16))] + [(C[a], h(b, 16)) for a in ("NH", "NL") for b in ("cc1", "cb2", "cc4")]))
        act(f("yb1", 8), ps(7, 0, 8), bias=C["bx1"])
        act(f("yb2", 8), ps(7, 8, 16), bias=C["bx2"], scale=-1.0)
        for nm, b, sc in (("a1", L["th3"], 1.0), ("a2", S1 - 0.5, -1.0), ("p6", 0.5 - DUMP, 1.0)):
            L[nm] = act(h("c" + nm, 8), cf, F.Sign, bias=b, scale=sc)
        other = [(IDF, cf), (dg(WS // 2), L["a1"]), (dg(WS // 2), L["a2"]), (dg(-WS // 2), L["b1"]), (dg(-WS // 2), L["b2"])]
        mm(lin(ps(7, 448, 456), other) + lin(ps(7, 456, 464), other + [(dg(-4096), L[x]) for x in ("a1", "a2", "b1", "b2")]))
        o2 = cp(sub("offg", 16, 24), ps(7, 448, 456))
        ts(sub("offg", 0, 8), ps(7, 456, 464), 8192.0, ADD, float(ZC), MIN)
        L["g2"] = act(f("g2"), ind(TGa, o2))
        L["tagb"] = act(h("tagb"), ps(3, 320, 448), bias=128.0, scale=1.0 / 4096)
        mm(lin(ps(3, 0, 128), [(ID, C["KF"]), (IDF, xg)]))
        f("s1", 8)
        f("s2", 8)
        nd = CFG["nd"] if rho == RO - 1 else 0
        if nd:
            mm(lin(ps(6, 0, 128), [(ID, C["KF"]), (IDF, xg)]))
            act(f("yb3", 8), sub("yb2", 0, 8), F.Copy, scale=-1.0)
            act(sub("s2", 8 - nd, 8), io(0, nd), F.Copy, scale=0.0)
            z = 640 * (me_c ^ PEER[3])
            for a in range(8 - nd, 8):
                n, y = 16 * a + 16, z + 256 * (a % 2)
                ts(sub("G", y, y + n), ps(6, 0, n), sub("yb1", a, a + 1), LT, 2.0, MUL)
                ts(sub("G", y + n, y + 2 * n), ps(6, 0, n), sub("yb3", a, a + 1), LT, -2.0, MUL)
                red(sub("s1", a, a + 1), sub("G", y, y + 2 * n))
        for a in range(8 - nd):
            for nm in ("1", "2"):
                act(sub("junk%d" % (int(nm) - 1), 0, 16 * a + 16), ps(3, 0, 16 * a + 16), F.Sign, bias=sub("yb" + nm, a, a + 1), scale=-1.0 if nm == "1" else 1.0,
                    acc=sub("s" + nm, a, a + 1))
        L["pg"] = cp(f("pg_", 256), ind(PTa, sub("offg", 0, 16)))
        L["pgop"] = len(ops) - 1
        L["rkb"] = act(h("rkb"), xg, bias=192.0 - 511.5 / 1024, scale=1.0 / 1024)

    def cand_b(rho, ovout):
        out = ps(7, 128, 256)
        mm(lin(out, [(dg(2, True), L["xg"]), (IDF, L["g1"]), (IDF, L["g2"])]))
        emp = act(h("emp"), out, F.Relu, bias=-1.0, scale=-1.0)
        mm([(ps(7, 256, 384), C["LSI"], emp, True, True)])
        L["nfs"] = act(h("nfs"), ps(7, 256, 384), F.Sign, bias=1.0)
        twice = [(IDF, sub("s1", 0, 8)), (IDF, sub("s2", 0, 8))]
        ov, tr = ps(2, 0, 8), ps(7, 392, 400)
        opens(2, [(ov, ID, L["p6"])] + [(ov, sumto(r), sub("emp", r, 128, 16)) for r in range(16)])
        closes(2, [(ov, a, b) for a, b in twice])
        mm(lin(tr, [(ID, L["p6"])] + twice))
        act(f("ov", 8), ov, F.Relu, scale=-1.0, acc=f("ovs", 1))
        L["tr"] = act(h("tr", 8), tr, F.Relu, scale=-1.0)
        ovout(f("ovs", 1))

    def cand_d(rho):
        nfs, xg = L["nfs"], L["xg"]
        last = rho == RO - 1
        w = 40 if last else 32
        key, pay = ps(0, 0, 128), ps(1, 0, 128)
        c128 = sub("C128", 0, 128)
        opens(0, [(key, dg(8192), L["tagb"]), (key, dg(-129 * 64), c128)])
        opens(1, [(pay, a, b) for a, b in ((dg(192 * U / 128), c128), (dg(-U), L["rkb"]), (dg(1024, True), xg), (ID, L["rkb"]), (dg(8), L["tagb"]), (dg(-(192 + 8 * 129) / 128), c128))])
        opens(4, [(ps(4, 0, 256), IDF, sub("pg_", 0, 256))])
        s4 = [(IDF, L["cf"]), (dg(-4096), L["b1"]), (dg(-4096), L["b2"])]
        lists = [s4, s4[:1], s4, [(IDF, L["cf"]), (dg(4096), L["b2"])], [(dg(-1, True), sub("yb2", 0, 8)), (dg((fin_lo - fin_hi) / 2, own=4), L["b2"])]][:w // 8]
        opens(5, [(ps(5, 0, w), ID, sub("ZB", 0, w))] + [(ps(5, 8 * k, 8 * k + 8), a, b) for k, x in enumerate(lists) for a, b in x])
        closes(4, [(ps(4, a, a + 128), dg(P21), nfs) for a in (128, 0)])
        closes(0, [(key, dg(-P21), nfs)])
        closes(1, [(pay, dg(-P21), nfs)])
        closes(5, [(ps(5, 8 * k, 8 * k + 8), dg(-16384 if k == 4 else -8192), L["tr"]) for k in range(w // 8)])
        kept = act(f("kept"), ps(4, 128, 256), F.Relu, bias=-P21)
        L["keptop"] = len(ops) - 1
        act(cols("UP", 0, 128), ps(4, 0, 128), F.Relu, bias=-P21)
        tt(cols("UP", 256, 384), key, L["g1"], MAX)
        L["np1"] = tt(cols("UP", 128, 256), pay, kept, MAX)
        tt(cols("UP", 384, 384 + w), ps(5, 0, w), sub("DM", 0, w), MIN)
        L["upop"] = range(len(ops) - 3, len(ops))
        msg = cols("UP", 128, 416)
        trs = [(nxt, T.UA[:, rho, :], msg, "aA%d" % rho, side_engines(core, nxt, topo, cores))]
        if rho < RO - 1:
            trs.append((prv, T.UB[:, rho, :], msg, "aB%d" % rho, side_engines(core, prv, topo, cores)))
        s = send(trs)
        arrive("aA%d" % rho, len(side_engines(prv, core, topo, cores)), [o("UA", rho)], CFG["far"] + CFG["a1" if last else "a0"], s)
        if rho < RO - 1:
            arrive("aB%d" % rho, len(side_engines(nxt, core, topo, cores)), [o("UB", rho)], CFG["far"] + CFG["a0"], s)

    def insert(rho):
        u("offs", 16)
        ts(sub("offs", 0, 16), cols("UP", 384, 400), C0, ADD)
        scat(TGa, sub("offs", 8, 16), cols("UP", 256, 384))
        scat(PTa, sub("offs", 0, 16), cols("UP", 0, 256))

    def sums(step):
        for b in range(8):
            a = (0 if b < 4 else S2) + 256 * (b % 4)
            x = cols("YS", a, a + 256)
            if step:
                mm([(ps(4 + b % 2, 0, 256), C["BLKF"], x, True, True)])
                act(x, ps(4 + b % 2, 0, 256), F.Copy)
            else:
                as_float(x, cols("PT", a, a + 256))

    def sums_of(parts, off):
        mm(lin(ps(4, 0, 128), [(C["BLKF"], x) for x in parts]))
        scat(YSa, off, act(f("sm1"), ps(4, 0, 128), F.Copy))

    def mirror(rho, buf, a, c):
        off = ts(u("offm" + buf, 8), o(buf, rho, slice(a, a + 8)), c, ADD)
        scat(TGa, off, o(buf, rho, slice(128, 256)))
        scat(PTa, off, o(buf, rho, slice(0, 128)))

    urgent(CFG["u2"], mirror_out)
    address(KI)
    spread(0)
    place()
    lc = len(ops)
    late_consts()
    lc = [op for op in ops[lc:] if op["q"] == "s" and op["lab"] not in ("XT", "GIF", "GIB", "YN")]
    for v in (8192, U / 2, -U / 2, 0.5):
        dg(v)
    pack()
    request(0)
    behind("go1", o("dki"), T.dk[:], 4000.0)
    iota(o("SR", slice(128, 192)), [[0, 1024]], 0, 0)
    ri16 = iota(f("ri16"), [[0, 8], [1, 16]], 0, 0)
    C["LSI"] = keep_if(h("LSI"), LS, A.not_equal, -1.0)
    C["DG"] = ts(h("DG"), ri16, pr, EQ, P21, MUL)
    C["RS16"] = act(f("RS16"), ri16, F.Sign)
    f("dk2", 384)
    for r in range(RO):
        ts(sub("dk2", 128 * r, 128 * r + 128), cols("dki", 128 * r, 128 * r + 128), (RO - 1 - r) * 2 * U + BIG * (r < RO - 1), ADD)
    dk_ops = ops[-RO:] if CFG["lp0"] else []
    boost[0] = CFG["u6"]
    homes(t, (4, 5))
    boost[0] = CFG["u8"]
    relative(0, 0, (4, 5))
    xw = ts(f("xw", 18), C["kA"], n0, ADD, -1024.0 * t, ADD)
    offw = ts(u("offw", 18), xw, 0.0, MAX, 1023.0, MIN)
    NX = act(f("NX", WIN), cols("XT", S3, S1), bias=-1.0, scale=-1.0)
    kg = cp(i_("kg", WIN), ind(cols("KR", 0, 1024), offw))
    pgw = cp(f("pgw", WIN), ind(cols("PT", 0, S3), offw))
    gw = act(f("gw", WIN), ind(cols("TG", 0, S3), offw))
    mv = ts(h("mv", WIN), ts(i_("kb", WIN), kg, -2147475456, AND), 8192.0, EQ)
    nmv = act(h("nmv", WIN), mv, bias=1.0, scale=-1.0)
    mvp, nmvp = act(ps(4, 0, WIN), mv, F.Copy), act(ps(5, 0, WIN), nmv, F.Copy)
    mm(lin(ps(7, 0, WIN), [(IDF, gw), (dg(-P21), mv)]))
    tt(cols("TG", S3, S1), ps(7, 0, WIN), NX, MAX)
    mm(lin(ps(3, 0, WIN), [(IDF, gw), (dg(-P21), nmv)]))
    t4 = tt(cols("TG", S4, S2), ps(3, 0, WIN), NX, MAX)
    p4 = tt(cols("PT", S4, S2), pgw, mvp, MUL)
    ea, eb = halves(core, nxt, topo)
    s = send([(nxt, T.TG[:, S5:DUMP], t4, "aW", ea), (nxt, T.PT[:, S5:DUMP], p4, "aW", eb)])
    arrive("aW", len(topo.engines(prv, core)), [cols("TG", S5, DUMP), cols("PT", S5, DUMP)], CFG["far"], s)
    tt(cols("PT", S3, S1), pgw, nmvp, MUL)
    boost[0] = 0.0

    for rho in range(RO):
        last = rho == RO - 1
        if rho or not CFG["lp0"]:
            lane_prep(rho, KI)
        if rho:
            urgent(CFG["u2"], pointer, rho, o("RQ", slice(4 * rho, 4 * rho + 4), slice(0, 96, 88)))
        for k in range(NP - 1):
            lookup(rho, k)

        def forward(rho=rho):
            urgent(CFG["u2"], miss_pre, rho)
            urgent(CFG["u7"], miss, rho)
        lookup(rho, NP - 1, forward if rho in CFG["ff"] else None)
        if rho not in CFG["ff"]:
            forward()
        if not rho:
            first = L["pr"]
            for op in dk_ops:
                op["soft"].add(first)
            if CFG["lp0"]:
                lane_prep(rho, KI)
            iota(cols("PT", DUMP, TW), [[0, TW - DUMP]], 0, 0, False)
            C["ZT"] = act(h("ZT"), ID, F.Copy, scale=0.0)
            tp = (t - 1) % N + 1
            for k, v in enumerate((-512 * (t + 1), WS // 2 - 512 * tp, -512 * tp, (fin_lo - fin_hi) / 2)):
                dg(v, own=k + 1)
            for v in (-WS // 2, WS // 2, -4096):
                dg(v)
            for a, r in ((0, t), (S2, (t - 1) % N), (S1, t)):
                iota(cols("XT", a, a + 1024), [[1, 1024]], 1024 * r, 0)
            for v in (4096, -129 * 64, 192 * U / 128, -U, 8, -(192 + 8 * 129) / 128, P21, -8192):
                dg(v)
        image(rho, cols("OY", 128, 256) if last else f("img"))
        if rho == RO - 2:
            sums(0)
        if not last:
            for k in range(2):
                urgent(CFG["u1"], count, rho, k)
            urgent(CFG["u1"], pick, rho)
            urgent(CFG["u1"], cand_a, rho)
            KI = unpack(rho)
            address(KI)
            spread(rho + 1)
            place()
            urgent(CFG["u1"], cand_b, rho, lambda s, rho=rho: ts(o("SQ", slice(8 * rho + 8, 8 * rho + 16), 40 * par), C["ONE"], s, MUL))
            urgent(CFG["u1"], cand_d, rho)
            pack()
            request(rho + 1)
            if rho == RO - 2:
                sums(1)
            insert(rho)
            mirror(rho, "UA", 272, C2)
            mirror(rho, "UB", 280, C3)

    rho = RO - 1
    dma("y", T.yi[:], cols("OY", 128, 256))
    z = len(ops)
    act(h("kB", 8), sub("kA", 0, 8), F.Copy)
    act(h("RS160", 640), io(0, 640), bias=1.0, scale=0.0)
    act(sub("RS160", 0, 640, 160), io(0, 4), F.Copy, scale=0.0)
    for op in ops[z:]:
        op["soft"].add(first)
    sums_of([L["np1"]], sub("offs", 8, 16))
    dn = L["dn"]

    def outside(nm, x, n):
        return act(f(nm, n), act(f(nm + "a", n), x, F.Abs, bias=-511.5), F.Relu, bias=-512.0 * 32768, scale=32768.0)

    def from_on(nm, x, first, n):
        return act(f(nm, n), x, F.Relu, bias=act(f(nm + "a", 1), first, bias=16384.0, scale=-16384.0), scale=16384.0)
    k12 = sub("kA", 0, 12)
    offl = cp(u("offl", 18), tt(f("z2", 18), tt(f("z1", 18), xw, outside("z0", xw, 18), ADD), act(f("dl_", 18), C["kA"], bias=float(S1)), MIN))
    for op in ops[-6:]:
        op["soft"].add(first)
    xh = act(f("xh", 12), k12, bias=act(f("xh0", 1), n0, bias=-1024.0 * ((t - 1) % N)))
    ops[-1]["soft"].add(first)
    zh = tt(f("z5", 12), tt(f("z4", 12), xh, outside("z3", xh, 12), SUB), from_on("sp", k12, dn, 12), SUB)
    offh = ts(u("offh", 12), tt(f("z6", 12), zh, act(f("dh_", 12), k12, bias=float(WIN - WS)), MAX), float(WS), ADD)
    half = act(f("half", 1), dn, bias=-0.5)
    done_ = act(h("mv", WIN), io(0, WIN), F.Sign, bias=half, scale=-1.0)
    m2 = tt(ps(5, 0, WIN), act(ps(1, 0, WIN), done_, bias=-U, scale=-U), cols("TG", S4, S2), ADD)
    low = tt(f("NX", WIN), m2, cols("TG", S3, S1), MAX)
    for a, b in ((0, 10), (10, 18)):
        scat(cols("TG", 0, S4), sub("offl", a, b), sub("NX", 16 * a, 16 * b))
    scat(cols("TG", S1, S5), offh, cols("TG", S5, S5 + 192))
    for k in range(2):
        urgent(CFG["u9"], count, rho, k)
    urgent(CFG["u9"], pick, rho)
    urgent(CFG["u9"], cand_a, rho)

    def free(nm, k, a, b):
        return sub(nm, 640 * (me_c ^ PEER[k]) + a, 640 * (me_c ^ PEER[k]) + b)
    p1 = tt(free("PR", 0, 320, 320 + WIN), act(ps(1, 0, WIN), done_, bias=0.5, scale=-0.5), cols("PT", S4, S2), MUL)
    pa = as_float(free("PR", 0, 0, WIN), cols("PT", S3, S1))
    pb = as_float(free("PR", 1, 0, 192), cols("PT", S5, S5 + 192))
    for a in (0, 96, 192):
        mm(lin(ps(4, a, a + 96), [(C["BLKF"], free("PR", 0, z + a, z + a + 96)) for z in (0, 320)]))
    for a in (0, 96):
        mm([(ps(5, a, a + 96), C["BLKF"], free("PR", 1, a, a + 96), True, True)])
    for k, n in enumerate((WIN, 192)):
        act(free("G", k, 0, n), ps(4 + k, 0, n), F.Copy)
    for a, b in ((0, 10), (10, 18)):
        scat(cols("YS", 0, S4), sub("offl", a, b), free("G", 0, 16 * a, 16 * b))
        if CFG["ysl"]:
            ops[-1]["soft"].add(L["pgop"])
    scat(cols("YS", S1, S5), offh, free("G", 1, 0, 192))

    def ov_last(s):
        act(cols("SO", 0, 1), s, F.Copy)
        calls = [pair_call(core, pairs[me_c ^ x], cores, topo) for x in PEER]
        thin = [(d, en[k * len(en) // 2:(k + 1) * len(en) // 2]) for k in range(2) for d, en in calls[k]]
        L["calls"] = [thin + calls[3], calls[2]]
        for call in L["calls"][:CFG["ao"]]:
            L["ao"] = send([(cores[d], T.RV[:, t, :], o("SO"), "aO", en) for d, en in call])
        act(o("RV", t), o("SO"), F.Copy)
    urgent(CFG["u1"], cand_b, rho, ov_last)
    cand_d(rho)
    for call in L["calls"][CFG["ao"]:]:
        L["ao"] = send([(cores[d], T.RV[:, t, :], o("SO"), "aO", en) for d, en in call])
    arrive("aO", sum(len(en) for call in L["calls"] for d, en in call), [o("RV", d) for d in range(N) if d != t], CFG["far"] + CFG["a1"], L["ao"])
    insert(rho)
    offf = ts(u("offf", 8), cols("UP", 416, 424), C4, ADD)
    scat(TGa, offf, tt(f("whole"), cols("UP", 256, 384), L["g2"], MAX))
    back = []
    for a in (0, S2):
        for k in range(2):
            for z in (0, 256):
                mm([(ps(2 + k, z, z + 256), IDF, cols("XT", a + 512 * k + z, a + 512 * k + z + 256), True, True)])
                back.append(ops[-1])
        for k in range(2):
            x = cols("TG", a + 512 * k, a + 512 * k + 512)
            tt(x, x, ps(2 + k, 0, 512), ADD)
    z = len(ops)
    KI = unpack(rho)
    turns = [k for k in range(z, len(ops)) if ops[k]["q"] == "p"]
    for k, op in enumerate(back):
        op["soft"].add(turns[min(k + CFG["tb"], 7)])
    sums_of([L["np1"], cols("UP", 0, 128)], offf)
    dma("y", T.yl[:], cp(cols("OY", 0, 128), ts(i_("w"), KI, 1048575, AND)))
    k6 = sub("kA", 0, 6)
    for nm in ("sec", "xx", "xb", "dx", "i12"):
        f(nm, 12)
    for k, (sec, r, base) in enumerate(((S3, t, 0), (S5, (t - 1) % N, S2))):
        act(sub("sec", 6 * k, 6 * k + 6), k6, bias=float(sec))
        act(sub("dx", 6 * k, 6 * k + 6), k6, bias=96.0 * k + DUMP)
        act(sub("i12", 6 * k, 6 * k + 6), k6, F.Copy)
        xx = act(sub("xx", 6 * k, 6 * k + 6), k6, bias=act(f("xx%d" % k, 1), NN[RO - 1], bias=-1024.0 * r))
        act(sub("xb", 6 * k, 6 * k + 6), xx, bias=float(base))
    offx = ts(u("offx", 12), f("sec", 12), dn, ADD)
    tt(f("tg0", 12), f("xb", 12), outside("xo", f("xx", 12), 12), ADD)
    mirror(rho, "UA", 272, C2)
    for k in range(2):
        act(ps(7, 96 * k, 96 * k + 96), io(0, 96), bias=NN[RO - 1])
    kx = tt(free("PR", 1, 320, 512), act(free("G", 2, 0, 192), ind(TGa, offx)), ps(7, 0, 192), ADD)
    mm([(ps(4, 0, 192), C["BLKF"], cp(free("PR", 2, 0, 192), ind(PTa, offx)), True, True)])
    sx = act(free("PR", 2, 320, 512), ps(4, 0, 192), F.Copy)
    cap = act(f("cap", 1), NN[RO - 1], bias=8192.0, scale=-1.0)
    tg1 = tt(f("tg1", 12), from_on("tg2", f("i12", 12), cap, 12), f("tg0", 12), ADD)
    boost[0] = CFG["u5"]
    v = ps(7, 320, 321)
    mm([(v, C["BLKF"], red(f("v", 1), o("RV", slice(None), 0)), True, True)])
    no = ts(f("no", 12), sub("i12", 0, 12), v, GE, BIG, MUL)
    offy = cp(u("offy", 12), tt(f("y2", 12), tt(ps(6, 384, 396), no, tg1, ADD), sub("dx", 0, 12), MIN))
    scat(TGa, offy, kx)
    dma("y", T.yk[:, 0:1024], cols("TG", 0, S3), CFG["st"])
    dma("s", T.yk[:, 1024:2048], cols("TG", S2, S5), CFG["st"])
    scat(YSa, offy, sx)
    boost[0] = 0.0
    dma("y", T.yn[:], ts(cols("OY", 256, 257), ts(f("v2", 1), v, 96.0, MIN, NN[RO - 1], ADD), 8192.0, MIN))
    dma("y", T.ys[:, 0:1024], (T.YS[0:128:16, 0:S3], cols("YS", 0, S3)[1], "s"))
    dma("s", T.ys[:, 1024:2048], (T.YS[0:128:16, S2:S5], cols("YS", S2, S5)[1], "s"))

    n = len(ops)
    pre = [op["deps"] | op["soft"] for op in ops]
    post = [[] for _ in ops]
    for me in range(n):
        for d in pre[me]:
            post[d].append(me)

    def plan(pre, post, prio, sign):
        left = [len(p) for p in pre]
        done, taken = [0.0] * n, {q: [] for q in ENG}
        ready = {me for me in range(n) if not left[me]}
        while ready:
            me = max(ready, key=lambda k: (prio[k] + sign * ops[k]["up"], -k))
            ready.remove(me)
            q = ops[me]["q"]
            at = max([done[d] + WAKE for d in pre[me]], default=0.0)
            if q != "x":
                hold = ops[me]["c"] if ops[me]["ev"] is None or q == "g" else 60.0
                row, k = taken[q], 0
                while k < len(row) and row[k][0] < at + hold - CFG["tol"]:
                    at = max(at, row[k][1])
                    k += 1
                row.insert(k, (at, at + hold))
            done[me] = at + ops[me]["c"]
            for k in post[me]:
                left[k] -= 1
                if not left[k]:
                    ready.add(k)
        return done, sorted(range(n), key=lambda k: done[k] - ops[k]["c"])

    def greedy(pre, post, prio, sign):
        left = [len(p) for p in pre]
        done, free, order = [0.0] * n, {}, []
        ready = {me: 0.0 for me in range(n) if not left[me]}
        while ready:
            start = {me: max(r, free.get(ops[me]["q"], 0.0)) for me, r in ready.items()}
            first = min(start, key=lambda k: start[k])
            q = ops[first]["q"]
            mine = [k for k in ready if ops[k]["q"] == q and start[k] <= start[first] + CFG["look"]]
            val = {k: prio[k] + sign * ops[k]["up"] for k in mine}
            me = top = max(mine, key=lambda k: (val[k], -k))
            if start[top] > start[first] and q != "x":
                late = {k: max(start[k] + val[k], max(start[top], start[k] + ops[k]["c"]) + val[top]) for k in mine if start[k] < start[top]}
                other = min(late, key=lambda k: (late[k], -val[k], k))
                if late[other] <= max(start[top] + val[top], start[top] + ops[top]["c"] + val[other]) + 30.0:
                    me = other
            done[me] = start[me] + ops[me]["c"]
            if q != "x":
                free[q] = done[me] if ops[me]["ev"] is None or q == "g" else start[me] + 60.0
            order.append(me)
            del ready[me]
            for k in post[me]:
                left[k] -= 1
                if not left[k]:
                    ready[k] = max(done[d] for d in pre[k]) + WAKE
        return done, order
    if not CFG["gaps"]:
        plan = greedy

    def first_order(look):
        CFG["look"] = look
        prio = [0.0] * n
        for me in range(n - 1, -1, -1):
            prio[me] = ops[me]["c"] + max([prio[k] + WAKE for k in post[me]], default=0.0)
        best = None
        for _ in range(CFG["passes"]):
            done, order = plan(pre, post, prio, 1.0)
            CFG.setdefault("log", []).append(int(max(done)))
            if best is None or max(done) < max(best[0]):
                best = (done, order)
            prio = plan(post, pre, done, -1.0)[0]
        return best[1]

    def clocked(rows):
        before, after_ = [-1] * n, [-1] * n
        for row in rows.values():
            for a, b in zip(row, row[1:]):
                before[b], after_[a] = a, b
        left = [len(pre[k]) + (before[k] >= 0) for k in range(n)]
        at, why, seen = [0.0] * n, [-1] * n, [k for k in range(n) if not left[k]]
        for k in seen:
            e = at[k] + cost_[k] + WAKE
            for j in post[k]:
                if e > at[j]:
                    at[j], why[j] = e, k
                left[j] -= 1
                if not left[j]:
                    seen.append(j)
            j = after_[k]
            if j >= 0:
                if at[k] + hold[k] > at[j]:
                    at[j], why[j] = at[k] + hold[k], k
                left[j] -= 1
                if not left[j]:
                    seen.append(j)
        if len(seen) < n:
            return None
        end = max(at[k] + cost_[k] for k in range(n))
        return end, at, why, seen, end + CFG["lam"] * sum(at[k] for k in marks) / len(marks)
    marks = [k for k in range(n) if ops[k]["q"] == "g" and ops[k]["ev"]]
    kids = [set(p) for p in post]

    def mend(order, steps):
        rows = {q: [k for k in order if ops[k]["q"] == q] for q in "vspy"}
        now = top = clocked(rows)
        barred = {}
        for step in range(steps):
            end, at, why, seen = now[:4]
            where = {k: i for row in rows.values() for i, k in enumerate(row)}
            tail, own = [0.0] * n, [0.0] * n
            for k in reversed(seen):
                own[k] = cost_[k] + max([WAKE + tail[j] for j in post[k]], default=0.0)
                row = rows.get(ops[k]["q"])
                tail[k] = max(own[k], hold[k] + tail[row[where[k] + 1]]) if row and where[k] + 1 < len(row) else own[k]
            k, runs, run = max(range(n), key=lambda k: at[k] + cost_[k]), [], []
            while k >= 0:
                if why[k] >= 0 and why[k] not in pre[k]:
                    run = run or [k]
                    run.append(why[k])
                elif run:
                    runs.append(run[::-1])
                    run = []
                k = why[k]
            moves = []
            for run in runs:
                row, m = rows[ops[run[0]]["q"]], len(run)
                ready = {k: max([at[d] + cost_[d] + WAKE for d in pre[k]], default=0.0) for k in run}
                for i in range(m - 1):
                    for j in sorted({i + 1, i + 2, i + 4, i + 8, m - 1}):
                        if j >= m:
                            continue
                        part = run[i:j + 1]
                        for back in (0, 1) if j > i + 1 else (0,):
                            x = part[-1] if back else part[0]
                            if barred.get(x, -1) >= step or (pre[x] if back else kids[x]) & set(part):
                                continue
                            new, p0, p1 = [x] + part[:-1] if back else part[1:] + [x], where[part[0]], where[part[-1]]
                            p, heads = at[row[p0 - 1]] + hold[row[p0 - 1]] if p0 else 0.0, []
                            for w in new:
                                p = max(p, ready[w])
                                heads.append(p)
                                p += hold[w]
                            p, worst = tail[row[p1 + 1]] if p1 + 1 < len(row) else 0.0, 0.0
                            for w, a in zip(reversed(new), reversed(heads)):
                                p = max(own[w], hold[w] + p)
                                worst = max(worst, a + p)
                            moves.append((worst, x, p0, new))
            moves.sort(key=lambda z: z[:3])
            for worst, x, p0, new in moves[:6]:
                row = rows[ops[x]["q"]]
                old = row[p0:p0 + len(new)]
                row[p0:p0 + len(new)] = new
                barred[x] = step + CFG["bar"]
                after = clocked(rows)
                if after and after[0] <= end + CFG["warm"]:
                    now = after
                    break
                row[p0:p0 + len(new)] = old
            if now[0] < top[0]:
                top = now
        place_ = {k: i for i, k in enumerate(top[3])}
        CFG["log"].append(int(top[0]))
        return top[0], sorted(range(n), key=lambda k: (top[1][k], place_[k]))
    cost_ = [op["c"] for op in ops]
    hold = [op["c"] if op["ev"] is None else 60.0 for op in ops]
    shape = tuple((op["q"], op["c"]) for op in ops)
    again = clocked({q: [k for k in ORDERS[shape] if ops[k]["q"] == q] for q in "vspy"}) if shape in ORDERS else None
    if again:
        place_ = {k: i for i, k in enumerate(again[3])}
        order = sorted(range(n), key=lambda k: (again[1][k], place_[k]))
    else:
        order = ORDERS[shape] = mend(min(mend(first_order(x), CFG["mend"] // 4) for x in CFG["looks"])[1], CFG["mend"])[1]
    PLAN.update(slots)
    pos = {me: k for k, me in enumerate(order)}
    ops = [ops[me] for me in order]
    for op in ops:
        op["deps"] = {pos[d] for d in op["deps"]}
    known = {q: {} for q in ENG}
    clock, need = [], set()
    for me, op in enumerate(ops):
        q = op["q"]
        op["waits"] = []
        kn = known.get(q, {})
        for d in sorted(op["deps"], reverse=True) if q != "x" else []:
            dq = ops[d]["q"] if ops[d]["ev"] is None else ops[d]["ev"][0]
            if kn.get(dq, -1) >= d:
                continue
            op["waits"].append(d)
            need.add(d)
            kn[dq] = d
            for k, v in clock[d].items():
                kn[k] = max(kn.get(k, -1), v)
        clock.append(dict(kn))
    tick = {"v": 0, "s": 0, "p": 0, "g": 0}
    evs = []
    for me, op in enumerate(ops):
        q = op["q"]
        if q != "x":
            e = ENG[q]
            for d in op["waits"]:
                e.wait_ge(T.sem[ops[d]["ev"][0]], ops[d]["ev"][1])
            ins = op["fn"](e)
            if op["ev"] is None and me in need:
                tick[q] += 1
                ins.then_inc(T.sem["q" + q], 1)
                op["ev"] = ("q" + q, tick[q])
                continue
        if op["ev"] is not None:
            evs.append(op["ev"])
    for s, k in evs:
        g.wait_ge(T.sem[s], k)
